import numpy as np
import ml_dtypes


def mxq(x, axis, fmt="e4m3"):
    dtype, down = {"e4m3": (ml_dtypes.float8_e4m3fn, 7), "e5m2": (ml_dtypes.float8_e5m2, 14)}[fmt]
    v = np.moveaxis(np.asarray(x, np.float32).astype(ml_dtypes.bfloat16).astype(np.float64), axis, -1)
    blocks = v.reshape(v.shape[:-1] + (-1, 32))
    amax = np.abs(blocks).max(-1, keepdims=True)
    byte = np.maximum(np.where(amax > 0, np.frexp(amax)[1] - 1 + 127, 0) - down, 1)
    scale = np.exp2(byte - 127.0)
    codes = (blocks / scale).astype(np.float32).astype(dtype).astype(np.float64)
    return np.moveaxis((codes * scale).reshape(v.shape), -1, axis)


WIDE = False


def mx_kscale(k):
    if not WIDE:
        return np.ones(k)
    levels = np.array([18, -18])
    if k % 512:
        return np.exp2(np.random.permutation(np.resize(levels, k // 32))).repeat(32)
    a = np.empty((k // 512, 16))
    for p in range(k // 512):
        a[p, :8] = np.random.permutation(np.resize(levels, 8))
        for g in range(8):
            far = levels[np.abs(levels - a[p, g]) >= 10]
            a[p, g + 8] = far[np.random.randint(len(far))]
    return np.exp2(a.ravel()).repeat(32)


def f64(x):
    return np.asarray(x).astype(np.float64)


def striped(idx):
    return np.tile(np.asarray(idx).reshape(-1, 16).T, (8, 1)).astype(np.uint16)


def unstriped(offs):
    return offs[:16].T.reshape(-1).astype(np.int64)


def setup_inputs():
    n = np.random.standard_normal
    uni = np.random.uniform
    idx = np.random.permutation(2048)[:1024]
    blk = np.random.permutation(np.repeat(np.arange(512), 2))
    slot = np.argsort(blk, kind="stable")
    f_d = mx_kscale(512)
    f_r = mx_kscale(512)
    return {
        "qT": (0.7 * n((512, 512)) * f_d[:, None] * f_r[None, :]).astype(np.float32),
        "kT": (n((512, 2048)) / np.sqrt(512) / f_d[:, None]).astype(np.float32),
        "us": (uni(0.75, 1.3, (512, 1)) / f_r[:, None]).astype(np.float32),
        "ts": np.tile(uni(0.75, 1.3, 2048), (128, 1)).astype(np.float32),
        "wb": (uni(0.5, 1.5, (512, 512))).astype(np.float32),
        "dp": (n((512, 1024))).astype(np.float32),
        "offs": striped(idx),
        "blkoffs": striped(blk),
        "slotoffs": striped(slot),
    }


def reference(qT, kT, us, ts, wb, dp, offs, blkoffs, slotoffs):
    idx = unstriped(offs)
    blk = unstriped(blkoffs)
    slot = unstriped(slotoffs)
    kT_c = f64(kT)[:, idx]
    ts_c = f64(ts)[:1][:, idx]
    a = mxq(f64(qT), 0, "e4m3").T @ mxq(kT_c, 0, "e4m3")
    e = np.exp(f64(us) * ts_c * a)
    es = e[:, slot]
    s = es.reshape(512, 512, 2).sum(-1)
    f = e * f64(dp)
    fs = f[:, slot]
    t = fs.reshape(512, 512, 2).sum(-1)
    h = f64(wb) / s
    m = t / s
    hc = h[:, blk]
    mc = m[:, blk]
    g = f64(us) * ts_c * e * hc * (f64(dp) - mc)
    dk = mxq(f64(qT), 1, "e4m3") @ mxq(g, 0, "e5m2")
    out = np.zeros((512, 2048))
    out[:, idx] = dk
    return out

@@ -1,0 +1,336 @@
+from contextlib import ExitStack
+
+import concourse.mybir as mybir
+from concourse.masks import make_identity
+
+D, R, C, T, X = 512, 512, 1024, 2048, 512
+FLOPS = 2 * 2 * D * R * C
+
+F32 = mybir.dt.float32
+BF16 = mybir.dt.bfloat16
+U32 = mybir.dt.uint32
+U16 = mybir.dt.uint16
+U8 = mybir.dt.uint8
+E4M3 = mybir.dt.float8_e4m3fn_x4
+E5M2 = mybir.dt.float8_e5m2_x4
+ACT = mybir.ActivationFunctionType
+ALU = mybir.AluOpType
+
+P = 128
+PACK = 4
+HALF = 512
+LIST_COLS = HALF // 16
+K_PIECE = 512
+H_WINDOW = X + 8
+M_WINDOW = 2 * X
+OUT_WINDOWS = 3
+
+
+def tile_attend_gblkatt_kernel(tc, qT, kT, us, ts, wb, dp, offs, blkoffs, slotoffs, out):
+    nc = tc.nc
+    with ExitStack() as ctx:
+        keep = ctx.enter_context(tc.tile_pool(name="keep", bufs=1))
+        work = ctx.enter_context(tc.tile_pool(name="work", bufs=1))
+        psum = ctx.enter_context(tc.psum_pool(name="psum", bufs=2))
+
+        def shared(shape, dtype, tag, bufs, name):
+            return work.tile(shape, dtype, tag=tag, bufs=bufs, name=name, align_bytes=64)
+
+        def bank(tag, name):
+            return psum.tile([P, PACK, P], F32, tag=tag, name=name)
+
+        def half_list(lst, half):
+            return lst[:, half * LIST_COLS : (half + 1) * LIST_COLS]
+
+        def turn(dst, src, start=True, stop=True):
+            nc.tensor.matmul(dst, lhsT=src, rhs=ident[:], is_transpose=True, start=start, stop=stop)
+
+        tok_list = keep.tile([P, C // 16], U16, name="tok_list")
+        blk_list = keep.tile([P, C // 16], U16, name="blk_list")
+        slot_list = keep.tile([P, C // 16], U16, name="slot_list")
+        ident = keep.tile([P, P], F32, name="ident")
+        ts_window = keep.tile([P, T], F32, name="ts_window")
+        nc.vector.memset(ts_window[:], 0.0)
+        nc.scalar.dma_start(out=ts_window[0:1, :], in_=ts[0:1, :])
+        nc.sync.dma_start(tok_list[:], offs)
+        make_identity(nc, ident[:])
+
+        k_rows = kT.rearrange("(p u e) n -> p u e n", u=2, e=2)
+        k_raw = []
+        for u in range(2):
+            for s in range(T // K_PIECE):
+                raw = shared([P, 2, K_PIECE], F32, ("ktr", "e")[u], 4, "k_raw_%d_%d" % (u, s))
+                nc.sync.dma_start(out=raw[:], in_=k_rows[:, u, :, s * K_PIECE : (s + 1) * K_PIECE])
+                k_raw.append(raw)
+        q_rows = qT.rearrange("(p t) r -> p t r", t=PACK)
+        q_raw = []
+        for s in range(2):
+            raw = shared([P, PACK, R // 2], F32, "y", 3, "q_raw_%d" % s)
+            nc.sync.dma_start(out=raw[:], in_=q_rows[:, :, s * (R // 2) : (s + 1) * (R // 2)])
+            q_raw.append(raw)
+        us_sb = keep.tile([P, PACK], F32, name="us_sb")
+        nc.sync.dma_start(out=us_sb[:], in_=us.rearrange("(p j) o -> p (j o)", j=PACK))
+        nc.sync.dma_start(slot_list[:], slotoffs)
+        dp_rows = dp.rearrange("(p j) c -> j p c", j=PACK)
+        dp_sb = []
+        for j in range(PACK):
+            tile = keep.tile([P, C], F32, name="dp_%d" % j)
+            nc.sync.dma_start(out=tile[:], in_=dp_rows[j])
+            dp_sb.append(tile)
+        wb_sb = keep.tile([P, PACK, X], F32, name="wb_sb")
+        nc.sync.dma_start(out=wb_sb[:], in_=wb.rearrange("(p j) x -> p j x", j=PACK))
+        nc.sync.dma_start(blk_list[:], blkoffs)
+
+        out_window = []
+        for w in range(OUT_WINDOWS):
+            tile = keep.tile([P, T], F32, name="out_window_%d" % w)
+            nc.vector.memset(tile[:], 0.0)
+            out_window.append(tile)
+        h_window, m_window = [], []
+        for j in range(PACK):
+            h_tile = keep.tile([P, H_WINDOW], F32, name="h_%d" % j)
+            m_tile = keep.tile([P, M_WINDOW], F32, name="m_%d" % j)
+            nc.vector.memset(h_tile[:, X:], 0.0)
+            nc.vector.memset(m_tile[:, X:], 0.0)
+            h_window.append(h_tile)
+            m_window.append(m_tile)
+        neg_us = keep.tile([P, PACK], F32, name="neg_us")
+        nc.vector.tensor_scalar(neg_us[:], us_sb[:], -1.0, None, ALU.mult)
+
+        ts_c = keep.tile([P, C], F32, name="ts_c")
+        nc.vector.tensor_copy(ts_c[:], ts_window[:].indirect(tok_list[:]))
+        ts_col = keep.tile([P, C // P], F32, name="ts_col")
+        for half in range(2):
+            ps = bank("fwd", "ts_turned")
+            for b in range(PACK):
+                blk = half * PACK + b
+                turn(ps[:, b, :], ts_c[:, blk * P : (blk + 1) * P])
+            nc.scalar.copy(ts_col[:, half * PACK : (half + 1) * PACK], ps[:, :, 0])
+
+        k_pairs = []
+        for u in range(2):
+            pairs = shared([P, T, 2], BF16, "kb", 2, "k_pairs_%d" % u)
+            for s in range(T // K_PIECE):
+                nc.scalar.activation(
+                    pairs[:, s * K_PIECE : (s + 1) * K_PIECE, :],
+                    k_raw[u * (T // K_PIECE) + s][:].rearrange("p e n -> p n e"),
+                    ACT.Copy,
+                )
+            k_pairs.append(pairs)
+        k_grouped = [shared([P, HALF * PACK], BF16, "kg", 2, "k_grouped_%d" % half) for half in range(2)]
+
+        def gather_keys(u, half):
+            window = k_pairs[u][:].rearrange("p n e -> p (n e)").bitcast(U32)
+            words = k_grouped[half][:].bitcast(U32).rearrange("p (c u) -> p c u", u=2)
+            nc.vector.tensor_copy(words[:, :, u], window.indirect(half_list(tok_list, half)))
+
+        for half in range(2):
+            gather_keys(0, half)
+        q_grouped = keep.tile([P, PACK, P, PACK], BF16, name="q_grouped", align_bytes=64)
+        for s in range(2):
+            nc.scalar.activation(
+                q_grouped[:, :, s * 64 : (s + 1) * 64, :].rearrange("p j m t -> p m j t"),
+                q_raw[s][:].rearrange("p t (m j) -> p m j t", j=PACK),
+                ACT.Copy,
+            )
+        q_codes = keep.tile([P, R], U32, name="q_codes", align_bytes=64)
+        q_scales = keep.tile([P, R], U8, name="q_scales", align_bytes=64)
+        nc.vector.quantize_mx(
+            out=q_codes[:].bitcast(E4M3), scales=q_scales[:], in_=q_grouped[:].rearrange("p j m t -> p (j m t)")
+        )
+        k_codes, k_scales = [], []
+        for half in range(2):
+            gather_keys(1, half)
+            codes = keep.tile([P, HALF], U32, name="k_codes_%d" % half, align_bytes=64)
+            scales = keep.tile([P, HALF], U8, name="k_scales_%d" % half, align_bytes=64)
+            nc.vector.quantize_mx(out=codes[:].bitcast(E4M3), scales=scales[:], in_=k_grouped[half][:])
+            k_codes.append(codes)
+            k_scales.append(scales)
+
+        e_sb = []
+        for j in range(PACK):
+            e_tile = shared([P, C], F32, "e", 4, "e_%d" % j)
+            scaled = shared([P, 2, PACK, P], F32, "y", 3, "scaled_%d" % j)
+            rows = slice(j * P, (j + 1) * P)
+            for half in range(2):
+                ps = bank("fwd", "scores")
+                for b in range(PACK):
+                    cols = slice(b * P, (b + 1) * P)
+                    nc.tensor.matmul_mx(
+                        out=ps[:, b, :],
+                        lhsT=k_codes[half][:, cols].bitcast(E4M3),
+                        lhsT_scale=k_scales[half][:, cols],
+                        rhs=q_codes[:, rows].bitcast(E4M3),
+                        rhs_scale=q_scales[:, rows],
+                        start=True,
+                        stop=True,
+                    )
+                for b in range(PACK):
+                    blk = half * PACK + b
+                    nc.scalar.activation(scaled[:, half, b, :], ps[:, b, :], ACT.Copy, scale=ts_col[:, blk : blk + 1])
+                back = bank("back", "scores_back")
+                for b in range(PACK):
+                    turn(back[:, b, :], scaled[:, half, b, :])
+                nc.scalar.activation(
+                    e_tile[:, half * HALF : (half + 1) * HALF],
+                    back[:].rearrange("p b c -> p (b c)"),
+                    ACT.Exp,
+                    scale=us_sb[:, j : j + 1],
+                )
+            e_sb.append(e_tile)
+
+        def by_slots(src, tag, bufs, name):
+            picked = shared([P, C], F32, tag, bufs, name)
+            for half in range(2):
+                nc.vector.tensor_copy(
+                    picked[:, half * HALF : (half + 1) * HALF], src[:].indirect(half_list(slot_list, half))
+                )
+            return picked
+
+        def pair_sums(picked, ps):
+            pairs = picked[:].rearrange("p (x i) -> p x i", i=2)
+            for b in range(PACK):
+                for i in range(2):
+                    turn(ps[:, b, :], pairs[:, b * P : (b + 1) * P, i], start=(i == 0), stop=(i == 1))
+
+        f_sb, e_slots = [], []
+        for j in range(PACK):
+            e_slots.append(by_slots(e_sb[j], "t4", 4, "e_slots_%d" % j))
+            f_tile = shared([P, C], F32, "f", 4, "f_%d" % j)
+            nc.vector.tensor_tensor(f_tile[:], e_sb[j][:], dp_sb[j][:], ALU.mult)
+            f_sb.append(f_tile)
+
+        log_s = shared([P, PACK, X], F32, "kb", 2, "log_s")
+        for j in range(PACK):
+            ps = bank("back", "s_turned")
+            pair_sums(e_slots[j], ps)
+            nc.scalar.activation(log_s[:, j, :], ps[:].rearrange("p b m -> p (b m)"), ACT.Ln)
+        inv_s = shared([P, PACK, X], F32, "kb", 2, "inv_s")
+        nc.scalar.activation(
+            inv_s[:].rearrange("p j x -> p (j x)"), log_s[:].rearrange("p j x -> p (j x)"), ACT.Exp, scale=-1.0
+        )
+
+        q_words = q_grouped[:].rearrange("p j m t -> p (j m t)").bitcast(F32).rearrange("p (j m u) -> p j m u", j=PACK, u=2)
+        q2_grouped = keep.tile([P, PACK, P, PACK], BF16, name="q2_grouped", align_bytes=64)
+        for u in range(2):
+            ps = bank("fwd", "q_turned")
+            for j in range(PACK):
+                turn(ps[:, j, :], q_words[:, j, :, u])
+            nc.scalar.copy(
+                q2_grouped[:, 2 * u : 2 * u + 2, :, :],
+                ps[:].rearrange("m j p -> m (j p)").bitcast(BF16).rearrange("m (j p e) -> m e p j", j=PACK, e=2),
+            )
+        q2_codes = keep.tile([P, D], U32, name="q2_codes", align_bytes=64)
+        q2_scales = keep.tile([P, D], U8, name="q2_scales", align_bytes=64)
+        nc.vector.quantize_mx(
+            out=q2_codes[:].bitcast(E4M3), scales=q2_scales[:], in_=q2_grouped[:].rearrange("m t p j -> m (t p j)")
+        )
+
+        te_turned = []
+        for pair in range(C // P // 2):
+            tile = shared([P, 2, R], F32, "ktr", 4, "te_turned_%d" % pair)
+            for i in range(2):
+                blk = 2 * pair + i
+                ps = bank("fwd", "e_turned")
+                for j in range(PACK):
+                    turn(ps[:, j, :], e_sb[j][:, blk * P : (blk + 1) * P])
+                nc.scalar.activation(
+                    tile[:, i, :], ps[:].rearrange("c j m -> c (j m)"), ACT.Copy, scale=ts_col[:, blk : blk + 1]
+                )
+            te_turned.append(tile)
+
+        t_turned = []
+        for j in range(PACK):
+            f_slots = by_slots(f_sb[j], "t4", 4, "f_slots_%d" % j)
+            ps = bank("sum", "t_turned")
+            pair_sums(f_slots, ps)
+            m_turned = shared([P, PACK, P], F32, "kg", 2, "m_turned_%d" % j)
+            nc.vector.tensor_tensor(
+                m_turned[:].rearrange("x b m -> x (b m)"), ps[:].rearrange("x b m -> x (b m)"), inv_s[:, j, :], ALU.mult
+            )
+            inv_back = bank("blk", "inv_back")
+            for b in range(PACK):
+                turn(inv_back[:, b, :], inv_s[:, j, b * P : (b + 1) * P])
+            nc.vector.tensor_tensor(
+                h_window[j][:, :X], inv_back[:].rearrange("m b x -> m (b x)"), wb_sb[:, j, :], ALU.mult
+            )
+            m_back = bank("blk", "m_back")
+            for b in range(PACK):
+                turn(m_back[:, b, :], m_turned[:, b, :])
+            nc.scalar.copy(m_window[j][:, :X], m_back[:].rearrange("m b x -> m (b x)"))
+
+        dk_sb = {}
+
+        def products(half, g_codes, g_scales, tiles):
+            for t in tiles:
+                ps = bank("blk", "dk")
+                flat = ps[:].rearrange("p b c -> p (b c)")
+                nc.tensor.matmul_mx(
+                    out=flat,
+                    lhsT=q2_codes[:, t * P : (t + 1) * P].bitcast(E4M3),
+                    lhsT_scale=q2_scales[:, t * P : (t + 1) * P],
+                    rhs=g_codes[:].bitcast(E5M2),
+                    rhs_scale=g_scales[:],
+                    start=True,
+                    stop=True,
+                )
+                tile = shared([P, HALF], F32, "t4", 4, "dk_%d_%d" % (t, half))
+                nc.scalar.copy(tile[:], flat)
+                dk_sb[(t, half)] = tile
+
+        out_rows = out.rearrange("(p t) n -> t p n", t=PACK)
+
+        def place(t, half):
+            window = out_window[t % OUT_WINDOWS]
+            nc.vector.tensor_copy(window[:].indirect(half_list(tok_list, half)), dk_sb[(t, half)][:])
+            if half == 1:
+                nc.sync.dma_start(out=out_rows[t], in_=window[:])
+
+        g_quant = []
+        for half in range(2):
+            cols = slice(half * HALF, (half + 1) * HALF)
+            g_planes = shared([P, PACK, HALF], BF16, "t4", 4, "g_planes_%d" % half)
+            parts = []
+            for step in range(PACK + 2):
+                if step < PACK:
+                    part = shared([P, 2, HALF], F32, "y", 3, "part_%d_%d" % (half, step))
+                    nc.vector.tensor_tensor(
+                        part[:, 0, :], m_window[step][:].indirect(half_list(blk_list, half)), dp_sb[step][:, cols], ALU.subtract
+                    )
+                    parts.append(part)
+                if 1 <= step <= PACK:
+                    j = step - 1
+                    nc.vector.tensor_tensor(
+                        parts[j][:, 1, :], h_window[j][:].indirect(half_list(blk_list, half)), parts[j][:, 0, :], ALU.mult
+                    )
+                if step >= 2:
+                    j = step - 2
+                    te = bank("back", "te")
+                    for b in range(PACK):
+                        blk = half * PACK + b
+                        turn(te[:, b, :], te_turned[blk // 2][:, blk % 2, j * P : (j + 1) * P])
+                    nc.vector.scalar_tensor_tensor(
+                        g_planes[:, j, :], parts[j][:, 1, :], neg_us[:, j : j + 1],
+                        te[:].rearrange("m b c -> m (b c)"), ALU.mult, ALU.mult,
+                    )
+            g_grouped = shared([P, HALF, PACK], BF16, "t4", 4, "g_grouped_%d" % half)
+            nc.scalar.copy(
+                g_grouped[:].rearrange("p (c i) j -> p c j i", i=4), g_planes[:].rearrange("p j (c i) -> p c j i", i=4)
+            )
+            g_codes = keep.tile([P, HALF], U32, name="g_codes_%d" % half, align_bytes=64)
+            g_scales = keep.tile([P, HALF], U8, name="g_scales_%d" % half, align_bytes=64)
+            nc.vector.quantize_mx(
+                out=g_codes[:].bitcast(E5M2), scales=g_scales[:], in_=g_grouped[:].rearrange("p c j -> p (c j)")
+            )
+            g_quant.append((g_codes, g_scales))
+
+        products(0, g_quant[0][0], g_quant[0][1], range(OUT_WINDOWS))
+        for t in range(OUT_WINDOWS):
+            place(t, 0)
+        for t in range(OUT_WINDOWS):
+            products(1, g_quant[1][0], g_quant[1][1], [t])
+            place(t, 1)
+        for t in range(OUT_WINDOWS, PACK):
+            for half in range(2):
+                products(half, g_quant[half][0], g_quant[half][1], [t])
+                place(t, half)

@@ -9,6 +9,7 @@ FLOPS = 2 * 2 * D * R * C
 F32 = mybir.dt.float32
 BF16 = mybir.dt.bfloat16
 U32 = mybir.dt.uint32
+I32 = mybir.dt.int32
 U16 = mybir.dt.uint16
 U8 = mybir.dt.uint8
 E4M3 = mybir.dt.float8_e4m3fn_x4
@@ -21,8 +22,10 @@ PACK = 4
 HALF = 512
 LIST_COLS = HALF // 16
 K_PIECE = 512
-H_WINDOW = X + 8
-M_WINDOW = 2 * X
+BLK_WINDOW = X + 8
+KB = 1024
+TS_ROWS = 32
+SCALAR_CASTS = (2, 3)
 OUT_WINDOWS = 3
 
 
@@ -31,10 +34,14 @@ def tile_attend_gblkatt_kernel(tc, qT, kT, us, ts, wb, dp, offs, blkoffs, slotof
     with ExitStack() as ctx:
         keep = ctx.enter_context(tc.tile_pool(name="keep", bufs=1))
         work = ctx.enter_context(tc.tile_pool(name="work", bufs=1))
+        arena = ctx.enter_context(tc.tile_pool(name="arena", bufs=1))
         psum = ctx.enter_context(tc.psum_pool(name="psum", bufs=2))
 
         def shared(shape, dtype, tag, bufs, name):
             return work.tile(shape, dtype, tag=tag, bufs=bufs, name=name, align_bytes=64)
+
+        def placed(shape, dtype, kb, name):
+            return arena.tile(shape, dtype, name=name, align_bytes=64, offset=kb * KB)
 
         def bank(tag, name):
             return psum.tile([P, PACK, P], F32, tag=tag, name=name)
@@ -49,9 +56,10 @@ def tile_attend_gblkatt_kernel(tc, qT, kT, us, ts, wb, dp, offs, blkoffs, slotof
         blk_list = keep.tile([P, C // 16], U16, name="blk_list")
         slot_list = keep.tile([P, C // 16], U16, name="slot_list")
         ident = keep.tile([P, P], F32, name="ident")
-        ts_window = keep.tile([P, T], F32, name="ts_window")
-        nc.vector.memset(ts_window[:], 0.0)
-        nc.scalar.dma_start(out=ts_window[0:1, :], in_=ts[0:1, :])
+        ts_window = placed([P, T], F32, 0, "ts_window")
+        nc.scalar.dma_start(out=ts_window[0:TS_ROWS, :], in_=ts[0:TS_ROWS, :])
+        nc.vector.memset(ts_window[TS_ROWS:64, :].bitcast(I32), 0)
+        nc.gpsimd.memset(ts_window[64:P, :].bitcast(I32), 0)
         nc.sync.dma_start(tok_list[:], offs)
         make_identity(nc, ident[:])
 
@@ -59,13 +67,13 @@ def tile_attend_gblkatt_kernel(tc, qT, kT, us, ts, wb, dp, offs, blkoffs, slotof
         k_raw = []
         for u in range(2):
             for s in range(T // K_PIECE):
-                raw = shared([P, 2, K_PIECE], F32, ("ktr", "e")[u], 4, "k_raw_%d_%d" % (u, s))
+                raw = placed([P, 2, K_PIECE], F32, 40 + 16 * u + 4 * s, "k_raw_%d_%d" % (u, s))
                 nc.sync.dma_start(out=raw[:], in_=k_rows[:, u, :, s * K_PIECE : (s + 1) * K_PIECE])
                 k_raw.append(raw)
         q_rows = qT.rearrange("(p t) r -> p t r", t=PACK)
         q_raw = []
         for s in range(2):
-            raw = shared([P, PACK, R // 2], F32, "y", 3, "q_raw_%d" % s)
+            raw = placed([P, PACK, R // 2], F32, 32 + 4 * s, "q_raw_%d" % s)
             nc.sync.dma_start(out=raw[:], in_=q_rows[:, :, s * (R // 2) : (s + 1) * (R // 2)])
             q_raw.append(raw)
         us_sb = keep.tile([P, PACK], F32, name="us_sb")
@@ -81,19 +89,15 @@ def tile_attend_gblkatt_kernel(tc, qT, kT, us, ts, wb, dp, offs, blkoffs, slotof
         nc.sync.dma_start(out=wb_sb[:], in_=wb.rearrange("(p j) x -> p j x", j=PACK))
         nc.sync.dma_start(blk_list[:], blkoffs)
 
+        h_window = [keep.tile([P, BLK_WINDOW], F32, name="h_%d" % j) for j in range(PACK)]
+        m_window = [keep.tile([P, BLK_WINDOW], F32, name="m_%d" % j) for j in range(PACK)]
+        for tile in h_window + m_window:
+            nc.gpsimd.memset(tile[:, X:], 0.0)
         out_window = []
         for w in range(OUT_WINDOWS):
             tile = keep.tile([P, T], F32, name="out_window_%d" % w)
-            nc.vector.memset(tile[:], 0.0)
+            nc.gpsimd.memset(tile[:], 0.0)
             out_window.append(tile)
-        h_window, m_window = [], []
-        for j in range(PACK):
-            h_tile = keep.tile([P, H_WINDOW], F32, name="h_%d" % j)
-            m_tile = keep.tile([P, M_WINDOW], F32, name="m_%d" % j)
-            nc.vector.memset(h_tile[:, X:], 0.0)
-            nc.vector.memset(m_tile[:, X:], 0.0)
-            h_window.append(h_tile)
-            m_window.append(m_tile)
         neg_us = keep.tile([P, PACK], F32, name="neg_us")
         nc.vector.tensor_scalar(neg_us[:], us_sb[:], -1.0, None, ALU.mult)
 
@@ -109,15 +113,16 @@ def tile_attend_gblkatt_kernel(tc, qT, kT, us, ts, wb, dp, offs, blkoffs, slotof
 
         k_pairs = []
         for u in range(2):
-            pairs = shared([P, T, 2], BF16, "kb", 2, "k_pairs_%d" % u)
+            pairs = placed([P, T, 2], BF16, 8 + 8 * u, "k_pairs_%d" % u)
             for s in range(T // K_PIECE):
-                nc.scalar.activation(
-                    pairs[:, s * K_PIECE : (s + 1) * K_PIECE, :],
-                    k_raw[u * (T // K_PIECE) + s][:].rearrange("p e n -> p n e"),
-                    ACT.Copy,
-                )
+                dst = pairs[:, s * K_PIECE : (s + 1) * K_PIECE, :]
+                src = k_raw[u * (T // K_PIECE) + s][:].rearrange("p e n -> p n e")
+                if s >= SCALAR_CASTS[u]:
+                    nc.vector.tensor_copy(dst, src)
+                else:
+                    nc.scalar.activation(dst, src, ACT.Copy)
             k_pairs.append(pairs)
-        k_grouped = [shared([P, HALF * PACK], BF16, "kg", 2, "k_grouped_%d" % half) for half in range(2)]
+        k_grouped = [placed([P, HALF * PACK], BF16, 24 + 4 * half, "k_grouped_%d" % half) for half in range(2)]
 
         def gather_keys(u, half):
             window = k_pairs[u][:].rearrange("p n e -> p (n e)").bitcast(U32)
@@ -147,37 +152,64 @@ def tile_attend_gblkatt_kernel(tc, qT, kT, us, ts, wb, dp, offs, blkoffs, slotof
             k_codes.append(codes)
             k_scales.append(scales)
 
-        e_sb = []
-        for j in range(PACK):
-            e_tile = shared([P, C], F32, "e", 4, "e_%d" % j)
-            scaled = shared([P, 2, PACK, P], F32, "y", 3, "scaled_%d" % j)
-            rows = slice(j * P, (j + 1) * P)
+        q_words = q_grouped[:].rearrange("p j m t -> p (j m t)").bitcast(F32).rearrange("p (j m u) -> p j m u", j=PACK, u=2)
+        q_turned = [bank("blk", "q_turned") for u in range(2)]
+        for u in range(2):
+            for j in range(PACK):
+                turn(q_turned[u][:, j, :], q_words[:, j, :, u])
+
+        e_sb = [placed([P, C], F32, 56 + 4 * j, "e_%d" % j) for j in range(PACK)]
+        for group in ((0,), (1,), (2,), (3,)):
+            width = len(group) * P
+            per_bank = HALF // width
+            rows = slice(group[0] * P, group[0] * P + width)
+            scaled = shared([P, C // P, width], F32, "y", 2, "scaled_%d" % group[0])
             for half in range(2):
-                ps = bank("fwd", "scores")
-                for b in range(PACK):
-                    cols = slice(b * P, (b + 1) * P)
-                    nc.tensor.matmul_mx(
-                        out=ps[:, b, :],
-                        lhsT=k_codes[half][:, cols].bitcast(E4M3),
-                        lhsT_scale=k_scales[half][:, cols],
-                        rhs=q_codes[:, rows].bitcast(E4M3),
-                        rhs_scale=q_scales[:, rows],
-                        start=True,
-                        stop=True,
+                for first in range(0, PACK, per_bank):
+                    ps = psum.tile([P, per_bank, width], F32, tag="sum" if group == (3,) else "fwd", name="scores")
+                    for i in range(per_bank):
+                        cols = slice((first + i) * P, (first + i + 1) * P)
+                        nc.tensor.matmul_mx(
+                            out=ps[:, i, :],
+                            lhsT=k_codes[half][:, cols].bitcast(E4M3),
+                            lhsT_scale=k_scales[half][:, cols],
+                            rhs=q_codes[:, rows].bitcast(E4M3),
+                            rhs_scale=q_scales[:, rows],
+                            start=True,
+                            stop=True,
+                        )
+                    for i in range(per_bank):
+                        blk = half * PACK + first + i
+                        if group == (0,) and half == 1:
+                            nc.vector.tensor_scalar(
+                                scaled[:, blk, :], ps[:, i, :], ts_col[:, blk : blk + 1], None, ALU.mult
+                            )
+                        else:
+                            nc.scalar.activation(
+                                scaled[:, blk, :], ps[:, i, :], ACT.Copy, scale=ts_col[:, blk : blk + 1]
+                            )
+                for i, j in enumerate(group):
+                    back = bank("back", "scores_back")
+                    for b in range(PACK):
+                        turn(back[:, b, :], scaled[:, half * PACK + b, i * P : (i + 1) * P])
+                    nc.scalar.activation(
+                        e_sb[j][:, half * HALF : (half + 1) * HALF],
+                        back[:].rearrange("p b c -> p (b c)"),
+                        ACT.Exp,
+                        scale=us_sb[:, j : j + 1],
                     )
-                for b in range(PACK):
-                    blk = half * PACK + b
-                    nc.scalar.activation(scaled[:, half, b, :], ps[:, b, :], ACT.Copy, scale=ts_col[:, blk : blk + 1])
-                back = bank("back", "scores_back")
-                for b in range(PACK):
-                    turn(back[:, b, :], scaled[:, half, b, :])
-                nc.scalar.activation(
-                    e_tile[:, half * HALF : (half + 1) * HALF],
-                    back[:].rearrange("p b c -> p (b c)"),
-                    ACT.Exp,
-                    scale=us_sb[:, j : j + 1],
-                )
-            e_sb.append(e_tile)
+
+        q2_grouped = keep.tile([P, PACK, P, PACK], BF16, name="q2_grouped", align_bytes=64)
+        for u in range(2):
+            nc.vector.tensor_copy(
+                q2_grouped[:, 2 * u : 2 * u + 2, :, :],
+                q_turned[u][:].rearrange("m j p -> m (j p)").bitcast(BF16).rearrange("m (j p e) -> m e p j", j=PACK, e=2),
+            )
+        q2_codes = keep.tile([P, D], U32, name="q2_codes", align_bytes=64)
+        q2_scales = keep.tile([P, D], U8, name="q2_scales", align_bytes=64)
+        nc.vector.quantize_mx(
+            out=q2_codes[:].bitcast(E4M3), scales=q2_scales[:], in_=q2_grouped[:].rearrange("m t p j -> m (t p j)")
+        )
 
         def by_slots(src, tag, bufs, name):
             picked = shared([P, C], F32, tag, bufs, name)
@@ -196,55 +228,25 @@ def tile_attend_gblkatt_kernel(tc, qT, kT, us, ts, wb, dp, offs, blkoffs, slotof
         f_sb, e_slots = [], []
         for j in range(PACK):
             e_slots.append(by_slots(e_sb[j], "t4", 4, "e_slots_%d" % j))
-            f_tile = shared([P, C], F32, "f", 4, "f_%d" % j)
-            nc.vector.tensor_tensor(f_tile[:], e_sb[j][:], dp_sb[j][:], ALU.mult)
+            f_tile = placed([P, C], F32, 40 + 4 * j, "f_%d" % j)
+            nc.gpsimd.tensor_tensor(f_tile[:], e_sb[j][:], dp_sb[j][:], ALU.mult)
             f_sb.append(f_tile)
 
-        log_s = shared([P, PACK, X], F32, "kb", 2, "log_s")
+        log_s = placed([P, PACK, X], F32, 16, "log_s")
         for j in range(PACK):
             ps = bank("back", "s_turned")
             pair_sums(e_slots[j], ps)
             nc.scalar.activation(log_s[:, j, :], ps[:].rearrange("p b m -> p (b m)"), ACT.Ln)
-        inv_s = shared([P, PACK, X], F32, "kb", 2, "inv_s")
+        inv_s = placed([P, PACK, X], F32, 32, "inv_s")
         nc.scalar.activation(
             inv_s[:].rearrange("p j x -> p (j x)"), log_s[:].rearrange("p j x -> p (j x)"), ACT.Exp, scale=-1.0
         )
 
-        q_words = q_grouped[:].rearrange("p j m t -> p (j m t)").bitcast(F32).rearrange("p (j m u) -> p j m u", j=PACK, u=2)
-        q2_grouped = keep.tile([P, PACK, P, PACK], BF16, name="q2_grouped", align_bytes=64)
-        for u in range(2):
-            ps = bank("fwd", "q_turned")
-            for j in range(PACK):
-                turn(ps[:, j, :], q_words[:, j, :, u])
-            nc.scalar.copy(
-                q2_grouped[:, 2 * u : 2 * u + 2, :, :],
-                ps[:].rearrange("m j p -> m (j p)").bitcast(BF16).rearrange("m (j p e) -> m e p j", j=PACK, e=2),
-            )
-        q2_codes = keep.tile([P, D], U32, name="q2_codes", align_bytes=64)
-        q2_scales = keep.tile([P, D], U8, name="q2_scales", align_bytes=64)
-        nc.vector.quantize_mx(
-            out=q2_codes[:].bitcast(E4M3), scales=q2_scales[:], in_=q2_grouped[:].rearrange("m t p j -> m (t p j)")
-        )
-
-        te_turned = []
-        for pair in range(C // P // 2):
-            tile = shared([P, 2, R], F32, "ktr", 4, "te_turned_%d" % pair)
-            for i in range(2):
-                blk = 2 * pair + i
-                ps = bank("fwd", "e_turned")
-                for j in range(PACK):
-                    turn(ps[:, j, :], e_sb[j][:, blk * P : (blk + 1) * P])
-                nc.scalar.activation(
-                    tile[:, i, :], ps[:].rearrange("c j m -> c (j m)"), ACT.Copy, scale=ts_col[:, blk : blk + 1]
-                )
-            te_turned.append(tile)
-
-        t_turned = []
         for j in range(PACK):
-            f_slots = by_slots(f_sb[j], "t4", 4, "f_slots_%d" % j)
+            f_slots = by_slots(f_sb[j], "fs" if j == 0 else "t4", 1 if j == 0 else 4, "f_slots_%d" % j)
             ps = bank("sum", "t_turned")
             pair_sums(f_slots, ps)
-            m_turned = shared([P, PACK, P], F32, "kg", 2, "m_turned_%d" % j)
+            m_turned = shared([P, PACK, P], F32, "mt", 2, "m_turned_%d" % j)
             nc.vector.tensor_tensor(
                 m_turned[:].rearrange("x b m -> x (b m)"), ps[:].rearrange("x b m -> x (b m)"), inv_s[:, j, :], ALU.mult
             )
@@ -258,6 +260,7 @@ def tile_attend_gblkatt_kernel(tc, qT, kT, us, ts, wb, dp, offs, blkoffs, slotof
             for b in range(PACK):
                 turn(m_back[:, b, :], m_turned[:, b, :])
             nc.scalar.copy(m_window[j][:, :X], m_back[:].rearrange("m b x -> m (b x)"))
+            nc.gpsimd.tensor_scalar(f_sb[j][:], f_sb[j][:], -1.0, 0.0, ALU.mult, ALU.add)
 
         dk_sb = {}
 
@@ -274,7 +277,10 @@ def tile_attend_gblkatt_kernel(tc, qT, kT, us, ts, wb, dp, offs, blkoffs, slotof
                     start=True,
                     stop=True,
                 )
-                tile = shared([P, HALF], F32, "t4", 4, "dk_%d_%d" % (t, half))
+                if (t, half) == (2, 0):
+                    tile = placed([P, HALF], F32, 8, "dk_held")
+                else:
+                    tile = shared([P, HALF], F32, "t4", 4, "dk_%d_%d" % (t, half))
                 nc.scalar.copy(tile[:], flat)
                 dk_sb[(t, half)] = tile
 
@@ -286,51 +292,68 @@ def tile_attend_gblkatt_kernel(tc, qT, kT, us, ts, wb, dp, offs, blkoffs, slotof
             if half == 1:
                 nc.sync.dma_start(out=out_rows[t], in_=window[:])
 
-        g_quant = []
-        for half in range(2):
-            cols = slice(half * HALF, (half + 1) * HALF)
-            g_planes = shared([P, PACK, HALF], BF16, "t4", 4, "g_planes_%d" % half)
-            parts = []
-            for step in range(PACK + 2):
-                if step < PACK:
-                    part = shared([P, 2, HALF], F32, "y", 3, "part_%d_%d" % (half, step))
-                    nc.vector.tensor_tensor(
-                        part[:, 0, :], m_window[step][:].indirect(half_list(blk_list, half)), dp_sb[step][:, cols], ALU.subtract
-                    )
-                    parts.append(part)
-                if 1 <= step <= PACK:
-                    j = step - 1
-                    nc.vector.tensor_tensor(
-                        parts[j][:, 1, :], h_window[j][:].indirect(half_list(blk_list, half)), parts[j][:, 0, :], ALU.mult
-                    )
-                if step >= 2:
-                    j = step - 2
-                    te = bank("back", "te")
-                    for b in range(PACK):
-                        blk = half * PACK + b
-                        turn(te[:, b, :], te_turned[blk // 2][:, blk % 2, j * P : (j + 1) * P])
-                    nc.vector.scalar_tensor_tensor(
-                        g_planes[:, j, :], parts[j][:, 1, :], neg_us[:, j : j + 1],
-                        te[:].rearrange("m b c -> m (b c)"), ALU.mult, ALU.mult,
-                    )
-            g_grouped = shared([P, HALF, PACK], BF16, "t4", 4, "g_grouped_%d" % half)
-            nc.scalar.copy(
-                g_grouped[:].rearrange("p (c i) j -> p c j i", i=4), g_planes[:].rearrange("p j (c i) -> p c j i", i=4)
-            )
-            g_codes = keep.tile([P, HALF], U32, name="g_codes_%d" % half, align_bytes=64)
-            g_scales = keep.tile([P, HALF], U8, name="g_scales_%d" % half, align_bytes=64)
-            nc.vector.quantize_mx(
-                out=g_codes[:].bitcast(E5M2), scales=g_scales[:], in_=g_grouped[:].rearrange("p c j -> p (c j)")
-            )
-            g_quant.append((g_codes, g_scales))
+        g_planes = [placed([P, PACK, HALF], F32, 8 * half, "g_planes_%d" % half) for half in range(2)]
+        g_codes = [keep.tile([P, HALF], U32, name="g_codes_%d" % half, align_bytes=64) for half in range(2)]
+        g_scales = [keep.tile([P, HALF], U8, name="g_scales_%d" % half, align_bytes=64) for half in range(2)]
 
-        products(0, g_quant[0][0], g_quant[0][1], range(OUT_WINDOWS))
+        def gradient(half, j):
+            cols = slice(half * HALF, (half + 1) * HALF)
+            me = shared([P, HALF], F32, "me", 3, "me_%d_%d" % (half, j))
+            nc.vector.tensor_tensor(
+                me[:], m_window[j][:].indirect(half_list(blk_list, half)), e_sb[j][:, cols], ALU.mult
+            )
+            ps = bank("fwd", "diff_turned")
+            if (half, j) == (1, 2):
+                diff = placed([P, PACK, P], F32, 72, "diff_held")
+            else:
+                diff = shared([P, PACK, P], F32, "xt", 2, "diff_%d_%d" % (half, j))
+            for b in range(PACK):
+                blk = half * PACK + b
+                turn(ps[:, b, :], me[:, b * P : (b + 1) * P], start=True, stop=False)
+                turn(ps[:, b, :], f_sb[j][:, blk * P : (blk + 1) * P], start=False, stop=True)
+            for b in range(PACK):
+                blk = half * PACK + b
+                nc.scalar.activation(diff[:, b, :], ps[:, b, :], ACT.Copy, scale=ts_col[:, blk : blk + 1])
+            back = bank("back", "diff_back")
+            for b in range(PACK):
+                turn(back[:, b, :], diff[:, b, :])
+            factor = shared([P, HALF], F32, "fa", 5, "factor_%d_%d" % (half, j))
+            nc.scalar.activation(
+                factor[:], back[:].rearrange("m b c -> m (b c)"), ACT.Copy, scale=neg_us[:, j : j + 1]
+            )
+            nc.vector.tensor_tensor(
+                g_planes[half][:, j, :], h_window[j][:].indirect(half_list(blk_list, half)), factor[:], ALU.mult
+            )
+
+        def quantize_gradient(half):
+            g_grouped = placed([P, HALF, PACK], BF16, 72 + 4 * half, "g_grouped_%d" % half)
+            nc.scalar.activation(
+                g_grouped[:].rearrange("p (c i) j -> p c j i", i=4),
+                g_planes[half][:].rearrange("p j (c i) -> p c j i", i=4),
+                ACT.Copy,
+            )
+            nc.vector.quantize_mx(
+                out=g_codes[half][:].bitcast(E5M2),
+                scales=g_scales[half][:],
+                in_=g_grouped[:].rearrange("p c j -> p (c j)"),
+            )
+
+        def place_product(t, half):
+            products(half, g_codes[half], g_scales[half], [t])
+            place(t, half)
+
+        for j in range(PACK):
+            gradient(0, j)
+        for j in range(PACK - 1):
+            gradient(1, j)
+        gradient(1, PACK - 1)
+        quantize_gradient(0)
+        place_product(0, 0)
+        quantize_gradient(1)
+        for t in range(1, OUT_WINDOWS):
+            place_product(t, 0)
         for t in range(OUT_WINDOWS):
-            place(t, 0)
-        for t in range(OUT_WINDOWS):
-            products(1, g_quant[1][0], g_quant[1][1], [t])
-            place(t, 1)
+            place_product(t, 1)
         for t in range(OUT_WINDOWS, PACK):
             for half in range(2):
-                products(half, g_quant[half][0], g_quant[half][1], [t])
-                place(t, half)
+                place_product(t, half)

@@ -25,6 +25,7 @@ K_PIECE = 512
 BLK_WINDOW = X + 8
 KB = 1024
 TS_ROWS = 32
+LAG = 4
 SCALAR_CASTS = (2, 3)
 OUT_WINDOWS = 3
 
@@ -59,7 +60,7 @@ def tile_attend_gblkatt_kernel(tc, qT, kT, us, ts, wb, dp, offs, blkoffs, slotof
         ts_window = placed([P, T], F32, 0, "ts_window")
         nc.scalar.dma_start(out=ts_window[0:TS_ROWS, :], in_=ts[0:TS_ROWS, :])
         nc.vector.memset(ts_window[TS_ROWS:64, :].bitcast(I32), 0)
-        nc.gpsimd.memset(ts_window[64:P, :].bitcast(I32), 0)
+        nc.vector.memset(ts_window[64:P, :].bitcast(I32), 0)
         nc.sync.dma_start(tok_list[:], offs)
         make_identity(nc, ident[:])
 
@@ -93,13 +94,8 @@ def tile_attend_gblkatt_kernel(tc, qT, kT, us, ts, wb, dp, offs, blkoffs, slotof
         m_window = [keep.tile([P, BLK_WINDOW], F32, name="m_%d" % j) for j in range(PACK)]
         for tile in h_window + m_window:
             nc.gpsimd.memset(tile[:, X:], 0.0)
-        out_window = []
-        for w in range(OUT_WINDOWS):
-            tile = keep.tile([P, T], F32, name="out_window_%d" % w)
-            nc.gpsimd.memset(tile[:], 0.0)
-            out_window.append(tile)
         neg_us = keep.tile([P, PACK], F32, name="neg_us")
-        nc.vector.tensor_scalar(neg_us[:], us_sb[:], -1.0, None, ALU.mult)
+        nc.gpsimd.tensor_scalar(neg_us[:], us_sb[:], -1.0, 0.0, ALU.mult, ALU.add)
 
         ts_c = keep.tile([P, C], F32, name="ts_c")
         nc.vector.tensor_copy(ts_c[:], ts_window[:].indirect(tok_list[:]))
@@ -146,7 +142,7 @@ def tile_attend_gblkatt_kernel(tc, qT, kT, us, ts, wb, dp, offs, blkoffs, slotof
         k_codes, k_scales = [], []
         for half in range(2):
             gather_keys(1, half)
-            codes = keep.tile([P, HALF], U32, name="k_codes_%d" % half, align_bytes=64)
+            codes = placed([P, HALF], U32, (88, 36)[half], "k_codes_%d" % half)
             scales = keep.tile([P, HALF], U8, name="k_scales_%d" % half, align_bytes=64)
             nc.vector.quantize_mx(out=codes[:].bitcast(E4M3), scales=scales[:], in_=k_grouped[half][:])
             k_codes.append(codes)
@@ -180,7 +176,7 @@ def tile_attend_gblkatt_kernel(tc, qT, kT, us, ts, wb, dp, offs, blkoffs, slotof
                         )
                     for i in range(per_bank):
                         blk = half * PACK + first + i
-                        if group == (0,) and half == 1:
+                        if group == (0,):
                             nc.vector.tensor_scalar(
                                 scaled[:, blk, :], ps[:, i, :], ts_col[:, blk : blk + 1], None, ALU.mult
                             )
@@ -200,8 +196,8 @@ def tile_attend_gblkatt_kernel(tc, qT, kT, us, ts, wb, dp, offs, blkoffs, slotof
                     )
 
         q2_grouped = keep.tile([P, PACK, P, PACK], BF16, name="q2_grouped", align_bytes=64)
-        for u in range(2):
-            nc.vector.tensor_copy(
+        for u, copy in enumerate((nc.scalar.copy, nc.scalar.copy)):
+            copy(
                 q2_grouped[:, 2 * u : 2 * u + 2, :, :],
                 q_turned[u][:].rearrange("m j p -> m (j p)").bitcast(BF16).rearrange("m (j p e) -> m e p j", j=PACK, e=2),
             )
@@ -229,38 +225,43 @@ def tile_attend_gblkatt_kernel(tc, qT, kT, us, ts, wb, dp, offs, blkoffs, slotof
         for j in range(PACK):
             e_slots.append(by_slots(e_sb[j], "t4", 4, "e_slots_%d" % j))
             f_tile = placed([P, C], F32, 40 + 4 * j, "f_%d" % j)
-            nc.gpsimd.tensor_tensor(f_tile[:], e_sb[j][:], dp_sb[j][:], ALU.mult)
+            nc.vector.tensor_tensor(f_tile[:], e_sb[j][:], dp_sb[j][:], ALU.mult)
             f_sb.append(f_tile)
 
-        log_s = placed([P, PACK, X], F32, 16, "log_s")
+        root = placed([P, PACK, X], F32, 80, "root")
+        inv_s = []
         for j in range(PACK):
             ps = bank("back", "s_turned")
             pair_sums(e_slots[j], ps)
-            nc.scalar.activation(log_s[:, j, :], ps[:].rearrange("p b m -> p (b m)"), ACT.Ln)
-        inv_s = placed([P, PACK, X], F32, 32, "inv_s")
-        nc.scalar.activation(
-            inv_s[:].rearrange("p j x -> p (j x)"), log_s[:].rearrange("p j x -> p (j x)"), ACT.Exp, scale=-1.0
-        )
-
-        for j in range(PACK):
-            f_slots = by_slots(f_sb[j], "fs" if j == 0 else "t4", 1 if j == 0 else 4, "f_slots_%d" % j)
-            ps = bank("sum", "t_turned")
-            pair_sums(f_slots, ps)
-            m_turned = shared([P, PACK, P], F32, "mt", 2, "m_turned_%d" % j)
-            nc.vector.tensor_tensor(
-                m_turned[:].rearrange("x b m -> x (b m)"), ps[:].rearrange("x b m -> x (b m)"), inv_s[:, j, :], ALU.mult
-            )
-            inv_back = bank("blk", "inv_back")
+            nc.scalar.activation(root[:, j, :], ps[:].rearrange("p b m -> p (b m)"), ACT.Abs_reciprocal_sqrt)
+            ps = bank("sum", "root_back")
             for b in range(PACK):
-                turn(inv_back[:, b, :], inv_s[:, j, b * P : (b + 1) * P])
-            nc.vector.tensor_tensor(
-                h_window[j][:, :X], inv_back[:].rearrange("m b x -> m (b x)"), wb_sb[:, j, :], ALU.mult
-            )
+                turn(ps[:, b, :], root[:, j, b * P : (b + 1) * P])
+            flat = ps[:].rearrange("m b x -> m (b x)")
+            inv = placed([P, X, 2], F32, (90, 94, 32, 36)[j], "inv_%d" % j)
+            nc.scalar.activation(inv[:], flat.unsqueeze(2).to_broadcast([P, X, 2]), ACT.Square)
+            inv_s.append(inv)
+
+        def block_terms(j):
+            f_slots = shared([P, C], F32, "t4", 4, "f_slots_%d" % j)
+            twice = inv_s[j][:].rearrange("p x i -> p (x i)")
+            for half in range(2):
+                cols = slice(half * HALF, (half + 1) * HALF)
+                nc.vector.tensor_tensor(
+                    f_slots[:, cols], f_sb[j][:].indirect(half_list(slot_list, half)), twice[:, cols], ALU.mult
+                )
+            ps = bank("back", "m_turned")
+            pair_sums(f_slots, ps)
+            m_turned = placed([P, PACK, P], F32, (98, 100, 23, 80)[j], "m_turned_%d" % j)
+            nc.scalar.copy(m_turned[:], ps[:])
             m_back = bank("blk", "m_back")
             for b in range(PACK):
                 turn(m_back[:, b, :], m_turned[:, b, :])
             nc.scalar.copy(m_window[j][:, :X], m_back[:].rearrange("m b x -> m (b x)"))
-            nc.gpsimd.tensor_scalar(f_sb[j][:], f_sb[j][:], -1.0, 0.0, ALU.mult, ALU.add)
+            nc.vector.tensor_tensor(h_window[j][:, :X], inv_s[j][:, :, 0], wb_sb[:, j, :], ALU.mult)
+            nc.scalar.activation(f_sb[j][:], f_sb[j][:], ACT.Copy, scale=-1.0)
+
+        out_window = []
 
         dk_sb = {}
 
@@ -298,7 +299,7 @@ def tile_attend_gblkatt_kernel(tc, qT, kT, us, ts, wb, dp, offs, blkoffs, slotof
 
         def gradient(half, j):
             cols = slice(half * HALF, (half + 1) * HALF)
-            me = shared([P, HALF], F32, "me", 3, "me_%d_%d" % (half, j))
+            me = shared([P, HALF], F32, "me", 4, "me_%d_%d" % (half, j))
             nc.vector.tensor_tensor(
                 me[:], m_window[j][:].indirect(half_list(blk_list, half)), e_sb[j][:, cols], ALU.mult
             )
@@ -342,8 +343,16 @@ def tile_attend_gblkatt_kernel(tc, qT, kT, us, ts, wb, dp, offs, blkoffs, slotof
             products(half, g_codes[half], g_scales[half], [t])
             place(t, half)
 
-        for j in range(PACK):
-            gradient(0, j)
+        for j in range(PACK + LAG):
+            if j < PACK:
+                block_terms(j)
+            if j >= LAG:
+                gradient(0, j - LAG)
+        for w, kb in enumerate((16, 24, 80)):
+            tile = placed([P, T], F32, kb, "out_window_%d" % w)
+            nc.gpsimd.memset(tile[:], 0.0)
+            out_window.append(tile)
+
         for j in range(PACK - 1):
             gradient(1, j)
         gradient(1, PACK - 1)

@@ -25,7 +25,10 @@ K_PIECE = 512
 BLK_WINDOW = X + 8
 KB = 1024
 TS_ROWS = 32
-LAG = 4
+LAG = 2
+DIRECT = (0, 1)
+M_ON_TENSOR = ()
+S_ON_VECTOR = (0,)
 SCALAR_CASTS = (2, 3)
 OUT_WINDOWS = 3
 
@@ -107,26 +110,27 @@ def tile_attend_gblkatt_kernel(tc, qT, kT, us, ts, wb, dp, offs, blkoffs, slotof
                 turn(ps[:, b, :], ts_c[:, blk * P : (blk + 1) * P])
             nc.scalar.copy(ts_col[:, half * PACK : (half + 1) * PACK], ps[:, :, 0])
 
-        k_pairs = []
-        for u in range(2):
-            pairs = placed([P, T, 2], BF16, 8 + 8 * u, "k_pairs_%d" % u)
+        k_pairs = [placed([P, T, 2], BF16, 8 + 8 * u, "k_pairs_%d" % u) for u in range(2)]
+        k_grouped = [placed([P, HALF * PACK], BF16, 24 + 4 * half, "k_grouped_%d" % half) for half in range(2)]
+
+        def round_keys(u):
             for s in range(T // K_PIECE):
-                dst = pairs[:, s * K_PIECE : (s + 1) * K_PIECE, :]
+                dst = k_pairs[u][:, s * K_PIECE : (s + 1) * K_PIECE, :]
                 src = k_raw[u * (T // K_PIECE) + s][:].rearrange("p e n -> p n e")
                 if s >= SCALAR_CASTS[u]:
                     nc.vector.tensor_copy(dst, src)
                 else:
                     nc.scalar.activation(dst, src, ACT.Copy)
-            k_pairs.append(pairs)
-        k_grouped = [placed([P, HALF * PACK], BF16, 24 + 4 * half, "k_grouped_%d" % half) for half in range(2)]
 
         def gather_keys(u, half):
             window = k_pairs[u][:].rearrange("p n e -> p (n e)").bitcast(U32)
             words = k_grouped[half][:].bitcast(U32).rearrange("p (c u) -> p c u", u=2)
             nc.vector.tensor_copy(words[:, :, u], window.indirect(half_list(tok_list, half)))
 
+        round_keys(0)
         for half in range(2):
             gather_keys(0, half)
+        round_keys(1)
         q_grouped = keep.tile([P, PACK, P, PACK], BF16, name="q_grouped", align_bytes=64)
         for s in range(2):
             nc.scalar.activation(
@@ -142,70 +146,71 @@ def tile_attend_gblkatt_kernel(tc, qT, kT, us, ts, wb, dp, offs, blkoffs, slotof
         k_codes, k_scales = [], []
         for half in range(2):
             gather_keys(1, half)
-            codes = placed([P, HALF], U32, (88, 36)[half], "k_codes_%d" % half)
+            codes = placed([P, HALF], U32, (80, 36)[half], "k_codes_%d" % half)
             scales = keep.tile([P, HALF], U8, name="k_scales_%d" % half, align_bytes=64)
             nc.vector.quantize_mx(out=codes[:].bitcast(E4M3), scales=scales[:], in_=k_grouped[half][:])
             k_codes.append(codes)
             k_scales.append(scales)
 
-        q_words = q_grouped[:].rearrange("p j m t -> p (j m t)").bitcast(F32).rearrange("p (j m u) -> p j m u", j=PACK, u=2)
-        q_turned = [bank("blk", "q_turned") for u in range(2)]
-        for u in range(2):
-            for j in range(PACK):
-                turn(q_turned[u][:, j, :], q_words[:, j, :, u])
+        ts_rows = placed([P, C], F32, 32, "ts_rows")
+        for half in range(2):
+            ps = bank("blk", "ts_spread")
+            for b in range(PACK):
+                blk = half * PACK + b
+                turn(ps[:, b, :], ts_col[:, blk : blk + 1].to_broadcast([P, P]))
+            nc.scalar.copy(ts_rows[:, half * HALF : (half + 1) * HALF], ps[:].rearrange("m b c -> m (b c)"))
 
         e_sb = [placed([P, C], F32, 56 + 4 * j, "e_%d" % j) for j in range(PACK)]
-        for group in ((0,), (1,), (2,), (3,)):
-            width = len(group) * P
-            per_bank = HALF // width
-            rows = slice(group[0] * P, group[0] * P + width)
-            scaled = shared([P, C // P, width], F32, "y", 2, "scaled_%d" % group[0])
-            for half in range(2):
-                for first in range(0, PACK, per_bank):
-                    ps = psum.tile([P, per_bank, width], F32, tag="sum" if group == (3,) else "fwd", name="scores")
-                    for i in range(per_bank):
-                        cols = slice((first + i) * P, (first + i + 1) * P)
-                        nc.tensor.matmul_mx(
-                            out=ps[:, i, :],
-                            lhsT=k_codes[half][:, cols].bitcast(E4M3),
-                            lhsT_scale=k_scales[half][:, cols],
-                            rhs=q_codes[:, rows].bitcast(E4M3),
-                            rhs_scale=q_scales[:, rows],
-                            start=True,
-                            stop=True,
-                        )
-                    for i in range(per_bank):
-                        blk = half * PACK + first + i
-                        if group == (0,):
-                            nc.vector.tensor_scalar(
-                                scaled[:, blk, :], ps[:, i, :], ts_col[:, blk : blk + 1], None, ALU.mult
-                            )
-                        else:
-                            nc.scalar.activation(
-                                scaled[:, blk, :], ps[:, i, :], ACT.Copy, scale=ts_col[:, blk : blk + 1]
-                            )
-                for i, j in enumerate(group):
-                    back = bank("back", "scores_back")
-                    for b in range(PACK):
-                        turn(back[:, b, :], scaled[:, half * PACK + b, i * P : (i + 1) * P])
-                    nc.scalar.activation(
-                        e_sb[j][:, half * HALF : (half + 1) * HALF],
-                        back[:].rearrange("p b c -> p (b c)"),
-                        ACT.Exp,
-                        scale=us_sb[:, j : j + 1],
+        for j in range(PACK):
+            rows = slice(j * P, (j + 1) * P)
+            if j == PACK - 1:
+                scaled = placed([P, 2, PACK, P], F32, 32, "scaled_last")
+            else:
+                scaled = shared([P, 2, PACK, P], F32, "y", 2, "scaled_%d" % j)
+            if j in DIRECT:
+                for half in range(2):
+                    ps = bank("sum", "scores_direct")
+                    flat = ps[:].rearrange("m b c -> m (b c)")
+                    nc.tensor.matmul_mx(
+                        out=flat,
+                        lhsT=q_codes[:, rows].bitcast(E4M3),
+                        lhsT_scale=q_scales[:, rows],
+                        rhs=k_codes[half][:].bitcast(E4M3),
+                        rhs_scale=k_scales[half][:],
+                        start=True,
+                        stop=True,
                     )
-
-        q2_grouped = keep.tile([P, PACK, P, PACK], BF16, name="q2_grouped", align_bytes=64)
-        for u, copy in enumerate((nc.scalar.copy, nc.scalar.copy)):
-            copy(
-                q2_grouped[:, 2 * u : 2 * u + 2, :, :],
-                q_turned[u][:].rearrange("m j p -> m (j p)").bitcast(BF16).rearrange("m (j p e) -> m e p j", j=PACK, e=2),
-            )
-        q2_codes = keep.tile([P, D], U32, name="q2_codes", align_bytes=64)
-        q2_scales = keep.tile([P, D], U8, name="q2_scales", align_bytes=64)
-        nc.vector.quantize_mx(
-            out=q2_codes[:].bitcast(E4M3), scales=q2_scales[:], in_=q2_grouped[:].rearrange("m t p j -> m (t p j)")
-        )
+                    cols = slice(half * HALF, (half + 1) * HALF)
+                    part = scaled[:, half, :, :].rearrange("m b c -> m (b c)")
+                    nc.vector.tensor_tensor(part, flat, ts_rows[:, cols], ALU.mult)
+                    nc.scalar.activation(e_sb[j][:, cols], part, ACT.Exp, scale=us_sb[:, j : j + 1])
+                continue
+            for half in range(2):
+                ps = bank("sum", "scores")
+                for b in range(PACK):
+                    cols = slice(b * P, (b + 1) * P)
+                    nc.tensor.matmul_mx(
+                        out=ps[:, b, :],
+                        lhsT=k_codes[half][:, cols].bitcast(E4M3),
+                        lhsT_scale=k_scales[half][:, cols],
+                        rhs=q_codes[:, rows].bitcast(E4M3),
+                        rhs_scale=q_scales[:, rows],
+                        start=True,
+                        stop=True,
+                    )
+                for b in range(PACK):
+                    blk = half * PACK + b
+                    nc.scalar.activation(scaled[:, half, b, :], ps[:, b, :], ACT.Copy, scale=ts_col[:, blk : blk + 1])
+            for half in range(2):
+                back = bank("back", "scores_back")
+                for b in range(PACK):
+                    turn(back[:, b, :], scaled[:, half, b, :])
+                nc.scalar.activation(
+                    e_sb[j][:, half * HALF : (half + 1) * HALF],
+                    back[:].rearrange("p b c -> p (b c)"),
+                    ACT.Exp,
+                    scale=us_sb[:, j : j + 1],
+                )
 
         def by_slots(src, tag, bufs, name):
             picked = shared([P, C], F32, tag, bufs, name)
@@ -225,22 +230,47 @@ def tile_attend_gblkatt_kernel(tc, qT, kT, us, ts, wb, dp, offs, blkoffs, slotof
         for j in range(PACK):
             e_slots.append(by_slots(e_sb[j], "t4", 4, "e_slots_%d" % j))
             f_tile = placed([P, C], F32, 40 + 4 * j, "f_%d" % j)
-            nc.vector.tensor_tensor(f_tile[:], e_sb[j][:], dp_sb[j][:], ALU.mult)
+            nc.gpsimd.tensor_tensor(f_tile[:], e_sb[j][:], dp_sb[j][:], ALU.mult)
             f_sb.append(f_tile)
 
-        root = placed([P, PACK, X], F32, 80, "root")
+        root = placed([P, PACK, X], F32, 32, "root")
         inv_s = []
         for j in range(PACK):
-            ps = bank("back", "s_turned")
-            pair_sums(e_slots[j], ps)
-            nc.scalar.activation(root[:, j, :], ps[:].rearrange("p b m -> p (b m)"), ACT.Abs_reciprocal_sqrt)
-            ps = bank("sum", "root_back")
-            for b in range(PACK):
-                turn(ps[:, b, :], root[:, j, b * P : (b + 1) * P])
-            flat = ps[:].rearrange("m b x -> m (b x)")
-            inv = placed([P, X, 2], F32, (90, 94, 32, 36)[j], "inv_%d" % j)
+            if j in S_ON_VECTOR:
+                sums = placed([P, X], F32, 82 + 2 * j, "sums_%d" % j)
+                pairs = e_slots[j][:].rearrange("p (x i) -> p x i", i=2)
+                nc.vector.tensor_reduce(sums[:], pairs, mybir.AxisListType.X, ALU.add)
+                nc.scalar.activation(root[:, j, :], sums[:], ACT.Abs_reciprocal_sqrt)
+                flat = root[:, j, :]
+            else:
+                ps = bank("back", "s_turned")
+                pair_sums(e_slots[j], ps)
+                nc.scalar.activation(root[:, j, :], ps[:].rearrange("p b m -> p (b m)"), ACT.Abs_reciprocal_sqrt)
+                ps = bank("sum", "root_back")
+                for b in range(PACK):
+                    turn(ps[:, b, :], root[:, j, b * P : (b + 1) * P])
+                flat = ps[:].rearrange("m b x -> m (b x)")
+            inv = placed([P, X, 2], F32, (16, 20, 24, 28)[j], "inv_%d" % j)
             nc.scalar.activation(inv[:], flat.unsqueeze(2).to_broadcast([P, X, 2]), ACT.Square)
             inv_s.append(inv)
+
+        q_words = q_grouped[:].rearrange("p j m t -> p (j m t)").bitcast(F32).rearrange("p (j m u) -> p j m u", j=PACK, u=2)
+        q2_grouped = keep.tile([P, PACK, P, PACK], BF16, name="q2_grouped", align_bytes=64)
+        q2_codes = keep.tile([P, D], U32, name="q2_codes", align_bytes=64)
+        q2_scales = keep.tile([P, D], U8, name="q2_scales", align_bytes=64)
+
+        def queries_along_rows():
+            for u in range(2):
+                ps = bank("sum", "q_turned")
+                for j in range(PACK):
+                    turn(ps[:, j, :], q_words[:, j, :, u])
+                nc.scalar.copy(
+                    q2_grouped[:, 2 * u : 2 * u + 2, :, :],
+                    ps[:].rearrange("m j p -> m (j p)").bitcast(BF16).rearrange("m (j p e) -> m e p j", j=PACK, e=2),
+                )
+            nc.vector.quantize_mx(
+                out=q2_codes[:].bitcast(E4M3), scales=q2_scales[:], in_=q2_grouped[:].rearrange("m t p j -> m (t p j)")
+            )
 
         def block_terms(j):
             f_slots = shared([P, C], F32, "t4", 4, "f_slots_%d" % j)
@@ -250,18 +280,21 @@ def tile_attend_gblkatt_kernel(tc, qT, kT, us, ts, wb, dp, offs, blkoffs, slotof
                 nc.vector.tensor_tensor(
                     f_slots[:, cols], f_sb[j][:].indirect(half_list(slot_list, half)), twice[:, cols], ALU.mult
                 )
-            ps = bank("back", "m_turned")
-            pair_sums(f_slots, ps)
-            m_turned = placed([P, PACK, P], F32, (98, 100, 23, 80)[j], "m_turned_%d" % j)
-            nc.scalar.copy(m_turned[:], ps[:])
-            m_back = bank("blk", "m_back")
-            for b in range(PACK):
-                turn(m_back[:, b, :], m_turned[:, b, :])
-            nc.scalar.copy(m_window[j][:, :X], m_back[:].rearrange("m b x -> m (b x)"))
             nc.vector.tensor_tensor(h_window[j][:, :X], inv_s[j][:, :, 0], wb_sb[:, j, :], ALU.mult)
+            if j in M_ON_TENSOR:
+                ps = bank("back", "m_turned")
+                pair_sums(f_slots, ps)
+                m_turned = shared([P, PACK, P], F32, "mt", 2, "m_turned_%d" % j)
+                nc.scalar.copy(m_turned[:], ps[:])
+                m_back = bank("blk", "m_back")
+                for b in range(PACK):
+                    turn(m_back[:, b, :], m_turned[:, b, :])
+                nc.scalar.copy(m_window[j][:, :X], m_back[:].rearrange("m b x -> m (b x)"))
+            else:
+                pairs = f_slots[:].rearrange("p (x i) -> p x i", i=2)
+                nc.vector.tensor_tensor(m_window[j][:, :X], pairs[:, :, 0], pairs[:, :, 1], ALU.add)
             nc.scalar.activation(f_sb[j][:], f_sb[j][:], ACT.Copy, scale=-1.0)
 
-        out_window = []
 
         dk_sb = {}
 
@@ -348,10 +381,10 @@ def tile_attend_gblkatt_kernel(tc, qT, kT, us, ts, wb, dp, offs, blkoffs, slotof
                 block_terms(j)
             if j >= LAG:
                 gradient(0, j - LAG)
-        for w, kb in enumerate((16, 24, 80)):
-            tile = placed([P, T], F32, kb, "out_window_%d" % w)
+        queries_along_rows()
+        out_window = [placed([P, T], F32, kb, "out_window_%d" % kb) for kb in (32, 16, 24)]
+        for tile in out_window:
             nc.gpsimd.memset(tile[:], 0.0)
-            out_window.append(tile)
 
         for j in range(PACK - 1):
             gradient(1, j)

@@ -19,18 +19,24 @@ ALU = mybir.AluOpType
 
 P = 128
 PACK = 4
+LAST = PACK - 1
 HALF = 512
+CHUNKS = HALF // P
 LIST_COLS = HALF // 16
 K_PIECE = 512
+K_PIECES = T // K_PIECE
+Q_PIECE = R // 2
 BLK_WINDOW = X + 8
-KB = 1024
-TS_ROWS = 32
-LAG = 2
-DIRECT = (0, 1)
-M_ON_TENSOR = ()
-S_ON_VECTOR = (0,)
-SCALAR_CASTS = (2, 3)
+QUADRANT = 32
 OUT_WINDOWS = 3
+DIRECT_TILES = 2
+
+AT_TS, AT_K_PAIRS, AT_K_GROUPED, AT_Q_RAW, AT_F, AT_E = 0, 8, 24, 32, 40, 56
+AT_G_GROUPED, AT_K_CODES, AT_SUMS, AT_BLK_WINDOWS = 72, 80, 82, 84
+BLK_WINDOW_KIB = 2.125
+AT_K_RAW = (AT_BLK_WINDOWS, AT_E)
+AT_G_PLANES = AT_TS
+AT_INVERSE = AT_K_PAIRS + 8
 
 
 def tile_attend_gblkatt_kernel(tc, qT, kT, us, ts, wb, dp, offs, blkoffs, slotoffs, out):
@@ -41,17 +47,26 @@ def tile_attend_gblkatt_kernel(tc, qT, kT, us, ts, wb, dp, offs, blkoffs, slotof
         arena = ctx.enter_context(tc.tile_pool(name="arena", bufs=1))
         psum = ctx.enter_context(tc.psum_pool(name="psum", bufs=2))
 
-        def shared(shape, dtype, tag, bufs, name):
-            return work.tile(shape, dtype, tag=tag, bufs=bufs, name=name, align_bytes=64)
+        def rotating(shape, tag, bufs, name):
+            return work.tile(shape, F32, tag=tag, bufs=bufs, name=name, align_bytes=64)
 
-        def placed(shape, dtype, kb, name):
-            return arena.tile(shape, dtype, name=name, align_bytes=64, offset=kb * KB)
+        def placed(shape, dtype, kib, name):
+            return arena.tile(shape, dtype, name=name, align_bytes=64, offset=int(kib * 1024))
 
         def bank(tag, name):
-            return psum.tile([P, PACK, P], F32, tag=tag, name=name)
+            return psum.tile([P, CHUNKS, P], F32, tag=tag, name=name)
 
-        def half_list(lst, half):
-            return lst[:, half * LIST_COLS : (half + 1) * LIST_COLS]
+        def flat(view):
+            return view.rearrange("p a b -> p (a b)")
+
+        def half_cols(half):
+            return slice(half * HALF, (half + 1) * HALF)
+
+        def chunk_cols(chunk):
+            return slice(chunk * P, (chunk + 1) * P)
+
+        def half_list(offsets, half):
+            return offsets[:, half * LIST_COLS : (half + 1) * LIST_COLS]
 
         def turn(dst, src, start=True, stop=True):
             nc.tensor.matmul(dst, lhsT=src, rhs=ident[:], is_transpose=True, start=start, stop=stop)
@@ -60,81 +75,86 @@ def tile_attend_gblkatt_kernel(tc, qT, kT, us, ts, wb, dp, offs, blkoffs, slotof
         blk_list = keep.tile([P, C // 16], U16, name="blk_list")
         slot_list = keep.tile([P, C // 16], U16, name="slot_list")
         ident = keep.tile([P, P], F32, name="ident")
-        ts_window = placed([P, T], F32, 0, "ts_window")
-        nc.scalar.dma_start(out=ts_window[0:TS_ROWS, :], in_=ts[0:TS_ROWS, :])
-        nc.vector.memset(ts_window[TS_ROWS:64, :].bitcast(I32), 0)
-        nc.vector.memset(ts_window[64:P, :].bitcast(I32), 0)
+
+        ts_window = placed([P, T], F32, AT_TS, "ts_window")
+        nc.scalar.dma_start(out=ts_window[0:QUADRANT, :], in_=ts[0:QUADRANT, :])
+        nc.vector.memset(ts_window[QUADRANT : 2 * QUADRANT, :].bitcast(I32), 0)
+        nc.vector.memset(ts_window[2 * QUADRANT : P, :].bitcast(I32), 0)
+        out_window = [keep.tile([P, T], F32, name="out_window_%d" % w) for w in range(OUT_WINDOWS)]
+        ts_listed = keep.tile([P, C], F32, name="ts_listed")
         nc.sync.dma_start(tok_list[:], offs)
+        for w in range(OUT_WINDOWS):
+            nc.vector.memset(out_window[w][:].bitcast(I32), 0)
+            if w == 0:
+                nc.vector.tensor_copy(ts_listed[:], ts_window[:].indirect(tok_list[:]))
         make_identity(nc, ident[:])
 
         k_rows = kT.rearrange("(p u e) n -> p u e n", u=2, e=2)
-        k_raw = []
+        k_raw = {}
         for u in range(2):
-            for s in range(T // K_PIECE):
-                raw = placed([P, 2, K_PIECE], F32, 40 + 16 * u + 4 * s, "k_raw_%d_%d" % (u, s))
-                nc.sync.dma_start(out=raw[:], in_=k_rows[:, u, :, s * K_PIECE : (s + 1) * K_PIECE])
-                k_raw.append(raw)
+            for s in range(K_PIECES):
+                k_raw[(u, s)] = placed([P, 2, K_PIECE], F32, AT_K_RAW[u] + 4 * s, "k_raw_%d_%d" % (u, s))
+                nc.sync.dma_start(out=k_raw[(u, s)][:], in_=k_rows[:, u, :, s * K_PIECE : (s + 1) * K_PIECE])
         q_rows = qT.rearrange("(p t) r -> p t r", t=PACK)
-        q_raw = []
+        q_raw = [placed([P, PACK, Q_PIECE], F32, AT_Q_RAW + 4 * s, "q_raw_%d" % s) for s in range(2)]
         for s in range(2):
-            raw = placed([P, PACK, R // 2], F32, 32 + 4 * s, "q_raw_%d" % s)
-            nc.sync.dma_start(out=raw[:], in_=q_rows[:, :, s * (R // 2) : (s + 1) * (R // 2)])
-            q_raw.append(raw)
+            nc.sync.dma_start(out=q_raw[s][:], in_=q_rows[:, :, s * Q_PIECE : (s + 1) * Q_PIECE])
         us_sb = keep.tile([P, PACK], F32, name="us_sb")
         nc.sync.dma_start(out=us_sb[:], in_=us.rearrange("(p j) o -> p (j o)", j=PACK))
         nc.sync.dma_start(slot_list[:], slotoffs)
         dp_rows = dp.rearrange("(p j) c -> j p c", j=PACK)
-        dp_sb = []
+        dp_sb = [keep.tile([P, C], F32, name="dp_%d" % j) for j in range(PACK)]
         for j in range(PACK):
-            tile = keep.tile([P, C], F32, name="dp_%d" % j)
-            nc.sync.dma_start(out=tile[:], in_=dp_rows[j])
-            dp_sb.append(tile)
+            nc.sync.dma_start(out=dp_sb[j][:], in_=dp_rows[j])
         wb_sb = keep.tile([P, PACK, X], F32, name="wb_sb")
         nc.sync.dma_start(out=wb_sb[:], in_=wb.rearrange("(p j) x -> p j x", j=PACK))
         nc.sync.dma_start(blk_list[:], blkoffs)
 
-        h_window = [keep.tile([P, BLK_WINDOW], F32, name="h_%d" % j) for j in range(PACK)]
-        m_window = [keep.tile([P, BLK_WINDOW], F32, name="m_%d" % j) for j in range(PACK)]
-        for tile in h_window + m_window:
-            nc.gpsimd.memset(tile[:, X:], 0.0)
+        blk_windows = [
+            placed([P, BLK_WINDOW], F32, AT_BLK_WINDOWS + BLK_WINDOW_KIB * n, "blk_window_%d" % n) for n in range(2 * PACK)
+        ]
+        h_window, m_window = blk_windows[:PACK], blk_windows[PACK:]
         neg_us = keep.tile([P, PACK], F32, name="neg_us")
         nc.gpsimd.tensor_scalar(neg_us[:], us_sb[:], -1.0, 0.0, ALU.mult, ALU.add)
 
-        ts_c = keep.tile([P, C], F32, name="ts_c")
-        nc.vector.tensor_copy(ts_c[:], ts_window[:].indirect(tok_list[:]))
         ts_col = keep.tile([P, C // P], F32, name="ts_col")
         for half in range(2):
-            ps = bank("fwd", "ts_turned")
-            for b in range(PACK):
-                blk = half * PACK + b
-                turn(ps[:, b, :], ts_c[:, blk * P : (blk + 1) * P])
-            nc.scalar.copy(ts_col[:, half * PACK : (half + 1) * PACK], ps[:, :, 0])
+            turned = bank("fwd", "ts_turned")
+            for b in range(CHUNKS):
+                turn(turned[:, b, :], ts_listed[:, chunk_cols(half * CHUNKS + b)])
+            nc.scalar.copy(ts_col[:, half * CHUNKS : (half + 1) * CHUNKS], turned[:, :, 0])
 
-        k_pairs = [placed([P, T, 2], BF16, 8 + 8 * u, "k_pairs_%d" % u) for u in range(2)]
-        k_grouped = [placed([P, HALF * PACK], BF16, 24 + 4 * half, "k_grouped_%d" % half) for half in range(2)]
+        def ts_of_chunk(half, b):
+            return ts_col[:, half * CHUNKS + b : half * CHUNKS + b + 1]
+
+        k_pairs = [placed([P, T, 2], BF16, AT_K_PAIRS + 8 * u, "k_pairs_%d" % u) for u in range(2)]
+        k_grouped = [placed([P, HALF * PACK], BF16, AT_K_GROUPED + 4 * half, "k_grouped_%d" % half) for half in range(2)]
 
         def round_keys(u):
-            for s in range(T // K_PIECE):
+            for s in range(K_PIECES):
                 dst = k_pairs[u][:, s * K_PIECE : (s + 1) * K_PIECE, :]
-                src = k_raw[u * (T // K_PIECE) + s][:].rearrange("p e n -> p n e")
-                if s >= SCALAR_CASTS[u]:
+                src = k_raw[(u, s)][:].rearrange("p e n -> p n e")
+                if (u, s) == (1, K_PIECES - 1):
                     nc.vector.tensor_copy(dst, src)
                 else:
                     nc.scalar.activation(dst, src, ACT.Copy)
 
         def gather_keys(u, half):
-            window = k_pairs[u][:].rearrange("p n e -> p (n e)").bitcast(U32)
+            window = flat(k_pairs[u][:]).bitcast(U32)
             words = k_grouped[half][:].bitcast(U32).rearrange("p (c u) -> p c u", u=2)
             nc.vector.tensor_copy(words[:, :, u], window.indirect(half_list(tok_list, half)))
 
         round_keys(0)
+        for window in blk_windows:
+            nc.gpsimd.memset(window[:, X:], 0.0)
         for half in range(2):
             gather_keys(0, half)
         round_keys(1)
+
         q_grouped = keep.tile([P, PACK, P, PACK], BF16, name="q_grouped", align_bytes=64)
         for s in range(2):
             nc.scalar.activation(
-                q_grouped[:, :, s * 64 : (s + 1) * 64, :].rearrange("p j m t -> p m j t"),
+                q_grouped[:, :, s * Q_PIECE // PACK : (s + 1) * Q_PIECE // PACK, :].rearrange("p j m t -> p m j t"),
                 q_raw[s][:].rearrange("p t (m j) -> p m j t", j=PACK),
                 ACT.Copy,
             )
@@ -143,259 +163,228 @@ def tile_attend_gblkatt_kernel(tc, qT, kT, us, ts, wb, dp, offs, blkoffs, slotof
         nc.vector.quantize_mx(
             out=q_codes[:].bitcast(E4M3), scales=q_scales[:], in_=q_grouped[:].rearrange("p j m t -> p (j m t)")
         )
-        k_codes, k_scales = [], []
+        k_codes = [
+            placed([P, HALF], U32, kib, "k_codes_%d" % half) for half, kib in enumerate((AT_K_CODES, AT_Q_RAW + 4))
+        ]
+        k_scales = [keep.tile([P, HALF], U8, name="k_scales_%d" % half, align_bytes=64) for half in range(2)]
         for half in range(2):
             gather_keys(1, half)
-            codes = placed([P, HALF], U32, (80, 36)[half], "k_codes_%d" % half)
-            scales = keep.tile([P, HALF], U8, name="k_scales_%d" % half, align_bytes=64)
-            nc.vector.quantize_mx(out=codes[:].bitcast(E4M3), scales=scales[:], in_=k_grouped[half][:])
-            k_codes.append(codes)
-            k_scales.append(scales)
+            nc.vector.quantize_mx(out=k_codes[half][:].bitcast(E4M3), scales=k_scales[half][:], in_=k_grouped[half][:])
 
-        ts_rows = placed([P, C], F32, 32, "ts_rows")
+        ts_rows = placed([P, C], F32, AT_Q_RAW, "ts_rows")
         for half in range(2):
-            ps = bank("blk", "ts_spread")
-            for b in range(PACK):
-                blk = half * PACK + b
-                turn(ps[:, b, :], ts_col[:, blk : blk + 1].to_broadcast([P, P]))
-            nc.scalar.copy(ts_rows[:, half * HALF : (half + 1) * HALF], ps[:].rearrange("m b c -> m (b c)"))
+            spread = bank("blk", "ts_spread")
+            for b in range(CHUNKS):
+                turn(spread[:, b, :], ts_of_chunk(half, b).to_broadcast([P, P]))
+            nc.scalar.copy(ts_rows[:, half_cols(half)], flat(spread[:]))
 
-        e_sb = [placed([P, C], F32, 56 + 4 * j, "e_%d" % j) for j in range(PACK)]
-        for j in range(PACK):
-            rows = slice(j * P, (j + 1) * P)
-            if j == PACK - 1:
-                scaled = placed([P, 2, PACK, P], F32, 32, "scaled_last")
-            else:
-                scaled = shared([P, 2, PACK, P], F32, "y", 2, "scaled_%d" % j)
-            if j in DIRECT:
-                for half in range(2):
-                    ps = bank("sum", "scores_direct")
-                    flat = ps[:].rearrange("m b c -> m (b c)")
-                    nc.tensor.matmul_mx(
-                        out=flat,
-                        lhsT=q_codes[:, rows].bitcast(E4M3),
-                        lhsT_scale=q_scales[:, rows],
-                        rhs=k_codes[half][:].bitcast(E4M3),
-                        rhs_scale=k_scales[half][:],
-                        start=True,
-                        stop=True,
-                    )
-                    cols = slice(half * HALF, (half + 1) * HALF)
-                    part = scaled[:, half, :, :].rearrange("m b c -> m (b c)")
-                    nc.vector.tensor_tensor(part, flat, ts_rows[:, cols], ALU.mult)
-                    nc.scalar.activation(e_sb[j][:, cols], part, ACT.Exp, scale=us_sb[:, j : j + 1])
-                continue
+        e_sb = [placed([P, C], F32, AT_E + 4 * j, "e_%d" % j) for j in range(PACK)]
+
+        def scores(dst, stationary, stationary_scales, moving, moving_scales):
+            nc.tensor.matmul_mx(
+                out=dst,
+                lhsT=stationary.bitcast(E4M3),
+                lhsT_scale=stationary_scales,
+                rhs=moving.bitcast(E4M3),
+                rhs_scale=moving_scales,
+                start=True,
+                stop=True,
+            )
+
+        def exp_into_e(j, half, src):
+            nc.scalar.activation(e_sb[j][:, half_cols(half)], src, ACT.Exp, scale=us_sb[:, j : j + 1])
+
+        def weights_direct(j, scaled):
+            rows = chunk_cols(j)
             for half in range(2):
-                ps = bank("sum", "scores")
-                for b in range(PACK):
-                    cols = slice(b * P, (b + 1) * P)
-                    nc.tensor.matmul_mx(
-                        out=ps[:, b, :],
-                        lhsT=k_codes[half][:, cols].bitcast(E4M3),
-                        lhsT_scale=k_scales[half][:, cols],
-                        rhs=q_codes[:, rows].bitcast(E4M3),
-                        rhs_scale=q_scales[:, rows],
-                        start=True,
-                        stop=True,
+                product = bank("sum", "scores_direct")
+                scores(flat(product[:]), q_codes[:, rows], q_scales[:, rows], k_codes[half][:], k_scales[half][:])
+                part = flat(scaled[:, half, :, :])
+                nc.vector.tensor_tensor(part, flat(product[:]), ts_rows[:, half_cols(half)], ALU.mult)
+                exp_into_e(j, half, part)
+
+        def weights_turned(j, scaled):
+            rows = chunk_cols(j)
+            for half in range(2):
+                product = bank("sum", "scores_turned")
+                for b in range(CHUNKS):
+                    cols = chunk_cols(b)
+                    scores(
+                        product[:, b, :], k_codes[half][:, cols], k_scales[half][:, cols],
+                        q_codes[:, rows], q_scales[:, rows],
                     )
-                for b in range(PACK):
-                    blk = half * PACK + b
-                    nc.scalar.activation(scaled[:, half, b, :], ps[:, b, :], ACT.Copy, scale=ts_col[:, blk : blk + 1])
+                for b in range(CHUNKS):
+                    nc.scalar.activation(scaled[:, half, b, :], product[:, b, :], ACT.Copy, scale=ts_of_chunk(half, b))
             for half in range(2):
                 back = bank("back", "scores_back")
-                for b in range(PACK):
+                for b in range(CHUNKS):
                     turn(back[:, b, :], scaled[:, half, b, :])
-                nc.scalar.activation(
-                    e_sb[j][:, half * HALF : (half + 1) * HALF],
-                    back[:].rearrange("p b c -> p (b c)"),
-                    ACT.Exp,
-                    scale=us_sb[:, j : j + 1],
-                )
+                exp_into_e(j, half, flat(back[:]))
 
-        def by_slots(src, tag, bufs, name):
-            picked = shared([P, C], F32, tag, bufs, name)
-            for half in range(2):
-                nc.vector.tensor_copy(
-                    picked[:, half * HALF : (half + 1) * HALF], src[:].indirect(half_list(slot_list, half))
-                )
-            return picked
-
-        def pair_sums(picked, ps):
-            pairs = picked[:].rearrange("p (x i) -> p x i", i=2)
-            for b in range(PACK):
-                for i in range(2):
-                    turn(ps[:, b, :], pairs[:, b * P : (b + 1) * P, i], start=(i == 0), stop=(i == 1))
-
-        f_sb, e_slots = [], []
         for j in range(PACK):
-            e_slots.append(by_slots(e_sb[j], "t4", 4, "e_slots_%d" % j))
-            f_tile = placed([P, C], F32, 40 + 4 * j, "f_%d" % j)
-            nc.gpsimd.tensor_tensor(f_tile[:], e_sb[j][:], dp_sb[j][:], ALU.mult)
-            f_sb.append(f_tile)
-
-        root = placed([P, PACK, X], F32, 32, "root")
-        inv_s = []
-        for j in range(PACK):
-            if j in S_ON_VECTOR:
-                sums = placed([P, X], F32, 82 + 2 * j, "sums_%d" % j)
-                pairs = e_slots[j][:].rearrange("p (x i) -> p x i", i=2)
-                nc.vector.tensor_reduce(sums[:], pairs, mybir.AxisListType.X, ALU.add)
-                nc.scalar.activation(root[:, j, :], sums[:], ACT.Abs_reciprocal_sqrt)
-                flat = root[:, j, :]
+            if j == LAST:
+                scaled = placed([P, 2, CHUNKS, P], F32, AT_Q_RAW, "scaled_last")
             else:
-                ps = bank("back", "s_turned")
-                pair_sums(e_slots[j], ps)
-                nc.scalar.activation(root[:, j, :], ps[:].rearrange("p b m -> p (b m)"), ACT.Abs_reciprocal_sqrt)
-                ps = bank("sum", "root_back")
-                for b in range(PACK):
-                    turn(ps[:, b, :], root[:, j, b * P : (b + 1) * P])
-                flat = ps[:].rearrange("m b x -> m (b x)")
-            inv = placed([P, X, 2], F32, (16, 20, 24, 28)[j], "inv_%d" % j)
-            nc.scalar.activation(inv[:], flat.unsqueeze(2).to_broadcast([P, X, 2]), ACT.Square)
-            inv_s.append(inv)
+                scaled = rotating([P, 2, CHUNKS, P], "scaled", 2, "scaled_%d" % j)
+            if j < DIRECT_TILES:
+                weights_direct(j, scaled)
+            else:
+                weights_turned(j, scaled)
+
+        e_slots, f_sb = [], []
+        for j in range(PACK):
+            picked = rotating([P, C], "slots", PACK, "e_slots_%d" % j)
+            for half in range(2):
+                nc.vector.tensor_copy(picked[:, half_cols(half)], e_sb[j][:].indirect(half_list(slot_list, half)))
+            e_slots.append(picked[:].rearrange("p (x i) -> p x i", i=2))
+            f_sb.append(placed([P, C], F32, AT_F + 4 * j, "f_%d" % j))
+            nc.gpsimd.tensor_tensor(f_sb[j][:], e_sb[j][:], dp_sb[j][:], ALU.mult)
+
+        root = placed([P, PACK, X], F32, AT_Q_RAW, "root")
+        inverse = []
+        for j in range(PACK):
+            if j == 0:
+                sums = placed([P, X], F32, AT_SUMS, "sums")
+                nc.vector.tensor_reduce(sums[:], e_slots[j], mybir.AxisListType.X, ALU.add)
+                nc.scalar.activation(root[:, j, :], sums[:], ACT.Abs_reciprocal_sqrt)
+                roots = root[:, j, :]
+            else:
+                sums_turned = bank("back", "sums_turned")
+                for b in range(CHUNKS):
+                    for i in range(2):
+                        turn(sums_turned[:, b, :], e_slots[j][:, chunk_cols(b), i], start=(i == 0), stop=(i == 1))
+                nc.scalar.activation(root[:, j, :], flat(sums_turned[:]), ACT.Abs_reciprocal_sqrt)
+                root_back = bank("sum", "root_back")
+                for b in range(CHUNKS):
+                    turn(root_back[:, b, :], root[:, j, chunk_cols(b)])
+                roots = flat(root_back[:])
+            inverse.append(placed([P, X, 2], F32, AT_INVERSE + 4 * j, "inverse_%d" % j))
+            nc.scalar.activation(inverse[j][:], roots.unsqueeze(2).to_broadcast([P, X, 2]), ACT.Square)
 
         q_words = q_grouped[:].rearrange("p j m t -> p (j m t)").bitcast(F32).rearrange("p (j m u) -> p j m u", j=PACK, u=2)
         q2_grouped = keep.tile([P, PACK, P, PACK], BF16, name="q2_grouped", align_bytes=64)
         q2_codes = keep.tile([P, D], U32, name="q2_codes", align_bytes=64)
         q2_scales = keep.tile([P, D], U8, name="q2_scales", align_bytes=64)
-
-        def queries_along_rows():
-            for u in range(2):
-                ps = bank("sum", "q_turned")
-                for j in range(PACK):
-                    turn(ps[:, j, :], q_words[:, j, :, u])
-                nc.scalar.copy(
-                    q2_grouped[:, 2 * u : 2 * u + 2, :, :],
-                    ps[:].rearrange("m j p -> m (j p)").bitcast(BF16).rearrange("m (j p e) -> m e p j", j=PACK, e=2),
-                )
-            nc.vector.quantize_mx(
-                out=q2_codes[:].bitcast(E4M3), scales=q2_scales[:], in_=q2_grouped[:].rearrange("m t p j -> m (t p j)")
+        for u in range(2):
+            q_turned = bank("sum", "q_turned")
+            for j in range(PACK):
+                turn(q_turned[:, j, :], q_words[:, j, :, u])
+            nc.scalar.copy(
+                q2_grouped[:, 2 * u : 2 * u + 2, :, :],
+                flat(q_turned[:]).bitcast(BF16).rearrange("m (j p e) -> m e p j", j=PACK, e=2),
             )
+        nc.vector.quantize_mx(
+            out=q2_codes[:].bitcast(E4M3), scales=q2_scales[:], in_=q2_grouped[:].rearrange("m t p j -> m (t p j)")
+        )
 
         def block_terms(j):
-            f_slots = shared([P, C], F32, "t4", 4, "f_slots_%d" % j)
-            twice = inv_s[j][:].rearrange("p x i -> p (x i)")
+            f_over_s = rotating([P, C], "slots", PACK, "f_over_s_%d" % j)
             for half in range(2):
-                cols = slice(half * HALF, (half + 1) * HALF)
+                cols = half_cols(half)
                 nc.vector.tensor_tensor(
-                    f_slots[:, cols], f_sb[j][:].indirect(half_list(slot_list, half)), twice[:, cols], ALU.mult
+                    f_over_s[:, cols], f_sb[j][:].indirect(half_list(slot_list, half)), flat(inverse[j][:])[:, cols], ALU.mult
                 )
-            nc.vector.tensor_tensor(h_window[j][:, :X], inv_s[j][:, :, 0], wb_sb[:, j, :], ALU.mult)
-            if j in M_ON_TENSOR:
-                ps = bank("back", "m_turned")
-                pair_sums(f_slots, ps)
-                m_turned = shared([P, PACK, P], F32, "mt", 2, "m_turned_%d" % j)
-                nc.scalar.copy(m_turned[:], ps[:])
-                m_back = bank("blk", "m_back")
-                for b in range(PACK):
-                    turn(m_back[:, b, :], m_turned[:, b, :])
-                nc.scalar.copy(m_window[j][:, :X], m_back[:].rearrange("m b x -> m (b x)"))
-            else:
-                pairs = f_slots[:].rearrange("p (x i) -> p x i", i=2)
-                nc.vector.tensor_tensor(m_window[j][:, :X], pairs[:, :, 0], pairs[:, :, 1], ALU.add)
+            nc.vector.tensor_tensor(h_window[j][:, :X], inverse[j][:, :, 0], wb_sb[:, j, :], ALU.mult)
+            pairs = f_over_s[:].rearrange("p (x i) -> p x i", i=2)
+            nc.vector.tensor_tensor(m_window[j][:, :X], pairs[:, :, 0], pairs[:, :, 1], ALU.add)
             nc.scalar.activation(f_sb[j][:], f_sb[j][:], ACT.Copy, scale=-1.0)
 
+        centred_back, factor, g_planes = {}, {}, {}
 
-        dk_sb = {}
+        def centred(half, j):
+            e_m = rotating([P, HALF], "e_m", PACK, "e_m_%d_%d" % (half, j))
+            nc.vector.tensor_tensor(
+                e_m[:], m_window[j][:].indirect(half_list(blk_list, half)), e_sb[j][:, half_cols(half)], ALU.mult
+            )
+            turned = bank("fwd", "centred_turned")
+            with_ts = rotating([P, CHUNKS, P], "with_ts", 2, "with_ts_%d_%d" % (half, j))
+            for b in range(CHUNKS):
+                turn(turned[:, b, :], e_m[:, chunk_cols(b)], start=True, stop=False)
+                turn(turned[:, b, :], f_sb[j][:, chunk_cols(half * CHUNKS + b)], start=False, stop=True)
+            for b in range(CHUNKS):
+                nc.scalar.activation(with_ts[:, b, :], turned[:, b, :], ACT.Copy, scale=ts_of_chunk(half, b))
+            centred_back[(half, j)] = bank("back", "centred_back")
+            for b in range(CHUNKS):
+                turn(centred_back[(half, j)][:, b, :], with_ts[:, b, :])
 
-        def products(half, g_codes, g_scales, tiles):
-            for t in tiles:
-                ps = bank("blk", "dk")
-                flat = ps[:].rearrange("p b c -> p (b c)")
-                nc.tensor.matmul_mx(
-                    out=flat,
-                    lhsT=q2_codes[:, t * P : (t + 1) * P].bitcast(E4M3),
-                    lhsT_scale=q2_scales[:, t * P : (t + 1) * P],
-                    rhs=g_codes[:].bitcast(E5M2),
-                    rhs_scale=g_scales[:],
-                    start=True,
-                    stop=True,
-                )
-                if (t, half) == (2, 0):
-                    tile = placed([P, HALF], F32, 8, "dk_held")
-                else:
-                    tile = shared([P, HALF], F32, "t4", 4, "dk_%d_%d" % (t, half))
-                nc.scalar.copy(tile[:], flat)
-                dk_sb[(t, half)] = tile
+        def fetch_factor(half, j):
+            name = "factor_%d_%d" % (half, j)
+            if j == LAST:
+                factor[(half, j)] = placed([P, HALF], F32, AT_G_PLANES + 8 * (1 - half), name)
+            else:
+                factor[(half, j)] = rotating([P, HALF], "factor", 2 * LAST, name)
+            nc.scalar.activation(
+                factor[(half, j)][:], flat(centred_back[(half, j)][:]), ACT.Copy, scale=neg_us[:, j : j + 1]
+            )
 
-        out_rows = out.rearrange("(p t) n -> t p n", t=PACK)
+        def gradient(half, j):
+            if j == 0:
+                g_planes[half] = placed([P, PACK, HALF], F32, AT_G_PLANES + 8 * half, "g_planes_%d" % half)
+            nc.vector.tensor_tensor(
+                g_planes[half][:, j, :], h_window[j][:].indirect(half_list(blk_list, half)), factor[(half, j)][:], ALU.mult
+            )
 
-        def place(t, half):
-            window = out_window[t % OUT_WINDOWS]
-            nc.vector.tensor_copy(window[:].indirect(half_list(tok_list, half)), dk_sb[(t, half)][:])
-            if half == 1:
-                nc.sync.dma_start(out=out_rows[t], in_=window[:])
-
-        g_planes = [placed([P, PACK, HALF], F32, 8 * half, "g_planes_%d" % half) for half in range(2)]
         g_codes = [keep.tile([P, HALF], U32, name="g_codes_%d" % half, align_bytes=64) for half in range(2)]
         g_scales = [keep.tile([P, HALF], U8, name="g_scales_%d" % half, align_bytes=64) for half in range(2)]
 
-        def gradient(half, j):
-            cols = slice(half * HALF, (half + 1) * HALF)
-            me = shared([P, HALF], F32, "me", 4, "me_%d_%d" % (half, j))
-            nc.vector.tensor_tensor(
-                me[:], m_window[j][:].indirect(half_list(blk_list, half)), e_sb[j][:, cols], ALU.mult
-            )
-            ps = bank("fwd", "diff_turned")
-            if (half, j) == (1, 2):
-                diff = placed([P, PACK, P], F32, 72, "diff_held")
-            else:
-                diff = shared([P, PACK, P], F32, "xt", 2, "diff_%d_%d" % (half, j))
-            for b in range(PACK):
-                blk = half * PACK + b
-                turn(ps[:, b, :], me[:, b * P : (b + 1) * P], start=True, stop=False)
-                turn(ps[:, b, :], f_sb[j][:, blk * P : (blk + 1) * P], start=False, stop=True)
-            for b in range(PACK):
-                blk = half * PACK + b
-                nc.scalar.activation(diff[:, b, :], ps[:, b, :], ACT.Copy, scale=ts_col[:, blk : blk + 1])
-            back = bank("back", "diff_back")
-            for b in range(PACK):
-                turn(back[:, b, :], diff[:, b, :])
-            factor = shared([P, HALF], F32, "fa", 5, "factor_%d_%d" % (half, j))
-            nc.scalar.activation(
-                factor[:], back[:].rearrange("m b c -> m (b c)"), ACT.Copy, scale=neg_us[:, j : j + 1]
-            )
-            nc.vector.tensor_tensor(
-                g_planes[half][:, j, :], h_window[j][:].indirect(half_list(blk_list, half)), factor[:], ALU.mult
-            )
-
         def quantize_gradient(half):
-            g_grouped = placed([P, HALF, PACK], BF16, 72 + 4 * half, "g_grouped_%d" % half)
+            g_grouped = placed([P, HALF, PACK], BF16, AT_G_GROUPED + 4 * half, "g_grouped_%d" % half)
             nc.scalar.activation(
                 g_grouped[:].rearrange("p (c i) j -> p c j i", i=4),
                 g_planes[half][:].rearrange("p j (c i) -> p c j i", i=4),
                 ACT.Copy,
             )
-            nc.vector.quantize_mx(
-                out=g_codes[half][:].bitcast(E5M2),
-                scales=g_scales[half][:],
-                in_=g_grouped[:].rearrange("p c j -> p (c j)"),
+            nc.vector.quantize_mx(out=g_codes[half][:].bitcast(E5M2), scales=g_scales[half][:], in_=flat(g_grouped[:]))
+
+        out_rows = out.rearrange("(p t) n -> t p n", t=PACK)
+
+        def place_result(t, half):
+            product = bank("blk", "dk")
+            nc.tensor.matmul_mx(
+                out=flat(product[:]),
+                lhsT=q2_codes[:, chunk_cols(t)].bitcast(E4M3),
+                lhsT_scale=q2_scales[:, chunk_cols(t)],
+                rhs=g_codes[half][:].bitcast(E5M2),
+                rhs_scale=g_scales[half][:],
+                start=True,
+                stop=True,
             )
+            name = "dk_%d_%d" % (t, half)
+            if (t, half) == (OUT_WINDOWS - 1, 0):
+                dk = placed([P, HALF], F32, AT_G_PLANES + 8, name)
+            else:
+                dk = rotating([P, HALF], "slots", PACK, name)
+            nc.scalar.copy(dk[:], flat(product[:]))
+            window = out_window[t % OUT_WINDOWS]
+            nc.vector.tensor_copy(window[:].indirect(half_list(tok_list, half)), dk[:])
+            if half == 1:
+                nc.sync.dma_start(out=out_rows[t], in_=window[:])
 
-        def place_product(t, half):
-            products(half, g_codes[half], g_scales[half], [t])
-            place(t, half)
+        def front(half, j):
+            centred(half, j)
+            fetch_factor(half, j)
 
-        for j in range(PACK + LAG):
-            if j < PACK:
-                block_terms(j)
-            if j >= LAG:
-                gradient(0, j - LAG)
-        queries_along_rows()
-        out_window = [placed([P, T], F32, kb, "out_window_%d" % kb) for kb in (32, 16, 24)]
-        for tile in out_window:
-            nc.gpsimd.memset(tile[:], 0.0)
-
-        for j in range(PACK - 1):
+        for j in range(PACK):
+            block_terms(j)
+            if 1 <= j < LAST:
+                for half in range(2):
+                    front(half, j - 1)
+        front(0, LAST - 1)
+        front(0, LAST)
+        front(1, LAST - 1)
+        centred(1, LAST)
+        for j in range(PACK):
+            gradient(0, j)
+        for j in range(LAST):
             gradient(1, j)
-        gradient(1, PACK - 1)
         quantize_gradient(0)
-        place_product(0, 0)
+        fetch_factor(1, LAST)
+        gradient(1, LAST)
+        place_result(0, 0)
         quantize_gradient(1)
         for t in range(1, OUT_WINDOWS):
-            place_product(t, 0)
+            place_result(t, 0)
         for t in range(OUT_WINDOWS):
-            place_product(t, 1)
-        for t in range(OUT_WINDOWS, PACK):
-            for half in range(2):
-                place_product(t, half)
+            place_result(t, 1)
+        for half in range(2):
+            place_result(LAST, half)

@@ -29,32 +29,28 @@ Q_PIECE = R // 2
 BLK_WINDOW = X + 8
 QUADRANT = 32
 OUT_WINDOWS = 3
-DIRECT_TILES = 2
+TURNED_ROWS = R - P
 
-AT_TS, AT_K_PAIRS, AT_K_GROUPED, AT_Q_RAW, AT_F, AT_E = 0, 8, 24, 32, 40, 56
-AT_G_GROUPED, AT_K_CODES, AT_SUMS, AT_BLK_WINDOWS = 72, 80, 82, 84
+AT_TS, AT_K_PAIRS, AT_K_GROUPED, AT_Q_RAW, AT_E, AT_K_LATE, AT_BLK, AT_DP, AT_WB = 0, 8, 24, 32, 40, 56, 72, 89, 105
+AT_F, AT_SLOTS, AT_WITH_TS, AT_T_TURNED, AT_T_FIRST, AT_SPARE = 113, 129, 145, 149, 153, 155
 BLK_WINDOW_KIB = 2.125
-AT_K_RAW = (AT_BLK_WINDOWS, AT_E)
-AT_G_PLANES = AT_TS
-AT_INVERSE = AT_K_PAIRS + 8
+AT_K_RAW = (AT_BLK, AT_K_LATE)
+AT_NEG_F = (AT_K_LATE, AT_SLOTS + 4, AT_SLOTS + 8, AT_SPARE)
+BANK_BYTES = 2048
 
 
 def tile_attend_gblkatt_kernel(tc, qT, kT, us, ts, wb, dp, offs, blkoffs, slotoffs, out):
     nc = tc.nc
     with ExitStack() as ctx:
         keep = ctx.enter_context(tc.tile_pool(name="keep", bufs=1))
-        work = ctx.enter_context(tc.tile_pool(name="work", bufs=1))
         arena = ctx.enter_context(tc.tile_pool(name="arena", bufs=1))
-        psum = ctx.enter_context(tc.psum_pool(name="psum", bufs=2))
-
-        def rotating(shape, tag, bufs, name):
-            return work.tile(shape, F32, tag=tag, bufs=bufs, name=name, align_bytes=64)
+        psum = ctx.enter_context(tc.psum_pool(name="psum", bufs=1))
 
         def placed(shape, dtype, kib, name):
             return arena.tile(shape, dtype, name=name, align_bytes=64, offset=int(kib * 1024))
 
-        def bank(tag, name):
-            return psum.tile([P, CHUNKS, P], F32, tag=tag, name=name)
+        def bank(index, name):
+            return psum.tile([P, CHUNKS, P], F32, name=name, offset=index * BANK_BYTES)
 
         def flat(view):
             return view.rearrange("p a b -> p (a b)")
@@ -80,14 +76,15 @@ def tile_attend_gblkatt_kernel(tc, qT, kT, us, ts, wb, dp, offs, blkoffs, slotof
         nc.scalar.dma_start(out=ts_window[0:QUADRANT, :], in_=ts[0:QUADRANT, :])
         nc.vector.memset(ts_window[QUADRANT : 2 * QUADRANT, :].bitcast(I32), 0)
         nc.vector.memset(ts_window[2 * QUADRANT : P, :].bitcast(I32), 0)
-        out_window = [keep.tile([P, T], F32, name="out_window_%d" % w) for w in range(OUT_WINDOWS)]
+        out_window = [keep.tile([P, T], F32, name="out_window_%d" % w) for w in range(OUT_WINDOWS - 1)]
         ts_listed = keep.tile([P, C], F32, name="ts_listed")
         nc.sync.dma_start(tok_list[:], offs)
-        for w in range(OUT_WINDOWS):
-            nc.vector.memset(out_window[w][:].bitcast(I32), 0)
-            if w == 0:
-                nc.vector.tensor_copy(ts_listed[:], ts_window[:].indirect(tok_list[:]))
         make_identity(nc, ident[:])
+        nc.vector.memset(out_window[0][:].bitcast(I32), 0)
+        nc.vector.tensor_copy(ts_listed[:], ts_window[:].indirect(tok_list[:]))
+        nc.vector.memset(out_window[1][:].bitcast(I32), 0)
+        out_window.append(placed([P, T], F32, AT_TS, "out_window_2"))
+        nc.gpsimd.memset(out_window[2][:], 0.0)
 
         k_rows = kT.rearrange("(p u e) n -> p u e n", u=2, e=2)
         k_raw = {}
@@ -103,26 +100,15 @@ def tile_attend_gblkatt_kernel(tc, qT, kT, us, ts, wb, dp, offs, blkoffs, slotof
         nc.sync.dma_start(out=us_sb[:], in_=us.rearrange("(p j) o -> p (j o)", j=PACK))
         nc.sync.dma_start(slot_list[:], slotoffs)
         dp_rows = dp.rearrange("(p j) c -> j p c", j=PACK)
-        dp_sb = [keep.tile([P, C], F32, name="dp_%d" % j) for j in range(PACK)]
+        dp_sb = [placed([P, C], F32, AT_DP + 4 * j, "dp_%d" % j) for j in range(PACK)]
         for j in range(PACK):
             nc.sync.dma_start(out=dp_sb[j][:], in_=dp_rows[j])
-        wb_sb = keep.tile([P, PACK, X], F32, name="wb_sb")
+        wb_sb = placed([P, PACK, X], F32, AT_WB, "wb_sb")
         nc.sync.dma_start(out=wb_sb[:], in_=wb.rearrange("(p j) x -> p j x", j=PACK))
         nc.sync.dma_start(blk_list[:], blkoffs)
 
-        blk_windows = [
-            placed([P, BLK_WINDOW], F32, AT_BLK_WINDOWS + BLK_WINDOW_KIB * n, "blk_window_%d" % n) for n in range(2 * PACK)
-        ]
+        blk_windows = [placed([P, BLK_WINDOW], F32, AT_BLK + BLK_WINDOW_KIB * n, "blk_window_%d" % n) for n in range(2 * PACK)]
         h_window, m_window = blk_windows[:PACK], blk_windows[PACK:]
-        neg_us = keep.tile([P, PACK], F32, name="neg_us")
-        nc.gpsimd.tensor_scalar(neg_us[:], us_sb[:], -1.0, 0.0, ALU.mult, ALU.add)
-
-        ts_col = keep.tile([P, C // P], F32, name="ts_col")
-        for half in range(2):
-            turned = bank("fwd", "ts_turned")
-            for b in range(CHUNKS):
-                turn(turned[:, b, :], ts_listed[:, chunk_cols(half * CHUNKS + b)])
-            nc.scalar.copy(ts_col[:, half * CHUNKS : (half + 1) * CHUNKS], turned[:, :, 0])
 
         def ts_of_chunk(half, b):
             return ts_col[:, half * CHUNKS + b : half * CHUNKS + b + 1]
@@ -151,6 +137,13 @@ def tile_attend_gblkatt_kernel(tc, qT, kT, us, ts, wb, dp, offs, blkoffs, slotof
             gather_keys(0, half)
         round_keys(1)
 
+        ts_col = placed([P, C // P], F32, AT_K_LATE + 8, "ts_col")
+        for half in range(2):
+            turned = bank(half, "ts_turned_%d" % half)
+            for b in range(CHUNKS):
+                turn(turned[:, b, :], ts_listed[:, chunk_cols(half * CHUNKS + b)])
+            nc.scalar.copy(ts_col[:, half * CHUNKS : (half + 1) * CHUNKS], turned[:, :, 0])
+
         q_grouped = keep.tile([P, PACK, P, PACK], BF16, name="q_grouped", align_bytes=64)
         for s in range(2):
             nc.scalar.activation(
@@ -158,25 +151,25 @@ def tile_attend_gblkatt_kernel(tc, qT, kT, us, ts, wb, dp, offs, blkoffs, slotof
                 q_raw[s][:].rearrange("p t (m j) -> p m j t", j=PACK),
                 ACT.Copy,
             )
-        q_codes = keep.tile([P, R], U32, name="q_codes", align_bytes=64)
-        q_scales = keep.tile([P, R], U8, name="q_scales", align_bytes=64)
-        nc.vector.quantize_mx(
-            out=q_codes[:].bitcast(E4M3), scales=q_scales[:], in_=q_grouped[:].rearrange("p j m t -> p (j m t)")
-        )
-        k_codes = [
-            placed([P, HALF], U32, kib, "k_codes_%d" % half) for half, kib in enumerate((AT_K_CODES, AT_Q_RAW + 4))
-        ]
-        k_scales = [keep.tile([P, HALF], U8, name="k_scales_%d" % half, align_bytes=64) for half in range(2)]
+        ts_rows = placed([P, C], F32, AT_Q_RAW + 2, "ts_rows")
         for half in range(2):
-            gather_keys(1, half)
-            nc.vector.quantize_mx(out=k_codes[half][:].bitcast(E4M3), scales=k_scales[half][:], in_=k_grouped[half][:])
-
-        ts_rows = placed([P, C], F32, AT_Q_RAW, "ts_rows")
-        for half in range(2):
-            spread = bank("blk", "ts_spread")
+            spread = bank(2 + half, "ts_spread_%d" % half)
             for b in range(CHUNKS):
                 turn(spread[:, b, :], ts_of_chunk(half, b).to_broadcast([P, P]))
             nc.scalar.copy(ts_rows[:, half_cols(half)], flat(spread[:]))
+        neg_us = keep.tile([P, PACK], F32, name="neg_us")
+        nc.scalar.activation(neg_us[:], us_sb[:], ACT.Copy, scale=-1.0)
+        q_codes = keep.tile([P, R], U32, name="q_codes", align_bytes=64)
+        q_scales = keep.tile([P, R], U8, name="q_scales", align_bytes=64)
+        k_codes = [keep.tile([P, HALF], U32, name="k_codes_0", align_bytes=64), placed([P, HALF], U32, AT_Q_RAW + 6, "k_codes_1")]
+        k_scales = [keep.tile([P, HALF], U8, name="k_scales_%d" % half, align_bytes=64) for half in range(2)]
+        for half in range(2):
+            gather_keys(1, half)
+            if half == 1:
+                nc.vector.quantize_mx(
+                    out=q_codes[:].bitcast(E4M3), scales=q_scales[:], in_=q_grouped[:].rearrange("p j m t -> p (j m t)")
+                )
+            nc.vector.quantize_mx(out=k_codes[half][:].bitcast(E4M3), scales=k_scales[half][:], in_=k_grouped[half][:])
 
         e_sb = [placed([P, C], F32, AT_E + 4 * j, "e_%d" % j) for j in range(PACK)]
 
@@ -194,132 +187,175 @@ def tile_attend_gblkatt_kernel(tc, qT, kT, us, ts, wb, dp, offs, blkoffs, slotof
         def exp_into_e(j, half, src):
             nc.scalar.activation(e_sb[j][:, half_cols(half)], src, ACT.Exp, scale=us_sb[:, j : j + 1])
 
-        def weights_direct(j, scaled):
-            rows = chunk_cols(j)
-            for half in range(2):
-                product = bank("sum", "scores_direct")
-                scores(flat(product[:]), q_codes[:, rows], q_scales[:, rows], k_codes[half][:], k_scales[half][:])
-                part = flat(scaled[:, half, :, :])
-                nc.vector.tensor_tensor(part, flat(product[:]), ts_rows[:, half_cols(half)], ALU.mult)
-                exp_into_e(j, half, part)
+        scaled_first = keep.tile([P, C], F32, name="scaled_first")
+        scaled_turned = {}
 
-        def weights_turned(j, scaled):
-            rows = chunk_cols(j)
+        def first_tile(half):
+            product = bank(half, "scores_direct_%d" % half)
+            scores(flat(product[:]), q_codes[:, :P], q_scales[:, :P], k_codes[half][:], k_scales[half][:])
+            part = scaled_first[:, half_cols(half)]
+            nc.vector.tensor_tensor(part, flat(product[:]), ts_rows[:, half_cols(half)], ALU.mult)
+            exp_into_e(0, half, part)
+
+        def turned_scores(half):
+            for b in range(CHUNKS):
+                product = flat(bank(4 + b, "scores_turned_%d_%d" % (half, b))[:])
+                cols = chunk_cols(b)
+                for rows in (slice(P, 2 * P), slice(2 * P, R)):
+                    dst = product[:, rows.start - P : rows.stop - P]
+                    scores(dst, k_codes[half][:, cols], k_scales[half][:, cols], q_codes[:, rows], q_scales[:, rows])
+                tile = placed([P, TURNED_ROWS], F32, AT_K_PAIRS + 8 * half + 1.5 * b, "scaled_turned_%d_%d" % (half, b))
+                nc.scalar.activation(tile[:], product[:, :TURNED_ROWS], ACT.Copy, scale=ts_of_chunk(half, b))
+                scaled_turned[(half, b)] = tile
+
+        def turned_tile(j):
             for half in range(2):
-                product = bank("sum", "scores_turned")
+                back = bank((2 * j + half) % 4, "scores_back_%d_%d" % (j, half))
                 for b in range(CHUNKS):
-                    cols = chunk_cols(b)
-                    scores(
-                        product[:, b, :], k_codes[half][:, cols], k_scales[half][:, cols],
-                        q_codes[:, rows], q_scales[:, rows],
-                    )
-                for b in range(CHUNKS):
-                    nc.scalar.activation(scaled[:, half, b, :], product[:, b, :], ACT.Copy, scale=ts_of_chunk(half, b))
-            for half in range(2):
-                back = bank("back", "scores_back")
-                for b in range(CHUNKS):
-                    turn(back[:, b, :], scaled[:, half, b, :])
+                    turn(back[:, b, :], scaled_turned[(half, b)][:, chunk_cols(j - 1)])
                 exp_into_e(j, half, flat(back[:]))
 
-        for j in range(PACK):
-            if j == LAST:
-                scaled = placed([P, 2, CHUNKS, P], F32, AT_Q_RAW, "scaled_last")
-            else:
-                scaled = rotating([P, 2, CHUNKS, P], "scaled", 2, "scaled_%d" % j)
-            if j < DIRECT_TILES:
-                weights_direct(j, scaled)
-            else:
-                weights_turned(j, scaled)
+        f_sb = [placed([P, C], F32, AT_F + 4 * j, "f_%d" % j) for j in range(PACK)]
+        e_slots, f_slots = {}, {}
 
-        e_slots, f_sb = [], []
-        for j in range(PACK):
-            picked = rotating([P, C], "slots", PACK, "e_slots_%d" % j)
+        def by_slots(window, place, name):
+            picked = placed([P, C], F32, AT_SLOTS + 4 * place, name)
             for half in range(2):
-                nc.vector.tensor_copy(picked[:, half_cols(half)], e_sb[j][:].indirect(half_list(slot_list, half)))
-            e_slots.append(picked[:].rearrange("p (x i) -> p x i", i=2))
-            f_sb.append(placed([P, C], F32, AT_F + 4 * j, "f_%d" % j))
+                nc.vector.tensor_copy(picked[:, half_cols(half)], window[:].indirect(half_list(slot_list, half)))
+            return picked[:].rearrange("p (x i) -> p x i", i=2)
+
+        def form_f(j):
             nc.gpsimd.tensor_tensor(f_sb[j][:], e_sb[j][:], dp_sb[j][:], ALU.mult)
 
-        root = placed([P, PACK, X], F32, AT_Q_RAW, "root")
-        inverse = []
-        for j in range(PACK):
-            if j == 0:
-                sums = placed([P, X], F32, AT_SUMS, "sums")
-                nc.vector.tensor_reduce(sums[:], e_slots[j], mybir.AxisListType.X, ALU.add)
-                nc.scalar.activation(root[:, j, :], sums[:], ACT.Abs_reciprocal_sqrt)
-                roots = root[:, j, :]
-            else:
-                sums_turned = bank("back", "sums_turned")
-                for b in range(CHUNKS):
-                    for i in range(2):
-                        turn(sums_turned[:, b, :], e_slots[j][:, chunk_cols(b), i], start=(i == 0), stop=(i == 1))
-                nc.scalar.activation(root[:, j, :], flat(sums_turned[:]), ACT.Abs_reciprocal_sqrt)
-                root_back = bank("sum", "root_back")
-                for b in range(CHUNKS):
-                    turn(root_back[:, b, :], root[:, j, chunk_cols(b)])
-                roots = flat(root_back[:])
-            inverse.append(placed([P, X, 2], F32, AT_INVERSE + 4 * j, "inverse_%d" % j))
-            nc.scalar.activation(inverse[j][:], roots.unsqueeze(2).to_broadcast([P, X, 2]), ACT.Square)
+        def pair_sums_turned(pairs, index, name):
+            sums = bank(index, name)
+            for b in range(CHUNKS):
+                for i in range(2):
+                    turn(sums[:, b, :], pairs[:, chunk_cols(b), i], start=(i == 0), stop=(i == 1))
+            return flat(sums[:])
+
+        def turn_back(src, index, name):
+            back = bank(index, name)
+            for b in range(CHUNKS):
+                turn(back[:, b, :], src[:, chunk_cols(b)])
+            return flat(back[:])
 
         q_words = q_grouped[:].rearrange("p j m t -> p (j m t)").bitcast(F32).rearrange("p (j m u) -> p j m u", j=PACK, u=2)
         q2_grouped = keep.tile([P, PACK, P, PACK], BF16, name="q2_grouped", align_bytes=64)
         q2_codes = keep.tile([P, D], U32, name="q2_codes", align_bytes=64)
         q2_scales = keep.tile([P, D], U8, name="q2_scales", align_bytes=64)
         for u in range(2):
-            q_turned = bank("sum", "q_turned")
+            q_turned = bank(4 + u, "q_turned_%d" % u)
             for j in range(PACK):
                 turn(q_turned[:, j, :], q_words[:, j, :, u])
             nc.scalar.copy(
                 q2_grouped[:, 2 * u : 2 * u + 2, :, :],
                 flat(q_turned[:]).bitcast(BF16).rearrange("m (j p e) -> m e p j", j=PACK, e=2),
             )
+        for half in range(2):
+            first_tile(half)
         nc.vector.quantize_mx(
             out=q2_codes[:].bitcast(E4M3), scales=q2_scales[:], in_=q2_grouped[:].rearrange("m t p j -> m (t p j)")
         )
+        for half in range(2):
+            turned_scores(half)
+        neg_f = {0: placed([P, C], F32, AT_NEG_F[0], "neg_f_0")}
+        e_slots[0] = by_slots(e_sb[0], 0, "e_slots_0")
+        form_f(0)
+        nc.gpsimd.tensor_scalar(neg_f[0][:], f_sb[0][:], -1.0, 0.0, ALU.mult, ALU.add)
+        f_slots[0] = by_slots(f_sb[0], 1, "f_slots_0")
+        for j in range(1, PACK):
+            turned_tile(j)
+            e_slots[j] = by_slots(e_sb[j], (j + 1) % PACK, "e_slots_%d" % j)
+            form_f(j)
 
-        def block_terms(j):
-            f_over_s = rotating([P, C], "slots", PACK, "f_over_s_%d" % j)
+        root, inverse, t_turned, t_back = {}, {}, {}, {}
+
+        def take_root(j, index):
+            sums = pair_sums_turned(e_slots[j], index, "s_turned_%d" % j)
+            root[j] = placed([P, X], F32, AT_K_PAIRS + 8 + 2 * j, "root_%d" % j)
+            nc.scalar.activation(root[j][:], sums, ACT.Abs_reciprocal_sqrt)
+
+        def take_inverse(j, index):
+            back = turn_back(root[j], index, "root_back_%d" % j)
+            inverse[j] = placed([P, X], F32, AT_K_GROUPED + 2 * j, "inverse_%d" % j)
+            nc.scalar.activation(inverse[j][:], back, ACT.Square)
+            nc.gpsimd.tensor_tensor(h_window[j][:, :X], inverse[j][:], wb_sb[:, j, :], ALU.mult)
+
+        def sum_f(j, index, index_back):
+            sums = pair_sums_turned(f_slots[j], index, "t_turned_%d" % j)
+            t_turned[j] = placed([P, X], F32, AT_T_TURNED + 2 * (j % 2), "t_turned_sb_%d" % j)
+            nc.scalar.copy(t_turned[j][:], sums)
+            t_back[j] = turn_back(t_turned[j], index_back, "t_back_%d" % j)
+
+        def negate_f(j):
+            neg_f[j] = placed([P, C], F32, AT_NEG_F[j], "neg_f_%d" % j)
             for half in range(2):
-                cols = half_cols(half)
-                nc.vector.tensor_tensor(
-                    f_over_s[:, cols], f_sb[j][:].indirect(half_list(slot_list, half)), flat(inverse[j][:])[:, cols], ALU.mult
-                )
-            nc.vector.tensor_tensor(h_window[j][:, :X], inverse[j][:, :, 0], wb_sb[:, j, :], ALU.mult)
-            pairs = f_over_s[:].rearrange("p (x i) -> p x i", i=2)
-            nc.vector.tensor_tensor(m_window[j][:, :X], pairs[:, :, 0], pairs[:, :, 1], ALU.add)
-            nc.scalar.activation(f_sb[j][:], f_sb[j][:], ACT.Copy, scale=-1.0)
+                nc.scalar.activation(neg_f[j][:, half_cols(half)], f_sb[j][:, half_cols(half)], ACT.Copy, scale=-1.0)
 
-        centred_back, factor, g_planes = {}, {}, {}
+        take_root(0, 7)
+        sum_f(0, 0, 1)
+        take_root(1, 3)
+        take_inverse(0, 4)
+        t_first = placed([P, X], F32, AT_T_FIRST, "t_first")
+        nc.scalar.copy(t_first[:], t_back[0])
+        nc.gpsimd.tensor_tensor(m_window[0][:, :X], t_first[:], inverse[0][:], ALU.mult)
+        take_root(2, 7)
+        take_inverse(1, 5)
+        negate_f(3)
+        take_root(3, 4)
+        take_inverse(2, 2)
+        for j in range(1, PACK):
+            f_slots[j] = by_slots(f_sb[j], j, "f_slots_%d" % j)
+        sum_f(1, 5, 0)
+        take_inverse(3, 6)
 
-        def centred(half, j):
-            e_m = rotating([P, HALF], "e_m", PACK, "e_m_%d_%d" % (half, j))
+        sum_f(2, 5, 1)
+        negate_f(1)
+
+        def form_m(j):
+            nc.vector.tensor_tensor(m_window[j][:, :X], t_back[j], inverse[j][:], ALU.mult)
+
+        e_m, factor, g_planes = {}, {}, {}
+        at_e_m = {(0, 0): AT_SLOTS + 12, (0, 1): AT_SLOTS + 14, (0, 2): AT_T_TURNED + 2, (0, 3): AT_F + 10, (1, 0): AT_SLOTS + 14, (1, 1): AT_T_TURNED + 2}
+        at_factor = {(0, j): AT_K_PAIRS + 2 * j for j in range(PACK)}
+        at_factor.update({(1, j): AT_DP + 8 + 2 * j for j in range(PACK)})
+        at_g_planes = (AT_WB, AT_K_GROUPED)
+
+        def look_up_m(half, j):
+            if (half, j) == (1, 2):
+                both = placed([P, 2, HALF], F32, AT_K_PAIRS + 4, "e_m_late")
+                e_m[(1, 2)], e_m[(1, 3)] = both[:, 0, :], both[:, 1, :]
+            elif (half, j) != (1, 3):
+                e_m[(half, j)] = placed([P, HALF], F32, at_e_m[(half, j)], "e_m_%d_%d" % (half, j))[:]
             nc.vector.tensor_tensor(
-                e_m[:], m_window[j][:].indirect(half_list(blk_list, half)), e_sb[j][:, half_cols(half)], ALU.mult
+                e_m[(half, j)], m_window[j][:].indirect(half_list(blk_list, half)), e_sb[j][:, half_cols(half)], ALU.mult
             )
-            turned = bank("fwd", "centred_turned")
-            with_ts = rotating([P, CHUNKS, P], "with_ts", 2, "with_ts_%d_%d" % (half, j))
+
+        centred_back = {}
+
+        def centre(half, j):
+            turned = bank(2 + j % 2, "centred_turned_%d_%d" % (half, j))
+            with_ts = placed([P, CHUNKS, P], F32, AT_WITH_TS + 2 * (j % 2), "with_ts_%d_%d" % (half, j))
             for b in range(CHUNKS):
-                turn(turned[:, b, :], e_m[:, chunk_cols(b)], start=True, stop=False)
-                turn(turned[:, b, :], f_sb[j][:, chunk_cols(half * CHUNKS + b)], start=False, stop=True)
+                turn(turned[:, b, :], e_m[(half, j)][:, chunk_cols(b)], start=True, stop=False)
+                turn(turned[:, b, :], neg_f[j][:, chunk_cols(half * CHUNKS + b)], start=False, stop=True)
             for b in range(CHUNKS):
                 nc.scalar.activation(with_ts[:, b, :], turned[:, b, :], ACT.Copy, scale=ts_of_chunk(half, b))
-            centred_back[(half, j)] = bank("back", "centred_back")
-            for b in range(CHUNKS):
-                turn(centred_back[(half, j)][:, b, :], with_ts[:, b, :])
+            centred_back[(half, j)] = turn_back(flat(with_ts[:]), 4 + j % 2, "centred_back_%d_%d" % (half, j))
 
         def fetch_factor(half, j):
-            name = "factor_%d_%d" % (half, j)
-            if j == LAST:
-                factor[(half, j)] = placed([P, HALF], F32, AT_G_PLANES + 8 * (1 - half), name)
-            else:
-                factor[(half, j)] = rotating([P, HALF], "factor", 2 * LAST, name)
-            nc.scalar.activation(
-                factor[(half, j)][:], flat(centred_back[(half, j)][:]), ACT.Copy, scale=neg_us[:, j : j + 1]
-            )
+            factor[(half, j)] = placed([P, HALF], F32, at_factor[(half, j)], "factor_%d_%d" % (half, j))
+            nc.scalar.activation(factor[(half, j)][:], centred_back[(half, j)], ACT.Copy, scale=neg_us[:, j : j + 1])
+
+        def front(half, j):
+            look_up_m(half, j)
+            centre(half, j)
+            fetch_factor(half, j)
 
         def gradient(half, j):
             if j == 0:
-                g_planes[half] = placed([P, PACK, HALF], F32, AT_G_PLANES + 8 * half, "g_planes_%d" % half)
+                g_planes[half] = placed([P, PACK, HALF], F32, at_g_planes[half], "g_planes_%d" % half)
             nc.vector.tensor_tensor(
                 g_planes[half][:, j, :], h_window[j][:].indirect(half_list(blk_list, half)), factor[(half, j)][:], ALU.mult
             )
@@ -328,7 +364,7 @@ def tile_attend_gblkatt_kernel(tc, qT, kT, us, ts, wb, dp, offs, blkoffs, slotof
         g_scales = [keep.tile([P, HALF], U8, name="g_scales_%d" % half, align_bytes=64) for half in range(2)]
 
         def quantize_gradient(half):
-            g_grouped = placed([P, HALF, PACK], BF16, AT_G_GROUPED + 4 * half, "g_grouped_%d" % half)
+            g_grouped = placed([P, HALF, PACK], BF16, AT_Q_RAW + 4 * half, "g_grouped_%d" % half)
             nc.scalar.activation(
                 g_grouped[:].rearrange("p (c i) j -> p c j i", i=4),
                 g_planes[half][:].rearrange("p j (c i) -> p c j i", i=4),
@@ -339,7 +375,7 @@ def tile_attend_gblkatt_kernel(tc, qT, kT, us, ts, wb, dp, offs, blkoffs, slotof
         out_rows = out.rearrange("(p t) n -> t p n", t=PACK)
 
         def place_result(t, half):
-            product = bank("blk", "dk")
+            product = bank((3, 5, 4, 1, 0, 1, 0, 0)[t + PACK * half], "dk_psum_%d_%d" % (t, half))
             nc.tensor.matmul_mx(
                 out=flat(product[:]),
                 lhsT=q2_codes[:, chunk_cols(t)].bitcast(E4M3),
@@ -351,35 +387,37 @@ def tile_attend_gblkatt_kernel(tc, qT, kT, us, ts, wb, dp, offs, blkoffs, slotof
             )
             name = "dk_%d_%d" % (t, half)
             if (t, half) == (OUT_WINDOWS - 1, 0):
-                dk = placed([P, HALF], F32, AT_G_PLANES + 8, name)
+                dk = placed([P, HALF], F32, at_g_planes[1], name)
             else:
-                dk = rotating([P, HALF], "slots", PACK, name)
+                dk = placed([P, HALF], F32, AT_SLOTS + 2 * (t + PACK * half), name)
             nc.scalar.copy(dk[:], flat(product[:]))
             window = out_window[t % OUT_WINDOWS]
             nc.vector.tensor_copy(window[:].indirect(half_list(tok_list, half)), dk[:])
             if half == 1:
                 nc.sync.dma_start(out=out_rows[t], in_=window[:])
 
-        def front(half, j):
-            centred(half, j)
-            fetch_factor(half, j)
-
-        for j in range(PACK):
-            block_terms(j)
-            if 1 <= j < LAST:
-                for half in range(2):
-                    front(half, j - 1)
-        front(0, LAST - 1)
-        front(0, LAST)
-        front(1, LAST - 1)
-        centred(1, LAST)
+        form_m(1)
+        form_m(2)
+        sum_f(3, 5, 7)
+        negate_f(2)
+        front(0, 0)
+        front(0, 1)
+        front(0, 2)
+        form_m(3)
+        front(0, 3)
+        front(1, 0)
+        front(1, 1)
         for j in range(PACK):
             gradient(0, j)
-        for j in range(LAST):
-            gradient(1, j)
+        look_up_m(1, 2)
+        look_up_m(1, 3)
         quantize_gradient(0)
-        fetch_factor(1, LAST)
-        gradient(1, LAST)
+        centre(1, 2)
+        fetch_factor(1, 2)
+        centre(1, 3)
+        fetch_factor(1, 3)
+        for j in range(PACK):
+            gradient(1, j)
         place_result(0, 0)
         quantize_gradient(1)
         for t in range(1, OUT_WINDOWS):

@@ -32,10 +32,10 @@ OUT_WINDOWS = 3
 TURNED_ROWS = R - P
 
 AT_TS, AT_K_PAIRS, AT_K_GROUPED, AT_Q_RAW, AT_E, AT_K_LATE, AT_BLK, AT_DP, AT_WB = 0, 8, 24, 32, 40, 56, 72, 89, 105
-AT_F, AT_SLOTS, AT_WITH_TS, AT_T_TURNED, AT_T_FIRST, AT_SPARE = 113, 129, 145, 149, 153, 155
+AT_F, AT_SLOTS, AT_WITH_TS, AT_T_TURNED, AT_T_FIRST, AT_SPARE, AT_S_FIRST = 113, 129, 145, 149, 153, 155, 159
 BLK_WINDOW_KIB = 2.125
 AT_K_RAW = (AT_BLK, AT_K_LATE)
-AT_NEG_F = (AT_K_LATE, AT_SLOTS + 4, AT_SLOTS + 8, AT_SPARE)
+AT_NEG_F = (AT_S_FIRST, AT_SLOTS + 4, AT_SLOTS + 8, AT_SPARE)
 BANK_BYTES = 2048
 
 
@@ -259,10 +259,11 @@ def tile_attend_gblkatt_kernel(tc, qT, kT, us, ts, wb, dp, offs, blkoffs, slotof
         )
         for half in range(2):
             turned_scores(half)
-        neg_f = {0: placed([P, C], F32, AT_NEG_F[0], "neg_f_0")}
+        neg_f = {}
         e_slots[0] = by_slots(e_sb[0], 0, "e_slots_0")
         form_f(0)
-        nc.gpsimd.tensor_scalar(neg_f[0][:], f_sb[0][:], -1.0, 0.0, ALU.mult, ALU.add)
+        s_first = placed([P, X], F32, AT_S_FIRST, "s_first")
+        nc.gpsimd.tensor_tensor(s_first[:], e_slots[0][:, :, 0], e_slots[0][:, :, 1], ALU.add)
         f_slots[0] = by_slots(f_sb[0], 1, "f_slots_0")
         for j in range(1, PACK):
             turned_tile(j)
@@ -272,12 +273,12 @@ def tile_attend_gblkatt_kernel(tc, qT, kT, us, ts, wb, dp, offs, blkoffs, slotof
         root, inverse, t_turned, t_back = {}, {}, {}, {}
 
         def take_root(j, index):
-            sums = pair_sums_turned(e_slots[j], index, "s_turned_%d" % j)
-            root[j] = placed([P, X], F32, AT_K_PAIRS + 8 + 2 * j, "root_%d" % j)
+            sums = s_first[:] if j == 0 else pair_sums_turned(e_slots[j], index, "s_turned_%d" % j)
+            root[j] = placed([P, X], F32, AT_K_PAIRS + 8 + 2 * ((j + 2) % PACK), "root_%d" % j)
             nc.scalar.activation(root[j][:], sums, ACT.Abs_reciprocal_sqrt)
 
         def take_inverse(j, index):
-            back = turn_back(root[j], index, "root_back_%d" % j)
+            back = root[j][:] if j == 0 else turn_back(root[j], index, "root_back_%d" % j)
             inverse[j] = placed([P, X], F32, AT_K_GROUPED + 2 * j, "inverse_%d" % j)
             nc.scalar.activation(inverse[j][:], back, ACT.Square)
             nc.gpsimd.tensor_tensor(h_window[j][:, :X], inverse[j][:], wb_sb[:, j, :], ALU.mult)
@@ -293,38 +294,40 @@ def tile_attend_gblkatt_kernel(tc, qT, kT, us, ts, wb, dp, offs, blkoffs, slotof
             for half in range(2):
                 nc.scalar.activation(neg_f[j][:, half_cols(half)], f_sb[j][:, half_cols(half)], ACT.Copy, scale=-1.0)
 
-        take_root(0, 7)
-        sum_f(0, 0, 1)
-        take_root(1, 3)
-        take_inverse(0, 4)
+        take_root(0, None)
+        take_inverse(0, None)
+        sum_f(0, 0, 5)
+        take_root(1, 1)
         t_first = placed([P, X], F32, AT_T_FIRST, "t_first")
         nc.scalar.copy(t_first[:], t_back[0])
         nc.gpsimd.tensor_tensor(m_window[0][:, :X], t_first[:], inverse[0][:], ALU.mult)
         take_root(2, 7)
-        take_inverse(1, 5)
+        take_inverse(1, 4)
         negate_f(3)
-        take_root(3, 4)
-        take_inverse(2, 2)
+        take_root(3, 1)
+        take_inverse(2, 6)
+        take_inverse(3, 4)
+        negate_f(0)
         for j in range(1, PACK):
             f_slots[j] = by_slots(f_sb[j], j, "f_slots_%d" % j)
-        sum_f(1, 5, 0)
-        take_inverse(3, 6)
-
-        sum_f(2, 5, 1)
+        sum_f(1, 1, 0)
         negate_f(1)
+        sum_f(2, 6, 5)
+        negate_f(2)
 
         def form_m(j):
             nc.vector.tensor_tensor(m_window[j][:, :X], t_back[j], inverse[j][:], ALU.mult)
 
         e_m, factor, g_planes = {}, {}, {}
-        at_e_m = {(0, 0): AT_SLOTS + 12, (0, 1): AT_SLOTS + 14, (0, 2): AT_T_TURNED + 2, (0, 3): AT_F + 10, (1, 0): AT_SLOTS + 14, (1, 1): AT_T_TURNED + 2}
+        units = [(0, 0), (0, 3), (0, 1), (0, 2), (1, 0), (1, 1), (1, 2), (1, 3)]
+        at_e_m = {(0, 0): AT_DP, (0, 3): AT_T_TURNED + 2, (0, 1): AT_DP + 2, (1, 0): AT_T_TURNED, (0, 2): AT_DP + 4, (1, 1): AT_K_GROUPED + 4}
         at_factor = {(0, j): AT_K_PAIRS + 2 * j for j in range(PACK)}
         at_factor.update({(1, j): AT_DP + 8 + 2 * j for j in range(PACK)})
-        at_g_planes = (AT_WB, AT_K_GROUPED)
+        at_g_planes = (AT_WB, AT_Q_RAW)
 
         def look_up_m(half, j):
             if (half, j) == (1, 2):
-                both = placed([P, 2, HALF], F32, AT_K_PAIRS + 4, "e_m_late")
+                both = placed([P, 2, HALF], F32, AT_K_PAIRS + 2, "e_m_late")
                 e_m[(1, 2)], e_m[(1, 3)] = both[:, 0, :], both[:, 1, :]
             elif (half, j) != (1, 3):
                 e_m[(half, j)] = placed([P, HALF], F32, at_e_m[(half, j)], "e_m_%d_%d" % (half, j))[:]
@@ -335,14 +338,15 @@ def tile_attend_gblkatt_kernel(tc, qT, kT, us, ts, wb, dp, offs, blkoffs, slotof
         centred_back = {}
 
         def centre(half, j):
-            turned = bank(2 + j % 2, "centred_turned_%d_%d" % (half, j))
-            with_ts = placed([P, CHUNKS, P], F32, AT_WITH_TS + 2 * (j % 2), "with_ts_%d_%d" % (half, j))
+            side = units.index((half, j)) % 2
+            turned = bank(1 + 5 * side, "centred_turned_%d_%d" % (half, j))
+            with_ts = placed([P, CHUNKS, P], F32, AT_WITH_TS + 2 * side, "with_ts_%d_%d" % (half, j))
             for b in range(CHUNKS):
                 turn(turned[:, b, :], e_m[(half, j)][:, chunk_cols(b)], start=True, stop=False)
                 turn(turned[:, b, :], neg_f[j][:, chunk_cols(half * CHUNKS + b)], start=False, stop=True)
             for b in range(CHUNKS):
                 nc.scalar.activation(with_ts[:, b, :], turned[:, b, :], ACT.Copy, scale=ts_of_chunk(half, b))
-            centred_back[(half, j)] = turn_back(flat(with_ts[:]), 4 + j % 2, "centred_back_%d_%d" % (half, j))
+            centred_back[(half, j)] = turn_back(flat(with_ts[:]), 4 + 3 * side, "centred_back_%d_%d" % (half, j))
 
         def fetch_factor(half, j):
             factor[(half, j)] = placed([P, HALF], F32, at_factor[(half, j)], "factor_%d_%d" % (half, j))
@@ -364,7 +368,7 @@ def tile_attend_gblkatt_kernel(tc, qT, kT, us, ts, wb, dp, offs, blkoffs, slotof
         g_scales = [keep.tile([P, HALF], U8, name="g_scales_%d" % half, align_bytes=64) for half in range(2)]
 
         def quantize_gradient(half):
-            g_grouped = placed([P, HALF, PACK], BF16, AT_Q_RAW + 4 * half, "g_grouped_%d" % half)
+            g_grouped = placed([P, HALF, PACK], BF16, (AT_Q_RAW, AT_K_GROUPED)[half], "g_grouped_%d" % half)
             nc.scalar.activation(
                 g_grouped[:].rearrange("p (c i) j -> p c j i", i=4),
                 g_planes[half][:].rearrange("p j (c i) -> p c j i", i=4),
@@ -375,7 +379,7 @@ def tile_attend_gblkatt_kernel(tc, qT, kT, us, ts, wb, dp, offs, blkoffs, slotof
         out_rows = out.rearrange("(p t) n -> t p n", t=PACK)
 
         def place_result(t, half):
-            product = bank((3, 5, 4, 1, 0, 1, 0, 0)[t + PACK * half], "dk_psum_%d_%d" % (t, half))
+            product = bank((6, 7, 4, 3, 3, 3, 3, 3)[t + PACK * half], "dk_psum_%d_%d" % (t, half))
             nc.tensor.matmul_mx(
                 out=flat(product[:]),
                 lhsT=q2_codes[:, chunk_cols(t)].bitcast(E4M3),
@@ -396,28 +400,33 @@ def tile_attend_gblkatt_kernel(tc, qT, kT, us, ts, wb, dp, offs, blkoffs, slotof
             if half == 1:
                 nc.sync.dma_start(out=out_rows[t], in_=window[:])
 
-        form_m(1)
-        form_m(2)
-        sum_f(3, 5, 7)
-        negate_f(2)
-        front(0, 0)
-        front(0, 1)
-        front(0, 2)
+        look_up_m(0, 0)
+        t_last = placed([P, X], F32, AT_T_FIRST, "t_last")
+        nc.vector.tensor_tensor(t_last[:], f_slots[LAST][:, :, 0], f_slots[LAST][:, :, 1], ALU.add)
+        t_back[LAST] = t_last[:]
         form_m(3)
-        front(0, 3)
-        front(1, 0)
-        front(1, 1)
-        for j in range(PACK):
+        form_m(1)
+        look_up_m(0, 3)
+        look_up_m(0, 1)
+        form_m(2)
+        look_up_m(1, 0)
+        look_up_m(0, 2)
+        look_up_m(1, 1)
+        for half, j in units[:6]:
+            centre(half, j)
+            fetch_factor(half, j)
+        for j in (0, 3, 1, 2):
             gradient(0, j)
         look_up_m(1, 2)
         look_up_m(1, 3)
         quantize_gradient(0)
-        centre(1, 2)
-        fetch_factor(1, 2)
-        centre(1, 3)
-        fetch_factor(1, 3)
-        for j in range(PACK):
-            gradient(1, j)
+        gradient(1, 0)
+        gradient(1, 1)
+        for half, j in units[6:]:
+            centre(half, j)
+            fetch_factor(half, j)
+        gradient(1, 2)
+        gradient(1, 3)
         place_result(0, 0)
         quantize_gradient(1)
         for t in range(1, OUT_WINDOWS):

@@ -29,13 +29,11 @@ Q_PIECE = R // 2
 BLK_WINDOW = X + 8
 QUADRANT = 32
 OUT_WINDOWS = 3
-TURNED_ROWS = R - P
 
 AT_TS, AT_K_PAIRS, AT_K_GROUPED, AT_Q_RAW, AT_E, AT_K_LATE, AT_BLK, AT_DP, AT_WB = 0, 8, 24, 32, 40, 56, 72, 89, 105
-AT_F, AT_SLOTS, AT_WITH_TS, AT_T_TURNED, AT_T_FIRST, AT_SPARE, AT_S_FIRST = 113, 129, 145, 149, 153, 155, 159
+AT_F, AT_SLOTS, AT_WITH_TS, AT_M_TURNED, AT_INVERSE = 113, 129, 145, 149, 153
 BLK_WINDOW_KIB = 2.125
 AT_K_RAW = (AT_BLK, AT_K_LATE)
-AT_NEG_F = (AT_S_FIRST, AT_SLOTS + 4, AT_SLOTS + 8, AT_SPARE)
 BANK_BYTES = 2048
 
 
@@ -197,31 +195,43 @@ def tile_attend_gblkatt_kernel(tc, qT, kT, us, ts, wb, dp, offs, blkoffs, slotof
             nc.vector.tensor_tensor(part, flat(product[:]), ts_rows[:, half_cols(half)], ALU.mult)
             exp_into_e(0, half, part)
 
-        def turned_scores(half):
-            for b in range(CHUNKS):
-                product = flat(bank(4 + b, "scores_turned_%d_%d" % (half, b))[:])
-                cols = chunk_cols(b)
-                for rows in (slice(P, 2 * P), slice(2 * P, R)):
-                    dst = product[:, rows.start - P : rows.stop - P]
-                    scores(dst, k_codes[half][:, cols], k_scales[half][:, cols], q_codes[:, rows], q_scales[:, rows])
-                tile = placed([P, TURNED_ROWS], F32, AT_K_PAIRS + 8 * half + 1.5 * b, "scaled_turned_%d_%d" % (half, b))
-                nc.scalar.activation(tile[:], product[:, :TURNED_ROWS], ACT.Copy, scale=ts_of_chunk(half, b))
-                scaled_turned[(half, b)] = tile
+        def turned_scores(tiles, half, first, index, kib):
+            rows = slice(tiles[0] * P, (tiles[-1] + 1) * P)
+            width = len(tiles) * P
+            product = flat(bank(index, "scores_turned_%d_%d_%d" % (tiles[0], half, first))[:])
+            count = HALF // width
+            for n in range(count):
+                cols = chunk_cols(first + n)
+                scores(
+                    product[:, n * width : (n + 1) * width], k_codes[half][:, cols], k_scales[half][:, cols],
+                    q_codes[:, rows], q_scales[:, rows],
+                )
+            for n in range(count):
+                name = "scaled_turned_%d_%d_%d" % (tiles[0], half, first + n)
+                tile = placed([P, width], F32, kib + n * width * 4 / 1024, name)
+                nc.scalar.activation(tile[:], product[:, n * width : (n + 1) * width], ACT.Copy, scale=ts_of_chunk(half, first + n))
+                for i, j in enumerate(tiles):
+                    scaled_turned[(j, half, first + n)] = tile[:, chunk_cols(i)]
 
-        def turned_tile(j):
+        def turned_tile(j, indices):
             for half in range(2):
-                back = bank((2 * j + half) % 4, "scores_back_%d_%d" % (j, half))
+                back = bank(indices[half], "scores_back_%d_%d" % (j, half))
                 for b in range(CHUNKS):
-                    turn(back[:, b, :], scaled_turned[(half, b)][:, chunk_cols(j - 1)])
+                    turn(back[:, b, :], scaled_turned[(j, half, b)])
                 exp_into_e(j, half, flat(back[:]))
 
         f_sb = [placed([P, C], F32, AT_F + 4 * j, "f_%d" % j) for j in range(PACK)]
         e_slots, f_slots = {}, {}
 
-        def by_slots(window, place, name):
-            picked = placed([P, C], F32, AT_SLOTS + 4 * place, name)
+        def by_slots(window, kib, name, other=None):
+            picked = placed([P, C], F32, kib, name)
             for half in range(2):
-                nc.vector.tensor_copy(picked[:, half_cols(half)], window[:].indirect(half_list(slot_list, half)))
+                cols = half_cols(half)
+                looked_up = window[:].indirect(half_list(slot_list, half))
+                if other is None:
+                    nc.vector.tensor_copy(picked[:, cols], looked_up)
+                else:
+                    nc.vector.tensor_tensor(picked[:, cols], looked_up, other[:, cols], ALU.mult)
             return picked[:].rearrange("p (x i) -> p x i", i=2)
 
         def form_f(j):
@@ -258,69 +268,89 @@ def tile_attend_gblkatt_kernel(tc, qT, kT, us, ts, wb, dp, offs, blkoffs, slotof
             out=q2_codes[:].bitcast(E4M3), scales=q2_scales[:], in_=q2_grouped[:].rearrange("m t p j -> m (t p j)")
         )
         for half in range(2):
-            turned_scores(half)
-        neg_f = {}
-        e_slots[0] = by_slots(e_sb[0], 0, "e_slots_0")
+            turned_scores([1], half, 0, 4 + half, AT_K_PAIRS + 2 * half)
+        e_slots[0] = by_slots(e_sb[0], AT_SLOTS, "e_slots_0")
         form_f(0)
-        s_first = placed([P, X], F32, AT_S_FIRST, "s_first")
-        nc.gpsimd.tensor_tensor(s_first[:], e_slots[0][:, :, 0], e_slots[0][:, :, 1], ALU.add)
-        f_slots[0] = by_slots(f_sb[0], 1, "f_slots_0")
-        for j in range(1, PACK):
-            turned_tile(j)
-            e_slots[j] = by_slots(e_sb[j], (j + 1) % PACK, "e_slots_%d" % j)
+        turned_tile(1, (2, 3))
+        e_slots[1] = by_slots(e_sb[1], AT_SLOTS + 4, "e_slots_1")
+        form_f(1)
+        for n, index in enumerate((5, 2, 3, 5)):
+            turned_scores([2, 3], n // 2, 2 * (n % 2), index, AT_K_PAIRS + 8 + 2 * n)
+        f_slots[0] = by_slots(f_sb[0], AT_Q_RAW + 4, "f_slots_0")
+        for j in (2, 3):
+            turned_tile(j, (0, 1) if j == 2 else (5, 0))
+            e_slots[j] = by_slots(e_sb[j], AT_SLOTS + 4 * j, "e_slots_%d" % j)
             form_f(j)
 
-        root, inverse, t_turned, t_back = {}, {}, {}, {}
+        root, inverse, doubled, neg_f = {}, {}, {}, {}
 
-        def take_root(j, index):
-            sums = s_first[:] if j == 0 else pair_sums_turned(e_slots[j], index, "s_turned_%d" % j)
-            root[j] = placed([P, X], F32, AT_K_PAIRS + 8 + 2 * ((j + 2) % PACK), "root_%d" % j)
+        def take_root(j, index, kib):
+            sums = pair_sums_turned(e_slots[j], index, "s_turned_%d" % j)
+            root[j] = placed([P, X], F32, kib, "root_%d" % j)
             nc.scalar.activation(root[j][:], sums, ACT.Abs_reciprocal_sqrt)
 
         def take_inverse(j, index):
-            back = root[j][:] if j == 0 else turn_back(root[j], index, "root_back_%d" % j)
-            inverse[j] = placed([P, X], F32, AT_K_GROUPED + 2 * j, "inverse_%d" % j)
-            nc.scalar.activation(inverse[j][:], back, ACT.Square)
-            nc.gpsimd.tensor_tensor(h_window[j][:, :X], inverse[j][:], wb_sb[:, j, :], ALU.mult)
+            back = turn_back(root[j], index, "root_back_%d" % j)
+            if j < 2:
+                tile = placed([P, X], F32, AT_INVERSE + 4 * j, "inverse_%d" % j)
+                nc.scalar.activation(tile[:], back, ACT.Square)
+                inverse[j] = tile[:]
+            else:
+                tile = placed([P, X, 2], F32, AT_INVERSE + 4 * j, "inverse_%d" % j)
+                nc.scalar.activation(tile[:], back.unsqueeze(2).to_broadcast([P, X, 2]), ACT.Square)
+                inverse[j], doubled[j] = tile[:, :, 0], flat(tile[:])
 
-        def sum_f(j, index, index_back):
-            sums = pair_sums_turned(f_slots[j], index, "t_turned_%d" % j)
-            t_turned[j] = placed([P, X], F32, AT_T_TURNED + 2 * (j % 2), "t_turned_sb_%d" % j)
-            nc.scalar.copy(t_turned[j][:], sums)
-            t_back[j] = turn_back(t_turned[j], index_back, "t_back_%d" % j)
+        def form_h(j):
+            nc.vector.tensor_tensor(h_window[j][:, :X], inverse[j], wb_sb[:, j, :], ALU.mult)
 
-        def negate_f(j):
-            neg_f[j] = placed([P, C], F32, AT_NEG_F[j], "neg_f_%d" % j)
+        def add_pairs(dst, pairs):
+            nc.vector.tensor_tensor(dst, pairs[:, :, 0], pairs[:, :, 1], ALU.add)
+
+        def negate_f(j, kib):
+            neg_f[j] = placed([P, C], F32, kib, "neg_f_%d" % j)
             for half in range(2):
                 nc.scalar.activation(neg_f[j][:, half_cols(half)], f_sb[j][:, half_cols(half)], ACT.Copy, scale=-1.0)
 
-        take_root(0, None)
-        take_inverse(0, None)
-        sum_f(0, 0, 5)
-        take_root(1, 1)
-        t_first = placed([P, X], F32, AT_T_FIRST, "t_first")
-        nc.scalar.copy(t_first[:], t_back[0])
-        nc.gpsimd.tensor_tensor(m_window[0][:, :X], t_first[:], inverse[0][:], ALU.mult)
-        take_root(2, 7)
-        take_inverse(1, 4)
-        negate_f(3)
-        take_root(3, 1)
-        take_inverse(2, 6)
-        take_inverse(3, 4)
-        negate_f(0)
-        for j in range(1, PACK):
-            f_slots[j] = by_slots(f_sb[j], j, "f_slots_%d" % j)
-        sum_f(1, 1, 0)
-        negate_f(1)
-        sum_f(2, 6, 5)
-        negate_f(2)
+        m_turned = {}
 
-        def form_m(j):
-            nc.vector.tensor_tensor(m_window[j][:, :X], t_back[j], inverse[j][:], ALU.mult)
+        def sum_m(j, index):
+            sums = pair_sums_turned(f_slots[j], index, "m_turned_%d" % j)
+            m_turned[j] = placed([P, X], F32, AT_M_TURNED + 2 * (j % 2), "m_turned_sb_%d" % j)
+            nc.scalar.copy(m_turned[j][:], sums)
+
+        def fetch_m(j, index):
+            nc.scalar.copy(m_window[j][:, :X], turn_back(m_turned[j], index, "m_back_%d" % j))
+
+        take_root(0, 1, AT_K_PAIRS + 14)
+        take_root(1, 5, AT_K_PAIRS + 12)
+        take_inverse(0, 7)
+        take_root(2, 1, AT_K_PAIRS + 10)
+        take_inverse(1, 2)
+        take_inverse(2, 3)
+        take_root(3, 1, AT_K_PAIRS + 8)
+        negate_f(0, AT_SLOTS + 8)
+        take_inverse(3, 7)
+        f_slots[1] = by_slots(f_sb[1], AT_SLOTS, "f_slots_1")
+        t_first = placed([P, X], F32, AT_DP + 12, "t_first")
+        add_pairs(t_first[:], f_slots[0])
+        form_h(0)
+        nc.vector.tensor_tensor(m_window[0][:, :X], t_first[:], inverse[0], ALU.mult)
+        form_h(1)
+        f_slots[2] = by_slots(f_sb[2], AT_SLOTS + 4, "f_slots_2", doubled[2])
+        form_h(2)
+        f_slots[3] = by_slots(f_sb[3], AT_K_LATE, "f_slots_3", doubled[3])
+        form_h(3)
+        sum_m(1, 1)
+        sum_m(2, 7)
+        negate_f(1, AT_SLOTS + 12)
+        t_second = turn_back(m_turned[1], 2, "t_back_1")
+        negate_f(3, AT_SLOTS)
+        fetch_m(2, 3)
+        negate_f(2, AT_SLOTS + 4)
 
         e_m, factor, g_planes = {}, {}, {}
         units = [(0, 0), (0, 3), (0, 1), (0, 2), (1, 0), (1, 1), (1, 2), (1, 3)]
-        at_e_m = {(0, 0): AT_DP, (0, 3): AT_T_TURNED + 2, (0, 1): AT_DP + 2, (1, 0): AT_T_TURNED, (0, 2): AT_DP + 4, (1, 1): AT_K_GROUPED + 4}
+        at_e_m = {(0, 0): AT_DP + 6, (0, 1): AT_DP, (0, 3): AT_DP + 2, (0, 2): AT_DP + 4, (1, 0): AT_M_TURNED, (1, 1): AT_DP}
         at_factor = {(0, j): AT_K_PAIRS + 2 * j for j in range(PACK)}
         at_factor.update({(1, j): AT_DP + 8 + 2 * j for j in range(PACK)})
         at_g_planes = (AT_WB, AT_Q_RAW)
@@ -335,7 +365,7 @@ def tile_attend_gblkatt_kernel(tc, qT, kT, us, ts, wb, dp, offs, blkoffs, slotof
                 e_m[(half, j)], m_window[j][:].indirect(half_list(blk_list, half)), e_sb[j][:, half_cols(half)], ALU.mult
             )
 
-        centred_back = {}
+        centred = {}
 
         def centre(half, j):
             side = units.index((half, j)) % 2
@@ -346,16 +376,13 @@ def tile_attend_gblkatt_kernel(tc, qT, kT, us, ts, wb, dp, offs, blkoffs, slotof
                 turn(turned[:, b, :], neg_f[j][:, chunk_cols(half * CHUNKS + b)], start=False, stop=True)
             for b in range(CHUNKS):
                 nc.scalar.activation(with_ts[:, b, :], turned[:, b, :], ACT.Copy, scale=ts_of_chunk(half, b))
-            centred_back[(half, j)] = turn_back(flat(with_ts[:]), 4 + 3 * side, "centred_back_%d_%d" % (half, j))
+            centred[(half, j)] = flat(with_ts[:])
 
         def fetch_factor(half, j):
+            side = units.index((half, j)) % 2
+            back = turn_back(centred[(half, j)], 4 + 3 * side, "centred_back_%d_%d" % (half, j))
             factor[(half, j)] = placed([P, HALF], F32, at_factor[(half, j)], "factor_%d_%d" % (half, j))
-            nc.scalar.activation(factor[(half, j)][:], centred_back[(half, j)], ACT.Copy, scale=neg_us[:, j : j + 1])
-
-        def front(half, j):
-            look_up_m(half, j)
-            centre(half, j)
-            fetch_factor(half, j)
+            nc.scalar.activation(factor[(half, j)][:], back, ACT.Copy, scale=neg_us[:, j : j + 1])
 
         def gradient(half, j):
             if j == 0:
@@ -393,7 +420,7 @@ def tile_attend_gblkatt_kernel(tc, qT, kT, us, ts, wb, dp, offs, blkoffs, slotof
             if (t, half) == (OUT_WINDOWS - 1, 0):
                 dk = placed([P, HALF], F32, at_g_planes[1], name)
             else:
-                dk = placed([P, HALF], F32, AT_SLOTS + 2 * (t + PACK * half), name)
+                dk = placed([P, HALF], F32, AT_F + 2 * (t + PACK * half), name)
             nc.scalar.copy(dk[:], flat(product[:]))
             window = out_window[t % OUT_WINDOWS]
             nc.vector.tensor_copy(window[:].indirect(half_list(tok_list, half)), dk[:])
@@ -401,32 +428,29 @@ def tile_attend_gblkatt_kernel(tc, qT, kT, us, ts, wb, dp, offs, blkoffs, slotof
                 nc.sync.dma_start(out=out_rows[t], in_=window[:])
 
         look_up_m(0, 0)
-        t_last = placed([P, X], F32, AT_T_FIRST, "t_last")
-        nc.vector.tensor_tensor(t_last[:], f_slots[LAST][:, :, 0], f_slots[LAST][:, :, 1], ALU.add)
-        t_back[LAST] = t_last[:]
-        form_m(3)
-        form_m(1)
+        add_pairs(m_window[LAST][:, :X], f_slots[LAST])
+        nc.vector.tensor_tensor(m_window[1][:, :X], t_second, inverse[1], ALU.mult)
         look_up_m(0, 3)
         look_up_m(0, 1)
-        form_m(2)
-        look_up_m(1, 0)
         look_up_m(0, 2)
+        look_up_m(1, 0)
         look_up_m(1, 1)
-        for half, j in units[:6]:
-            centre(half, j)
-            fetch_factor(half, j)
+        centre(*units[0])
+        for n in range(1, 6):
+            centre(*units[n])
+            fetch_factor(*units[n - 1])
         for j in (0, 3, 1, 2):
             gradient(0, j)
         look_up_m(1, 2)
         look_up_m(1, 3)
         quantize_gradient(0)
-        gradient(1, 0)
-        gradient(1, 1)
-        for half, j in units[6:]:
-            centre(half, j)
-            fetch_factor(half, j)
-        gradient(1, 2)
-        gradient(1, 3)
+        fetch_factor(1, 1)
+        centre(1, 2)
+        centre(1, 3)
+        fetch_factor(1, 2)
+        fetch_factor(1, 3)
+        for j in range(PACK):
+            gradient(1, j)
         place_result(0, 0)
         quantize_gradient(1)
         for t in range(1, OUT_WINDOWS):

@@ -161,13 +161,31 @@ def tile_attend_gblkatt_kernel(tc, qT, kT, us, ts, wb, dp, offs, blkoffs, slotof
         q_scales = keep.tile([P, R], U8, name="q_scales", align_bytes=64)
         k_codes = [keep.tile([P, HALF], U32, name="k_codes_0", align_bytes=64), placed([P, HALF], U32, AT_Q_RAW + 6, "k_codes_1")]
         k_scales = [keep.tile([P, HALF], U8, name="k_scales_%d" % half, align_bytes=64) for half in range(2)]
+
+        def parts_of(half):
+            return (slice(0, HALF),) if half == 0 else (slice(0, HALF // 2), slice(HALF // 2, HALF))
+
+        def quantize_queries(first, count):
+            rows = slice(first * P, (first + count) * P)
+            nc.vector.quantize_mx(
+                out=q_codes[:, rows].bitcast(E4M3),
+                scales=q_scales[:, rows],
+                in_=q_grouped[:, first : first + count, :, :].rearrange("p j m t -> p (j m t)"),
+            )
+
         for half in range(2):
             gather_keys(1, half)
-            if half == 1:
+        for half in range(2):
+            for part in parts_of(half):
                 nc.vector.quantize_mx(
-                    out=q_codes[:].bitcast(E4M3), scales=q_scales[:], in_=q_grouped[:].rearrange("p j m t -> p (j m t)")
+                    out=k_codes[half][:, part].bitcast(E4M3),
+                    scales=k_scales[half][:, part],
+                    in_=k_grouped[half][:, part.start * PACK : part.stop * PACK],
                 )
-            nc.vector.quantize_mx(out=k_codes[half][:].bitcast(E4M3), scales=k_scales[half][:], in_=k_grouped[half][:])
+            if half == 0:
+                quantize_queries(0, 1)
+        quantize_queries(1, 1)
+        quantize_queries(2, 2)
 
         e_sb = [placed([P, C], F32, AT_E + 4 * j, "e_%d" % j) for j in range(PACK)]
 
@@ -189,11 +207,12 @@ def tile_attend_gblkatt_kernel(tc, qT, kT, us, ts, wb, dp, offs, blkoffs, slotof
         scaled_turned = {}
 
         def first_tile(half):
-            product = bank(half, "scores_direct_%d" % half)
-            scores(flat(product[:]), q_codes[:, :P], q_scales[:, :P], k_codes[half][:], k_scales[half][:])
-            part = scaled_first[:, half_cols(half)]
-            nc.vector.tensor_tensor(part, flat(product[:]), ts_rows[:, half_cols(half)], ALU.mult)
-            exp_into_e(0, half, part)
+            for n, part in enumerate(parts_of(half)):
+                product = flat(bank(half + 2 * n, "scores_direct_%d_%d" % (half, n))[:])[:, part]
+                scores(product, q_codes[:, :P], q_scales[:, :P], k_codes[half][:, part], k_scales[half][:, part])
+                cols = slice(half * HALF + part.start, half * HALF + part.stop)
+                nc.vector.tensor_tensor(scaled_first[:, cols], product, ts_rows[:, cols], ALU.mult)
+                nc.scalar.activation(e_sb[0][:, cols], scaled_first[:, cols], ACT.Exp, scale=us_sb[:, 0:1])
 
         def turned_scores(tiles, half, first, index, kib):
             rows = slice(tiles[0] * P, (tiles[-1] + 1) * P)
@@ -214,7 +233,7 @@ def tile_attend_gblkatt_kernel(tc, qT, kT, us, ts, wb, dp, offs, blkoffs, slotof
                     scaled_turned[(j, half, first + n)] = tile[:, chunk_cols(i)]
 
         def turned_tile(j, indices):
-            for half in range(2):
+            for half in range(len(indices)):
                 back = bank(indices[half], "scores_back_%d_%d" % (j, half))
                 for b in range(CHUNKS):
                     turn(back[:, b, :], scaled_turned[(j, half, b)])
@@ -223,15 +242,11 @@ def tile_attend_gblkatt_kernel(tc, qT, kT, us, ts, wb, dp, offs, blkoffs, slotof
         f_sb = [placed([P, C], F32, AT_F + 4 * j, "f_%d" % j) for j in range(PACK)]
         e_slots, f_slots = {}, {}
 
-        def by_slots(window, kib, name, other=None):
+        def by_slots(window, kib, name):
             picked = placed([P, C], F32, kib, name)
             for half in range(2):
                 cols = half_cols(half)
-                looked_up = window[:].indirect(half_list(slot_list, half))
-                if other is None:
-                    nc.vector.tensor_copy(picked[:, cols], looked_up)
-                else:
-                    nc.vector.tensor_tensor(picked[:, cols], looked_up, other[:, cols], ALU.mult)
+                nc.vector.tensor_copy(picked[:, cols], window[:].indirect(half_list(slot_list, half)))
             return picked[:].rearrange("p (x i) -> p x i", i=2)
 
         def form_f(j):
@@ -267,22 +282,26 @@ def tile_attend_gblkatt_kernel(tc, qT, kT, us, ts, wb, dp, offs, blkoffs, slotof
         nc.vector.quantize_mx(
             out=q2_codes[:].bitcast(E4M3), scales=q2_scales[:], in_=q2_grouped[:].rearrange("m t p j -> m (t p j)")
         )
-        for half in range(2):
-            turned_scores([1], half, 0, 4 + half, AT_K_PAIRS + 2 * half)
+        product = flat(bank(6, "scores_direct_second")[:])
+        scores(product, q_codes[:, P : 2 * P], q_scales[:, P : 2 * P], k_codes[1][:], k_scales[1][:])
+        scaled_second = placed([P, HALF], F32, AT_K_PAIRS + 2, "scaled_second")
+        nc.vector.tensor_tensor(scaled_second[:], product, ts_rows[:, half_cols(1)], ALU.mult)
+        turned_scores([1], 0, 0, 4, AT_K_PAIRS)
         e_slots[0] = by_slots(e_sb[0], AT_SLOTS, "e_slots_0")
         form_f(0)
-        turned_tile(1, (2, 3))
+        exp_into_e(1, 1, scaled_second[:])
+        turned_tile(1, (2,))
         e_slots[1] = by_slots(e_sb[1], AT_SLOTS + 4, "e_slots_1")
         form_f(1)
-        for n, index in enumerate((5, 2, 3, 5)):
+        for n, index in enumerate((3, 4, 2, 3)):
             turned_scores([2, 3], n // 2, 2 * (n % 2), index, AT_K_PAIRS + 8 + 2 * n)
         f_slots[0] = by_slots(f_sb[0], AT_Q_RAW + 4, "f_slots_0")
         for j in (2, 3):
-            turned_tile(j, (0, 1) if j == 2 else (5, 0))
+            turned_tile(j, (0, 1) if j == 2 else (3, 0))
             e_slots[j] = by_slots(e_sb[j], AT_SLOTS + 4 * j, "e_slots_%d" % j)
             form_f(j)
 
-        root, inverse, doubled, neg_f = {}, {}, {}, {}
+        root, inverse, neg_f, t_sums = {}, {}, {}, {}
 
         def take_root(j, index, kib):
             sums = pair_sums_turned(e_slots[j], index, "s_turned_%d" % j)
@@ -291,17 +310,9 @@ def tile_attend_gblkatt_kernel(tc, qT, kT, us, ts, wb, dp, offs, blkoffs, slotof
 
         def take_inverse(j, index):
             back = turn_back(root[j], index, "root_back_%d" % j)
-            if j < 2:
-                tile = placed([P, X], F32, AT_INVERSE + 4 * j, "inverse_%d" % j)
-                nc.scalar.activation(tile[:], back, ACT.Square)
-                inverse[j] = tile[:]
-            else:
-                tile = placed([P, X, 2], F32, AT_INVERSE + 4 * j, "inverse_%d" % j)
-                nc.scalar.activation(tile[:], back.unsqueeze(2).to_broadcast([P, X, 2]), ACT.Square)
-                inverse[j], doubled[j] = tile[:, :, 0], flat(tile[:])
-
-        def form_h(j):
-            nc.vector.tensor_tensor(h_window[j][:, :X], inverse[j], wb_sb[:, j, :], ALU.mult)
+            inverse[j] = placed([P, X], F32, AT_INVERSE + 2 * j, "inverse_%d" % j)[:]
+            nc.scalar.activation(inverse[j], back, ACT.Square)
+            nc.gpsimd.tensor_tensor(h_window[j][:, :X], inverse[j], wb_sb[:, j, :], ALU.mult)
 
         def add_pairs(dst, pairs):
             nc.vector.tensor_tensor(dst, pairs[:, :, 0], pairs[:, :, 1], ALU.add)
@@ -318,46 +329,40 @@ def tile_attend_gblkatt_kernel(tc, qT, kT, us, ts, wb, dp, offs, blkoffs, slotof
             m_turned[j] = placed([P, X], F32, AT_M_TURNED + 2 * (j % 2), "m_turned_sb_%d" % j)
             nc.scalar.copy(m_turned[j][:], sums)
 
-        def fetch_m(j, index):
-            nc.scalar.copy(m_window[j][:, :X], turn_back(m_turned[j], index, "m_back_%d" % j))
+        def form_m(j):
+            nc.vector.tensor_tensor(m_window[j][:, :X], t_sums[j], inverse[j], ALU.mult)
 
         take_root(0, 1, AT_K_PAIRS + 14)
-        take_root(1, 5, AT_K_PAIRS + 12)
+        take_root(1, 3, AT_K_PAIRS + 12)
         take_inverse(0, 7)
         take_root(2, 1, AT_K_PAIRS + 10)
-        take_inverse(1, 2)
-        take_inverse(2, 3)
-        take_root(3, 1, AT_K_PAIRS + 8)
-        negate_f(0, AT_SLOTS + 8)
+        take_inverse(1, 5)
+        take_root(3, 3, AT_K_PAIRS + 8)
+        take_inverse(2, 2)
         take_inverse(3, 7)
-        f_slots[1] = by_slots(f_sb[1], AT_SLOTS, "f_slots_1")
-        t_first = placed([P, X], F32, AT_DP + 12, "t_first")
-        add_pairs(t_first[:], f_slots[0])
-        form_h(0)
-        nc.vector.tensor_tensor(m_window[0][:, :X], t_first[:], inverse[0], ALU.mult)
-        form_h(1)
-        f_slots[2] = by_slots(f_sb[2], AT_SLOTS + 4, "f_slots_2", doubled[2])
-        form_h(2)
-        f_slots[3] = by_slots(f_sb[3], AT_K_LATE, "f_slots_3", doubled[3])
-        form_h(3)
-        sum_m(1, 1)
-        sum_m(2, 7)
-        negate_f(1, AT_SLOTS + 12)
-        t_second = turn_back(m_turned[1], 2, "t_back_1")
-        negate_f(3, AT_SLOTS)
-        fetch_m(2, 3)
+        for j, kib in ((1, AT_SLOTS), (2, AT_SLOTS + 4), (3, AT_K_LATE)):
+            f_slots[j] = by_slots(f_sb[j], kib, "f_slots_%d" % j)
+        sum_m(0, 1)
+        negate_f(0, AT_SLOTS + 8)
+        sum_m(1, 3)
+        t_sums[0] = turn_back(m_turned[0], 5, "t_back_0")
+        negate_f(3, AT_SLOTS + 12)
+        sum_m(2, 2)
+        t_sums[1] = turn_back(m_turned[1], 7, "t_back_1")
+        negate_f(1, AT_SLOTS)
+        t_sums[2] = turn_back(m_turned[2], 1, "t_back_2")
         negate_f(2, AT_SLOTS + 4)
 
         e_m, factor, g_planes = {}, {}, {}
-        units = [(0, 0), (0, 3), (0, 1), (0, 2), (1, 0), (1, 1), (1, 2), (1, 3)]
-        at_e_m = {(0, 0): AT_DP + 6, (0, 1): AT_DP, (0, 3): AT_DP + 2, (0, 2): AT_DP + 4, (1, 0): AT_M_TURNED, (1, 1): AT_DP}
+        units = [(0, 0), (0, 1), (0, 3), (0, 2), (1, 0), (1, 1), (1, 2), (1, 3)]
+        at_e_m = {(0, 0): AT_WB + 2, (0, 1): AT_DP, (0, 3): AT_M_TURNED + 2, (0, 2): AT_DP + 4, (1, 0): AT_M_TURNED, (1, 1): AT_INVERSE + 4}
         at_factor = {(0, j): AT_K_PAIRS + 2 * j for j in range(PACK)}
         at_factor.update({(1, j): AT_DP + 8 + 2 * j for j in range(PACK)})
-        at_g_planes = (AT_WB, AT_Q_RAW)
+        at_g_planes = (AT_WB, AT_K_GROUPED)
 
         def look_up_m(half, j):
             if (half, j) == (1, 2):
-                both = placed([P, 2, HALF], F32, AT_K_PAIRS + 2, "e_m_late")
+                both = placed([P, 2, HALF], F32, AT_K_PAIRS + 4, "e_m_late")
                 e_m[(1, 2)], e_m[(1, 3)] = both[:, 0, :], both[:, 1, :]
             elif (half, j) != (1, 3):
                 e_m[(half, j)] = placed([P, HALF], F32, at_e_m[(half, j)], "e_m_%d_%d" % (half, j))[:]
@@ -369,7 +374,7 @@ def tile_attend_gblkatt_kernel(tc, qT, kT, us, ts, wb, dp, offs, blkoffs, slotof
 
         def centre(half, j):
             side = units.index((half, j)) % 2
-            turned = bank(1 + 5 * side, "centred_turned_%d_%d" % (half, j))
+            turned = bank(3 + 3 * side, "centred_turned_%d_%d" % (half, j))
             with_ts = placed([P, CHUNKS, P], F32, AT_WITH_TS + 2 * side, "with_ts_%d_%d" % (half, j))
             for b in range(CHUNKS):
                 turn(turned[:, b, :], e_m[(half, j)][:, chunk_cols(b)], start=True, stop=False)
@@ -380,7 +385,7 @@ def tile_attend_gblkatt_kernel(tc, qT, kT, us, ts, wb, dp, offs, blkoffs, slotof
 
         def fetch_factor(half, j):
             side = units.index((half, j)) % 2
-            back = turn_back(centred[(half, j)], 4 + 3 * side, "centred_back_%d_%d" % (half, j))
+            back = turn_back(centred[(half, j)], 4 - 2 * side, "centred_back_%d_%d" % (half, j))
             factor[(half, j)] = placed([P, HALF], F32, at_factor[(half, j)], "factor_%d_%d" % (half, j))
             nc.scalar.activation(factor[(half, j)][:], back, ACT.Copy, scale=neg_us[:, j : j + 1])
 
@@ -395,7 +400,7 @@ def tile_attend_gblkatt_kernel(tc, qT, kT, us, ts, wb, dp, offs, blkoffs, slotof
         g_scales = [keep.tile([P, HALF], U8, name="g_scales_%d" % half, align_bytes=64) for half in range(2)]
 
         def quantize_gradient(half):
-            g_grouped = placed([P, HALF, PACK], BF16, (AT_Q_RAW, AT_K_GROUPED)[half], "g_grouped_%d" % half)
+            g_grouped = placed([P, HALF, PACK], BF16, AT_K_LATE + 4 * half + 8 * half, "g_grouped_%d" % half)
             nc.scalar.activation(
                 g_grouped[:].rearrange("p (c i) j -> p c j i", i=4),
                 g_planes[half][:].rearrange("p j (c i) -> p c j i", i=4),
@@ -406,7 +411,7 @@ def tile_attend_gblkatt_kernel(tc, qT, kT, us, ts, wb, dp, offs, blkoffs, slotof
         out_rows = out.rearrange("(p t) n -> t p n", t=PACK)
 
         def place_result(t, half):
-            product = bank((6, 7, 4, 3, 3, 3, 3, 3)[t + PACK * half], "dk_psum_%d_%d" % (t, half))
+            product = bank((6, 2, 4, 7, 7, 7, 7, 7)[t + PACK * half], "dk_psum_%d_%d" % (t, half))
             nc.tensor.matmul_mx(
                 out=flat(product[:]),
                 lhsT=q2_codes[:, chunk_cols(t)].bitcast(E4M3),
@@ -417,29 +422,36 @@ def tile_attend_gblkatt_kernel(tc, qT, kT, us, ts, wb, dp, offs, blkoffs, slotof
                 stop=True,
             )
             name = "dk_%d_%d" % (t, half)
-            if (t, half) == (OUT_WINDOWS - 1, 0):
-                dk = placed([P, HALF], F32, at_g_planes[1], name)
-            else:
-                dk = placed([P, HALF], F32, AT_F + 2 * (t + PACK * half), name)
-            nc.scalar.copy(dk[:], flat(product[:]))
             window = out_window[t % OUT_WINDOWS]
-            nc.vector.tensor_copy(window[:].indirect(half_list(tok_list, half)), dk[:])
+            if t == LAST:
+                nc.scalar.copy(dk_last[:, half_cols(half)], flat(product[:]))
+                if half == 1:
+                    nc.vector.tensor_copy(window[:].indirect(tok_list[:]), dk_last[:])
+            else:
+                kib = at_g_planes[1] if (t, half) == (OUT_WINDOWS - 1, 0) else AT_F + 2 * (t + PACK * half)
+                dk = placed([P, HALF], F32, kib, name)
+                nc.scalar.copy(dk[:], flat(product[:]))
+                nc.vector.tensor_copy(window[:].indirect(half_list(tok_list, half)), dk[:])
             if half == 1:
                 nc.sync.dma_start(out=out_rows[t], in_=window[:])
 
+        form_m(0)
+        t_sums[LAST] = placed([P, X], F32, AT_WB, "t_last")[:]
+        add_pairs(t_sums[LAST], f_slots[LAST])
         look_up_m(0, 0)
-        add_pairs(m_window[LAST][:, :X], f_slots[LAST])
-        nc.vector.tensor_tensor(m_window[1][:, :X], t_second, inverse[1], ALU.mult)
-        look_up_m(0, 3)
+        form_m(1)
+        form_m(3)
         look_up_m(0, 1)
-        look_up_m(0, 2)
+        look_up_m(0, 3)
+        form_m(2)
         look_up_m(1, 0)
+        look_up_m(0, 2)
         look_up_m(1, 1)
         centre(*units[0])
         for n in range(1, 6):
             centre(*units[n])
             fetch_factor(*units[n - 1])
-        for j in (0, 3, 1, 2):
+        for j in (0, 1, 3, 2):
             gradient(0, j)
         look_up_m(1, 2)
         look_up_m(1, 3)
@@ -457,5 +469,6 @@ def tile_attend_gblkatt_kernel(tc, qT, kT, us, ts, wb, dp, offs, blkoffs, slotof
             place_result(t, 0)
         for t in range(OUT_WINDOWS):
             place_result(t, 1)
+        dk_last = placed([P, C], F32, AT_SLOTS, "dk_last")
         for half in range(2):
             place_result(LAST, half)

@@ -34,6 +34,7 @@ AT_TS, AT_K_PAIRS, AT_K_GROUPED, AT_Q_RAW, AT_E, AT_K_LATE, AT_BLK, AT_DP, AT_WB
 AT_F, AT_SLOTS, AT_WITH_TS, AT_M_TURNED, AT_INVERSE = 113, 129, 145, 149, 153
 BLK_WINDOW_KIB = 2.125
 AT_K_RAW = (AT_BLK, AT_K_LATE)
+AT_WINDOW = 169
 BANK_BYTES = 2048
 
 
@@ -74,21 +75,19 @@ def tile_attend_gblkatt_kernel(tc, qT, kT, us, ts, wb, dp, offs, blkoffs, slotof
         nc.scalar.dma_start(out=ts_window[0:QUADRANT, :], in_=ts[0:QUADRANT, :])
         nc.vector.memset(ts_window[QUADRANT : 2 * QUADRANT, :].bitcast(I32), 0)
         nc.vector.memset(ts_window[2 * QUADRANT : P, :].bitcast(I32), 0)
-        out_window = [keep.tile([P, T], F32, name="out_window_%d" % w) for w in range(OUT_WINDOWS - 1)]
+        out_window = [keep.tile([P, T], F32, name="out_window_0")]
         ts_listed = keep.tile([P, C], F32, name="ts_listed")
         nc.sync.dma_start(tok_list[:], offs)
         make_identity(nc, ident[:])
         nc.vector.memset(out_window[0][:].bitcast(I32), 0)
         nc.vector.tensor_copy(ts_listed[:], ts_window[:].indirect(tok_list[:]))
-        nc.vector.memset(out_window[1][:].bitcast(I32), 0)
-        out_window.append(placed([P, T], F32, AT_TS, "out_window_2"))
-        nc.gpsimd.memset(out_window[2][:], 0.0)
 
         k_rows = kT.rearrange("(p u e) n -> p u e n", u=2, e=2)
         k_raw = {}
         for u in range(2):
             for s in range(K_PIECES):
-                k_raw[(u, s)] = placed([P, 2, K_PIECE], F32, AT_K_RAW[u] + 4 * s, "k_raw_%d_%d" % (u, s))
+                kib = AT_WINDOW if (u, s) == (0, K_PIECES - 1) else AT_K_RAW[u] + 4 * s
+                k_raw[(u, s)] = placed([P, 2, K_PIECE], F32, kib, "k_raw_%d_%d" % (u, s))
                 nc.sync.dma_start(out=k_raw[(u, s)][:], in_=k_rows[:, u, :, s * K_PIECE : (s + 1) * K_PIECE])
         q_rows = qT.rearrange("(p t) r -> p t r", t=PACK)
         q_raw = [placed([P, PACK, Q_PIECE], F32, AT_Q_RAW + 4 * s, "q_raw_%d" % s) for s in range(2)]
@@ -118,7 +117,7 @@ def tile_attend_gblkatt_kernel(tc, qT, kT, us, ts, wb, dp, offs, blkoffs, slotof
             for s in range(K_PIECES):
                 dst = k_pairs[u][:, s * K_PIECE : (s + 1) * K_PIECE, :]
                 src = k_raw[(u, s)][:].rearrange("p e n -> p n e")
-                if (u, s) == (1, K_PIECES - 1):
+                if s == K_PIECES - 1:
                     nc.vector.tensor_copy(dst, src)
                 else:
                     nc.scalar.activation(dst, src, ACT.Copy)
@@ -131,16 +130,26 @@ def tile_attend_gblkatt_kernel(tc, qT, kT, us, ts, wb, dp, offs, blkoffs, slotof
         round_keys(0)
         for window in blk_windows:
             nc.gpsimd.memset(window[:, X:], 0.0)
+        out_window.append(placed([P, T], F32, AT_WINDOW, "out_window_1"))
+        nc.gpsimd.memset(out_window[1][:], 0.0)
         for half in range(2):
             gather_keys(0, half)
-        round_keys(1)
-
-        ts_col = placed([P, C // P], F32, AT_K_LATE + 8, "ts_col")
+        ts_col = placed([P, C // P], F32, AT_K_LATE, "ts_col")
         for half in range(2):
             turned = bank(half, "ts_turned_%d" % half)
             for b in range(CHUNKS):
                 turn(turned[:, b, :], ts_listed[:, chunk_cols(half * CHUNKS + b)])
             nc.scalar.copy(ts_col[:, half * CHUNKS : (half + 1) * CHUNKS], turned[:, :, 0])
+
+        ts_rows = placed([P, C], F32, AT_TS + 4, "ts_rows")
+        for half in range(2):
+            spread = bank(2 + half, "ts_spread_%d" % half)
+            for b in range(CHUNKS):
+                turn(spread[:, b, :], ts_of_chunk(half, b).to_broadcast([P, P]))
+            nc.scalar.copy(ts_rows[:, half_cols(half)], flat(spread[:]))
+        round_keys(1)
+        out_window.append(placed([P, T], F32, AT_K_LATE + 8, "out_window_2"))
+        nc.gpsimd.memset(out_window[2][:], 0.0)
 
         q_grouped = keep.tile([P, PACK, P, PACK], BF16, name="q_grouped", align_bytes=64)
         for s in range(2):
@@ -149,12 +158,6 @@ def tile_attend_gblkatt_kernel(tc, qT, kT, us, ts, wb, dp, offs, blkoffs, slotof
                 q_raw[s][:].rearrange("p t (m j) -> p m j t", j=PACK),
                 ACT.Copy,
             )
-        ts_rows = placed([P, C], F32, AT_Q_RAW + 2, "ts_rows")
-        for half in range(2):
-            spread = bank(2 + half, "ts_spread_%d" % half)
-            for b in range(CHUNKS):
-                turn(spread[:, b, :], ts_of_chunk(half, b).to_broadcast([P, P]))
-            nc.scalar.copy(ts_rows[:, half_cols(half)], flat(spread[:]))
         neg_us = keep.tile([P, PACK], F32, name="neg_us")
         nc.scalar.activation(neg_us[:], us_sb[:], ACT.Copy, scale=-1.0)
         q_codes = keep.tile([P, R], U32, name="q_codes", align_bytes=64)
@@ -293,6 +296,8 @@ def tile_attend_gblkatt_kernel(tc, qT, kT, us, ts, wb, dp, offs, blkoffs, slotof
         turned_tile(1, (2,))
         e_slots[1] = by_slots(e_sb[1], AT_SLOTS + 4, "e_slots_1")
         form_f(1)
+        s_first = placed([P, X], F32, AT_INVERSE + 8, "s_first")
+        nc.gpsimd.tensor_tensor(s_first[:], e_slots[0][:, :, 0], e_slots[0][:, :, 1], ALU.add)
         for n, index in enumerate((3, 4, 2, 3)):
             turned_scores([2, 3], n // 2, 2 * (n % 2), index, AT_K_PAIRS + 8 + 2 * n)
         f_slots[0] = by_slots(f_sb[0], AT_Q_RAW + 4, "f_slots_0")
@@ -304,18 +309,15 @@ def tile_attend_gblkatt_kernel(tc, qT, kT, us, ts, wb, dp, offs, blkoffs, slotof
         root, inverse, neg_f, t_sums = {}, {}, {}, {}
 
         def take_root(j, index, kib):
-            sums = pair_sums_turned(e_slots[j], index, "s_turned_%d" % j)
+            sums = s_first[:] if j == 0 else pair_sums_turned(e_slots[j], index, "s_turned_%d" % j)
             root[j] = placed([P, X], F32, kib, "root_%d" % j)
             nc.scalar.activation(root[j][:], sums, ACT.Abs_reciprocal_sqrt)
 
         def take_inverse(j, index):
-            back = turn_back(root[j], index, "root_back_%d" % j)
+            back = root[j][:] if j == 0 else turn_back(root[j], index, "root_back_%d" % j)
             inverse[j] = placed([P, X], F32, AT_INVERSE + 2 * j, "inverse_%d" % j)[:]
             nc.scalar.activation(inverse[j], back, ACT.Square)
             nc.gpsimd.tensor_tensor(h_window[j][:, :X], inverse[j], wb_sb[:, j, :], ALU.mult)
-
-        def add_pairs(dst, pairs):
-            nc.vector.tensor_tensor(dst, pairs[:, :, 0], pairs[:, :, 1], ALU.add)
 
         def negate_f(j, kib):
             neg_f[j] = placed([P, C], F32, kib, "neg_f_%d" % j)
@@ -326,45 +328,53 @@ def tile_attend_gblkatt_kernel(tc, qT, kT, us, ts, wb, dp, offs, blkoffs, slotof
 
         def sum_m(j, index):
             sums = pair_sums_turned(f_slots[j], index, "m_turned_%d" % j)
-            m_turned[j] = placed([P, X], F32, AT_M_TURNED + 2 * (j % 2), "m_turned_sb_%d" % j)
+            m_turned[j] = placed([P, X], F32, AT_INVERSE + 12 if j == 2 else AT_M_TURNED + 2 * (j % 2), "m_turned_sb_%d" % j)
             nc.scalar.copy(m_turned[j][:], sums)
 
         def form_m(j):
             nc.vector.tensor_tensor(m_window[j][:, :X], t_sums[j], inverse[j], ALU.mult)
 
-        take_root(0, 1, AT_K_PAIRS + 14)
-        take_root(1, 3, AT_K_PAIRS + 12)
-        take_inverse(0, 7)
+        take_root(0, None, AT_K_PAIRS + 14)
+        take_root(1, 1, AT_K_PAIRS + 12)
+        take_inverse(0, None)
+        sum_m(0, 3)
         take_root(2, 1, AT_K_PAIRS + 10)
         take_inverse(1, 5)
+        t_first = placed([P, X], F32, AT_INVERSE + 10, "t_first")
+        nc.scalar.copy(t_first[:], turn_back(m_turned[0], 7, "t_back_0"))
+        nc.gpsimd.tensor_tensor(m_window[0][:, :X], t_first[:], inverse[0], ALU.mult)
         take_root(3, 3, AT_K_PAIRS + 8)
         take_inverse(2, 2)
-        take_inverse(3, 7)
-        for j, kib in ((1, AT_SLOTS), (2, AT_SLOTS + 4), (3, AT_K_LATE)):
-            f_slots[j] = by_slots(f_sb[j], kib, "f_slots_%d" % j)
-        sum_m(0, 1)
+        take_inverse(3, 5)
         negate_f(0, AT_SLOTS + 8)
+        for j, kib in ((1, AT_DP + 8), (2, AT_SLOTS + 4), (3, AT_K_LATE + 4)):
+            f_slots[j] = by_slots(f_sb[j], kib, "f_slots_%d" % j)
         sum_m(1, 3)
-        t_sums[0] = turn_back(m_turned[0], 5, "t_back_0")
-        negate_f(3, AT_SLOTS + 12)
+        t_sums[1] = turn_back(m_turned[1], 1, "t_back_1")
+        negate_f(1, AT_DP + 8)
         sum_m(2, 2)
-        t_sums[1] = turn_back(m_turned[1], 7, "t_back_1")
-        negate_f(1, AT_SLOTS)
-        t_sums[2] = turn_back(m_turned[2], 1, "t_back_2")
+        t_sums[2] = turn_back(m_turned[2], 7, "t_back_2")
         negate_f(2, AT_SLOTS + 4)
+        sum_m(3, 2)
+        t_sums[3] = turn_back(m_turned[3], 5, "t_back_3")
+        negate_f(3, AT_SLOTS + 12)
 
         e_m, factor, g_planes = {}, {}, {}
-        units = [(0, 0), (0, 1), (0, 3), (0, 2), (1, 0), (1, 1), (1, 2), (1, 3)]
-        at_e_m = {(0, 0): AT_WB + 2, (0, 1): AT_DP, (0, 3): AT_M_TURNED + 2, (0, 2): AT_DP + 4, (1, 0): AT_M_TURNED, (1, 1): AT_INVERSE + 4}
+        units = [(half, j) for half in range(2) for j in range(PACK)]
+        at_e_m = {
+            (0, 2): AT_DP + 2, (0, 3): AT_DP + 4,
+            (1, 0): AT_M_TURNED + 2, (1, 1): AT_INVERSE + 6,
+        }
+        at_e_m_pair = {(0, 0): AT_INVERSE + 12, (1, 2): AT_K_PAIRS + 4}
         at_factor = {(0, j): AT_K_PAIRS + 2 * j for j in range(PACK)}
-        at_factor.update({(1, j): AT_DP + 8 + 2 * j for j in range(PACK)})
+        at_factor.update({(1, 0): AT_SLOTS, (1, 1): AT_SLOTS + 2, (1, 2): AT_DP + 12, (1, 3): AT_DP + 14})
         at_g_planes = (AT_WB, AT_K_GROUPED)
 
         def look_up_m(half, j):
-            if (half, j) == (1, 2):
-                both = placed([P, 2, HALF], F32, AT_K_PAIRS + 4, "e_m_late")
-                e_m[(1, 2)], e_m[(1, 3)] = both[:, 0, :], both[:, 1, :]
-            elif (half, j) != (1, 3):
+            if (half, j) in at_e_m_pair:
+                both = placed([P, 2, HALF], F32, at_e_m_pair[(half, j)], "e_m_pair_%d" % half)
+                e_m[(half, j)], e_m[(half, j + 1)] = both[:, 0, :], both[:, 1, :]
+            elif (half, j) in at_e_m:
                 e_m[(half, j)] = placed([P, HALF], F32, at_e_m[(half, j)], "e_m_%d_%d" % (half, j))[:]
             nc.vector.tensor_tensor(
                 e_m[(half, j)], m_window[j][:].indirect(half_list(blk_list, half)), e_sb[j][:, half_cols(half)], ALU.mult
@@ -374,7 +384,7 @@ def tile_attend_gblkatt_kernel(tc, qT, kT, us, ts, wb, dp, offs, blkoffs, slotof
 
         def centre(half, j):
             side = units.index((half, j)) % 2
-            turned = bank(3 + 3 * side, "centred_turned_%d_%d" % (half, j))
+            turned = bank(7 - 5 * side, "centred_turned_%d_%d" % (half, j))
             with_ts = placed([P, CHUNKS, P], F32, AT_WITH_TS + 2 * side, "with_ts_%d_%d" % (half, j))
             for b in range(CHUNKS):
                 turn(turned[:, b, :], e_m[(half, j)][:, chunk_cols(b)], start=True, stop=False)
@@ -385,7 +395,7 @@ def tile_attend_gblkatt_kernel(tc, qT, kT, us, ts, wb, dp, offs, blkoffs, slotof
 
         def fetch_factor(half, j):
             side = units.index((half, j)) % 2
-            back = turn_back(centred[(half, j)], 4 - 2 * side, "centred_back_%d_%d" % (half, j))
+            back = turn_back(centred[(half, j)], 4 - side, "centred_back_%d_%d" % (half, j))
             factor[(half, j)] = placed([P, HALF], F32, at_factor[(half, j)], "factor_%d_%d" % (half, j))
             nc.scalar.activation(factor[(half, j)][:], back, ACT.Copy, scale=neg_us[:, j : j + 1])
 
@@ -400,7 +410,7 @@ def tile_attend_gblkatt_kernel(tc, qT, kT, us, ts, wb, dp, offs, blkoffs, slotof
         g_scales = [keep.tile([P, HALF], U8, name="g_scales_%d" % half, align_bytes=64) for half in range(2)]
 
         def quantize_gradient(half):
-            g_grouped = placed([P, HALF, PACK], BF16, AT_K_LATE + 4 * half + 8 * half, "g_grouped_%d" % half)
+            g_grouped = placed([P, HALF, PACK], BF16, (AT_K_LATE + 4, AT_TS)[half], "g_grouped_%d" % half)
             nc.scalar.activation(
                 g_grouped[:].rearrange("p (c i) j -> p c j i", i=4),
                 g_planes[half][:].rearrange("p j (c i) -> p c j i", i=4),
@@ -411,7 +421,7 @@ def tile_attend_gblkatt_kernel(tc, qT, kT, us, ts, wb, dp, offs, blkoffs, slotof
         out_rows = out.rearrange("(p t) n -> t p n", t=PACK)
 
         def place_result(t, half):
-            product = bank((6, 2, 4, 7, 7, 7, 7, 7)[t + PACK * half], "dk_psum_%d_%d" % (t, half))
+            product = bank((2, 3, 4, 1, 1, 1, 1, 1)[t + PACK * half], "dk_psum_%d_%d" % (t, half))
             nc.tensor.matmul_mx(
                 out=flat(product[:]),
                 lhsT=q2_codes[:, chunk_cols(t)].bitcast(E4M3),
@@ -435,23 +445,20 @@ def tile_attend_gblkatt_kernel(tc, qT, kT, us, ts, wb, dp, offs, blkoffs, slotof
             if half == 1:
                 nc.sync.dma_start(out=out_rows[t], in_=window[:])
 
-        form_m(0)
-        t_sums[LAST] = placed([P, X], F32, AT_WB, "t_last")[:]
-        add_pairs(t_sums[LAST], f_slots[LAST])
-        look_up_m(0, 0)
         form_m(1)
-        form_m(3)
-        look_up_m(0, 1)
-        look_up_m(0, 3)
         form_m(2)
-        look_up_m(1, 0)
+        look_up_m(0, 0)
+        look_up_m(0, 1)
         look_up_m(0, 2)
+        form_m(3)
+        look_up_m(1, 0)
+        look_up_m(0, 3)
         look_up_m(1, 1)
         centre(*units[0])
         for n in range(1, 6):
             centre(*units[n])
             fetch_factor(*units[n - 1])
-        for j in (0, 1, 3, 2):
+        for j in range(PACK):
             gradient(0, j)
         look_up_m(1, 2)
         look_up_m(1, 3)

@@ -122,10 +122,11 @@ def tile_attend_gblkatt_kernel(tc, qT, kT, us, ts, wb, dp, offs, blkoffs, slotof
                 else:
                     nc.scalar.activation(dst, src, ACT.Copy)
 
+        k_listed = [placed([P, 2, HALF], U32, AT_F + 4 * half, "k_listed_%d" % half) for half in range(2)]
+
         def gather_keys(u, half):
             window = flat(k_pairs[u][:]).bitcast(U32)
-            words = k_grouped[half][:].bitcast(U32).rearrange("p (c u) -> p c u", u=2)
-            nc.vector.tensor_copy(words[:, :, u], window.indirect(half_list(tok_list, half)))
+            nc.vector.tensor_copy(k_listed[half][:, u, :], window.indirect(half_list(tok_list, half)))
 
         round_keys(0)
         for window in blk_windows:
@@ -178,6 +179,9 @@ def tile_attend_gblkatt_kernel(tc, qT, kT, us, ts, wb, dp, offs, blkoffs, slotof
 
         for half in range(2):
             gather_keys(1, half)
+        for half in range(2):
+            words = k_grouped[half][:].bitcast(U32).rearrange("p (c u) -> p c u", u=2)
+            nc.vector.tensor_copy(words, k_listed[half][:].rearrange("p u c -> p c u"))
         for half in range(2):
             for part in parts_of(half):
                 nc.vector.quantize_mx(
@@ -351,13 +355,13 @@ def tile_attend_gblkatt_kernel(tc, qT, kT, us, ts, wb, dp, offs, blkoffs, slotof
             f_slots[j] = by_slots(f_sb[j], kib, "f_slots_%d" % j)
         sum_m(1, 3)
         t_sums[1] = turn_back(m_turned[1], 1, "t_back_1")
-        negate_f(1, AT_DP + 8)
+        negate_f(3, AT_SLOTS + 12)
         sum_m(2, 2)
         t_sums[2] = turn_back(m_turned[2], 7, "t_back_2")
-        negate_f(2, AT_SLOTS + 4)
+        negate_f(1, AT_SLOTS + 4)
         sum_m(3, 2)
         t_sums[3] = turn_back(m_turned[3], 5, "t_back_3")
-        negate_f(3, AT_SLOTS + 12)
+        negate_f(2, AT_K_LATE + 4)
 
         e_m, factor, g_planes = {}, {}, {}
         units = [(half, j) for half in range(2) for j in range(PACK)]
@@ -410,7 +414,7 @@ def tile_attend_gblkatt_kernel(tc, qT, kT, us, ts, wb, dp, offs, blkoffs, slotof
         g_scales = [keep.tile([P, HALF], U8, name="g_scales_%d" % half, align_bytes=64) for half in range(2)]
 
         def quantize_gradient(half):
-            g_grouped = placed([P, HALF, PACK], BF16, (AT_K_LATE + 4, AT_TS)[half], "g_grouped_%d" % half)
+            g_grouped = placed([P, HALF, PACK], BF16, (AT_DP + 8, AT_TS)[half], "g_grouped_%d" % half)
             nc.scalar.activation(
                 g_grouped[:].rearrange("p (c i) j -> p c j i", i=4),
                 g_planes[half][:].rearrange("p j (c i) -> p c j i", i=4),
@@ -442,8 +446,11 @@ def tile_attend_gblkatt_kernel(tc, qT, kT, us, ts, wb, dp, offs, blkoffs, slotof
                 dk = placed([P, HALF], F32, kib, name)
                 nc.scalar.copy(dk[:], flat(product[:]))
                 nc.vector.tensor_copy(window[:].indirect(half_list(tok_list, half)), dk[:])
-            if half == 1:
+            if half == 1 and t < LAST:
                 nc.sync.dma_start(out=out_rows[t], in_=window[:])
+            elif half == 1:
+                nc.sync.dma_start(out=out_rows[t][:, : T // 2], in_=window[:, : T // 2])
+                nc.scalar.dma_start(out=out_rows[t][:, T // 2 :], in_=window[:, T // 2 :])
 
         form_m(1)
         form_m(2)

@@ -83,12 +83,17 @@ def tile_attend_gblkatt_kernel(tc, qT, kT, us, ts, wb, dp, offs, blkoffs, slotof
         nc.vector.tensor_copy(ts_listed[:], ts_window[:].indirect(tok_list[:]))
 
         k_rows = kT.rearrange("(p u e) n -> p u e n", u=2, e=2)
+        k_pieces = [
+            [slice(first, first + K_PIECE) for first in range(0, T, K_PIECE)],
+            [slice(first, first + K_PIECE) for first in range(0, T - K_PIECE, K_PIECE)]
+            + [slice(T - K_PIECE, T - K_PIECE // 2), slice(T - K_PIECE // 2, T)],
+        ]
         k_raw = {}
         for u in range(2):
-            for s in range(K_PIECES):
-                kib = AT_WINDOW if (u, s) == (0, K_PIECES - 1) else AT_K_RAW[u] + 4 * s
-                k_raw[(u, s)] = placed([P, 2, K_PIECE], F32, kib, "k_raw_%d_%d" % (u, s))
-                nc.sync.dma_start(out=k_raw[(u, s)][:], in_=k_rows[:, u, :, s * K_PIECE : (s + 1) * K_PIECE])
+            for s, tokens in enumerate(k_pieces[u]):
+                kib = AT_WINDOW if (u, s) == (0, K_PIECES - 1) else AT_K_RAW[u] + tokens.start * 8 / 1024
+                k_raw[(u, s)] = placed([P, 2, tokens.stop - tokens.start], F32, kib, "k_raw_%d_%d" % (u, s))
+                nc.sync.dma_start(out=k_raw[(u, s)][:], in_=k_rows[:, u, :, tokens])
         q_rows = qT.rearrange("(p t) r -> p t r", t=PACK)
         q_raw = [placed([P, PACK, Q_PIECE], F32, AT_Q_RAW + 4 * s, "q_raw_%d" % s) for s in range(2)]
         for s in range(2):
@@ -114,10 +119,10 @@ def tile_attend_gblkatt_kernel(tc, qT, kT, us, ts, wb, dp, offs, blkoffs, slotof
         k_grouped = [placed([P, HALF * PACK], BF16, AT_K_GROUPED + 4 * half, "k_grouped_%d" % half) for half in range(2)]
 
         def round_keys(u):
-            for s in range(K_PIECES):
-                dst = k_pairs[u][:, s * K_PIECE : (s + 1) * K_PIECE, :]
+            for s, tokens in enumerate(k_pieces[u]):
+                dst = k_pairs[u][:, tokens, :]
                 src = k_raw[(u, s)][:].rearrange("p e n -> p n e")
-                if s == K_PIECES - 1:
+                if s >= K_PIECES - 1:
                     nc.vector.tensor_copy(dst, src)
                 else:
                     nc.scalar.activation(dst, src, ACT.Copy)
@@ -149,8 +154,6 @@ def tile_attend_gblkatt_kernel(tc, qT, kT, us, ts, wb, dp, offs, blkoffs, slotof
                 turn(spread[:, b, :], ts_of_chunk(half, b).to_broadcast([P, P]))
             nc.scalar.copy(ts_rows[:, half_cols(half)], flat(spread[:]))
         round_keys(1)
-        out_window.append(placed([P, T], F32, AT_K_LATE + 8, "out_window_2"))
-        nc.gpsimd.memset(out_window[2][:], 0.0)
 
         q_grouped = keep.tile([P, PACK, P, PACK], BF16, name="q_grouped", align_bytes=64)
         for s in range(2):
@@ -477,6 +480,8 @@ def tile_attend_gblkatt_kernel(tc, qT, kT, us, ts, wb, dp, offs, blkoffs, slotof
         fetch_factor(1, 3)
         for j in range(PACK):
             gradient(1, j)
+        out_window.append(placed([P, T], F32, AT_DP + 8, "out_window_2"))
+        nc.gpsimd.memset(out_window[2][:], 0.0)
         place_result(0, 0)
         quantize_gradient(1)
         for t in range(1, OUT_WINDOWS):

@@ -24,7 +24,6 @@ HALF = 512
 CHUNKS = HALF // P
 LIST_COLS = HALF // 16
 K_PIECE = 512
-K_PIECES = T // K_PIECE
 Q_PIECE = R // 2
 BLK_WINDOW = X + 8
 QUADRANT = 32
@@ -33,7 +32,6 @@ OUT_WINDOWS = 3
 AT_TS, AT_K_PAIRS, AT_K_GROUPED, AT_Q_RAW, AT_E, AT_K_LATE, AT_BLK, AT_DP, AT_WB = 0, 8, 24, 32, 40, 56, 72, 89, 105
 AT_F, AT_SLOTS, AT_WITH_TS, AT_M_TURNED, AT_INVERSE = 113, 129, 145, 149, 153
 BLK_WINDOW_KIB = 2.125
-AT_K_RAW = (AT_BLK, AT_K_LATE)
 AT_WINDOW = 169
 BANK_BYTES = 2048
 
@@ -83,15 +81,12 @@ def tile_attend_gblkatt_kernel(tc, qT, kT, us, ts, wb, dp, offs, blkoffs, slotof
         nc.vector.tensor_copy(ts_listed[:], ts_window[:].indirect(tok_list[:]))
 
         k_rows = kT.rearrange("(p u e) n -> p u e n", u=2, e=2)
-        k_pieces = [
-            [slice(first, first + K_PIECE) for first in range(0, T, K_PIECE)],
-            [slice(first, first + K_PIECE) for first in range(0, T - K_PIECE, K_PIECE)]
-            + [slice(T - K_PIECE, T - K_PIECE // 2), slice(T - K_PIECE // 2, T)],
-        ]
+        k_ends = ((T // 2, T), (T // 2, 3 * T // 4, 7 * T // 8, T))
+        k_pieces = [[slice(first, last) for first, last in zip((0,) + ends[:-1], ends)] for ends in k_ends]
         k_raw = {}
         for u in range(2):
             for s, tokens in enumerate(k_pieces[u]):
-                kib = AT_WINDOW if (u, s) == (0, K_PIECES - 1) else AT_K_RAW[u] + tokens.start * 8 / 1024
+                kib = (AT_WINDOW + 8 - 8 * s) if u == 0 else AT_K_LATE + tokens.start * 8 / 1024
                 k_raw[(u, s)] = placed([P, 2, tokens.stop - tokens.start], F32, kib, "k_raw_%d_%d" % (u, s))
                 nc.sync.dma_start(out=k_raw[(u, s)][:], in_=k_rows[:, u, :, tokens])
         q_rows = qT.rearrange("(p t) r -> p t r", t=PACK)
@@ -118,11 +113,13 @@ def tile_attend_gblkatt_kernel(tc, qT, kT, us, ts, wb, dp, offs, blkoffs, slotof
         k_pairs = [placed([P, T, 2], BF16, AT_K_PAIRS + 8 * u, "k_pairs_%d" % u) for u in range(2)]
         k_grouped = [placed([P, HALF * PACK], BF16, AT_K_GROUPED + 4 * half, "k_grouped_%d" % half) for half in range(2)]
 
-        def round_keys(u):
-            for s, tokens in enumerate(k_pieces[u]):
-                dst = k_pairs[u][:, tokens, :]
-                src = k_raw[(u, s)][:].rearrange("p e n -> p n e")
-                if s >= K_PIECES - 1:
+        def round_keys(u, cuts, on_vector):
+            for n, (first, last) in enumerate(zip((0,) + cuts[:-1], cuts)):
+                s = [tokens.start <= first < tokens.stop for tokens in k_pieces[u]].index(True)
+                start = k_pieces[u][s].start
+                dst = k_pairs[u][:, first:last, :]
+                src = k_raw[(u, s)][:, :, first - start : last - start].rearrange("p e n -> p n e")
+                if n in on_vector:
                     nc.vector.tensor_copy(dst, src)
                 else:
                     nc.scalar.activation(dst, src, ACT.Copy)
@@ -133,27 +130,27 @@ def tile_attend_gblkatt_kernel(tc, qT, kT, us, ts, wb, dp, offs, blkoffs, slotof
             window = flat(k_pairs[u][:]).bitcast(U32)
             nc.vector.tensor_copy(k_listed[half][:, u, :], window.indirect(half_list(tok_list, half)))
 
-        round_keys(0)
+        round_keys(0, (1024, 1408, 2048), (2,))
         for window in blk_windows:
             nc.gpsimd.memset(window[:, X:], 0.0)
         out_window.append(placed([P, T], F32, AT_WINDOW, "out_window_1"))
         nc.gpsimd.memset(out_window[1][:], 0.0)
         for half in range(2):
             gather_keys(0, half)
-        ts_col = placed([P, C // P], F32, AT_K_LATE, "ts_col")
+        ts_col = placed([P, C // P], F32, AT_WINDOW + 8, "ts_col")
         for half in range(2):
             turned = bank(half, "ts_turned_%d" % half)
             for b in range(CHUNKS):
                 turn(turned[:, b, :], ts_listed[:, chunk_cols(half * CHUNKS + b)])
             nc.scalar.copy(ts_col[:, half * CHUNKS : (half + 1) * CHUNKS], turned[:, :, 0])
 
-        ts_rows = placed([P, C], F32, AT_TS + 4, "ts_rows")
+        ts_rows = placed([P, C], F32, AT_WINDOW + 9, "ts_rows")
         for half in range(2):
             spread = bank(2 + half, "ts_spread_%d" % half)
             for b in range(CHUNKS):
                 turn(spread[:, b, :], ts_of_chunk(half, b).to_broadcast([P, P]))
             nc.scalar.copy(ts_rows[:, half_cols(half)], flat(spread[:]))
-        round_keys(1)
+        round_keys(1, (512, 1024, 1536, 1792, 2048), (1, 3, 4))
 
         q_grouped = keep.tile([P, PACK, P, PACK], BF16, name="q_grouped", align_bytes=64)
         for s in range(2):

@@ -26,7 +26,7 @@ LIST_COLS = HALF // 16
 K_PIECE = 512
 Q_PIECE = R // 2
 BLK_WINDOW = X + 8
-QUADRANT = 32
+TS_ROW = P - 1
 OUT_WINDOWS = 3
 
 AT_TS, AT_K_PAIRS, AT_K_GROUPED, AT_Q_RAW, AT_E, AT_K_LATE, AT_BLK, AT_DP, AT_WB = 0, 8, 24, 32, 40, 56, 72, 89, 105
@@ -70,9 +70,8 @@ def tile_attend_gblkatt_kernel(tc, qT, kT, us, ts, wb, dp, offs, blkoffs, slotof
         ident = keep.tile([P, P], F32, name="ident")
 
         ts_window = placed([P, T], F32, AT_TS, "ts_window")
-        nc.scalar.dma_start(out=ts_window[0:QUADRANT, :], in_=ts[0:QUADRANT, :])
-        nc.vector.memset(ts_window[QUADRANT : 2 * QUADRANT, :].bitcast(I32), 0)
-        nc.vector.memset(ts_window[2 * QUADRANT : P, :].bitcast(I32), 0)
+        nc.scalar.dma_start(out=ts_window[TS_ROW:P, :], in_=ts[0:1, :])
+        nc.vector.memset(ts_window[0:TS_ROW, :].bitcast(I32), 0)
         out_window = [keep.tile([P, T], F32, name="out_window_0")]
         ts_listed = keep.tile([P, C], F32, name="ts_listed")
         nc.sync.dma_start(tok_list[:], offs)
@@ -142,7 +141,7 @@ def tile_attend_gblkatt_kernel(tc, qT, kT, us, ts, wb, dp, offs, blkoffs, slotof
             turned = bank(half, "ts_turned_%d" % half)
             for b in range(CHUNKS):
                 turn(turned[:, b, :], ts_listed[:, chunk_cols(half * CHUNKS + b)])
-            nc.scalar.copy(ts_col[:, half * CHUNKS : (half + 1) * CHUNKS], turned[:, :, 0])
+            nc.scalar.copy(ts_col[:, half * CHUNKS : (half + 1) * CHUNKS], turned[:, :, TS_ROW])
 
         ts_rows = placed([P, C], F32, AT_WINDOW + 9, "ts_rows")
         for half in range(2):

@@ -21,19 +21,17 @@ P = 128
 PACK = 4
 LAST = PACK - 1
 HALF = 512
+QUARTER = 256
 CHUNKS = HALF // P
-LIST_COLS = HALF // 16
-K_PIECE = 512
 Q_PIECE = R // 2
 BLK_WINDOW = X + 8
-TS_ROW = P - 1
-OUT_WINDOWS = 3
-
-AT_TS, AT_K_PAIRS, AT_K_GROUPED, AT_Q_RAW, AT_E, AT_K_LATE, AT_BLK, AT_DP, AT_WB = 0, 8, 24, 32, 40, 56, 72, 89, 105
-AT_F, AT_SLOTS, AT_WITH_TS, AT_M_TURNED, AT_INVERSE = 113, 129, 145, 149, 153
 BLK_WINDOW_KIB = 2.125
-AT_WINDOW = 169
+TS_ROW = P - 1
 BANK_BYTES = 2048
+
+AT_TS, AT_K_PAIRS, AT_K_LISTED, AT_K_GROUPED, AT_Q_RAW, AT_K_EARLY, AT_K_LATE = 0, 8, 24, 32, 40, 48, 64
+AT_E, AT_F, AT_DP, AT_WB, AT_BLK, AT_TS_LISTED, AT_E_SLOTS, AT_INVERSE, AT_F_SLOTS = 80, 96, 112, 128, 136, 153, 157, 174, 182
+AT_TS_ROWS = 198
 
 
 def tile_attend_gblkatt_kernel(tc, qT, kT, us, ts, wb, dp, offs, blkoffs, slotoffs, out):
@@ -52,17 +50,31 @@ def tile_attend_gblkatt_kernel(tc, qT, kT, us, ts, wb, dp, offs, blkoffs, slotof
         def flat(view):
             return view.rearrange("p a b -> p (a b)")
 
-        def half_cols(half):
-            return slice(half * HALF, (half + 1) * HALF)
+        def cols(index, width):
+            return slice(index * width, (index + 1) * width)
 
-        def chunk_cols(chunk):
-            return slice(chunk * P, (chunk + 1) * P)
-
-        def half_list(offsets, half):
-            return offsets[:, half * LIST_COLS : (half + 1) * LIST_COLS]
+        def part_of(offsets, index, width):
+            return offsets[:, cols(index, width // 16)]
 
         def turn(dst, src, start=True, stop=True):
             nc.tensor.matmul(dst, lhsT=src, rhs=ident[:], is_transpose=True, start=start, stop=stop)
+
+        def turn_back(src, index, name):
+            back = bank(index, name)
+            for b in range(CHUNKS):
+                turn(back[:, b, :], src[:, cols(b, P)])
+            return flat(back[:])
+
+        def product_mx(dst, stationary, stationary_scales, moving, moving_scales, moving_format=E4M3):
+            nc.tensor.matmul_mx(
+                out=dst,
+                lhsT=stationary.bitcast(E4M3),
+                lhsT_scale=stationary_scales,
+                rhs=moving.bitcast(moving_format),
+                rhs_scale=moving_scales,
+                start=True,
+                stop=True,
+            )
 
         tok_list = keep.tile([P, C // 16], U16, name="tok_list")
         blk_list = keep.tile([P, C // 16], U16, name="blk_list")
@@ -73,7 +85,7 @@ def tile_attend_gblkatt_kernel(tc, qT, kT, us, ts, wb, dp, offs, blkoffs, slotof
         nc.scalar.dma_start(out=ts_window[TS_ROW:P, :], in_=ts[0:1, :])
         nc.vector.memset(ts_window[0:TS_ROW, :].bitcast(I32), 0)
         out_window = [keep.tile([P, T], F32, name="out_window_0")]
-        ts_listed = keep.tile([P, C], F32, name="ts_listed")
+        ts_listed = placed([P, C], F32, AT_TS_LISTED, "ts_listed")
         nc.sync.dma_start(tok_list[:], offs)
         make_identity(nc, ident[:])
         nc.vector.memset(out_window[0][:].bitcast(I32), 0)
@@ -85,14 +97,14 @@ def tile_attend_gblkatt_kernel(tc, qT, kT, us, ts, wb, dp, offs, blkoffs, slotof
         k_raw = {}
         for u in range(2):
             for s, tokens in enumerate(k_pieces[u]):
-                kib = (AT_WINDOW + 8 - 8 * s) if u == 0 else AT_K_LATE + tokens.start * 8 / 1024
+                kib = (AT_K_EARLY, AT_K_LATE)[u] + tokens.start * 8 / 1024
                 k_raw[(u, s)] = placed([P, 2, tokens.stop - tokens.start], F32, kib, "k_raw_%d_%d" % (u, s))
                 nc.sync.dma_start(out=k_raw[(u, s)][:], in_=k_rows[:, u, :, tokens])
         q_rows = qT.rearrange("(p t) r -> p t r", t=PACK)
         q_raw = [placed([P, PACK, Q_PIECE], F32, AT_Q_RAW + 4 * s, "q_raw_%d" % s) for s in range(2)]
         for s in range(2):
-            nc.sync.dma_start(out=q_raw[s][:], in_=q_rows[:, :, s * Q_PIECE : (s + 1) * Q_PIECE])
-        us_sb = keep.tile([P, PACK], F32, name="us_sb")
+            nc.sync.dma_start(out=q_raw[s][:], in_=q_rows[:, :, cols(s, Q_PIECE)])
+        us_sb = placed([P, PACK], F32, AT_F_SLOTS + 4, "us_sb")
         nc.sync.dma_start(out=us_sb[:], in_=us.rearrange("(p j) o -> p (j o)", j=PACK))
         nc.sync.dma_start(slot_list[:], slotoffs)
         dp_rows = dp.rearrange("(p j) c -> j p c", j=PACK)
@@ -106,11 +118,9 @@ def tile_attend_gblkatt_kernel(tc, qT, kT, us, ts, wb, dp, offs, blkoffs, slotof
         blk_windows = [placed([P, BLK_WINDOW], F32, AT_BLK + BLK_WINDOW_KIB * n, "blk_window_%d" % n) for n in range(2 * PACK)]
         h_window, m_window = blk_windows[:PACK], blk_windows[PACK:]
 
-        def ts_of_chunk(half, b):
-            return ts_col[:, half * CHUNKS + b : half * CHUNKS + b + 1]
-
         k_pairs = [placed([P, T, 2], BF16, AT_K_PAIRS + 8 * u, "k_pairs_%d" % u) for u in range(2)]
-        k_grouped = [placed([P, HALF * PACK], BF16, AT_K_GROUPED + 4 * half, "k_grouped_%d" % half) for half in range(2)]
+        k_listed = [placed([P, 2, QUARTER], U32, AT_K_LISTED + 2 * n, "k_listed_%d" % n) for n in range(4)]
+        k_grouped = [placed([P, QUARTER * PACK], BF16, AT_K_GROUPED + 2 * n, "k_grouped_%d" % n) for n in range(4)]
 
         def round_keys(u, cuts, on_vector):
             for n, (first, last) in enumerate(zip((0,) + cuts[:-1], cuts)):
@@ -123,127 +133,113 @@ def tile_attend_gblkatt_kernel(tc, qT, kT, us, ts, wb, dp, offs, blkoffs, slotof
                 else:
                     nc.scalar.activation(dst, src, ACT.Copy)
 
-        k_listed = [placed([P, 2, HALF], U32, AT_F + 4 * half, "k_listed_%d" % half) for half in range(2)]
-
-        def gather_keys(u, half):
+        def gather_keys(u):
             window = flat(k_pairs[u][:]).bitcast(U32)
-            nc.vector.tensor_copy(k_listed[half][:, u, :], window.indirect(half_list(tok_list, half)))
+            for n in range(4):
+                nc.vector.tensor_copy(k_listed[n][:, u, :], window.indirect(part_of(tok_list, n, QUARTER)))
 
         round_keys(0, (1024, 1408, 2048), (2,))
         for window in blk_windows:
             nc.gpsimd.memset(window[:, X:], 0.0)
-        out_window.append(placed([P, T], F32, AT_WINDOW, "out_window_1"))
+        out_window.append(placed([P, T], F32, AT_K_EARLY + 8, "out_window_1"))
         nc.gpsimd.memset(out_window[1][:], 0.0)
-        for half in range(2):
-            gather_keys(0, half)
-        ts_col = placed([P, C // P], F32, AT_WINDOW + 8, "ts_col")
+        gather_keys(0)
+
+        ts_col = keep.tile([P, C // P], F32, name="ts_col")
+        ts_rows = [placed([P, HALF], F32, AT_TS_ROWS + 2 * half, "ts_rows_%d" % half) for half in range(2)]
         for half in range(2):
             turned = bank(half, "ts_turned_%d" % half)
             for b in range(CHUNKS):
-                turn(turned[:, b, :], ts_listed[:, chunk_cols(half * CHUNKS + b)])
-            nc.scalar.copy(ts_col[:, half * CHUNKS : (half + 1) * CHUNKS], turned[:, :, TS_ROW])
+                turn(turned[:, b, :], ts_listed[:, cols(half * CHUNKS + b, P)])
+            nc.vector.tensor_copy(ts_col[:, cols(half, CHUNKS)], turned[:, :, TS_ROW])
 
-        ts_rows = placed([P, C], F32, AT_WINDOW + 9, "ts_rows")
+        def ts_of_chunk(half, b):
+            return ts_col[:, cols(half * CHUNKS + b, 1)]
+
         for half in range(2):
             spread = bank(2 + half, "ts_spread_%d" % half)
             for b in range(CHUNKS):
                 turn(spread[:, b, :], ts_of_chunk(half, b).to_broadcast([P, P]))
-            nc.scalar.copy(ts_rows[:, half_cols(half)], flat(spread[:]))
-        round_keys(1, (512, 1024, 1536, 1792, 2048), (1, 3, 4))
+            nc.scalar.copy(ts_rows[half][:], flat(spread[:]))
+        round_keys(1, (1024, 1536, 1792, 2048), (1, 2, 3))
+        gather_keys(1)
 
         q_grouped = keep.tile([P, PACK, P, PACK], BF16, name="q_grouped", align_bytes=64)
-        for s in range(2):
-            nc.scalar.activation(
-                q_grouped[:, :, s * Q_PIECE // PACK : (s + 1) * Q_PIECE // PACK, :].rearrange("p j m t -> p m j t"),
-                q_raw[s][:].rearrange("p t (m j) -> p m j t", j=PACK),
-                ACT.Copy,
-            )
-        neg_us = keep.tile([P, PACK], F32, name="neg_us")
-        nc.scalar.activation(neg_us[:], us_sb[:], ACT.Copy, scale=-1.0)
-        q_codes = keep.tile([P, R], U32, name="q_codes", align_bytes=64)
-        q_scales = keep.tile([P, R], U8, name="q_scales", align_bytes=64)
-        k_codes = [keep.tile([P, HALF], U32, name="k_codes_0", align_bytes=64), placed([P, HALF], U32, AT_Q_RAW + 6, "k_codes_1")]
-        k_scales = [keep.tile([P, HALF], U8, name="k_scales_%d" % half, align_bytes=64) for half in range(2)]
 
-        def parts_of(half):
-            return (slice(0, HALF),) if half == 0 else (slice(0, HALF // 2), slice(HALF // 2, HALF))
+        def rounded_queries(s):
+            dst = q_grouped[:, :, cols(s, Q_PIECE // PACK), :].rearrange("p j m t -> p m j t")
+            return dst, q_raw[s][:].rearrange("p t (m j) -> p m j t", j=PACK)
+
+        def weave(n):
+            words = k_grouped[n][:].bitcast(U32).rearrange("p (c u) -> p c u", u=2)
+            return words, k_listed[n][:].rearrange("p u c -> p c u")
+
+        nc.scalar.copy(*weave(0))
+        nc.scalar.copy(*weave(1))
+        nc.scalar.activation(*rounded_queries(0), ACT.Copy)
+        nc.vector.tensor_copy(*weave(2))
+        nc.scalar.copy(*weave(3))
+        nc.vector.tensor_copy(*rounded_queries(1))
+        q_codes = {
+            0: keep.tile([P, P], U32, name="q_codes_0", align_bytes=64),
+            1: placed([P, P], U32, AT_K_GROUPED + 4, "q_codes_1"),
+            2: placed([P, 2 * P], U32, AT_K_GROUPED + 4.5, "q_codes_2"),
+        }
+        q_scales = keep.tile([P, R], U8, name="q_scales", align_bytes=64)
+        k_codes = [placed([P, QUARTER], U32, AT_K_LATE if n == 0 else AT_Q_RAW + n, "k_codes_%d" % n) for n in range(4)]
+        k_scales = [keep.tile([P, QUARTER], U8, name="k_scales_%d" % n, align_bytes=64) for n in range(4)]
 
         def quantize_queries(first, count):
             rows = slice(first * P, (first + count) * P)
             nc.vector.quantize_mx(
-                out=q_codes[:, rows].bitcast(E4M3),
+                out=q_codes[first][:].bitcast(E4M3),
                 scales=q_scales[:, rows],
                 in_=q_grouped[:, first : first + count, :, :].rearrange("p j m t -> p (j m t)"),
             )
 
-        for half in range(2):
-            gather_keys(1, half)
-        for half in range(2):
-            words = k_grouped[half][:].bitcast(U32).rearrange("p (c u) -> p c u", u=2)
-            nc.vector.tensor_copy(words, k_listed[half][:].rearrange("p u c -> p c u"))
-        for half in range(2):
-            for part in parts_of(half):
-                nc.vector.quantize_mx(
-                    out=k_codes[half][:, part].bitcast(E4M3),
-                    scales=k_scales[half][:, part],
-                    in_=k_grouped[half][:, part.start * PACK : part.stop * PACK],
-                )
-            if half == 0:
+        for n in range(4):
+            nc.vector.quantize_mx(out=k_codes[n][:].bitcast(E4M3), scales=k_scales[n][:], in_=k_grouped[n][:])
+            if n == 0:
                 quantize_queries(0, 1)
+
+        neg_us = keep.tile([P, PACK], F32, name="neg_us")
+        nc.scalar.activation(neg_us[:], us_sb[:], ACT.Copy, scale=-1.0)
+        e_sb = [placed([P, C], F32, AT_E + 4 * j, "e_%d" % j) for j in range(PACK)]
+        scaled_first = [placed([P, QUARTER], F32, AT_K_GROUPED + (5.5, 6.5, 7.5, 0)[n], "scaled_first_%d" % n) for n in range(4)]
+        for n in range(4):
+            product = flat(bank(n, "scores_direct_%d" % n)[:])[:, :QUARTER]
+            product_mx(product, q_codes[0][:], q_scales[:, :P], k_codes[n][:], k_scales[n][:])
+            nc.vector.tensor_tensor(scaled_first[n][:], product, ts_rows[n // 2][:, cols(n % 2, QUARTER)], ALU.mult)
+            nc.scalar.activation(e_sb[0][:, cols(n, QUARTER)], scaled_first[n][:], ACT.Exp, scale=us_sb[:, 0:1])
         quantize_queries(1, 1)
         quantize_queries(2, 2)
 
-        e_sb = [placed([P, C], F32, AT_E + 4 * j, "e_%d" % j) for j in range(PACK)]
-
-        def scores(dst, stationary, stationary_scales, moving, moving_scales):
-            nc.tensor.matmul_mx(
-                out=dst,
-                lhsT=stationary.bitcast(E4M3),
-                lhsT_scale=stationary_scales,
-                rhs=moving.bitcast(E4M3),
-                rhs_scale=moving_scales,
-                start=True,
-                stop=True,
-            )
-
-        def exp_into_e(j, half, src):
-            nc.scalar.activation(e_sb[j][:, half_cols(half)], src, ACT.Exp, scale=us_sb[:, j : j + 1])
-
-        scaled_first = keep.tile([P, C], F32, name="scaled_first")
         scaled_turned = {}
 
-        def first_tile(half):
-            for n, part in enumerate(parts_of(half)):
-                product = flat(bank(half + 2 * n, "scores_direct_%d_%d" % (half, n))[:])[:, part]
-                scores(product, q_codes[:, :P], q_scales[:, :P], k_codes[half][:, part], k_scales[half][:, part])
-                cols = slice(half * HALF + part.start, half * HALF + part.stop)
-                nc.vector.tensor_tensor(scaled_first[:, cols], product, ts_rows[:, cols], ALU.mult)
-                nc.scalar.activation(e_sb[0][:, cols], scaled_first[:, cols], ACT.Exp, scale=us_sb[:, 0:1])
-
-        def turned_scores(tiles, half, first, index, kib):
+        def turned_scores(tiles, first, index, kib):
             rows = slice(tiles[0] * P, (tiles[-1] + 1) * P)
             width = len(tiles) * P
-            product = flat(bank(index, "scores_turned_%d_%d_%d" % (tiles[0], half, first))[:])
-            count = HALF // width
-            for n in range(count):
-                cols = chunk_cols(first + n)
-                scores(
-                    product[:, n * width : (n + 1) * width], k_codes[half][:, cols], k_scales[half][:, cols],
-                    q_codes[:, rows], q_scales[:, rows],
+            product = flat(bank(index, "scores_turned_%d_%d" % (tiles[0], first))[:])
+            chunks = range(first, first + HALF // width)
+            for n, chunk in enumerate(chunks):
+                slots = cols(chunk % 2, P)
+                product_mx(
+                    product[:, cols(n, width)], k_codes[chunk // 2][:, slots], k_scales[chunk // 2][:, slots],
+                    q_codes[tiles[0]][:], q_scales[:, rows],
                 )
-            for n in range(count):
-                name = "scaled_turned_%d_%d_%d" % (tiles[0], half, first + n)
-                tile = placed([P, width], F32, kib + n * width * 4 / 1024, name)
-                nc.scalar.activation(tile[:], product[:, n * width : (n + 1) * width], ACT.Copy, scale=ts_of_chunk(half, first + n))
+            for n, chunk in enumerate(chunks):
+                tile = placed([P, width], F32, kib + n * width * 4 / 1024, "scaled_turned_%d_%d" % (tiles[0], chunk))
+                scale = ts_of_chunk(chunk // CHUNKS, chunk % CHUNKS)
+                nc.scalar.activation(tile[:], product[:, cols(n, width)], ACT.Copy, scale=scale)
                 for i, j in enumerate(tiles):
-                    scaled_turned[(j, half, first + n)] = tile[:, chunk_cols(i)]
+                    scaled_turned[(j, chunk)] = tile[:, cols(i, P)]
 
         def turned_tile(j, indices):
-            for half in range(len(indices)):
+            for half in range(2):
                 back = bank(indices[half], "scores_back_%d_%d" % (j, half))
                 for b in range(CHUNKS):
-                    turn(back[:, b, :], scaled_turned[(j, half, b)])
-                exp_into_e(j, half, flat(back[:]))
+                    turn(back[:, b, :], scaled_turned[(j, half * CHUNKS + b)])
+                nc.scalar.activation(e_sb[j][:, cols(half, HALF)], flat(back[:]), ACT.Exp, scale=us_sb[:, cols(j, 1)])
 
         f_sb = [placed([P, C], F32, AT_F + 4 * j, "f_%d" % j) for j in range(PACK)]
         e_slots, f_slots = {}, {}
@@ -251,69 +247,43 @@ def tile_attend_gblkatt_kernel(tc, qT, kT, us, ts, wb, dp, offs, blkoffs, slotof
         def by_slots(window, kib, name):
             picked = placed([P, C], F32, kib, name)
             for half in range(2):
-                cols = half_cols(half)
-                nc.vector.tensor_copy(picked[:, cols], window[:].indirect(half_list(slot_list, half)))
+                nc.vector.tensor_copy(picked[:, cols(half, HALF)], window[:].indirect(part_of(slot_list, half, HALF)))
             return picked[:].rearrange("p (x i) -> p x i", i=2)
 
-        def form_f(j):
-            nc.gpsimd.tensor_tensor(f_sb[j][:], e_sb[j][:], dp_sb[j][:], ALU.mult)
+        def gather_e(j):
+            e_slots[j] = by_slots(e_sb[j], AT_E_SLOTS + 4 * j, "e_slots_%d" % j)
+            for part in (slice(0, C),) if j == 1 else (cols(0, HALF), cols(1, HALF)):
+                nc.gpsimd.tensor_tensor(f_sb[j][:, part], e_sb[j][:, part], dp_sb[j][:, part], ALU.mult)
+
+        def gather_f(j):
+            f_slots[j] = by_slots(f_sb[j], AT_F_SLOTS + 4 * j, "f_slots_%d" % j)
+
+        gather_e(0)
+        for half in range(2):
+            turned_scores([1], half * CHUNKS, 2 + half, AT_K_PAIRS + 2 * half)
+        turned_tile(1, (6, 7))
+        gather_f(0)
+        gather_e(1)
+        s_first = placed([P, X], F32, AT_TS_LISTED + 2, "s_first")
+        nc.gpsimd.tensor_tensor(s_first[:], e_slots[0][:, :, 0], e_slots[0][:, :, 1], ALU.add)
+        for n in range(4):
+            turned_scores([2, 3], 2 * n, (3, 6, 7, 3)[n], AT_K_PAIRS + 4 + 2 * n)
+        for j in (2, 3):
+            turned_tile(j, (0, 1) if j == 2 else (7, 3))
+            gather_e(j)
 
         def pair_sums_turned(pairs, index, name):
             sums = bank(index, name)
             for b in range(CHUNKS):
                 for i in range(2):
-                    turn(sums[:, b, :], pairs[:, chunk_cols(b), i], start=(i == 0), stop=(i == 1))
+                    turn(sums[:, b, :], pairs[:, cols(b, P), i], start=(i == 0), stop=(i == 1))
             return flat(sums[:])
 
-        def turn_back(src, index, name):
-            back = bank(index, name)
-            for b in range(CHUNKS):
-                turn(back[:, b, :], src[:, chunk_cols(b)])
-            return flat(back[:])
+        root, inverse, t_turned, t_sums, neg_f = {}, {}, {}, {}, {}
 
-        q_words = q_grouped[:].rearrange("p j m t -> p (j m t)").bitcast(F32).rearrange("p (j m u) -> p j m u", j=PACK, u=2)
-        q2_grouped = keep.tile([P, PACK, P, PACK], BF16, name="q2_grouped", align_bytes=64)
-        q2_codes = keep.tile([P, D], U32, name="q2_codes", align_bytes=64)
-        q2_scales = keep.tile([P, D], U8, name="q2_scales", align_bytes=64)
-        for u in range(2):
-            q_turned = bank(4 + u, "q_turned_%d" % u)
-            for j in range(PACK):
-                turn(q_turned[:, j, :], q_words[:, j, :, u])
-            nc.scalar.copy(
-                q2_grouped[:, 2 * u : 2 * u + 2, :, :],
-                flat(q_turned[:]).bitcast(BF16).rearrange("m (j p e) -> m e p j", j=PACK, e=2),
-            )
-        for half in range(2):
-            first_tile(half)
-        nc.vector.quantize_mx(
-            out=q2_codes[:].bitcast(E4M3), scales=q2_scales[:], in_=q2_grouped[:].rearrange("m t p j -> m (t p j)")
-        )
-        product = flat(bank(6, "scores_direct_second")[:])
-        scores(product, q_codes[:, P : 2 * P], q_scales[:, P : 2 * P], k_codes[1][:], k_scales[1][:])
-        scaled_second = placed([P, HALF], F32, AT_K_PAIRS + 2, "scaled_second")
-        nc.vector.tensor_tensor(scaled_second[:], product, ts_rows[:, half_cols(1)], ALU.mult)
-        turned_scores([1], 0, 0, 4, AT_K_PAIRS)
-        e_slots[0] = by_slots(e_sb[0], AT_SLOTS, "e_slots_0")
-        form_f(0)
-        exp_into_e(1, 1, scaled_second[:])
-        turned_tile(1, (2,))
-        e_slots[1] = by_slots(e_sb[1], AT_SLOTS + 4, "e_slots_1")
-        form_f(1)
-        s_first = placed([P, X], F32, AT_INVERSE + 8, "s_first")
-        nc.gpsimd.tensor_tensor(s_first[:], e_slots[0][:, :, 0], e_slots[0][:, :, 1], ALU.add)
-        for n, index in enumerate((3, 4, 2, 3)):
-            turned_scores([2, 3], n // 2, 2 * (n % 2), index, AT_K_PAIRS + 8 + 2 * n)
-        f_slots[0] = by_slots(f_sb[0], AT_Q_RAW + 4, "f_slots_0")
-        for j in (2, 3):
-            turned_tile(j, (0, 1) if j == 2 else (3, 0))
-            e_slots[j] = by_slots(e_sb[j], AT_SLOTS + 4 * j, "e_slots_%d" % j)
-            form_f(j)
-
-        root, inverse, neg_f, t_sums = {}, {}, {}, {}
-
-        def take_root(j, index, kib):
+        def take_root(j, index):
             sums = s_first[:] if j == 0 else pair_sums_turned(e_slots[j], index, "s_turned_%d" % j)
-            root[j] = placed([P, X], F32, kib, "root_%d" % j)
+            root[j] = placed([P, X], F32, AT_K_PAIRS + (9.5, 11.5, 0, 2)[j], "root_%d" % j)
             nc.scalar.activation(root[j][:], sums, ACT.Abs_reciprocal_sqrt)
 
         def take_inverse(j, index):
@@ -322,98 +292,120 @@ def tile_attend_gblkatt_kernel(tc, qT, kT, us, ts, wb, dp, offs, blkoffs, slotof
             nc.scalar.activation(inverse[j], back, ACT.Square)
             nc.gpsimd.tensor_tensor(h_window[j][:, :X], inverse[j], wb_sb[:, j, :], ALU.mult)
 
-        def negate_f(j, kib):
-            neg_f[j] = placed([P, C], F32, kib, "neg_f_%d" % j)
-            for half in range(2):
-                nc.scalar.activation(neg_f[j][:, half_cols(half)], f_sb[j][:, half_cols(half)], ACT.Copy, scale=-1.0)
+        def fetch_t(j):
+            t_turned[j] = placed([P, X], F32, AT_K_PAIRS + 11.5 if j == 0 else AT_K_LISTED + 2 * j, "t_turned_sb_%d" % j)
+            nc.scalar.copy(t_turned[j][:], t_banks[j])
 
-        m_turned = {}
-
-        def sum_m(j, index):
-            sums = pair_sums_turned(f_slots[j], index, "m_turned_%d" % j)
-            m_turned[j] = placed([P, X], F32, AT_INVERSE + 12 if j == 2 else AT_M_TURNED + 2 * (j % 2), "m_turned_sb_%d" % j)
-            nc.scalar.copy(m_turned[j][:], sums)
+        def negate_f(half, j, kib):
+            neg_f[(half, j)] = placed([P, HALF], F32, kib, "neg_f_%d_%d" % (half, j))
+            nc.scalar.activation(neg_f[(half, j)][:], f_sb[j][:, cols(half, HALF)], ACT.Copy, scale=-1.0)
 
         def form_m(j):
             nc.vector.tensor_tensor(m_window[j][:, :X], t_sums[j], inverse[j], ALU.mult)
 
-        take_root(0, None, AT_K_PAIRS + 14)
-        take_root(1, 1, AT_K_PAIRS + 12)
-        take_inverse(0, None)
-        sum_m(0, 3)
-        take_root(2, 1, AT_K_PAIRS + 10)
-        take_inverse(1, 5)
-        t_first = placed([P, X], F32, AT_INVERSE + 10, "t_first")
-        nc.scalar.copy(t_first[:], turn_back(m_turned[0], 7, "t_back_0"))
-        nc.gpsimd.tensor_tensor(m_window[0][:, :X], t_first[:], inverse[0], ALU.mult)
-        take_root(3, 3, AT_K_PAIRS + 8)
-        take_inverse(2, 2)
-        take_inverse(3, 5)
-        negate_f(0, AT_SLOTS + 8)
-        for j, kib in ((1, AT_DP + 8), (2, AT_SLOTS + 4), (3, AT_K_LATE + 4)):
-            f_slots[j] = by_slots(f_sb[j], kib, "f_slots_%d" % j)
-        sum_m(1, 3)
-        t_sums[1] = turn_back(m_turned[1], 1, "t_back_1")
-        negate_f(3, AT_SLOTS + 12)
-        sum_m(2, 2)
-        t_sums[2] = turn_back(m_turned[2], 7, "t_back_2")
-        negate_f(1, AT_SLOTS + 4)
-        sum_m(3, 2)
-        t_sums[3] = turn_back(m_turned[3], 5, "t_back_3")
-        negate_f(2, AT_K_LATE + 4)
+        q_words = q_grouped[:].rearrange("p j m t -> p (j m t)").bitcast(F32).rearrange("p (j m u) -> p j m u", j=PACK, u=2)
+        q2_codes = placed([P, D], U32, AT_DP + 7, "q2_codes")
+        q_turned, q2_grouped = {}, {}
+        q2_scales = keep.tile([P, D], U8, name="q2_scales", align_bytes=64)
 
-        e_m, factor, g_planes = {}, {}, {}
-        units = [(half, j) for half in range(2) for j in range(PACK)]
-        at_e_m = {
-            (0, 2): AT_DP + 2, (0, 3): AT_DP + 4,
-            (1, 0): AT_M_TURNED + 2, (1, 1): AT_INVERSE + 6,
-        }
-        at_e_m_pair = {(0, 0): AT_INVERSE + 12, (1, 2): AT_K_PAIRS + 4}
-        at_factor = {(0, j): AT_K_PAIRS + 2 * j for j in range(PACK)}
-        at_factor.update({(1, 0): AT_SLOTS, (1, 1): AT_SLOTS + 2, (1, 2): AT_DP + 12, (1, 3): AT_DP + 14})
-        at_g_planes = (AT_WB, AT_K_GROUPED)
+        def turn_queries(u, index):
+            q_turned[u] = bank(index, "q_turned_%d" % u)
+            for j in range(PACK):
+                turn(q_turned[u][:, j, :], q_words[:, j, :, u])
 
-        def look_up_m(half, j):
-            if (half, j) in at_e_m_pair:
-                both = placed([P, 2, HALF], F32, at_e_m_pair[(half, j)], "e_m_pair_%d" % half)
-                e_m[(half, j)], e_m[(half, j + 1)] = both[:, 0, :], both[:, 1, :]
-            elif (half, j) in at_e_m:
-                e_m[(half, j)] = placed([P, HALF], F32, at_e_m[(half, j)], "e_m_%d_%d" % (half, j))[:]
-            nc.vector.tensor_tensor(
-                e_m[(half, j)], m_window[j][:].indirect(half_list(blk_list, half)), e_sb[j][:, half_cols(half)], ALU.mult
+        def regroup_queries(u, kib):
+            q2_grouped[u] = placed([P, 2, P, PACK], BF16, kib, "q2_grouped_%d" % u)
+            nc.scalar.copy(q2_grouped[u][:], flat(q_turned[u][:]).bitcast(BF16).rearrange("m (j p e) -> m e p j", j=PACK, e=2))
+
+        def quantize_regrouped(u):
+            nc.vector.quantize_mx(
+                out=q2_codes[:, cols(u, 2 * P)].bitcast(E4M3),
+                scales=q2_scales[:, cols(u, 2 * P)],
+                in_=q2_grouped[u][:].rearrange("m t p j -> m (t p j)"),
             )
 
-        centred = {}
+        def turn_t(j, index):
+            t_banks[j] = pair_sums_turned(f_slots[j], index, "t_turned_%d" % j)
+
+        take_root(0, None)
+        take_root(1, 1)
+        take_inverse(0, None)
+        t_banks = {}
+        turn_t(0, 0)
+        turn_queries(1, 7)
+        turn_queries(0, 3)
+        take_root(2, 2)
+        for j in range(1, PACK):
+            gather_f(j)
+        take_inverse(1, 5)
+        fetch_t(0)
+        take_root(3, 4)
+        take_inverse(2, 6)
+        t_first = placed([P, X], F32, AT_TS_LISTED, "t_first")
+        nc.scalar.copy(t_first[:], turn_back(t_turned[0], 1, "t_back_0"))
+        nc.gpsimd.tensor_tensor(m_window[0][:, :X], t_first[:], inverse[0], ALU.mult)
+        take_inverse(3, 2)
+        negate_f(0, 0, AT_K_PAIRS + 2)
+        turn_t(1, 4)
+        fetch_t(1)
+        negate_f(0, 2, AT_F_SLOTS + 4)
+        negate_f(0, 3, AT_F_SLOTS + 6)
+        turn_t(2, 5)
+        fetch_t(2)
+        t_sums[1] = turn_back(t_turned[1], 6, "t_back_1")
+        regroup_queries(0, AT_F_SLOTS + 8)
+        negate_f(1, 0, AT_F_SLOTS + 10)
+        turn_t(3, 1)
+        fetch_t(3)
+        t_sums[2] = turn_back(t_turned[2], 2, "t_back_2")
+        t_sums[3] = turn_back(t_turned[3], 0, "t_back_3")
+        negate_f(0, 1, AT_F_SLOTS + 12)
+        negate_f(1, 1, AT_F_SLOTS + 14)
+        regroup_queries(1, AT_K_LISTED + 7)
+
+        e_m, centred, factor, g_planes = {}, {}, {}, {}
+        units = [(half, j) for half in range(2) for j in range(PACK)]
+        at_g_grouped = (AT_K_EARLY - 4, AT_TS)
+        at_g_planes = (AT_WB, AT_K_LATE)
+        at_e_m = {(0, 0): AT_K_LISTED + 2, (0, 1): AT_E_SLOTS, (0, 2): AT_K_LISTED + 5, (0, 3): AT_E_SLOTS + 2}
+        at_e_m.update({(1, 0): AT_INVERSE + 6, (1, 1): AT_K_PAIRS, (1, 2): AT_DP + 5, (1, 3): at_g_planes[0]})
+        at_factor = {(0, j): AT_DP + 2 * j for j in range(PACK)}
+        at_factor.update({(1, 0): AT_DP + 10, (1, 1): AT_DP + 12, (1, 2): AT_E_SLOTS + 6, (1, 3): AT_K_EARLY})
+
+        def look_up_m(half, j):
+            e_m[(half, j)] = placed([P, HALF], F32, at_e_m[(half, j)], "e_m_%d_%d" % (half, j))
+            nc.vector.tensor_tensor(
+                e_m[(half, j)][:], m_window[j][:].indirect(part_of(blk_list, half, HALF)), e_sb[j][:, cols(half, HALF)], ALU.mult
+            )
 
         def centre(half, j):
-            side = units.index((half, j)) % 2
-            turned = bank(7 - 5 * side, "centred_turned_%d_%d" % (half, j))
-            with_ts = placed([P, CHUNKS, P], F32, AT_WITH_TS + 2 * side, "with_ts_%d_%d" % (half, j))
+            side = j % 2
+            turned = bank(4 + side, "centred_turned_%d_%d" % (half, j))
+            with_ts = placed([P, CHUNKS, P], F32, AT_K_PAIRS + (0 if (half, j) == (0, 1) else 4 + 2 * side), "with_ts_%d_%d" % (half, j))
             for b in range(CHUNKS):
-                turn(turned[:, b, :], e_m[(half, j)][:, chunk_cols(b)], start=True, stop=False)
-                turn(turned[:, b, :], neg_f[j][:, chunk_cols(half * CHUNKS + b)], start=False, stop=True)
+                turn(turned[:, b, :], neg_f[(half, j)][:, cols(b, P)], start=True, stop=False)
+                turn(turned[:, b, :], e_m[(half, j)][:, cols(b, P)], start=False, stop=True)
             for b in range(CHUNKS):
                 nc.scalar.activation(with_ts[:, b, :], turned[:, b, :], ACT.Copy, scale=ts_of_chunk(half, b))
             centred[(half, j)] = flat(with_ts[:])
 
         def fetch_factor(half, j):
-            side = units.index((half, j)) % 2
-            back = turn_back(centred[(half, j)], 4 - side, "centred_back_%d_%d" % (half, j))
+            back = turn_back(centred[(half, j)], 1 + 5 * (j % 2), "centred_back_%d_%d" % (half, j))
             factor[(half, j)] = placed([P, HALF], F32, at_factor[(half, j)], "factor_%d_%d" % (half, j))
-            nc.scalar.activation(factor[(half, j)][:], back, ACT.Copy, scale=neg_us[:, j : j + 1])
+            nc.scalar.activation(factor[(half, j)][:], back, ACT.Copy, scale=neg_us[:, cols(j, 1)])
 
         def gradient(half, j):
             if j == 0:
                 g_planes[half] = placed([P, PACK, HALF], F32, at_g_planes[half], "g_planes_%d" % half)
             nc.vector.tensor_tensor(
-                g_planes[half][:, j, :], h_window[j][:].indirect(half_list(blk_list, half)), factor[(half, j)][:], ALU.mult
+                g_planes[half][:, j, :], h_window[j][:].indirect(part_of(blk_list, half, HALF)), factor[(half, j)][:], ALU.mult
             )
 
         g_codes = [keep.tile([P, HALF], U32, name="g_codes_%d" % half, align_bytes=64) for half in range(2)]
         g_scales = [keep.tile([P, HALF], U8, name="g_scales_%d" % half, align_bytes=64) for half in range(2)]
 
         def quantize_gradient(half):
-            g_grouped = placed([P, HALF, PACK], BF16, (AT_DP + 8, AT_TS)[half], "g_grouped_%d" % half)
+            g_grouped = placed([P, HALF, PACK], BF16, at_g_grouped[half], "g_grouped_%d" % half)
             nc.scalar.activation(
                 g_grouped[:].rearrange("p (c i) j -> p c j i", i=4),
                 g_planes[half][:].rearrange("p j (c i) -> p c j i", i=4),
@@ -424,66 +416,63 @@ def tile_attend_gblkatt_kernel(tc, qT, kT, us, ts, wb, dp, offs, blkoffs, slotof
         out_rows = out.rearrange("(p t) n -> t p n", t=PACK)
 
         def place_result(t, half):
-            product = bank((2, 3, 4, 1, 1, 1, 1, 1)[t + PACK * half], "dk_psum_%d_%d" % (t, half))
-            nc.tensor.matmul_mx(
-                out=flat(product[:]),
-                lhsT=q2_codes[:, chunk_cols(t)].bitcast(E4M3),
-                lhsT_scale=q2_scales[:, chunk_cols(t)],
-                rhs=g_codes[half][:].bitcast(E5M2),
-                rhs_scale=g_scales[half][:],
-                start=True,
-                stop=True,
-            )
-            name = "dk_%d_%d" % (t, half)
-            window = out_window[t % OUT_WINDOWS]
-            if t == LAST:
-                nc.scalar.copy(dk_last[:, half_cols(half)], flat(product[:]))
-                if half == 1:
-                    nc.vector.tensor_copy(window[:].indirect(tok_list[:]), dk_last[:])
-            else:
-                kib = at_g_planes[1] if (t, half) == (OUT_WINDOWS - 1, 0) else AT_F + 2 * (t + PACK * half)
-                dk = placed([P, HALF], F32, kib, name)
-                nc.scalar.copy(dk[:], flat(product[:]))
-                nc.vector.tensor_copy(window[:].indirect(half_list(tok_list, half)), dk[:])
+            product = bank((0, 2, 6, 3, 7, 0, 2, 3)[t + PACK * half], "dk_psum_%d_%d" % (t, half))
+            product_mx(flat(product[:]), q2_codes[:, cols(t, P)], q2_scales[:, cols(t, P)], g_codes[half][:], g_scales[half][:], E5M2)
+            at_dk = {(0, 0): AT_K_LATE + 8, (LAST, 0): at_g_planes[1]}
+            dk = placed([P, HALF], F32, at_dk.get((t, half), AT_F_SLOTS + 2 * (t + PACK * half)), "dk_%d_%d" % (t, half))
+            nc.scalar.copy(dk[:], flat(product[:]))
+            nc.vector.tensor_copy(out_window[t][:].indirect(part_of(tok_list, half, HALF)), dk[:])
             if half == 1 and t < LAST:
-                nc.sync.dma_start(out=out_rows[t], in_=window[:])
+                nc.sync.dma_start(out=out_rows[t], in_=out_window[t][:])
             elif half == 1:
-                nc.sync.dma_start(out=out_rows[t][:, : T // 2], in_=window[:, : T // 2])
-                nc.scalar.dma_start(out=out_rows[t][:, T // 2 :], in_=window[:, T // 2 :])
+                nc.sync.dma_start(out=out_rows[t][:, : T // 2], in_=out_window[t][:, : T // 2])
+                nc.scalar.dma_start(out=out_rows[t][:, T // 2 :], in_=out_window[t][:, T // 2 :])
+
+        def clear_window(kib):
+            out_window.append(placed([P, T], F32, kib, "out_window_%d" % len(out_window)))
+            nc.gpsimd.memset(out_window[-1][:], 0.0)
 
         form_m(1)
-        form_m(2)
         look_up_m(0, 0)
         look_up_m(0, 1)
+        form_m(2)
+        form_m(LAST)
         look_up_m(0, 2)
-        form_m(3)
+        look_up_m(0, LAST)
         look_up_m(1, 0)
-        look_up_m(0, 3)
+        centre(0, 0)
+        for j in range(1, PACK):
+            centre(0, j)
+            fetch_factor(0, j - 1)
+        centre(1, 0)
+        fetch_factor(0, LAST)
+        gradient(0, 0)
         look_up_m(1, 1)
-        centre(*units[0])
-        for n in range(1, 6):
-            centre(*units[n])
-            fetch_factor(*units[n - 1])
-        for j in range(PACK):
+        centre(1, 1)
+        fetch_factor(1, 0)
+        for j in range(1, PACK):
             gradient(0, j)
+        gradient(1, 0)
         look_up_m(1, 2)
-        look_up_m(1, 3)
+        for u in range(2):
+            quantize_regrouped(u)
         quantize_gradient(0)
         fetch_factor(1, 1)
-        centre(1, 2)
-        centre(1, 3)
-        fetch_factor(1, 2)
-        fetch_factor(1, 3)
-        for j in range(PACK):
-            gradient(1, j)
-        out_window.append(placed([P, T], F32, AT_DP + 8, "out_window_2"))
-        nc.gpsimd.memset(out_window[2][:], 0.0)
+        look_up_m(1, LAST)
+        gradient(1, 1)
         place_result(0, 0)
+        place_result(1, 0)
+        clear_window(AT_K_LATE + 8)
+        for j in range(2, PACK):
+            negate_f(1, j, at_g_planes[0] + 2 * j)
+        for j in range(2, PACK):
+            centre(1, j)
+        for j in range(2, PACK):
+            fetch_factor(1, j)
+            gradient(1, j)
+        place_result(2, 0)
+        clear_window(AT_K_EARLY)
         quantize_gradient(1)
-        for t in range(1, OUT_WINDOWS):
-            place_result(t, 0)
-        for t in range(OUT_WINDOWS):
+        place_result(LAST, 0)
+        for t in range(PACK):
             place_result(t, 1)
-        dk_last = placed([P, C], F32, AT_SLOTS, "dk_last")
-        for half in range(2):
-            place_result(LAST, half)

@@ -104,8 +104,8 @@ def tile_attend_gblkatt_kernel(tc, qT, kT, us, ts, wb, dp, offs, blkoffs, slotof
         q_raw = [placed([P, PACK, Q_PIECE], F32, AT_Q_RAW + 4 * s, "q_raw_%d" % s) for s in range(2)]
         for s in range(2):
             nc.sync.dma_start(out=q_raw[s][:], in_=q_rows[:, :, cols(s, Q_PIECE)])
-        us_sb = placed([P, PACK], F32, AT_F_SLOTS + 4, "us_sb")
-        nc.sync.dma_start(out=us_sb[:], in_=us.rearrange("(p j) o -> p (j o)", j=PACK))
+        us_sb = placed([P, 32], F32, AT_F_SLOTS + 8 - 1 / 16, "us_sb")
+        nc.sync.dma_start(out=us_sb[:, :PACK], in_=us.rearrange("(p j) o -> p (j o)", j=PACK))
         nc.sync.dma_start(slot_list[:], slotoffs)
         dp_rows = dp.rearrange("(p j) c -> j p c", j=PACK)
         dp_sb = [placed([P, C], F32, AT_DP + 4 * j, "dp_%d" % j) for j in range(PACK)]
@@ -119,7 +119,7 @@ def tile_attend_gblkatt_kernel(tc, qT, kT, us, ts, wb, dp, offs, blkoffs, slotof
         h_window, m_window = blk_windows[:PACK], blk_windows[PACK:]
 
         k_pairs = [placed([P, T, 2], BF16, AT_K_PAIRS + 8 * u, "k_pairs_%d" % u) for u in range(2)]
-        k_listed = [placed([P, 2, QUARTER], U32, AT_K_LISTED + 2 * n, "k_listed_%d" % n) for n in range(4)]
+        k_listed = [placed([P, 2, QUARTER], U32, AT_K_LISTED + 2 * n if n else AT_TS, "k_listed_%d" % n) for n in range(4)]
         k_grouped = [placed([P, QUARTER * PACK], BF16, AT_K_GROUPED + 2 * n, "k_grouped_%d" % n) for n in range(4)]
 
         def round_keys(u, cuts, on_vector):
@@ -164,7 +164,7 @@ def tile_attend_gblkatt_kernel(tc, qT, kT, us, ts, wb, dp, offs, blkoffs, slotof
         round_keys(1, (1024, 1536, 1792, 2048), (1, 2, 3))
         gather_keys(1)
 
-        q_grouped = keep.tile([P, PACK, P, PACK], BF16, name="q_grouped", align_bytes=64)
+        q_grouped = placed([P, PACK, P, PACK], BF16, AT_TS, "q_grouped")
 
         def rounded_queries(s):
             dst = q_grouped[:, :, cols(s, Q_PIECE // PACK), :].rearrange("p j m t -> p m j t")
@@ -183,10 +183,10 @@ def tile_attend_gblkatt_kernel(tc, qT, kT, us, ts, wb, dp, offs, blkoffs, slotof
         q_codes = {
             0: keep.tile([P, P], U32, name="q_codes_0", align_bytes=64),
             1: placed([P, P], U32, AT_K_GROUPED + 4, "q_codes_1"),
-            2: placed([P, 2 * P], U32, AT_K_GROUPED + 4.5, "q_codes_2"),
+            2: placed([P, 2 * P], U32, AT_TS_ROWS, "q_codes_2"),
         }
         q_scales = keep.tile([P, R], U8, name="q_scales", align_bytes=64)
-        k_codes = [placed([P, QUARTER], U32, AT_K_LATE if n == 0 else AT_Q_RAW + n, "k_codes_%d" % n) for n in range(4)]
+        k_codes = [placed([P, QUARTER], U32, (AT_K_LATE, AT_Q_RAW + 1, AT_K_LISTED + 6, AT_K_LISTED + 7)[n], "k_codes_%d" % n) for n in range(4)]
         k_scales = [keep.tile([P, QUARTER], U8, name="k_scales_%d" % n, align_bytes=64) for n in range(4)]
 
         def quantize_queries(first, count):
@@ -202,8 +202,10 @@ def tile_attend_gblkatt_kernel(tc, qT, kT, us, ts, wb, dp, offs, blkoffs, slotof
             if n == 0:
                 quantize_queries(0, 1)
 
+        quantize_queries(1, 1)
+
         neg_us = keep.tile([P, PACK], F32, name="neg_us")
-        nc.scalar.activation(neg_us[:], us_sb[:], ACT.Copy, scale=-1.0)
+        nc.scalar.activation(neg_us[:], us_sb[:, :PACK], ACT.Copy, scale=-1.0)
         e_sb = [placed([P, C], F32, AT_E + 4 * j, "e_%d" % j) for j in range(PACK)]
         scaled_first = [placed([P, QUARTER], F32, AT_K_GROUPED + (5.5, 6.5, 7.5, 0)[n], "scaled_first_%d" % n) for n in range(4)]
         for n in range(4):
@@ -211,7 +213,6 @@ def tile_attend_gblkatt_kernel(tc, qT, kT, us, ts, wb, dp, offs, blkoffs, slotof
             product_mx(product, q_codes[0][:], q_scales[:, :P], k_codes[n][:], k_scales[n][:])
             nc.vector.tensor_tensor(scaled_first[n][:], product, ts_rows[n // 2][:, cols(n % 2, QUARTER)], ALU.mult)
             nc.scalar.activation(e_sb[0][:, cols(n, QUARTER)], scaled_first[n][:], ACT.Exp, scale=us_sb[:, 0:1])
-        quantize_queries(1, 1)
         quantize_queries(2, 2)
 
         scaled_turned = {}
@@ -345,22 +346,22 @@ def tile_attend_gblkatt_kernel(tc, qT, kT, us, ts, wb, dp, offs, blkoffs, slotof
         nc.scalar.copy(t_first[:], turn_back(t_turned[0], 1, "t_back_0"))
         nc.gpsimd.tensor_tensor(m_window[0][:, :X], t_first[:], inverse[0], ALU.mult)
         take_inverse(3, 2)
-        negate_f(0, 0, AT_K_PAIRS + 2)
+        negate_f(1, 1, AT_K_PAIRS + 2)
         turn_t(1, 4)
         fetch_t(1)
         negate_f(0, 2, AT_F_SLOTS + 4)
         negate_f(0, 3, AT_F_SLOTS + 6)
-        turn_t(2, 5)
-        fetch_t(2)
         t_sums[1] = turn_back(t_turned[1], 6, "t_back_1")
+        turn_t(2, 2)
+        fetch_t(2)
+        t_sums[2] = turn_back(t_turned[2], 5, "t_back_2")
         regroup_queries(0, AT_F_SLOTS + 8)
         negate_f(1, 0, AT_F_SLOTS + 10)
-        turn_t(3, 1)
+        turn_t(3, 4)
         fetch_t(3)
-        t_sums[2] = turn_back(t_turned[2], 2, "t_back_2")
         t_sums[3] = turn_back(t_turned[3], 0, "t_back_3")
-        negate_f(0, 1, AT_F_SLOTS + 12)
-        negate_f(1, 1, AT_F_SLOTS + 14)
+        negate_f(0, 0, AT_F_SLOTS + 12)
+        negate_f(0, 1, AT_F_SLOTS + 14)
         regroup_queries(1, AT_K_LISTED + 7)
 
         e_m, centred, factor, g_planes = {}, {}, {}, {}
@@ -380,7 +381,7 @@ def tile_attend_gblkatt_kernel(tc, qT, kT, us, ts, wb, dp, offs, blkoffs, slotof
 
         def centre(half, j):
             side = j % 2
-            turned = bank(4 + side, "centred_turned_%d_%d" % (half, j))
+            turned = bank(2 + 2 * side, "centred_turned_%d_%d" % (half, j))
             with_ts = placed([P, CHUNKS, P], F32, AT_K_PAIRS + (0 if (half, j) == (0, 1) else 4 + 2 * side), "with_ts_%d_%d" % (half, j))
             for b in range(CHUNKS):
                 turn(turned[:, b, :], neg_f[(half, j)][:, cols(b, P)], start=True, stop=False)
@@ -416,7 +417,7 @@ def tile_attend_gblkatt_kernel(tc, qT, kT, us, ts, wb, dp, offs, blkoffs, slotof
         out_rows = out.rearrange("(p t) n -> t p n", t=PACK)
 
         def place_result(t, half):
-            product = bank((0, 2, 6, 3, 7, 0, 2, 3)[t + PACK * half], "dk_psum_%d_%d" % (t, half))
+            product = bank((0, 5, 6, 3, 7, 0, 5, 3)[t + PACK * half], "dk_psum_%d_%d" % (t, half))
             product_mx(flat(product[:]), q2_codes[:, cols(t, P)], q2_scales[:, cols(t, P)], g_codes[half][:], g_scales[half][:], E5M2)
             at_dk = {(0, 0): AT_K_LATE + 8, (LAST, 0): at_g_planes[1]}
             dk = placed([P, HALF], F32, at_dk.get((t, half), AT_F_SLOTS + 2 * (t + PACK * half)), "dk_%d_%d" % (t, half))

@@ -270,7 +270,7 @@ def tile_attend_gblkatt_kernel(tc, qT, kT, us, ts, wb, dp, offs, blkoffs, slotof
         for n in range(4):
             turned_scores([2, 3], 2 * n, (3, 6, 7, 3)[n], AT_K_PAIRS + 4 + 2 * n)
         for j in (2, 3):
-            turned_tile(j, (0, 1) if j == 2 else (7, 3))
+            turned_tile(j, (0, 1) if j == 2 else (3, 0))
             gather_e(j)
 
         def pair_sums_turned(pairs, index, name):
@@ -332,10 +332,9 @@ def tile_attend_gblkatt_kernel(tc, qT, kT, us, ts, wb, dp, offs, blkoffs, slotof
         take_root(1, 1)
         take_inverse(0, None)
         t_banks = {}
-        turn_t(0, 0)
-        turn_queries(1, 7)
-        turn_queries(0, 3)
-        take_root(2, 2)
+        turn_t(0, 3)
+        turn_queries(0, 0)
+        take_root(2, 7)
         for j in range(1, PACK):
             gather_f(j)
         take_inverse(1, 5)
@@ -343,23 +342,24 @@ def tile_attend_gblkatt_kernel(tc, qT, kT, us, ts, wb, dp, offs, blkoffs, slotof
         take_root(3, 4)
         take_inverse(2, 6)
         t_first = placed([P, X], F32, AT_TS_LISTED, "t_first")
-        nc.scalar.copy(t_first[:], turn_back(t_turned[0], 1, "t_back_0"))
+        nc.scalar.copy(t_first[:], turn_back(t_turned[0], 2, "t_back_0"))
         nc.gpsimd.tensor_tensor(m_window[0][:, :X], t_first[:], inverse[0], ALU.mult)
-        take_inverse(3, 2)
+        take_inverse(3, 7)
         negate_f(1, 1, AT_K_PAIRS + 2)
         turn_t(1, 4)
         fetch_t(1)
         negate_f(0, 2, AT_F_SLOTS + 4)
         negate_f(0, 3, AT_F_SLOTS + 6)
         t_sums[1] = turn_back(t_turned[1], 6, "t_back_1")
-        turn_t(2, 2)
+        turn_t(2, 7)
         fetch_t(2)
         t_sums[2] = turn_back(t_turned[2], 5, "t_back_2")
+        turn_queries(1, 1)
         regroup_queries(0, AT_F_SLOTS + 8)
         negate_f(1, 0, AT_F_SLOTS + 10)
         turn_t(3, 4)
         fetch_t(3)
-        t_sums[3] = turn_back(t_turned[3], 0, "t_back_3")
+        t_sums[3] = turn_back(t_turned[3], 3, "t_back_3")
         negate_f(0, 0, AT_F_SLOTS + 12)
         negate_f(0, 1, AT_F_SLOTS + 14)
         regroup_queries(1, AT_K_LISTED + 7)
@@ -381,7 +381,7 @@ def tile_attend_gblkatt_kernel(tc, qT, kT, us, ts, wb, dp, offs, blkoffs, slotof
 
         def centre(half, j):
             side = j % 2
-            turned = bank(2 + 2 * side, "centred_turned_%d_%d" % (half, j))
+            turned = bank(7 - 3 * side, "centred_turned_%d_%d" % (half, j))
             with_ts = placed([P, CHUNKS, P], F32, AT_K_PAIRS + (0 if (half, j) == (0, 1) else 4 + 2 * side), "with_ts_%d_%d" % (half, j))
             for b in range(CHUNKS):
                 turn(turned[:, b, :], neg_f[(half, j)][:, cols(b, P)], start=True, stop=False)
@@ -391,7 +391,7 @@ def tile_attend_gblkatt_kernel(tc, qT, kT, us, ts, wb, dp, offs, blkoffs, slotof
             centred[(half, j)] = flat(with_ts[:])
 
         def fetch_factor(half, j):
-            back = turn_back(centred[(half, j)], 1 + 5 * (j % 2), "centred_back_%d_%d" % (half, j))
+            back = turn_back(centred[(half, j)], 2 + 4 * (j % 2), "centred_back_%d_%d" % (half, j))
             factor[(half, j)] = placed([P, HALF], F32, at_factor[(half, j)], "factor_%d_%d" % (half, j))
             nc.scalar.activation(factor[(half, j)][:], back, ACT.Copy, scale=neg_us[:, cols(j, 1)])
 
@@ -417,7 +417,7 @@ def tile_attend_gblkatt_kernel(tc, qT, kT, us, ts, wb, dp, offs, blkoffs, slotof
         out_rows = out.rearrange("(p t) n -> t p n", t=PACK)
 
         def place_result(t, half):
-            product = bank((0, 5, 6, 3, 7, 0, 5, 3)[t + PACK * half], "dk_psum_%d_%d" % (t, half))
+            product = bank((0, 5, 6, 3, 1, 0, 5, 3)[t + PACK * half], "dk_psum_%d_%d" % (t, half))
             product_mx(flat(product[:]), q2_codes[:, cols(t, P)], q2_scales[:, cols(t, P)], g_codes[half][:], g_scales[half][:], E5M2)
             at_dk = {(0, 0): AT_K_LATE + 8, (LAST, 0): at_g_planes[1]}
             dk = placed([P, HALF], F32, at_dk.get((t, half), AT_F_SLOTS + 2 * (t + PACK * half)), "dk_%d_%d" % (t, half))

@@ -31,7 +31,7 @@ BANK_BYTES = 2048
 
 AT_TS, AT_K_PAIRS, AT_K_LISTED, AT_K_GROUPED, AT_Q_RAW, AT_K_EARLY, AT_K_LATE = 0, 8, 24, 32, 40, 48, 64
 AT_E, AT_F, AT_DP, AT_WB, AT_BLK, AT_TS_LISTED, AT_E_SLOTS, AT_INVERSE, AT_F_SLOTS = 80, 96, 112, 128, 136, 153, 157, 174, 182
-AT_TS_ROWS = 198
+AT_TS_ROWS, AT_LATE = 198, 204
 
 
 def tile_attend_gblkatt_kernel(tc, qT, kT, us, ts, wb, dp, offs, blkoffs, slotoffs, out):
@@ -204,8 +204,9 @@ def tile_attend_gblkatt_kernel(tc, qT, kT, us, ts, wb, dp, offs, blkoffs, slotof
 
         quantize_queries(1, 1)
 
-        neg_us = keep.tile([P, PACK], F32, name="neg_us")
-        nc.scalar.activation(neg_us[:], us_sb[:, :PACK], ACT.Copy, scale=-1.0)
+        neg_us = [placed([P, 32], F32, AT_LATE - 1 / 16, "neg_us_0"), keep.tile([P, PACK], F32, name="neg_us_1")]
+        for half in range(2):
+            nc.scalar.activation(neg_us[half][:, :PACK], us_sb[:, :PACK], ACT.Copy, scale=-1.0)
         e_sb = [placed([P, C], F32, AT_E + 4 * j, "e_%d" % j) for j in range(PACK)]
         scaled_first = [placed([P, QUARTER], F32, AT_K_GROUPED + (5.5, 6.5, 7.5, 0)[n], "scaled_first_%d" % n) for n in range(4)]
         for n in range(4):
@@ -305,7 +306,7 @@ def tile_attend_gblkatt_kernel(tc, qT, kT, us, ts, wb, dp, offs, blkoffs, slotof
             nc.vector.tensor_tensor(m_window[j][:, :X], t_sums[j], inverse[j], ALU.mult)
 
         q_words = q_grouped[:].rearrange("p j m t -> p (j m t)").bitcast(F32).rearrange("p (j m u) -> p j m u", j=PACK, u=2)
-        q2_codes = placed([P, D], U32, AT_DP + 7, "q2_codes")
+        q2_codes = placed([P, D], U32, AT_LATE, "q2_codes")
         q_turned, q2_grouped = {}, {}
         q2_scales = keep.tile([P, D], U8, name="q2_scales", align_bytes=64)
 
@@ -369,7 +370,7 @@ def tile_attend_gblkatt_kernel(tc, qT, kT, us, ts, wb, dp, offs, blkoffs, slotof
         at_g_grouped = (AT_K_EARLY - 4, AT_TS)
         at_g_planes = (AT_WB, AT_K_LATE)
         at_e_m = {(0, 0): AT_K_LISTED + 2, (0, 1): AT_E_SLOTS, (0, 2): AT_K_LISTED + 5, (0, 3): AT_E_SLOTS + 2}
-        at_e_m.update({(1, 0): AT_INVERSE + 6, (1, 1): AT_K_PAIRS, (1, 2): AT_DP + 5, (1, 3): at_g_planes[0]})
+        at_e_m.update({(1, 0): AT_INVERSE + 6, (1, 1): AT_K_PAIRS, (1, 2): AT_LATE - 2, (1, 3): at_g_planes[0]})
         at_factor = {(0, j): AT_DP + 2 * j for j in range(PACK)}
         at_factor.update({(1, 0): AT_DP + 10, (1, 1): AT_DP + 12, (1, 2): AT_E_SLOTS + 6, (1, 3): AT_K_EARLY})
 
@@ -382,7 +383,7 @@ def tile_attend_gblkatt_kernel(tc, qT, kT, us, ts, wb, dp, offs, blkoffs, slotof
         def centre(half, j):
             side = j % 2
             turned = bank(7 - 3 * side, "centred_turned_%d_%d" % (half, j))
-            with_ts = placed([P, CHUNKS, P], F32, AT_K_PAIRS + (0 if (half, j) == (0, 1) else 4 + 2 * side), "with_ts_%d_%d" % (half, j))
+            with_ts = placed([P, CHUNKS, P], F32, {(0, 1): AT_K_PAIRS, (1, 0): at_g_grouped[0]}.get((half, j), AT_K_PAIRS + 4 + 2 * side), "with_ts_%d_%d" % (half, j))
             for b in range(CHUNKS):
                 turn(turned[:, b, :], neg_f[(half, j)][:, cols(b, P)], start=True, stop=False)
                 turn(turned[:, b, :], e_m[(half, j)][:, cols(b, P)], start=False, stop=True)
@@ -393,7 +394,7 @@ def tile_attend_gblkatt_kernel(tc, qT, kT, us, ts, wb, dp, offs, blkoffs, slotof
         def fetch_factor(half, j):
             back = turn_back(centred[(half, j)], 2 + 4 * (j % 2), "centred_back_%d_%d" % (half, j))
             factor[(half, j)] = placed([P, HALF], F32, at_factor[(half, j)], "factor_%d_%d" % (half, j))
-            nc.scalar.activation(factor[(half, j)][:], back, ACT.Copy, scale=neg_us[:, cols(j, 1)])
+            nc.scalar.activation(factor[(half, j)][:], back, ACT.Copy, scale=neg_us[half][:, cols(j, 1)])
 
         def gradient(half, j):
             if j == 0:

@@ -424,11 +424,8 @@ def tile_attend_gblkatt_kernel(tc, qT, kT, us, ts, wb, dp, offs, blkoffs, slotof
             dk = placed([P, HALF], F32, at_dk.get((t, half), AT_F_SLOTS + 2 * (t + PACK * half)), "dk_%d_%d" % (t, half))
             nc.scalar.copy(dk[:], flat(product[:]))
             nc.vector.tensor_copy(out_window[t][:].indirect(part_of(tok_list, half, HALF)), dk[:])
-            if half == 1 and t < LAST:
+            if half == 1:
                 nc.sync.dma_start(out=out_rows[t], in_=out_window[t][:])
-            elif half == 1:
-                nc.sync.dma_start(out=out_rows[t][:, : T // 2], in_=out_window[t][:, : T // 2])
-                nc.scalar.dma_start(out=out_rows[t][:, T // 2 :], in_=out_window[t][:, T // 2 :])
 
         def clear_window(kib):
             out_window.append(placed([P, T], F32, kib, "out_window_%d" % len(out_window)))

@@ -21,17 +21,18 @@ P = 128
 PACK = 4
 LAST = PACK - 1
 HALF = 512
-QUARTER = 256
+PART = 256
+PARTS = C // PART
 CHUNKS = HALF // P
 Q_PIECE = R // 2
-BLK_WINDOW = X + 8
-BLK_WINDOW_KIB = 2.125
 TS_ROW = P - 1
 BANK_BYTES = 2048
+BLK_WINDOW = X + 8
+BLK_WINDOW_KIB = 2.125
 
-AT_TS, AT_K_PAIRS, AT_K_LISTED, AT_K_GROUPED, AT_Q_RAW, AT_K_EARLY, AT_K_LATE = 0, 8, 24, 32, 40, 48, 64
-AT_E, AT_F, AT_DP, AT_WB, AT_BLK, AT_TS_LISTED, AT_E_SLOTS, AT_INVERSE, AT_F_SLOTS = 80, 96, 112, 128, 136, 153, 157, 174, 182
-AT_TS_ROWS, AT_LATE = 198, 204
+AT_K_RAW, AT_OUT, AT_E, AT_F, AT_W, AT_DP, AT_UTS, AT_WB, AT_INV = 0, 32, 64, 80, 96, 112, 128, 144, 152
+AT_K_PLANES, AT_TS, AT_TS_LISTED, AT_TS_ROWS, AT_Q_RAW, AT_Q_GROUPED, AT_K_CODES, AT_Z, AT_LATE = 160, 168, 176, 180, 184, 192, 196, 200, 204
+AT_H, AT_M = 208, 216.5
 
 
 def tile_attend_gblkatt_kernel(tc, qT, kT, us, ts, wb, dp, offs, blkoffs, slotoffs, out):
@@ -76,402 +77,373 @@ def tile_attend_gblkatt_kernel(tc, qT, kT, us, ts, wb, dp, offs, blkoffs, slotof
                 stop=True,
             )
 
+        def move(engine, dst, src):
+            if engine == "vector":
+                nc.vector.tensor_copy(dst, src)
+            else:
+                nc.scalar.activation(dst, src, ACT.Copy)
+
+        def by_fours(woven, planes):
+            return woven.rearrange("p (c i) t -> p c t i", i=4), planes.rearrange("p t (c i) -> p c t i", i=4)
+
         tok_list = keep.tile([P, C // 16], U16, name="tok_list")
         blk_list = keep.tile([P, C // 16], U16, name="blk_list")
         slot_list = keep.tile([P, C // 16], U16, name="slot_list")
         ident = keep.tile([P, P], F32, name="ident")
+        us_sb = keep.tile([P, 8], F32, name="us_sb")
 
         ts_window = placed([P, T], F32, AT_TS, "ts_window")
         nc.scalar.dma_start(out=ts_window[TS_ROW:P, :], in_=ts[0:1, :])
         nc.vector.memset(ts_window[0:TS_ROW, :].bitcast(I32), 0)
-        out_window = [keep.tile([P, T], F32, name="out_window_0")]
-        ts_listed = placed([P, C], F32, AT_TS_LISTED, "ts_listed")
         nc.sync.dma_start(tok_list[:], offs)
         make_identity(nc, ident[:])
-        nc.vector.memset(out_window[0][:].bitcast(I32), 0)
-        nc.vector.tensor_copy(ts_listed[:], ts_window[:].indirect(tok_list[:]))
-
-        k_rows = kT.rearrange("(p u e) n -> p u e n", u=2, e=2)
-        k_ends = ((T // 2, T), (T // 2, 3 * T // 4, 7 * T // 8, T))
-        k_pieces = [[slice(first, last) for first, last in zip((0,) + ends[:-1], ends)] for ends in k_ends]
-        k_raw = {}
-        for u in range(2):
-            for s, tokens in enumerate(k_pieces[u]):
-                kib = (AT_K_EARLY, AT_K_LATE)[u] + tokens.start * 8 / 1024
-                k_raw[(u, s)] = placed([P, 2, tokens.stop - tokens.start], F32, kib, "k_raw_%d_%d" % (u, s))
-                nc.sync.dma_start(out=k_raw[(u, s)][:], in_=k_rows[:, u, :, tokens])
-        q_rows = qT.rearrange("(p t) r -> p t r", t=PACK)
-        q_raw = [placed([P, PACK, Q_PIECE], F32, AT_Q_RAW + 4 * s, "q_raw_%d" % s) for s in range(2)]
-        for s in range(2):
-            nc.sync.dma_start(out=q_raw[s][:], in_=q_rows[:, :, cols(s, Q_PIECE)])
-        us_sb = placed([P, 32], F32, AT_F_SLOTS + 8 - 1 / 16, "us_sb")
+        q_raw = placed([P, PACK, R], F32, AT_Q_RAW, "q_raw")
+        nc.sync.dma_start(out=q_raw[:], in_=qT.rearrange("(p t) r -> p t r", t=PACK))
         nc.sync.dma_start(out=us_sb[:, :PACK], in_=us.rearrange("(p j) o -> p (j o)", j=PACK))
-        nc.sync.dma_start(slot_list[:], slotoffs)
+        k_rows = kT.rearrange("(p t) n -> t p n", t=PACK)
+        k_raw = [placed([P, T], F32, AT_K_RAW + 8 * t, "k_raw_%d" % t) for t in range(PACK)]
+        for t in range(PACK):
+            nc.sync.dma_start(out=k_raw[t][:], in_=k_rows[t])
         dp_rows = dp.rearrange("(p j) c -> j p c", j=PACK)
         dp_sb = [placed([P, C], F32, AT_DP + 4 * j, "dp_%d" % j) for j in range(PACK)]
-        for j in range(PACK):
+        nc.sync.dma_start(out=dp_sb[0][:], in_=dp_rows[0])
+        nc.sync.dma_start(slot_list[:], slotoffs)
+        for j in range(1, PACK):
             nc.sync.dma_start(out=dp_sb[j][:], in_=dp_rows[j])
         wb_sb = placed([P, PACK, X], F32, AT_WB, "wb_sb")
         nc.sync.dma_start(out=wb_sb[:], in_=wb.rearrange("(p j) x -> p j x", j=PACK))
         nc.sync.dma_start(blk_list[:], blkoffs)
 
-        blk_windows = [placed([P, BLK_WINDOW], F32, AT_BLK + BLK_WINDOW_KIB * n, "blk_window_%d" % n) for n in range(2 * PACK)]
-        h_window, m_window = blk_windows[:PACK], blk_windows[PACK:]
-
-        k_pairs = [placed([P, T, 2], BF16, AT_K_PAIRS + 8 * u, "k_pairs_%d" % u) for u in range(2)]
-        k_listed = [placed([P, 2, QUARTER], U32, AT_K_LISTED + 2 * n if n else AT_TS, "k_listed_%d" % n) for n in range(4)]
-        k_grouped = [placed([P, QUARTER * PACK], BF16, AT_K_GROUPED + 2 * n, "k_grouped_%d" % n) for n in range(4)]
-
-        def round_keys(u, cuts, on_vector):
-            for n, (first, last) in enumerate(zip((0,) + cuts[:-1], cuts)):
-                s = [tokens.start <= first < tokens.stop for tokens in k_pieces[u]].index(True)
-                start = k_pieces[u][s].start
-                dst = k_pairs[u][:, first:last, :]
-                src = k_raw[(u, s)][:, :, first - start : last - start].rearrange("p e n -> p n e")
-                if n in on_vector:
-                    nc.vector.tensor_copy(dst, src)
-                else:
-                    nc.scalar.activation(dst, src, ACT.Copy)
-
-        def gather_keys(u):
-            window = flat(k_pairs[u][:]).bitcast(U32)
-            for n in range(4):
-                nc.vector.tensor_copy(k_listed[n][:, u, :], window.indirect(part_of(tok_list, n, QUARTER)))
-
-        round_keys(0, (1024, 1408, 2048), (2,))
-        for window in blk_windows:
-            nc.gpsimd.memset(window[:, X:], 0.0)
-        out_window.append(placed([P, T], F32, AT_K_EARLY + 8, "out_window_1"))
+        out_window = [placed([P, T], F32, AT_OUT + 8 * t, "out_window_%d" % t) for t in range(PACK)]
+        nc.vector.memset(out_window[0][:].bitcast(I32), 0)
+        ts_listed = placed([P, C], F32, AT_TS_LISTED, "ts_listed")
+        nc.vector.tensor_copy(ts_listed[:], ts_window[:].indirect(tok_list[:]))
         nc.gpsimd.memset(out_window[1][:], 0.0)
-        gather_keys(0)
+        nc.vector.memset(out_window[2][:].bitcast(I32), 0)
+        nc.gpsimd.memset(out_window[3][:], 0.0)
+        h_window = [placed([P, BLK_WINDOW], F32, AT_H + BLK_WINDOW_KIB * j, "h_window_%d" % j) for j in range(PACK)]
+        m_window = [placed([P, BLK_WINDOW], F32, AT_M + BLK_WINDOW_KIB * j, "m_window_%d" % j) for j in range(PACK)]
+        for window in h_window + m_window:
+            nc.gpsimd.memset(window[:, X:], 0.0)
+
+        q_grouped = placed([P, PACK, P, PACK], BF16, AT_Q_GROUPED, "q_grouped")
+        q_codes = keep.tile([P, R], U32, name="q_codes", align_bytes=64)
+        q_scales = keep.tile([P, R], U8, name="q_scales", align_bytes=64)
+        nc.scalar.activation(q_grouped[:].rearrange("p j m t -> p m t j"), q_raw[:].rearrange("p t (m j) -> p m t j", j=PACK), ACT.Copy)
 
         ts_col = keep.tile([P, C // P], F32, name="ts_col")
-        ts_rows = [placed([P, HALF], F32, AT_TS_ROWS + 2 * half, "ts_rows_%d" % half) for half in range(2)]
         for half in range(2):
             turned = bank(half, "ts_turned_%d" % half)
             for b in range(CHUNKS):
                 turn(turned[:, b, :], ts_listed[:, cols(half * CHUNKS + b, P)])
             nc.vector.tensor_copy(ts_col[:, cols(half, CHUNKS)], turned[:, :, TS_ROW])
-
-        def ts_of_chunk(half, b):
-            return ts_col[:, cols(half * CHUNKS + b, 1)]
-
+        ts_rows = placed([P, C], F32, AT_TS_ROWS, "ts_rows")
         for half in range(2):
             spread = bank(2 + half, "ts_spread_%d" % half)
             for b in range(CHUNKS):
-                turn(spread[:, b, :], ts_of_chunk(half, b).to_broadcast([P, P]))
-            nc.scalar.copy(ts_rows[half][:], flat(spread[:]))
-        round_keys(1, (1024, 1536, 1792, 2048), (1, 2, 3))
-        gather_keys(1)
+                turn(spread[:, b, :], ts_col[:, cols(half * CHUNKS + b, 1)].to_broadcast([P, P]))
+            nc.scalar.copy(ts_rows[:, cols(half, HALF)], flat(spread[:]))
+        nc.vector.quantize_mx(out=q_codes[:].bitcast(E4M3), scales=q_scales[:], in_=q_grouped[:].rearrange("p j m t -> p (j m t)"))
 
-        q_grouped = placed([P, PACK, P, PACK], BF16, AT_TS, "q_grouped")
+        k_planes = [placed([P, PACK, PART], BF16, AT_K_PLANES + 2 * n, "k_planes_%d" % n) for n in range(PARTS)]
 
-        def rounded_queries(s):
-            dst = q_grouped[:, :, cols(s, Q_PIECE // PACK), :].rearrange("p j m t -> p m j t")
-            return dst, q_raw[s][:].rearrange("p t (m j) -> p m j t", j=PACK)
+        def gather_keys(engine, t, parts):
+            for n in parts:
+                move(engine, k_planes[n][:, t, :], k_raw[t][:].indirect(part_of(tok_list, n, PART)))
 
-        def weave(n):
-            words = k_grouped[n][:].bitcast(U32).rearrange("p (c u) -> p c u", u=2)
-            return words, k_listed[n][:].rearrange("p u c -> p c u")
+        gather_keys("vector", 0, range(PARTS))
+        uts = [placed([P, C], F32, AT_UTS + 4 * j, "uts_%d" % j) for j in range(PACK)]
+        for j in range(PACK):
+            nc.gpsimd.tensor_scalar(uts[j][:], ts_rows[:], us_sb[:, cols(j, 1)], 0.0, ALU.mult, ALU.add)
+        neg_ts_col = keep.tile([P, C // P], F32, name="neg_ts_col")
+        nc.scalar.activation(neg_ts_col[:], ts_col[:], ACT.Copy, scale=-1.0)
 
-        nc.scalar.copy(*weave(0))
-        nc.scalar.copy(*weave(1))
-        nc.scalar.activation(*rounded_queries(0), ACT.Copy)
-        nc.vector.tensor_copy(*weave(2))
-        nc.scalar.copy(*weave(3))
-        nc.vector.tensor_copy(*rounded_queries(1))
-        q_codes = {
-            0: keep.tile([P, P], U32, name="q_codes_0", align_bytes=64),
-            1: placed([P, P], U32, AT_K_GROUPED + 4, "q_codes_1"),
-            2: placed([P, 2 * P], U32, AT_TS_ROWS, "q_codes_2"),
-        }
-        q_scales = keep.tile([P, R], U8, name="q_scales", align_bytes=64)
-        k_codes = [placed([P, QUARTER], U32, (AT_K_LATE, AT_Q_RAW + 1, AT_K_LISTED + 6, AT_K_LISTED + 7)[n], "k_codes_%d" % n) for n in range(4)]
-        k_scales = [keep.tile([P, QUARTER], U8, name="k_scales_%d" % n, align_bytes=64) for n in range(4)]
+        q_words = q_grouped[:].rearrange("p j m t -> p (j m t)").bitcast(F32).rearrange("p (j m u) -> p j m u", j=PACK, u=2)
+        q2_codes = keep.tile([P, D], U32, name="q2_codes", align_bytes=64)
+        q2_scales = keep.tile([P, D], U8, name="q2_scales", align_bytes=64)
+        q2_grouped = placed([P, PACK, P, PACK], BF16, AT_LATE, "q2_grouped")
+        for u in range(2):
+            turned = bank(4 + u, "q_turned_%d" % u)
+            for j in range(PACK):
+                turn(turned[:, j, :], q_words[:, j, :, u])
+            nc.scalar.copy(q2_grouped[:, cols(u, 2), :, :], flat(turned[:]).bitcast(BF16).rearrange("m (j p e) -> m e p j", j=PACK, e=2))
+        gather_keys("scalar", 1, range(PARTS))
+        nc.vector.quantize_mx(out=q2_codes[:].bitcast(E4M3), scales=q2_scales[:], in_=q2_grouped[:].rearrange("m t p j -> m (t p j)"))
+        gather_keys("vector", 2, range(PARTS))
 
-        def quantize_queries(first, count):
-            rows = slice(first * P, (first + count) * P)
+        k_grouped = [placed([P, PART, PACK], BF16, AT_TS + 2 * n, "k_grouped_%d" % n) for n in range(PARTS)]
+        k_codes = [placed([P, HALF], U32, AT_K_CODES + 2 * half, "k_codes_%d" % half) for half in range(2)]
+        k_scales = [keep.tile([P, HALF], U8, name="k_scales_%d" % half, align_bytes=64) for half in range(2)]
+
+        def weave_keys(engine, n):
+            woven, planes = by_fours(k_grouped[n][:], k_planes[n][:])
+            if engine == "vector":
+                nc.vector.tensor_copy(woven, planes)
+            else:
+                nc.scalar.copy(woven, planes)
+
+        def quantize_keys(n):
             nc.vector.quantize_mx(
-                out=q_codes[first][:].bitcast(E4M3),
-                scales=q_scales[:, rows],
-                in_=q_grouped[:, first : first + count, :, :].rearrange("p j m t -> p (j m t)"),
+                out=k_codes[n // 2][:, cols(n % 2, PART)].bitcast(E4M3), scales=k_scales[n // 2][:, cols(n % 2, PART)], in_=flat(k_grouped[n][:])
             )
 
-        for n in range(4):
-            nc.vector.quantize_mx(out=k_codes[n][:].bitcast(E4M3), scales=k_scales[n][:], in_=k_grouped[n][:])
-            if n == 0:
-                quantize_queries(0, 1)
+        gather_keys("vector", LAST, (0, 1))
+        gather_keys("scalar", LAST, (2, 3))
+        weave_keys("vector", 0)
+        weave_keys("scalar", 2)
+        weave_keys("vector", 1)
+        weave_keys("scalar", 3)
+        for n in range(PARTS):
+            quantize_keys(n)
 
-        quantize_queries(1, 1)
-
-        neg_us = [placed([P, 32], F32, AT_LATE - 1 / 16, "neg_us_0"), keep.tile([P, PACK], F32, name="neg_us_1")]
-        for half in range(2):
-            nc.scalar.activation(neg_us[half][:, :PACK], us_sb[:, :PACK], ACT.Copy, scale=-1.0)
         e_sb = [placed([P, C], F32, AT_E + 4 * j, "e_%d" % j) for j in range(PACK)]
-        scaled_first = [placed([P, QUARTER], F32, AT_K_GROUPED + (5.5, 6.5, 7.5, 0)[n], "scaled_first_%d" % n) for n in range(4)]
-        for n in range(4):
-            product = flat(bank(n, "scores_direct_%d" % n)[:])[:, :QUARTER]
-            product_mx(product, q_codes[0][:], q_scales[:, :P], k_codes[n][:], k_scales[n][:])
-            nc.vector.tensor_tensor(scaled_first[n][:], product, ts_rows[n // 2][:, cols(n % 2, QUARTER)], ALU.mult)
-            nc.scalar.activation(e_sb[0][:, cols(n, QUARTER)], scaled_first[n][:], ACT.Exp, scale=us_sb[:, 0:1])
-        quantize_queries(2, 2)
-
-        scaled_turned = {}
-
-        def turned_scores(tiles, first, index, kib):
-            rows = slice(tiles[0] * P, (tiles[-1] + 1) * P)
-            width = len(tiles) * P
-            product = flat(bank(index, "scores_turned_%d_%d" % (tiles[0], first))[:])
-            chunks = range(first, first + HALF // width)
-            for n, chunk in enumerate(chunks):
-                slots = cols(chunk % 2, P)
-                product_mx(
-                    product[:, cols(n, width)], k_codes[chunk // 2][:, slots], k_scales[chunk // 2][:, slots],
-                    q_codes[tiles[0]][:], q_scales[:, rows],
-                )
-            for n, chunk in enumerate(chunks):
-                tile = placed([P, width], F32, kib + n * width * 4 / 1024, "scaled_turned_%d_%d" % (tiles[0], chunk))
-                scale = ts_of_chunk(chunk // CHUNKS, chunk % CHUNKS)
-                nc.scalar.activation(tile[:], product[:, cols(n, width)], ACT.Copy, scale=scale)
-                for i, j in enumerate(tiles):
-                    scaled_turned[(j, chunk)] = tile[:, cols(i, P)]
-
-        def turned_tile(j, indices):
-            for half in range(2):
-                back = bank(indices[half], "scores_back_%d_%d" % (j, half))
-                for b in range(CHUNKS):
-                    turn(back[:, b, :], scaled_turned[(j, half * CHUNKS + b)])
-                nc.scalar.activation(e_sb[j][:, cols(half, HALF)], flat(back[:]), ACT.Exp, scale=us_sb[:, cols(j, 1)])
-
         f_sb = [placed([P, C], F32, AT_F + 4 * j, "f_%d" % j) for j in range(PACK)]
-        e_slots, f_slots = {}, {}
-
-        def by_slots(window, kib, name):
-            picked = placed([P, C], F32, kib, name)
+        ue_sb = [placed([P, C], F32, AT_W + 4 * j, "ue_%d" % j) for j in range(PACK)]
+        for j in range(PACK):
             for half in range(2):
-                nc.vector.tensor_copy(picked[:, cols(half, HALF)], window[:].indirect(part_of(slot_list, half, HALF)))
-            return picked[:].rearrange("p (x i) -> p x i", i=2)
+                step = 2 * j + half
+                scores = flat(bank(step, "scores_%d_%d" % (j, half))[:])
+                product_mx(scores, q_codes[:, cols(j, P)], q_scales[:, cols(j, P)], k_codes[half][:], k_scales[half][:])
+                z_sb = placed([P, HALF], F32, AT_K_RAW + (8, 10, 12, 14, 24, 26, 28, 30)[step], "z_sb_%d_%d" % (j, half))
+                nc.vector.tensor_tensor(z_sb[:], scores, uts[j][:, cols(half, HALF)], ALU.mult)
+                nc.scalar.activation(e_sb[j][:, cols(half, HALF)], z_sb[:], ACT.Exp)
+            nc.gpsimd.tensor_tensor(f_sb[j][:], e_sb[j][:], dp_sb[j][:], ALU.mult)
 
-        def gather_e(j):
-            e_slots[j] = by_slots(e_sb[j], AT_E_SLOTS + 4 * j, "e_slots_%d" % j)
-            for part in (slice(0, C),) if j == 1 else (cols(0, HALF), cols(1, HALF)):
-                nc.gpsimd.tensor_tensor(f_sb[j][:, part], e_sb[j][:, part], dp_sb[j][:, part], ALU.mult)
+        e_slots = [placed([P, C], F32, AT_K_RAW + (0, 4, 8)[j], "e_slots_%d" % j) for j in range(LAST)]
+        f_slots = [placed([P, C], F32, AT_K_RAW + (16, 20, 12)[j], "f_slots_%d" % j) for j in range(LAST)]
+        e_slots.append(placed([P, C], F32, AT_K_RAW + 4, "e_slots_3"))
+        f_slots.append(placed([P, C], F32, AT_K_RAW + 4, "f_slots_3"))
 
-        def gather_f(j):
-            f_slots[j] = by_slots(f_sb[j], AT_F_SLOTS + 4 * j, "f_slots_%d" % j)
+        def by_slots(engine, picked, window, halves):
+            for half in halves:
+                move(engine, picked[:, cols(half, HALF)], window[:].indirect(part_of(slot_list, half, HALF)))
 
-        gather_e(0)
-        for half in range(2):
-            turned_scores([1], half * CHUNKS, 2 + half, AT_K_PAIRS + 2 * half)
-        turned_tile(1, (6, 7))
-        gather_f(0)
-        gather_e(1)
-        s_first = placed([P, X], F32, AT_TS_LISTED + 2, "s_first")
-        nc.gpsimd.tensor_tensor(s_first[:], e_slots[0][:, :, 0], e_slots[0][:, :, 1], ALU.add)
-        for n in range(4):
-            turned_scores([2, 3], 2 * n, (3, 6, 7, 3)[n], AT_K_PAIRS + 4 + 2 * n)
-        for j in (2, 3):
-            turned_tile(j, (0, 1) if j == 2 else (3, 0))
-            gather_e(j)
+        def gather_e(engine, j, halves=(0, 1)):
+            by_slots(engine, e_slots[j], e_sb[j], halves)
 
-        def pair_sums_turned(pairs, index, name):
+        def gather_f(engine, j, halves=(0, 1)):
+            by_slots(engine, f_slots[j], f_sb[j], halves)
+
+        def pair_sums_turned(picked, index, name):
+            pairs = picked[:].rearrange("p (x i) -> p x i", i=2)
             sums = bank(index, name)
             for b in range(CHUNKS):
                 for i in range(2):
                     turn(sums[:, b, :], pairs[:, cols(b, P), i], start=(i == 0), stop=(i == 1))
             return flat(sums[:])
 
-        root, inverse, t_turned, t_sums, neg_f = {}, {}, {}, {}, {}
+        s_turned, root, root_back, inverse, t_turned, t_fetched, t_back = {}, {}, {}, {}, {}, {}, {}
 
-        def take_root(j, index):
-            sums = s_first[:] if j == 0 else pair_sums_turned(e_slots[j], index, "s_turned_%d" % j)
-            root[j] = placed([P, X], F32, AT_K_PAIRS + (9.5, 11.5, 0, 2)[j], "root_%d" % j)
-            nc.scalar.activation(root[j][:], sums, ACT.Abs_reciprocal_sqrt)
+        def sum_e(j, index):
+            s_turned[j] = pair_sums_turned(e_slots[j], index, "s_turned_%d" % j)
 
-        def take_inverse(j, index):
-            back = root[j][:] if j == 0 else turn_back(root[j], index, "root_back_%d" % j)
-            inverse[j] = placed([P, X], F32, AT_INVERSE + 2 * j, "inverse_%d" % j)[:]
-            nc.scalar.activation(inverse[j], back, ACT.Square)
-            nc.gpsimd.tensor_tensor(h_window[j][:, :X], inverse[j], wb_sb[:, j, :], ALU.mult)
+        def take_root(j):
+            root[j] = placed([P, X], F32, AT_K_RAW + (30, 28, 24, 26)[j], "root_%d" % j)
+            nc.scalar.activation(root[j][:], s_turned[j], ACT.Abs_reciprocal_sqrt)
+
+        def return_root(j, index):
+            root_back[j] = turn_back(root[j], index, "root_back_%d" % j)
+
+        def take_inverse(j):
+            inverse[j] = placed([P, X], F32, (AT_INV, AT_INV + 2, AT_TS_LISTED, AT_TS)[j], "inverse_%d" % j)
+            nc.scalar.activation(inverse[j][:], root_back[j], ACT.Square)
+
+        def sum_f(j, index):
+            t_turned[j] = pair_sums_turned(f_slots[j], index, "t_turned_%d" % j)
 
         def fetch_t(j):
-            t_turned[j] = placed([P, X], F32, AT_K_PAIRS + 11.5 if j == 0 else AT_K_LISTED + 2 * j, "t_turned_sb_%d" % j)
-            nc.scalar.copy(t_turned[j][:], t_banks[j])
+            t_fetched[j] = placed([P, X], F32, AT_Q_RAW + 2 * j, "t_fetched_%d" % j)
+            nc.scalar.copy(t_fetched[j][:], t_turned[j])
 
-        def negate_f(half, j, kib):
-            neg_f[(half, j)] = placed([P, HALF], F32, kib, "neg_f_%d_%d" % (half, j))
-            nc.scalar.activation(neg_f[(half, j)][:], f_sb[j][:, cols(half, HALF)], ACT.Copy, scale=-1.0)
+        def return_t(j, index):
+            t_back[j] = turn_back(t_fetched[j], index, "t_back_%d" % j)
 
         def form_m(j):
-            nc.vector.tensor_tensor(m_window[j][:, :X], t_sums[j], inverse[j], ALU.mult)
+            nc.vector.tensor_tensor(m_window[j][:, :X], t_back[j], inverse[j][:], ALU.mult)
 
-        q_words = q_grouped[:].rearrange("p j m t -> p (j m t)").bitcast(F32).rearrange("p (j m u) -> p j m u", j=PACK, u=2)
-        q2_codes = placed([P, D], U32, AT_LATE, "q2_codes")
-        q_turned, q2_grouped = {}, {}
-        q2_scales = keep.tile([P, D], U8, name="q2_scales", align_bytes=64)
+        def form_h(engine, j):
+            engine.tensor_tensor(h_window[j][:, :X], inverse[j][:], wb_sb[:, j, :], ALU.mult)
 
-        def turn_queries(u, index):
-            q_turned[u] = bank(index, "q_turned_%d" % u)
-            for j in range(PACK):
-                turn(q_turned[u][:, j, :], q_words[:, j, :, u])
+        def form_ue(j):
+            nc.gpsimd.tensor_scalar(ue_sb[j][:], e_sb[j][:], us_sb[:, cols(j, 1)], 0.0, ALU.mult, ALU.add)
 
-        def regroup_queries(u, kib):
-            q2_grouped[u] = placed([P, 2, P, PACK], BF16, kib, "q2_grouped_%d" % u)
-            nc.scalar.copy(q2_grouped[u][:], flat(q_turned[u][:]).bitcast(BF16).rearrange("m (j p e) -> m e p j", j=PACK, e=2))
-
-        def quantize_regrouped(u):
-            nc.vector.quantize_mx(
-                out=q2_codes[:, cols(u, 2 * P)].bitcast(E4M3),
-                scales=q2_scales[:, cols(u, 2 * P)],
-                in_=q2_grouped[u][:].rearrange("m t p j -> m (t p j)"),
-            )
-
-        def turn_t(j, index):
-            t_banks[j] = pair_sums_turned(f_slots[j], index, "t_turned_%d" % j)
-
-        take_root(0, None)
-        take_root(1, 1)
-        take_inverse(0, None)
-        t_banks = {}
-        turn_t(0, 3)
-        turn_queries(0, 0)
-        take_root(2, 7)
-        for j in range(1, PACK):
-            gather_f(j)
-        take_inverse(1, 5)
+        gather_e("vector", 0)
+        gather_e("scalar", 1)
+        sum_e(0, 0)
+        sum_e(1, 1)
+        gather_f("vector", 0)
+        take_root(0)
+        take_root(1)
+        sum_f(0, 2)
+        return_root(0, 3)
+        return_root(1, 4)
+        gather_e("vector", 2)
+        gather_e("scalar", 3)
+        form_ue(0)
+        form_ue(1)
+        sum_e(2, 5)
+        sum_e(3, 6)
+        gather_f("vector", 1)
+        take_inverse(0)
+        take_inverse(1)
+        form_h(nc.gpsimd, 0)
+        form_h(nc.gpsimd, 1)
+        sum_f(1, 7)
+        take_root(2)
+        take_root(3)
+        return_root(2, 0)
+        return_root(3, 1)
         fetch_t(0)
-        take_root(3, 4)
-        take_inverse(2, 6)
-        t_first = placed([P, X], F32, AT_TS_LISTED, "t_first")
-        nc.scalar.copy(t_first[:], turn_back(t_turned[0], 2, "t_back_0"))
-        nc.gpsimd.tensor_tensor(m_window[0][:, :X], t_first[:], inverse[0], ALU.mult)
-        take_inverse(3, 7)
-        negate_f(1, 1, AT_K_PAIRS + 2)
-        turn_t(1, 4)
         fetch_t(1)
-        negate_f(0, 2, AT_F_SLOTS + 4)
-        negate_f(0, 3, AT_F_SLOTS + 6)
-        t_sums[1] = turn_back(t_turned[1], 6, "t_back_1")
-        turn_t(2, 7)
+        return_t(0, 3)
+        return_t(1, 4)
+        gather_f("vector", 2)
+        form_ue(2)
+        form_ue(3)
+        take_inverse(2)
+        take_inverse(3)
+        sum_f(2, 5)
+        form_h(nc.gpsimd, 2)
+        gather_f("vector", 3, (0,))
+        gather_f("scalar", 3, (1,))
+        sum_f(3, 6)
         fetch_t(2)
-        t_sums[2] = turn_back(t_turned[2], 5, "t_back_2")
-        turn_queries(1, 1)
-        regroup_queries(0, AT_F_SLOTS + 8)
-        negate_f(1, 0, AT_F_SLOTS + 10)
-        turn_t(3, 4)
-        fetch_t(3)
-        t_sums[3] = turn_back(t_turned[3], 3, "t_back_3")
-        negate_f(0, 0, AT_F_SLOTS + 12)
-        negate_f(0, 1, AT_F_SLOTS + 14)
-        regroup_queries(1, AT_K_LISTED + 7)
+        return_t(2, 2)
+        form_m(0)
+        form_m(1)
+        form_h(nc.vector, 3)
 
-        e_m, centred, factor, g_planes = {}, {}, {}, {}
-        units = [(half, j) for half in range(2) for j in range(PACK)]
-        at_g_grouped = (AT_K_EARLY - 4, AT_TS)
-        at_g_planes = (AT_WB, AT_K_LATE)
-        at_e_m = {(0, 0): AT_K_LISTED + 2, (0, 1): AT_E_SLOTS, (0, 2): AT_K_LISTED + 5, (0, 3): AT_E_SLOTS + 2}
-        at_e_m.update({(1, 0): AT_INVERSE + 6, (1, 1): AT_K_PAIRS, (1, 2): AT_LATE - 2, (1, 3): at_g_planes[0]})
-        at_factor = {(0, j): AT_DP + 2 * j for j in range(PACK)}
-        at_factor.update({(1, 0): AT_DP + 10, (1, 1): AT_DP + 12, (1, 2): AT_E_SLOTS + 6, (1, 3): AT_K_EARLY})
+        neg_m_first = [placed([P, HALF], F32, AT_K_RAW + (12, 4, 6, 14)[j], "neg_m_first_%d" % j) for j in range(PACK)]
+        neg_m_third = placed([P, PACK, PART], F32, AT_K_RAW + 13, "neg_m_third")
+        m_less_dp = placed([P, PACK, PART], F32, AT_TS_LISTED, "m_less_dp")
+        g_grouped = [placed([P, PART, PACK], BF16, AT_K_PLANES + 2 * n if n else AT_UTS, "g_grouped_%d" % n) for n in range(PARTS)]
+        weighted = [placed([P, PACK, HALF], F32, (AT_TS, AT_UTS)[half], "weighted_%d" % half) for half in range(2)]
+        g_codes = [keep.tile([P, PART], U32, name="g_codes_%d" % n, align_bytes=64) for n in range(PARTS)]
+        g_scales = [keep.tile([P, PART], U8, name="g_scales_%d" % n, align_bytes=64) for n in range(PARTS)]
+        centred_turned, centred, centred_back, dk_banks, dk = {}, {}, {}, {}, {}
 
-        def look_up_m(half, j):
-            e_m[(half, j)] = placed([P, HALF], F32, at_e_m[(half, j)], "e_m_%d_%d" % (half, j))
-            nc.vector.tensor_tensor(
-                e_m[(half, j)][:], m_window[j][:].indirect(part_of(blk_list, half, HALF)), e_sb[j][:, cols(half, HALF)], ALU.mult
-            )
+        def look_up_h(j, half):
+            nc.vector.tensor_tensor(weighted[half][:, j, :], h_window[j][:].indirect(part_of(blk_list, half, HALF)), ue_sb[j][:, cols(half, HALF)], ALU.mult)
 
-        def centre(half, j):
-            side = j % 2
-            turned = bank(7 - 3 * side, "centred_turned_%d_%d" % (half, j))
-            with_ts = placed([P, CHUNKS, P], F32, {(0, 1): AT_K_PAIRS, (1, 0): at_g_grouped[0]}.get((half, j), AT_K_PAIRS + 4 + 2 * side), "with_ts_%d_%d" % (half, j))
-            for b in range(CHUNKS):
-                turn(turned[:, b, :], neg_f[(half, j)][:, cols(b, P)], start=True, stop=False)
-                turn(turned[:, b, :], e_m[(half, j)][:, cols(b, P)], start=False, stop=True)
-            for b in range(CHUNKS):
-                nc.scalar.activation(with_ts[:, b, :], turned[:, b, :], ACT.Copy, scale=ts_of_chunk(half, b))
-            centred[(half, j)] = flat(with_ts[:])
+        def look_up_neg_m(dst, j, offsets):
+            nc.scalar.activation(dst, m_window[j][:].indirect(offsets), ACT.Copy, scale=-1.0)
 
-        def fetch_factor(half, j):
-            back = turn_back(centred[(half, j)], 2 + 4 * (j % 2), "centred_back_%d_%d" % (half, j))
-            factor[(half, j)] = placed([P, HALF], F32, at_factor[(half, j)], "factor_%d_%d" % (half, j))
-            nc.scalar.activation(factor[(half, j)][:], back, ACT.Copy, scale=neg_us[half][:, cols(j, 1)])
+        def look_up_m_less_dp(j):
+            nc.vector.tensor_tensor(m_less_dp[:, j, :], m_window[j][:].indirect(part_of(blk_list, LAST, PART)), dp_sb[j][:, cols(LAST, PART)], ALU.subtract)
 
-        def gradient(half, j):
+        def turn_centred(chunk, j):
             if j == 0:
-                g_planes[half] = placed([P, PACK, HALF], F32, at_g_planes[half], "g_planes_%d" % half)
-            nc.vector.tensor_tensor(
-                g_planes[half][:, j, :], h_window[j][:].indirect(part_of(blk_list, half, HALF)), factor[(half, j)][:], ALU.mult
-            )
+                centred_turned[chunk] = bank((7, 0, 1, 5, 1, 5, 7, 0)[chunk], "centred_turned_%d" % chunk)
+            dst = centred_turned[chunk][:, j, :]
+            if chunk >= 6:
+                turn(dst, m_less_dp[:, j, cols(chunk - 6, P)])
+            else:
+                turn(dst, dp_sb[j][:, cols(chunk, P)], start=True, stop=False)
+                neg_m = neg_m_first[j][:, cols(chunk, P)] if chunk < CHUNKS else neg_m_third[:, j, cols(chunk - CHUNKS, P)]
+                turn(dst, neg_m, start=False, stop=True)
 
-        g_codes = [keep.tile([P, HALF], U32, name="g_codes_%d" % half, align_bytes=64) for half in range(2)]
-        g_scales = [keep.tile([P, HALF], U8, name="g_scales_%d" % half, align_bytes=64) for half in range(2)]
+        def scale_centred(chunk):
+            centred[chunk] = placed([P, HALF], F32, AT_E + 2 * chunk, "centred_%d" % chunk)
+            nc.scalar.activation(centred[chunk][:], flat(centred_turned[chunk][:]), ACT.Copy, scale=(neg_ts_col if chunk >= 6 else ts_col)[:, cols(chunk, 1)])
 
-        def quantize_gradient(half):
-            g_grouped = placed([P, HALF, PACK], BF16, at_g_grouped[half], "g_grouped_%d" % half)
-            nc.scalar.activation(
-                g_grouped[:].rearrange("p (c i) j -> p c j i", i=4),
-                g_planes[half][:].rearrange("p j (c i) -> p c j i", i=4),
-                ACT.Copy,
-            )
-            nc.vector.quantize_mx(out=g_codes[half][:].bitcast(E5M2), scales=g_scales[half][:], in_=flat(g_grouped[:]))
+        def return_centred(chunk):
+            centred_back[chunk] = turn_back(centred[chunk], (3, 4, 2, 6)[chunk % 4], "centred_back_%d" % chunk).rearrange("p (j c) -> p j c", j=PACK)
+
+        def gradient(chunk):
+            half, b = divmod(chunk, CHUNKS)
+            woven, planes = by_fours(g_grouped[chunk // 2][:, cols(chunk % 2, P), :], centred_back[chunk])
+            nc.vector.tensor_tensor(woven, planes, weighted[half][:, :, cols(b, P)].rearrange("p t (c i) -> p c t i", i=4), ALU.mult)
+
+        def quantize_gradient(n):
+            nc.vector.quantize_mx(out=g_codes[n][:].bitcast(E5M2), scales=g_scales[n][:], in_=flat(g_grouped[n][:]))
+
+        def multiply(n):
+            for pair in range(2):
+                product = flat(bank((7, 0, 1, 5)[2 * (n % 2) + pair], "dk_psum_%d_%d" % (n, pair))[:])
+                for i in range(2):
+                    t = 2 * pair + i
+                    product_mx(product[:, cols(i, PART)], q2_codes[:, cols(t, P)], q2_scales[:, cols(t, P)], g_codes[n][:], g_scales[n][:], E5M2)
+                dk_banks[(n, pair)] = product
+
+        def fetch_dk(n):
+            for pair in range(2):
+                dk[(n, pair)] = placed([P, HALF], F32, (AT_F + 4 * n if n else AT_K_RAW + 13) + 2 * pair, "dk_%d_%d" % (n, pair))
+                nc.scalar.copy(dk[(n, pair)][:], dk_banks[(n, pair)])
 
         out_rows = out.rearrange("(p t) n -> t p n", t=PACK)
 
-        def place_result(t, half):
-            product = bank((0, 5, 6, 3, 1, 0, 5, 3)[t + PACK * half], "dk_psum_%d_%d" % (t, half))
-            product_mx(flat(product[:]), q2_codes[:, cols(t, P)], q2_scales[:, cols(t, P)], g_codes[half][:], g_scales[half][:], E5M2)
-            at_dk = {(0, 0): AT_K_LATE + 8, (LAST, 0): at_g_planes[1]}
-            dk = placed([P, HALF], F32, at_dk.get((t, half), AT_F_SLOTS + 2 * (t + PACK * half)), "dk_%d_%d" % (t, half))
-            nc.scalar.copy(dk[:], flat(product[:]))
-            nc.vector.tensor_copy(out_window[t][:].indirect(part_of(tok_list, half, HALF)), dk[:])
-            if half == 1:
+        def place(engine, t, n):
+            move(engine, out_window[t][:].indirect(part_of(tok_list, n, PART)), dk[(n, t // 2)][:, cols(t % 2, PART)])
+            if n == PARTS - 1:
                 nc.sync.dma_start(out=out_rows[t], in_=out_window[t][:])
 
-        def clear_window(kib):
-            out_window.append(placed([P, T], F32, kib, "out_window_%d" % len(out_window)))
-            nc.gpsimd.memset(out_window[-1][:], 0.0)
+        def first_half(j):
+            look_up_neg_m(neg_m_first[j][:], j, part_of(blk_list, 0, HALF))
+            for chunk in range(CHUNKS):
+                turn_centred(chunk, j)
 
-        form_m(1)
-        look_up_m(0, 0)
-        look_up_m(0, 1)
+        look_up_neg_m(neg_m_first[0][:], 0, part_of(blk_list, 0, HALF))
+        fetch_t(3)
+        return_t(3, 6)
         form_m(2)
-        form_m(LAST)
-        look_up_m(0, 2)
-        look_up_m(0, LAST)
-        look_up_m(1, 0)
-        centre(0, 0)
-        for j in range(1, PACK):
-            centre(0, j)
-            fetch_factor(0, j - 1)
-        centre(1, 0)
-        fetch_factor(0, LAST)
-        gradient(0, 0)
-        look_up_m(1, 1)
-        centre(1, 1)
-        fetch_factor(1, 0)
-        for j in range(1, PACK):
-            gradient(0, j)
-        gradient(1, 0)
-        look_up_m(1, 2)
-        for u in range(2):
-            quantize_regrouped(u)
+        for chunk in range(CHUNKS):
+            turn_centred(chunk, 0)
+        first_half(1)
+        look_up_m_less_dp(0)
+        look_up_m_less_dp(1)
+        form_m(3)
+        first_half(2)
+        first_half(3)
+        for j in range(PACK):
+            look_up_h(j, 0)
+        look_up_m_less_dp(2)
+        look_up_m_less_dp(3)
+        for chunk in range(CHUNKS):
+            scale_centred(chunk)
+            return_centred(chunk)
+        for j in range(PACK):
+            look_up_neg_m(neg_m_third[:, j, :], j, part_of(blk_list, 2, PART))
+        for chunk in (6, 7, 4, 5):
+            for j in range(PACK):
+                turn_centred(chunk, j)
+        gradient(0)
+        gradient(1)
+        gradient(2)
         quantize_gradient(0)
-        fetch_factor(1, 1)
-        look_up_m(1, LAST)
-        gradient(1, 1)
-        place_result(0, 0)
-        place_result(1, 0)
-        clear_window(AT_K_LATE + 8)
-        for j in range(2, PACK):
-            negate_f(1, j, at_g_planes[0] + 2 * j)
-        for j in range(2, PACK):
-            centre(1, j)
-        for j in range(2, PACK):
-            fetch_factor(1, j)
-            gradient(1, j)
-        place_result(2, 0)
-        clear_window(AT_K_EARLY)
+        gradient(3)
+        for chunk in (6, 7, 4, 5):
+            scale_centred(chunk)
+        multiply(0)
+        look_up_h(0, 1)
         quantize_gradient(1)
-        place_result(LAST, 0)
-        for t in range(PACK):
-            place_result(t, 1)
+        fetch_dk(0)
+        multiply(1)
+        for chunk in range(CHUNKS, 2 * CHUNKS):
+            return_centred(chunk)
+        for j in range(1, PACK):
+            look_up_h(j, 1)
+        place("scalar", 0, 0)
+        fetch_dk(1)
+        place("scalar", 1, 0)
+        place("scalar", 0, 1)
+        gradient(4)
+        gradient(5)
+        gradient(6)
+        quantize_gradient(2)
+        gradient(7)
+        multiply(2)
+        fetch_dk(2)
+        quantize_gradient(3)
+        multiply(3)
+        fetch_dk(3)
+        place("vector", 0, 2)
+        place("vector", 2, 0)
+        place("vector", 0, 3)
+        place("scalar", 1, 1)
+        place("scalar", 3, 0)
+        place("scalar", 1, 2)
+        place("scalar", 1, 3)
+        for n in range(1, PARTS):
+            place("vector", 2, n)
+        for n in range(1, PARTS):
+            place("scalar", 3, n)

@@ -92,12 +92,12 @@ def tile_attend_gblkatt_kernel(tc, qT, kT, us, ts, wb, dp, offs, blkoffs, slotof
         ident = keep.tile([P, P], F32, name="ident")
         us_sb = keep.tile([P, 8], F32, name="us_sb")
 
-        ts_window = placed([P, T], F32, AT_TS, "ts_window")
+        ts_window = placed([P, T], F32, AT_OUT + 16, "ts_window")
         nc.scalar.dma_start(out=ts_window[TS_ROW:P, :], in_=ts[0:1, :])
         nc.vector.memset(ts_window[0:TS_ROW, :].bitcast(I32), 0)
         nc.sync.dma_start(tok_list[:], offs)
         make_identity(nc, ident[:])
-        q_raw = placed([P, PACK, R], F32, AT_Q_RAW, "q_raw")
+        q_raw = placed([P, PACK, R], F32, AT_OUT + 24, "q_raw")
         nc.sync.dma_start(out=q_raw[:], in_=qT.rearrange("(p t) r -> p t r", t=PACK))
         nc.sync.dma_start(out=us_sb[:, :PACK], in_=us.rearrange("(p j) o -> p (j o)", j=PACK))
         k_rows = kT.rearrange("(p t) n -> t p n", t=PACK)
@@ -118,11 +118,10 @@ def tile_attend_gblkatt_kernel(tc, qT, kT, us, ts, wb, dp, offs, blkoffs, slotof
         nc.vector.memset(out_window[0][:].bitcast(I32), 0)
         ts_listed = placed([P, C], F32, AT_TS_LISTED, "ts_listed")
         nc.vector.tensor_copy(ts_listed[:], ts_window[:].indirect(tok_list[:]))
-        nc.gpsimd.memset(out_window[1][:], 0.0)
-        nc.vector.memset(out_window[2][:].bitcast(I32), 0)
-        nc.gpsimd.memset(out_window[3][:], 0.0)
         h_window = [placed([P, BLK_WINDOW], F32, AT_H + BLK_WINDOW_KIB * j, "h_window_%d" % j) for j in range(PACK)]
         m_window = [placed([P, BLK_WINDOW], F32, AT_M + BLK_WINDOW_KIB * j, "m_window_%d" % j) for j in range(PACK)]
+        for t in (1, 2):
+            nc.gpsimd.memset(out_window[t][:], 0.0)
         for window in h_window + m_window:
             nc.gpsimd.memset(window[:, X:], 0.0)
 
@@ -132,31 +131,21 @@ def tile_attend_gblkatt_kernel(tc, qT, kT, us, ts, wb, dp, offs, blkoffs, slotof
         nc.scalar.activation(q_grouped[:].rearrange("p j m t -> p m t j"), q_raw[:].rearrange("p t (m j) -> p m t j", j=PACK), ACT.Copy)
 
         ts_col = keep.tile([P, C // P], F32, name="ts_col")
+        neg_ts_col = keep.tile([P, CHUNKS], F32, name="neg_ts_col")
         for half in range(2):
             turned = bank(half, "ts_turned_%d" % half)
             for b in range(CHUNKS):
                 turn(turned[:, b, :], ts_listed[:, cols(half * CHUNKS + b, P)])
             nc.vector.tensor_copy(ts_col[:, cols(half, CHUNKS)], turned[:, :, TS_ROW])
-        ts_rows = placed([P, C], F32, AT_TS_ROWS, "ts_rows")
+        nc.vector.tensor_scalar(neg_ts_col[:], turned[:, :, TS_ROW], -1.0, None, ALU.mult)
+        nc.vector.quantize_mx(out=q_codes[:].bitcast(E4M3), scales=q_scales[:], in_=q_grouped[:].rearrange("p j m t -> p (j m t)"))
+
+        ts_rows = placed([P, C], F32, AT_OUT + 24, "ts_rows")
         for half in range(2):
             spread = bank(2 + half, "ts_spread_%d" % half)
             for b in range(CHUNKS):
                 turn(spread[:, b, :], ts_col[:, cols(half * CHUNKS + b, 1)].to_broadcast([P, P]))
             nc.scalar.copy(ts_rows[:, cols(half, HALF)], flat(spread[:]))
-        nc.vector.quantize_mx(out=q_codes[:].bitcast(E4M3), scales=q_scales[:], in_=q_grouped[:].rearrange("p j m t -> p (j m t)"))
-
-        k_planes = [placed([P, PACK, PART], BF16, AT_K_PLANES + 2 * n, "k_planes_%d" % n) for n in range(PARTS)]
-
-        def gather_keys(engine, t, parts):
-            for n in parts:
-                move(engine, k_planes[n][:, t, :], k_raw[t][:].indirect(part_of(tok_list, n, PART)))
-
-        gather_keys("vector", 0, range(PARTS))
-        uts = [placed([P, C], F32, AT_UTS + 4 * j, "uts_%d" % j) for j in range(PACK)]
-        for j in range(PACK):
-            nc.gpsimd.tensor_scalar(uts[j][:], ts_rows[:], us_sb[:, cols(j, 1)], 0.0, ALU.mult, ALU.add)
-        neg_ts_col = keep.tile([P, C // P], F32, name="neg_ts_col")
-        nc.scalar.activation(neg_ts_col[:], ts_col[:], ACT.Copy, scale=-1.0)
 
         q_words = q_grouped[:].rearrange("p j m t -> p (j m t)").bitcast(F32).rearrange("p (j m u) -> p j m u", j=PACK, u=2)
         q2_codes = keep.tile([P, D], U32, name="q2_codes", align_bytes=64)
@@ -167,52 +156,69 @@ def tile_attend_gblkatt_kernel(tc, qT, kT, us, ts, wb, dp, offs, blkoffs, slotof
             for j in range(PACK):
                 turn(turned[:, j, :], q_words[:, j, :, u])
             nc.scalar.copy(q2_grouped[:, cols(u, 2), :, :], flat(turned[:]).bitcast(BF16).rearrange("m (j p e) -> m e p j", j=PACK, e=2))
-        gather_keys("scalar", 1, range(PARTS))
-        nc.vector.quantize_mx(out=q2_codes[:].bitcast(E4M3), scales=q2_scales[:], in_=q2_grouped[:].rearrange("m t p j -> m (t p j)"))
-        gather_keys("vector", 2, range(PARTS))
 
-        k_grouped = [placed([P, PART, PACK], BF16, AT_TS + 2 * n, "k_grouped_%d" % n) for n in range(PARTS)]
+        k_grouped = [placed([P, PART, PACK], BF16, AT_TS + 2 * n if n < LAST else AT_OUT + 28, "k_grouped_%d" % n) for n in range(PARTS)]
+        k_planes = {n: placed([P, PACK, PART], BF16, AT_K_PLANES + 2 * n, "k_planes_%d" % n) for n in (2, 3)}
         k_codes = [placed([P, HALF], U32, AT_K_CODES + 2 * half, "k_codes_%d" % half) for half in range(2)]
         k_scales = [keep.tile([P, HALF], U8, name="k_scales_%d" % half, align_bytes=64) for half in range(2)]
 
-        def weave_keys(engine, n):
-            woven, planes = by_fours(k_grouped[n][:], k_planes[n][:])
-            if engine == "vector":
-                nc.vector.tensor_copy(woven, planes)
-            else:
-                nc.scalar.copy(woven, planes)
+        def gather_keys(t):
+            for n in (0, 1):
+                nc.vector.tensor_copy(k_grouped[n][:, :, t], k_raw[t][:].indirect(part_of(tok_list, n, PART)))
+            for n in (2, 3):
+                nc.scalar.activation(k_planes[n][:, t, :], k_raw[t][:].indirect(part_of(tok_list, n, PART)), ACT.Copy)
+
+        gather_keys(0)
+        uts = [placed([P, C], F32, AT_UTS + 4 * j, "uts_%d" % j) for j in range(PACK)]
+        for j in range(PACK):
+            nc.gpsimd.tensor_scalar(uts[j][:], ts_rows[:], us_sb[:, cols(j, 1)], 0.0, ALU.mult, ALU.add)
+        gather_keys(1)
+        nc.vector.quantize_mx(out=q2_codes[:].bitcast(E4M3), scales=q2_scales[:], in_=q2_grouped[:].rearrange("m t p j -> m (t p j)"))
+        gather_keys(2)
+        gather_keys(3)
+        for n in (2, 3):
+            nc.scalar.copy(*by_fours(k_grouped[n][:], k_planes[n][:]))
 
         def quantize_keys(n):
             nc.vector.quantize_mx(
                 out=k_codes[n // 2][:, cols(n % 2, PART)].bitcast(E4M3), scales=k_scales[n // 2][:, cols(n % 2, PART)], in_=flat(k_grouped[n][:])
             )
 
-        gather_keys("vector", LAST, (0, 1))
-        gather_keys("scalar", LAST, (2, 3))
-        weave_keys("vector", 0)
-        weave_keys("scalar", 2)
-        weave_keys("vector", 1)
-        weave_keys("scalar", 3)
-        for n in range(PARTS):
-            quantize_keys(n)
-
         e_sb = [placed([P, C], F32, AT_E + 4 * j, "e_%d" % j) for j in range(PACK)]
         f_sb = [placed([P, C], F32, AT_F + 4 * j, "f_%d" % j) for j in range(PACK)]
-        ue_sb = [placed([P, C], F32, AT_W + 4 * j, "ue_%d" % j) for j in range(PACK)]
-        for j in range(PACK):
-            for half in range(2):
-                step = 2 * j + half
-                scores = flat(bank(step, "scores_%d_%d" % (j, half))[:])
-                product_mx(scores, q_codes[:, cols(j, P)], q_scales[:, cols(j, P)], k_codes[half][:], k_scales[half][:])
-                z_sb = placed([P, HALF], F32, AT_K_RAW + (8, 10, 12, 14, 24, 26, 28, 30)[step], "z_sb_%d_%d" % (j, half))
-                nc.vector.tensor_tensor(z_sb[:], scores, uts[j][:, cols(half, HALF)], ALU.mult)
-                nc.scalar.activation(e_sb[j][:, cols(half, HALF)], z_sb[:], ACT.Exp)
+        ue_sb = [placed([P, C], F32, AT_W + 4 * j, "ue_%d" % j) for j in range(LAST)]
+        def score(j, half, index, kib):
+            scores = flat(bank(index, "scores_%d_%d" % (j, half))[:])
+            product_mx(scores, q_codes[:, cols(j, P)], q_scales[:, cols(j, P)], k_codes[half][:], k_scales[half][:])
+            z_sb = placed([P, HALF], F32, kib, "z_sb_%d_%d" % (j, half))
+            nc.vector.tensor_tensor(z_sb[:], scores, uts[j][:, cols(half, HALF)], ALU.mult)
+            nc.scalar.activation(e_sb[j][:, cols(half, HALF)], z_sb[:], ACT.Exp)
+
+        def form_f(j):
             nc.gpsimd.tensor_tensor(f_sb[j][:], e_sb[j][:], dp_sb[j][:], ALU.mult)
 
-        e_slots = [placed([P, C], F32, AT_K_RAW + (0, 4, 8)[j], "e_slots_%d" % j) for j in range(LAST)]
-        f_slots = [placed([P, C], F32, AT_K_RAW + (16, 20, 12)[j], "f_slots_%d" % j) for j in range(LAST)]
-        e_slots.append(placed([P, C], F32, AT_K_RAW + 4, "e_slots_3"))
-        f_slots.append(placed([P, C], F32, AT_K_RAW + 4, "f_slots_3"))
+        quantize_keys(0)
+        quantize_keys(1)
+        quantize_keys(2)
+        score(0, 0, 0, AT_K_PLANES + 4)
+        quantize_keys(3)
+        nc.gpsimd.memset(out_window[LAST][:], 0.0)
+        score(1, 0, 1, AT_K_PLANES + 6)
+        score(0, 1, 2, AT_K_RAW)
+        form_f(0)
+        score(1, 1, 3, AT_K_RAW + 4)
+        form_f(1)
+        score(2, 0, 4, AT_K_PLANES + 6)
+        score(2, 1, 5, AT_K_RAW + 8)
+        form_f(2)
+        score(3, 0, 6, AT_K_RAW)
+        score(3, 1, 7, AT_K_RAW + 23)
+        form_f(3)
+
+        e_slots = [placed([P, C], F32, AT_K_RAW + (26, 20, 8)[j], "e_slots_%d" % j) for j in range(LAST)]
+        f_slots = [placed([P, C], F32, AT_K_RAW + (4, 12, 16)[j], "f_slots_%d" % j) for j in range(LAST)]
+        e_slots.append(placed([P, C], F32, AT_K_RAW + 20, "e_slots_3"))
+        f_slots.append(placed([P, C], F32, AT_K_RAW + 20, "f_slots_3"))
 
         def by_slots(engine, picked, window, halves):
             for half in halves:
@@ -238,7 +244,7 @@ def tile_attend_gblkatt_kernel(tc, qT, kT, us, ts, wb, dp, offs, blkoffs, slotof
             s_turned[j] = pair_sums_turned(e_slots[j], index, "s_turned_%d" % j)
 
         def take_root(j):
-            root[j] = placed([P, X], F32, AT_K_RAW + (30, 28, 24, 26)[j], "root_%d" % j)
+            root[j] = placed([P, X], F32, AT_K_RAW + (24, 30, 0, 2)[j], "root_%d" % j)
             nc.scalar.activation(root[j][:], s_turned[j], ACT.Abs_reciprocal_sqrt)
 
         def return_root(j, index):
@@ -252,7 +258,7 @@ def tile_attend_gblkatt_kernel(tc, qT, kT, us, ts, wb, dp, offs, blkoffs, slotof
             t_turned[j] = pair_sums_turned(f_slots[j], index, "t_turned_%d" % j)
 
         def fetch_t(j):
-            t_fetched[j] = placed([P, X], F32, AT_Q_RAW + 2 * j, "t_fetched_%d" % j)
+            t_fetched[j] = placed([P, X], F32, (AT_TS_ROWS, AT_TS_ROWS + 2, AT_Z, AT_Z + 2)[j], "t_fetched_%d" % j)
             nc.scalar.copy(t_fetched[j][:], t_turned[j])
 
         def return_t(j, index):
@@ -261,66 +267,68 @@ def tile_attend_gblkatt_kernel(tc, qT, kT, us, ts, wb, dp, offs, blkoffs, slotof
         def form_m(j):
             nc.vector.tensor_tensor(m_window[j][:, :X], t_back[j], inverse[j][:], ALU.mult)
 
-        def form_h(engine, j):
-            engine.tensor_tensor(h_window[j][:, :X], inverse[j][:], wb_sb[:, j, :], ALU.mult)
+        def form_h(j):
+            nc.gpsimd.tensor_tensor(h_window[j][:, :X], inverse[j][:], wb_sb[:, j, :], ALU.mult)
 
         def form_ue(j):
             nc.gpsimd.tensor_scalar(ue_sb[j][:], e_sb[j][:], us_sb[:, cols(j, 1)], 0.0, ALU.mult, ALU.add)
 
+        ue_sb.append(placed([P, C], F32, AT_K_RAW + 16, "ue_3"))
         gather_e("vector", 0)
         gather_e("scalar", 1)
         sum_e(0, 0)
         sum_e(1, 1)
         gather_f("vector", 0)
+        sum_f(0, 6)
         take_root(0)
         take_root(1)
-        sum_f(0, 2)
-        return_root(0, 3)
-        return_root(1, 4)
+        return_root(0, 2)
+        return_root(1, 3)
         gather_e("vector", 2)
         gather_e("scalar", 3)
         form_ue(0)
         form_ue(1)
-        sum_e(2, 5)
-        sum_e(3, 6)
+        sum_e(2, 1)
+        sum_e(3, 4)
         gather_f("vector", 1)
         take_inverse(0)
         take_inverse(1)
-        form_h(nc.gpsimd, 0)
-        form_h(nc.gpsimd, 1)
-        sum_f(1, 7)
+        form_h(0)
+        form_h(1)
+        sum_f(1, 2)
         take_root(2)
         take_root(3)
-        return_root(2, 0)
-        return_root(3, 1)
+        return_root(2, 3)
+        return_root(3, 5)
         fetch_t(0)
         fetch_t(1)
-        return_t(0, 3)
-        return_t(1, 4)
         gather_f("vector", 2)
+        sum_f(2, 4)
+        return_t(0, 0)
+        return_t(1, 7)
         form_ue(2)
-        form_ue(3)
         take_inverse(2)
         take_inverse(3)
-        sum_f(2, 5)
-        form_h(nc.gpsimd, 2)
-        gather_f("vector", 3, (0,))
-        gather_f("scalar", 3, (1,))
-        sum_f(3, 6)
+        form_h(2)
+        form_h(3)
+        gather_f("vector", 3)
         fetch_t(2)
-        return_t(2, 2)
-        form_m(0)
-        form_m(1)
-        form_h(nc.vector, 3)
+        nc.scalar.activation(ue_sb[LAST][:], e_sb[LAST][:], ACT.Copy, scale=us_sb[:, cols(LAST, 1)])
+        sum_f(3, 2)
+        return_t(2, 1)
+        fetch_t(3)
+        return_t(3, 6)
+        for j in range(PACK):
+            form_m(j)
 
-        neg_m_first = [placed([P, HALF], F32, AT_K_RAW + (12, 4, 6, 14)[j], "neg_m_first_%d" % j) for j in range(PACK)]
-        neg_m_third = placed([P, PACK, PART], F32, AT_K_RAW + 13, "neg_m_third")
-        m_less_dp = placed([P, PACK, PART], F32, AT_TS_LISTED, "m_less_dp")
-        g_grouped = [placed([P, PART, PACK], BF16, AT_K_PLANES + 2 * n if n else AT_UTS, "g_grouped_%d" % n) for n in range(PARTS)]
-        weighted = [placed([P, PACK, HALF], F32, (AT_TS, AT_UTS)[half], "weighted_%d" % half) for half in range(2)]
+        neg_m_first = [placed([P, HALF], F32, AT_K_RAW + (20, 22, 8, 4)[j], "neg_m_first_%d" % j) for j in range(PACK)]
+        neg_m_third = placed([P, PACK, PART], F32, AT_K_RAW + 4, "neg_m_third")
+        g_grouped = [placed([P, PART, PACK], BF16, AT_K_PLANES + 2 * n if n > 1 else AT_UTS + 1 + 3 * n, "g_grouped_%d" % n) for n in range(PARTS)]
+        m_less_dp = [placed([P, PART], F32, (AT_TS_LISTED, AT_UTS + 1.0625, AT_UTS + 2.0625, AT_UTS + 0.0625)[j], "m_less_dp_%d" % j) for j in range(PACK)]
+        weighted = [placed([P, PACK, HALF], F32, (AT_TS, AT_UTS + 4)[half], "weighted_%d" % half) for half in range(2)]
         g_codes = [keep.tile([P, PART], U32, name="g_codes_%d" % n, align_bytes=64) for n in range(PARTS)]
         g_scales = [keep.tile([P, PART], U8, name="g_scales_%d" % n, align_bytes=64) for n in range(PARTS)]
-        centred_turned, centred, centred_back, dk_banks, dk = {}, {}, {}, {}, {}
+        centred_turned, centred, centred_back, dk_banks = {}, {}, {}, {}
 
         def look_up_h(j, half):
             nc.vector.tensor_tensor(weighted[half][:, j, :], h_window[j][:].indirect(part_of(blk_list, half, HALF)), ue_sb[j][:, cols(half, HALF)], ALU.mult)
@@ -329,25 +337,27 @@ def tile_attend_gblkatt_kernel(tc, qT, kT, us, ts, wb, dp, offs, blkoffs, slotof
             nc.scalar.activation(dst, m_window[j][:].indirect(offsets), ACT.Copy, scale=-1.0)
 
         def look_up_m_less_dp(j):
-            nc.vector.tensor_tensor(m_less_dp[:, j, :], m_window[j][:].indirect(part_of(blk_list, LAST, PART)), dp_sb[j][:, cols(LAST, PART)], ALU.subtract)
+            nc.vector.tensor_tensor(m_less_dp[j][:], m_window[j][:].indirect(part_of(blk_list, LAST, PART)), dp_sb[j][:, cols(LAST, PART)], ALU.subtract)
 
-        def turn_centred(chunk, j):
-            if j == 0:
-                centred_turned[chunk] = bank((7, 0, 1, 5, 1, 5, 7, 0)[chunk], "centred_turned_%d" % chunk)
-            dst = centred_turned[chunk][:, j, :]
-            if chunk >= 6:
-                turn(dst, m_less_dp[:, j, cols(chunk - 6, P)])
-            else:
-                turn(dst, dp_sb[j][:, cols(chunk, P)], start=True, stop=False)
-                neg_m = neg_m_first[j][:, cols(chunk, P)] if chunk < CHUNKS else neg_m_third[:, j, cols(chunk - CHUNKS, P)]
-                turn(dst, neg_m, start=False, stop=True)
+        def turn_centred(chunks, j):
+            for chunk in chunks:
+                if j == 0:
+                    centred_turned[chunk] = bank((2, 4, 3, 5, 2, 4, 2, 4)[chunk], "centred_turned_%d" % chunk)
+                if chunk < 6:
+                    turn(centred_turned[chunk][:, j, :], dp_sb[j][:, cols(chunk, P)], start=True, stop=False)
+            for chunk in chunks:
+                if chunk >= 6:
+                    term = m_less_dp[j][:, cols(chunk - 6, P)]
+                else:
+                    term = neg_m_first[j][:, cols(chunk, P)] if chunk < CHUNKS else neg_m_third[:, j, cols(chunk - CHUNKS, P)]
+                turn(centred_turned[chunk][:, j, :], term, start=(chunk >= 6), stop=True)
 
         def scale_centred(chunk):
             centred[chunk] = placed([P, HALF], F32, AT_E + 2 * chunk, "centred_%d" % chunk)
-            nc.scalar.activation(centred[chunk][:], flat(centred_turned[chunk][:]), ACT.Copy, scale=(neg_ts_col if chunk >= 6 else ts_col)[:, cols(chunk, 1)])
+            nc.scalar.activation(centred[chunk][:], flat(centred_turned[chunk][:]), ACT.Copy, scale=neg_ts_col[:, cols(chunk - CHUNKS, 1)] if chunk >= 6 else ts_col[:, cols(chunk, 1)])
 
         def return_centred(chunk):
-            centred_back[chunk] = turn_back(centred[chunk], (3, 4, 2, 6)[chunk % 4], "centred_back_%d" % chunk).rearrange("p (j c) -> p j c", j=PACK)
+            centred_back[chunk] = turn_back(centred[chunk], (0, 7, 1, 6, 3, 5, 2, 4)[chunk], "centred_back_%d" % chunk).rearrange("p (j c) -> p j c", j=PACK)
 
         def gradient(chunk):
             half, b = divmod(chunk, CHUNKS)
@@ -357,93 +367,104 @@ def tile_attend_gblkatt_kernel(tc, qT, kT, us, ts, wb, dp, offs, blkoffs, slotof
         def quantize_gradient(n):
             nc.vector.quantize_mx(out=g_codes[n][:].bitcast(E5M2), scales=g_scales[n][:], in_=flat(g_grouped[n][:]))
 
-        def multiply(n):
-            for pair in range(2):
-                product = flat(bank((7, 0, 1, 5)[2 * (n % 2) + pair], "dk_psum_%d_%d" % (n, pair))[:])
-                for i in range(2):
-                    t = 2 * pair + i
-                    product_mx(product[:, cols(i, PART)], q2_codes[:, cols(t, P)], q2_scales[:, cols(t, P)], g_codes[n][:], g_scales[n][:], E5M2)
-                dk_banks[(n, pair)] = product
+        dk_early = [placed([P, 2, PART], F32, (AT_K_RAW + 6, AT_UTS, AT_F + 8, AT_F + 10)[n], "dk_early_%d" % n) for n in range(PARTS)]
+        dk_late = placed([P, 2, C], F32, AT_F, "dk_late")
 
-        def fetch_dk(n):
-            for pair in range(2):
-                dk[(n, pair)] = placed([P, HALF], F32, (AT_F + 4 * n if n else AT_K_RAW + 13) + 2 * pair, "dk_%d_%d" % (n, pair))
-                nc.scalar.copy(dk[(n, pair)][:], dk_banks[(n, pair)])
+        def multiply(n, pair):
+            product = flat(bank(((0, 7, 1, 6), (6, 3, 5, 2))[pair][n], "dk_psum_%d_%d" % (n, pair))[:])
+            for i in range(2):
+                t = 2 * pair + i
+                product_mx(product[:, cols(i, PART)], q2_codes[:, cols(t, P)], q2_scales[:, cols(t, P)], g_codes[n][:], g_scales[n][:], E5M2)
+            dk_banks[(n, pair)] = product.rearrange("p (i c) -> p i c", i=2)
+
+        def fetch_dk(engine, n, pair):
+            move(engine, dk_late[:, :, cols(n, PART)] if pair else dk_early[n][:], dk_banks[(n, pair)])
 
         out_rows = out.rearrange("(p t) n -> t p n", t=PACK)
 
-        def place(engine, t, n):
-            move(engine, out_window[t][:].indirect(part_of(tok_list, n, PART)), dk[(n, t // 2)][:, cols(t % 2, PART)])
-            if n == PARTS - 1:
-                nc.sync.dma_start(out=out_rows[t], in_=out_window[t][:])
+        def place(engine, t, first, last):
+            values = dk_late[:, t % 2, first:last] if t // 2 else dk_early[first // PART][:, t, :]
+            move(engine, out_window[t][:].indirect(tok_list[:, first // 16 : last // 16]), values)
+
+        def store(t):
+            nc.sync.dma_start(out=out_rows[t], in_=out_window[t][:])
+
+        def place_part(engine, t, n):
+            place(engine, t, n * PART, (n + 1) * PART)
 
         def first_half(j):
             look_up_neg_m(neg_m_first[j][:], j, part_of(blk_list, 0, HALF))
-            for chunk in range(CHUNKS):
-                turn_centred(chunk, j)
+            turn_centred(range(CHUNKS), j)
 
-        look_up_neg_m(neg_m_first[0][:], 0, part_of(blk_list, 0, HALF))
-        fetch_t(3)
-        return_t(3, 6)
-        form_m(2)
-        for chunk in range(CHUNKS):
-            turn_centred(chunk, 0)
-        first_half(1)
-        look_up_m_less_dp(0)
-        look_up_m_less_dp(1)
-        form_m(3)
-        first_half(2)
-        first_half(3)
+        def third_part(j):
+            look_up_neg_m(neg_m_third[:, j, :], j, part_of(blk_list, 2, PART))
+
+        for j in range(PACK):
+            first_half(j)
         for j in range(PACK):
             look_up_h(j, 0)
-        look_up_m_less_dp(2)
-        look_up_m_less_dp(3)
+        look_up_m_less_dp(0)
         for chunk in range(CHUNKS):
             scale_centred(chunk)
             return_centred(chunk)
         for j in range(PACK):
-            look_up_neg_m(neg_m_third[:, j, :], j, part_of(blk_list, 2, PART))
-        for chunk in (6, 7, 4, 5):
-            for j in range(PACK):
-                turn_centred(chunk, j)
+            third_part(j)
+            turn_centred((4, 5), j)
         gradient(0)
         gradient(1)
         gradient(2)
         quantize_gradient(0)
         gradient(3)
-        for chunk in (6, 7, 4, 5):
-            scale_centred(chunk)
-        multiply(0)
-        look_up_h(0, 1)
+        multiply(0, 0)
+        look_up_m_less_dp(1)
         quantize_gradient(1)
-        fetch_dk(0)
-        multiply(1)
+        look_up_m_less_dp(2)
+        look_up_m_less_dp(3)
+        for chunk in (4, 5):
+            scale_centred(chunk)
+        fetch_dk("scalar", 0, 0)
+        for j in range(PACK):
+            turn_centred((6, 7), j)
+        place_part("scalar", 0, 0)
+        for chunk in (6, 7):
+            scale_centred(chunk)
+        multiply(1, 0)
         for chunk in range(CHUNKS, 2 * CHUNKS):
             return_centred(chunk)
-        for j in range(1, PACK):
+        for j in range(PACK):
             look_up_h(j, 1)
-        place("scalar", 0, 0)
-        fetch_dk(1)
-        place("scalar", 1, 0)
-        place("scalar", 0, 1)
+        fetch_dk("scalar", 1, 0)
+        place_part("scalar", 1, 0)
+        place_part("scalar", 0, 1)
+        place_part("scalar", 1, 1)
         gradient(4)
         gradient(5)
+        multiply(1, 1)
         gradient(6)
         quantize_gradient(2)
         gradient(7)
-        multiply(2)
-        fetch_dk(2)
+        multiply(2, 0)
+        multiply(2, 1)
+        fetch_dk("vector", 2, 0)
         quantize_gradient(3)
-        multiply(3)
-        fetch_dk(3)
-        place("vector", 0, 2)
-        place("vector", 2, 0)
-        place("vector", 0, 3)
-        place("scalar", 1, 1)
-        place("scalar", 3, 0)
-        place("scalar", 1, 2)
-        place("scalar", 1, 3)
-        for n in range(1, PARTS):
-            place("vector", 2, n)
-        for n in range(1, PARTS):
-            place("scalar", 3, n)
+        multiply(3, 0)
+        multiply(3, 1)
+        fetch_dk("scalar", 1, 1)
+        fetch_dk("scalar", 3, 0)
+        multiply(0, 1)
+        fetch_dk("scalar", 2, 1)
+        fetch_dk("scalar", 3, 1)
+        fetch_dk("scalar", 0, 1)
+        place_part("vector", 0, 2)
+        place_part("vector", 0, 3)
+        store(0)
+        place_part("scalar", 1, 3)
+        place_part("scalar", 3, 3)
+        place_part("scalar", 1, 2)
+        store(1)
+        place_part("vector", 2, 3)
+        place("vector", 2, 0, 768)
+        store(2)
+        place("scalar", 3, 0, 384)
+        place("scalar", 3, 384, 768)
+        store(3)

@@ -97,7 +97,7 @@ def tile_attend_gblkatt_kernel(tc, qT, kT, us, ts, wb, dp, offs, blkoffs, slotof
         nc.vector.memset(ts_window[0:TS_ROW, :].bitcast(I32), 0)
         nc.sync.dma_start(tok_list[:], offs)
         make_identity(nc, ident[:])
-        q_raw = placed([P, PACK, R], F32, AT_OUT + 24, "q_raw")
+        q_raw = placed([P, PACK, R], F32, AT_Q_RAW, "q_raw")
         nc.sync.dma_start(out=q_raw[:], in_=qT.rearrange("(p t) r -> p t r", t=PACK))
         nc.sync.dma_start(out=us_sb[:, :PACK], in_=us.rearrange("(p j) o -> p (j o)", j=PACK))
         k_rows = kT.rearrange("(p t) n -> t p n", t=PACK)
@@ -122,8 +122,6 @@ def tile_attend_gblkatt_kernel(tc, qT, kT, us, ts, wb, dp, offs, blkoffs, slotof
         m_window = [placed([P, BLK_WINDOW], F32, AT_M + BLK_WINDOW_KIB * j, "m_window_%d" % j) for j in range(PACK)]
         for t in (1, 2):
             nc.gpsimd.memset(out_window[t][:], 0.0)
-        for window in h_window + m_window:
-            nc.gpsimd.memset(window[:, X:], 0.0)
 
         q_grouped = placed([P, PACK, P, PACK], BF16, AT_Q_GROUPED, "q_grouped")
         q_codes = keep.tile([P, R], U32, name="q_codes", align_bytes=64)
@@ -140,7 +138,7 @@ def tile_attend_gblkatt_kernel(tc, qT, kT, us, ts, wb, dp, offs, blkoffs, slotof
         nc.vector.tensor_scalar(neg_ts_col[:], turned[:, :, TS_ROW], -1.0, None, ALU.mult)
         nc.vector.quantize_mx(out=q_codes[:].bitcast(E4M3), scales=q_scales[:], in_=q_grouped[:].rearrange("p j m t -> p (j m t)"))
 
-        ts_rows = placed([P, C], F32, AT_OUT + 24, "ts_rows")
+        ts_rows = placed([P, C], F32, AT_Q_RAW, "ts_rows")
         for half in range(2):
             spread = bank(2 + half, "ts_spread_%d" % half)
             for b in range(CHUNKS):
@@ -150,14 +148,14 @@ def tile_attend_gblkatt_kernel(tc, qT, kT, us, ts, wb, dp, offs, blkoffs, slotof
         q_words = q_grouped[:].rearrange("p j m t -> p (j m t)").bitcast(F32).rearrange("p (j m u) -> p j m u", j=PACK, u=2)
         q2_codes = keep.tile([P, D], U32, name="q2_codes", align_bytes=64)
         q2_scales = keep.tile([P, D], U8, name="q2_scales", align_bytes=64)
-        q2_grouped = placed([P, PACK, P, PACK], BF16, AT_LATE, "q2_grouped")
+        q2_grouped = placed([P, PACK, P, PACK], BF16, AT_OUT + 24, "q2_grouped")
         for u in range(2):
             turned = bank(4 + u, "q_turned_%d" % u)
             for j in range(PACK):
                 turn(turned[:, j, :], q_words[:, j, :, u])
             nc.scalar.copy(q2_grouped[:, cols(u, 2), :, :], flat(turned[:]).bitcast(BF16).rearrange("m (j p e) -> m e p j", j=PACK, e=2))
 
-        k_grouped = [placed([P, PART, PACK], BF16, AT_TS + 2 * n if n < LAST else AT_OUT + 28, "k_grouped_%d" % n) for n in range(PARTS)]
+        k_grouped = [placed([P, PART, PACK], BF16, AT_TS + 2 * n, "k_grouped_%d" % n) for n in range(PARTS)]
         k_planes = {n: placed([P, PACK, PART], BF16, AT_K_PLANES + 2 * n, "k_planes_%d" % n) for n in (2, 3)}
         k_codes = [placed([P, HALF], U32, AT_K_CODES + 2 * half, "k_codes_%d" % half) for half in range(2)]
         k_scales = [keep.tile([P, HALF], U8, name="k_scales_%d" % half, align_bytes=64) for half in range(2)]
@@ -169,11 +167,11 @@ def tile_attend_gblkatt_kernel(tc, qT, kT, us, ts, wb, dp, offs, blkoffs, slotof
                 nc.scalar.activation(k_planes[n][:, t, :], k_raw[t][:].indirect(part_of(tok_list, n, PART)), ACT.Copy)
 
         gather_keys(0)
-        uts = [placed([P, C], F32, AT_UTS + 4 * j, "uts_%d" % j) for j in range(PACK)]
-        for j in range(PACK):
-            nc.gpsimd.tensor_scalar(uts[j][:], ts_rows[:], us_sb[:, cols(j, 1)], 0.0, ALU.mult, ALU.add)
         gather_keys(1)
         nc.vector.quantize_mx(out=q2_codes[:].bitcast(E4M3), scales=q2_scales[:], in_=q2_grouped[:].rearrange("m t p j -> m (t p j)"))
+        nc.gpsimd.memset(out_window[LAST][:], 0.0)
+        for window in h_window + m_window:
+            nc.gpsimd.memset(window[:, X:], 0.0)
         gather_keys(2)
         gather_keys(3)
         for n in (2, 3):
@@ -186,13 +184,13 @@ def tile_attend_gblkatt_kernel(tc, qT, kT, us, ts, wb, dp, offs, blkoffs, slotof
 
         e_sb = [placed([P, C], F32, AT_E + 4 * j, "e_%d" % j) for j in range(PACK)]
         f_sb = [placed([P, C], F32, AT_F + 4 * j, "f_%d" % j) for j in range(PACK)]
-        ue_sb = [placed([P, C], F32, AT_W + 4 * j, "ue_%d" % j) for j in range(LAST)]
+        ue_sb = {j: placed([P, C], F32, AT_W + 4 * j, "ue_%d" % j) for j in range(2)}
         def score(j, half, index, kib):
             scores = flat(bank(index, "scores_%d_%d" % (j, half))[:])
             product_mx(scores, q_codes[:, cols(j, P)], q_scales[:, cols(j, P)], k_codes[half][:], k_scales[half][:])
             z_sb = placed([P, HALF], F32, kib, "z_sb_%d_%d" % (j, half))
-            nc.vector.tensor_tensor(z_sb[:], scores, uts[j][:, cols(half, HALF)], ALU.mult)
-            nc.scalar.activation(e_sb[j][:, cols(half, HALF)], z_sb[:], ACT.Exp)
+            nc.vector.tensor_tensor(z_sb[:], scores, ts_rows[:, cols(half, HALF)], ALU.mult)
+            nc.scalar.activation(e_sb[j][:, cols(half, HALF)], z_sb[:], ACT.Exp, scale=us_sb[:, cols(j, 1)])
 
         def form_f(j):
             nc.gpsimd.tensor_tensor(f_sb[j][:], e_sb[j][:], dp_sb[j][:], ALU.mult)
@@ -202,7 +200,6 @@ def tile_attend_gblkatt_kernel(tc, qT, kT, us, ts, wb, dp, offs, blkoffs, slotof
         quantize_keys(2)
         score(0, 0, 0, AT_K_PLANES + 4)
         quantize_keys(3)
-        nc.gpsimd.memset(out_window[LAST][:], 0.0)
         score(1, 0, 1, AT_K_PLANES + 6)
         score(0, 1, 2, AT_K_RAW)
         form_f(0)
@@ -258,7 +255,7 @@ def tile_attend_gblkatt_kernel(tc, qT, kT, us, ts, wb, dp, offs, blkoffs, slotof
             t_turned[j] = pair_sums_turned(f_slots[j], index, "t_turned_%d" % j)
 
         def fetch_t(j):
-            t_fetched[j] = placed([P, X], F32, (AT_TS_ROWS, AT_TS_ROWS + 2, AT_Z, AT_Z + 2)[j], "t_fetched_%d" % j)
+            t_fetched[j] = placed([P, X], F32, (AT_TS_ROWS, AT_TS, AT_W + 8, AT_Z + 2)[j], "t_fetched_%d" % j)
             nc.scalar.copy(t_fetched[j][:], t_turned[j])
 
         def return_t(j, index):
@@ -273,7 +270,6 @@ def tile_attend_gblkatt_kernel(tc, qT, kT, us, ts, wb, dp, offs, blkoffs, slotof
         def form_ue(j):
             nc.gpsimd.tensor_scalar(ue_sb[j][:], e_sb[j][:], us_sb[:, cols(j, 1)], 0.0, ALU.mult, ALU.add)
 
-        ue_sb.append(placed([P, C], F32, AT_K_RAW + 16, "ue_3"))
         gather_e("vector", 0)
         gather_e("scalar", 1)
         sum_e(0, 0)
@@ -306,20 +302,23 @@ def tile_attend_gblkatt_kernel(tc, qT, kT, us, ts, wb, dp, offs, blkoffs, slotof
         sum_f(2, 4)
         return_t(0, 0)
         return_t(1, 7)
-        form_ue(2)
         take_inverse(2)
-        take_inverse(3)
         form_h(2)
-        form_h(3)
         gather_f("vector", 3)
         fetch_t(2)
+        take_inverse(3)
+        ue_sb[LAST] = placed([P, C], F32, AT_K_RAW + 16, "ue_3")
         nc.scalar.activation(ue_sb[LAST][:], e_sb[LAST][:], ACT.Copy, scale=us_sb[:, cols(LAST, 1)])
         sum_f(3, 2)
         return_t(2, 1)
         fetch_t(3)
         return_t(3, 6)
-        for j in range(PACK):
+        for j in range(LAST):
             form_m(j)
+        ue_sb[2] = placed([P, C], F32, AT_W + 8, "ue_2")
+        nc.vector.tensor_scalar(ue_sb[2][:], e_sb[2][:], us_sb[:, cols(2, 1)], None, ALU.mult)
+        nc.vector.tensor_tensor(h_window[LAST][:, :X], inverse[LAST][:], wb_sb[:, LAST, :], ALU.mult)
+        form_m(LAST)
 
         neg_m_first = [placed([P, HALF], F32, AT_K_RAW + (20, 22, 8, 4)[j], "neg_m_first_%d" % j) for j in range(PACK)]
         neg_m_third = placed([P, PACK, PART], F32, AT_K_RAW + 4, "neg_m_third")

@@ -92,7 +92,7 @@ def tile_attend_gblkatt_kernel(tc, qT, kT, us, ts, wb, dp, offs, blkoffs, slotof
         ident = keep.tile([P, P], F32, name="ident")
         us_sb = keep.tile([P, 8], F32, name="us_sb")
 
-        ts_window = placed([P, T], F32, AT_OUT + 16, "ts_window")
+        ts_window = placed([P, T], F32, AT_UTS, "ts_window")
         nc.scalar.dma_start(out=ts_window[TS_ROW:P, :], in_=ts[0:1, :])
         nc.vector.memset(ts_window[0:TS_ROW, :].bitcast(I32), 0)
         nc.sync.dma_start(tok_list[:], offs)
@@ -117,16 +117,15 @@ def tile_attend_gblkatt_kernel(tc, qT, kT, us, ts, wb, dp, offs, blkoffs, slotof
         out_window = [placed([P, T], F32, AT_OUT + 8 * t, "out_window_%d" % t) for t in range(PACK)]
         nc.vector.memset(out_window[0][:].bitcast(I32), 0)
         ts_listed = placed([P, C], F32, AT_TS_LISTED, "ts_listed")
-        nc.vector.tensor_copy(ts_listed[:], ts_window[:].indirect(tok_list[:]))
+        move("scalar", ts_listed[:], ts_window[:].indirect(tok_list[:]))
         h_window = [placed([P, BLK_WINDOW], F32, AT_H + BLK_WINDOW_KIB * j, "h_window_%d" % j) for j in range(PACK)]
         m_window = [placed([P, BLK_WINDOW], F32, AT_M + BLK_WINDOW_KIB * j, "m_window_%d" % j) for j in range(PACK)]
-        for t in (1, 2):
-            nc.gpsimd.memset(out_window[t][:], 0.0)
+        nc.gpsimd.memset(out_window[1][:], 0.0)
 
-        q_grouped = placed([P, PACK, P, PACK], BF16, AT_Q_GROUPED, "q_grouped")
+        q_grouped = placed([P, PACK, P, PACK], BF16, AT_OUT + 16, "q_grouped")
         q_codes = keep.tile([P, R], U32, name="q_codes", align_bytes=64)
         q_scales = keep.tile([P, R], U8, name="q_scales", align_bytes=64)
-        nc.scalar.activation(q_grouped[:].rearrange("p j m t -> p m t j"), q_raw[:].rearrange("p t (m j) -> p m t j", j=PACK), ACT.Copy)
+        nc.vector.tensor_copy(q_grouped[:].rearrange("p j m t -> p m j t"), q_raw[:].rearrange("p t (m j) -> p m j t", j=PACK))
 
         ts_col = keep.tile([P, C // P], F32, name="ts_col")
         neg_ts_col = keep.tile([P, CHUNKS], F32, name="neg_ts_col")
@@ -138,7 +137,7 @@ def tile_attend_gblkatt_kernel(tc, qT, kT, us, ts, wb, dp, offs, blkoffs, slotof
         nc.vector.tensor_scalar(neg_ts_col[:], turned[:, :, TS_ROW], -1.0, None, ALU.mult)
         nc.vector.quantize_mx(out=q_codes[:].bitcast(E4M3), scales=q_scales[:], in_=q_grouped[:].rearrange("p j m t -> p (j m t)"))
 
-        ts_rows = placed([P, C], F32, AT_Q_RAW, "ts_rows")
+        ts_rows = placed([P, C], F32, AT_LATE, "ts_rows")
         for half in range(2):
             spread = bank(2 + half, "ts_spread_%d" % half)
             for b in range(CHUNKS):
@@ -164,9 +163,10 @@ def tile_attend_gblkatt_kernel(tc, qT, kT, us, ts, wb, dp, offs, blkoffs, slotof
             for n in (0, 1):
                 nc.vector.tensor_copy(k_grouped[n][:, :, t], k_raw[t][:].indirect(part_of(tok_list, n, PART)))
             for n in (2, 3):
-                nc.scalar.activation(k_planes[n][:, t, :], k_raw[t][:].indirect(part_of(tok_list, n, PART)), ACT.Copy)
+                move("scalar", k_planes[n][:, t, :], k_raw[t][:].indirect(part_of(tok_list, n, PART)))
 
         gather_keys(0)
+        nc.gpsimd.memset(out_window[2][:], 0.0)
         gather_keys(1)
         nc.vector.quantize_mx(out=q2_codes[:].bitcast(E4M3), scales=q2_scales[:], in_=q2_grouped[:].rearrange("m t p j -> m (t p j)"))
         nc.gpsimd.memset(out_window[LAST][:], 0.0)

@@ -116,7 +116,7 @@ def tile_attend_gblkatt_kernel(tc, qT, kT, us, ts, wb, dp, offs, blkoffs, slotof
 
         out_window = [placed([P, T], F32, AT_OUT + 8 * t, "out_window_%d" % t) for t in range(PACK)]
         nc.vector.memset(out_window[0][:].bitcast(I32), 0)
-        ts_listed = placed([P, C], F32, AT_TS_LISTED, "ts_listed")
+        ts_listed = placed([P, C], F32, AT_TS, "ts_listed")
         move("scalar", ts_listed[:], ts_window[:].indirect(tok_list[:]))
         h_window = [placed([P, BLK_WINDOW], F32, AT_H + BLK_WINDOW_KIB * j, "h_window_%d" % j) for j in range(PACK)]
         m_window = [placed([P, BLK_WINDOW], F32, AT_M + BLK_WINDOW_KIB * j, "m_window_%d" % j) for j in range(PACK)]
@@ -163,7 +163,7 @@ def tile_attend_gblkatt_kernel(tc, qT, kT, us, ts, wb, dp, offs, blkoffs, slotof
             for n in (0, 1):
                 nc.vector.tensor_copy(k_grouped[n][:, :, t], k_raw[t][:].indirect(part_of(tok_list, n, PART)))
             for n in (2, 3):
-                move("scalar", k_planes[n][:, t, :], k_raw[t][:].indirect(part_of(tok_list, n, PART)))
+                move("scalar" if t else "vector", k_planes[n][:, t, :], k_raw[t][:].indirect(part_of(tok_list, n, PART)))
 
         gather_keys(0)
         nc.gpsimd.memset(out_window[2][:], 0.0)
@@ -248,14 +248,14 @@ def tile_attend_gblkatt_kernel(tc, qT, kT, us, ts, wb, dp, offs, blkoffs, slotof
             root_back[j] = turn_back(root[j], index, "root_back_%d" % j)
 
         def take_inverse(j):
-            inverse[j] = placed([P, X], F32, (AT_INV, AT_INV + 2, AT_TS_LISTED, AT_TS)[j], "inverse_%d" % j)
+            inverse[j] = placed([P, X], F32, (AT_INV, AT_INV + 2, AT_TS_LISTED, AT_TS - 1)[j], "inverse_%d" % j)
             nc.scalar.activation(inverse[j][:], root_back[j], ACT.Square)
 
         def sum_f(j, index):
             t_turned[j] = pair_sums_turned(f_slots[j], index, "t_turned_%d" % j)
 
         def fetch_t(j):
-            t_fetched[j] = placed([P, X], F32, (AT_TS_ROWS, AT_TS, AT_W + 8, AT_Z + 2)[j], "t_fetched_%d" % j)
+            t_fetched[j] = placed([P, X], F32, (AT_TS_ROWS, AT_TS - 1, AT_W + 8, AT_Z + 2)[j], "t_fetched_%d" % j)
             nc.scalar.copy(t_fetched[j][:], t_turned[j])
 
         def return_t(j, index):
@@ -305,10 +305,10 @@ def tile_attend_gblkatt_kernel(tc, qT, kT, us, ts, wb, dp, offs, blkoffs, slotof
         take_inverse(2)
         form_h(2)
         gather_f("vector", 3)
+        ue_sb[LAST] = placed([P, C], F32, AT_K_RAW, "ue_3")
+        nc.scalar.activation(ue_sb[LAST][:], e_sb[LAST][:], ACT.Copy, scale=us_sb[:, cols(LAST, 1)])
         fetch_t(2)
         take_inverse(3)
-        ue_sb[LAST] = placed([P, C], F32, AT_K_RAW + 16, "ue_3")
-        nc.scalar.activation(ue_sb[LAST][:], e_sb[LAST][:], ACT.Copy, scale=us_sb[:, cols(LAST, 1)])
         sum_f(3, 2)
         return_t(2, 1)
         fetch_t(3)
@@ -320,11 +320,11 @@ def tile_attend_gblkatt_kernel(tc, qT, kT, us, ts, wb, dp, offs, blkoffs, slotof
         nc.vector.tensor_tensor(h_window[LAST][:, :X], inverse[LAST][:], wb_sb[:, LAST, :], ALU.mult)
         form_m(LAST)
 
-        neg_m_first = [placed([P, HALF], F32, AT_K_RAW + (20, 22, 8, 4)[j], "neg_m_first_%d" % j) for j in range(PACK)]
-        neg_m_third = placed([P, PACK, PART], F32, AT_K_RAW + 4, "neg_m_third")
-        g_grouped = [placed([P, PART, PACK], BF16, AT_K_PLANES + 2 * n if n > 1 else AT_UTS + 1 + 3 * n, "g_grouped_%d" % n) for n in range(PARTS)]
-        m_less_dp = [placed([P, PART], F32, (AT_TS_LISTED, AT_UTS + 1.0625, AT_UTS + 2.0625, AT_UTS + 0.0625)[j], "m_less_dp_%d" % j) for j in range(PACK)]
-        weighted = [placed([P, PACK, HALF], F32, (AT_TS, AT_UTS + 4)[half], "weighted_%d" % half) for half in range(2)]
+        neg_m_first = [placed([P, HALF], F32, AT_K_RAW + (20, 22, 8, 5)[j], "neg_m_first_%d" % j) for j in range(PACK)]
+        neg_m_third = [placed([P, PART], F32, AT_K_RAW + 3.0625 + j if j else AT_TS - 1, "neg_m_third_%d" % j) for j in range(PACK)]
+        g_grouped = [placed([P, PART, PACK], BF16, AT_K_PLANES + 2 * n if n < LAST else AT_UTS + 8, "g_grouped_%d" % n) for n in range(PARTS)]
+        m_less_dp = [placed([P, PART], F32, (AT_TS_LISTED, AT_K_RAW + 20, AT_E + 2, AT_E + 4)[j], "m_less_dp_%d" % j) for j in range(PACK)]
+        weighted = [placed([P, PACK, HALF], F32, (AT_TS, AT_E + 6)[half], "weighted_%d" % half) for half in range(2)]
         g_codes = [keep.tile([P, PART], U32, name="g_codes_%d" % n, align_bytes=64) for n in range(PARTS)]
         g_scales = [keep.tile([P, PART], U8, name="g_scales_%d" % n, align_bytes=64) for n in range(PARTS)]
         centred_turned, centred, centred_back, dk_banks = {}, {}, {}, {}
@@ -348,11 +348,11 @@ def tile_attend_gblkatt_kernel(tc, qT, kT, us, ts, wb, dp, offs, blkoffs, slotof
                 if chunk >= 6:
                     term = m_less_dp[j][:, cols(chunk - 6, P)]
                 else:
-                    term = neg_m_first[j][:, cols(chunk, P)] if chunk < CHUNKS else neg_m_third[:, j, cols(chunk - CHUNKS, P)]
+                    term = neg_m_first[j][:, cols(chunk, P)] if chunk < CHUNKS else neg_m_third[j][:, cols(chunk - CHUNKS, P)]
                 turn(centred_turned[chunk][:, j, :], term, start=(chunk >= 6), stop=True)
 
         def scale_centred(chunk):
-            centred[chunk] = placed([P, HALF], F32, AT_E + 2 * chunk, "centred_%d" % chunk)
+            centred[chunk] = placed([P, HALF], F32, AT_E + 2 * chunk if chunk < CHUNKS else AT_UTS + 2 * chunk - 2 * CHUNKS, "centred_%d" % chunk)
             nc.scalar.activation(centred[chunk][:], flat(centred_turned[chunk][:]), ACT.Copy, scale=neg_ts_col[:, cols(chunk - CHUNKS, 1)] if chunk >= 6 else ts_col[:, cols(chunk, 1)])
 
         def return_centred(chunk):
@@ -366,18 +366,19 @@ def tile_attend_gblkatt_kernel(tc, qT, kT, us, ts, wb, dp, offs, blkoffs, slotof
         def quantize_gradient(n):
             nc.vector.quantize_mx(out=g_codes[n][:].bitcast(E5M2), scales=g_scales[n][:], in_=flat(g_grouped[n][:]))
 
-        dk_early = [placed([P, 2, PART], F32, (AT_K_RAW + 6, AT_UTS, AT_F + 8, AT_F + 10)[n], "dk_early_%d" % n) for n in range(PARTS)]
+        dk_early = [placed([P, 2, PART], F32, (AT_F + 12, AT_E + 4, AT_F + 8, AT_F + 10)[n], "dk_early_%d" % n) for n in range(PARTS)]
         dk_late = placed([P, 2, C], F32, AT_F, "dk_late")
 
         def multiply(n, pair):
-            product = flat(bank(((0, 7, 1, 6), (6, 3, 5, 2))[pair][n], "dk_psum_%d_%d" % (n, pair))[:])
+            product = flat(bank(((0, 7, 1, 6), (0, 3, 5, 2))[pair][n], "dk_psum_%d_%d" % (n, pair))[:])
             for i in range(2):
                 t = 2 * pair + i
                 product_mx(product[:, cols(i, PART)], q2_codes[:, cols(t, P)], q2_scales[:, cols(t, P)], g_codes[n][:], g_scales[n][:], E5M2)
             dk_banks[(n, pair)] = product.rearrange("p (i c) -> p i c", i=2)
 
         def fetch_dk(engine, n, pair):
-            move(engine, dk_late[:, :, cols(n, PART)] if pair else dk_early[n][:], dk_banks[(n, pair)])
+            engine_copy = nc.vector.tensor_copy if engine == "vector" else nc.scalar.copy
+            engine_copy(dk_late[:, :, cols(n, PART)] if pair else dk_early[n][:], dk_banks[(n, pair)])
 
         out_rows = out.rearrange("(p t) n -> t p n", t=PACK)
 
@@ -396,32 +397,34 @@ def tile_attend_gblkatt_kernel(tc, qT, kT, us, ts, wb, dp, offs, blkoffs, slotof
             turn_centred(range(CHUNKS), j)
 
         def third_part(j):
-            look_up_neg_m(neg_m_third[:, j, :], j, part_of(blk_list, 2, PART))
+            look_up_neg_m(neg_m_third[j][:], j, part_of(blk_list, 2, PART))
 
         for j in range(PACK):
             first_half(j)
+        look_up_m_less_dp(0)
         for j in range(PACK):
             look_up_h(j, 0)
-        look_up_m_less_dp(0)
+        third_part(0)
         for chunk in range(CHUNKS):
             scale_centred(chunk)
             return_centred(chunk)
-        for j in range(PACK):
+        turn_centred((4, 5), 0)
+        for j in range(1, PACK):
             third_part(j)
             turn_centred((4, 5), j)
+        look_up_m_less_dp(1)
         gradient(0)
         gradient(1)
         gradient(2)
         quantize_gradient(0)
+        look_up_m_less_dp(2)
         gradient(3)
         multiply(0, 0)
-        look_up_m_less_dp(1)
-        quantize_gradient(1)
-        look_up_m_less_dp(2)
         look_up_m_less_dp(3)
+        quantize_gradient(1)
+        fetch_dk("scalar", 0, 0)
         for chunk in (4, 5):
             scale_centred(chunk)
-        fetch_dk("scalar", 0, 0)
         for j in range(PACK):
             turn_centred((6, 7), j)
         place_part("scalar", 0, 0)
@@ -449,12 +452,12 @@ def tile_attend_gblkatt_kernel(tc, qT, kT, us, ts, wb, dp, offs, blkoffs, slotof
         multiply(3, 0)
         multiply(3, 1)
         fetch_dk("scalar", 1, 1)
-        fetch_dk("scalar", 3, 0)
         multiply(0, 1)
         fetch_dk("scalar", 2, 1)
         fetch_dk("scalar", 3, 1)
         fetch_dk("scalar", 0, 1)
         place_part("vector", 0, 2)
+        fetch_dk("vector", 3, 0)
         place_part("vector", 0, 3)
         store(0)
         place_part("scalar", 1, 3)

@@ -219,7 +219,10 @@ def tile_attend_gblkatt_kernel(tc, qT, kT, us, ts, wb, dp, offs, blkoffs, slotof
 
         def by_slots(engine, picked, window, halves):
             for half in halves:
-                move(engine, picked[:, cols(half, HALF)], window[:].indirect(part_of(slot_list, half, HALF)))
+                dst = picked[:, cols(half, HALF)]
+                if engine == "vector":
+                    dst = dst.rearrange("p (i x) -> p x i", i=2)
+                move(engine, dst, window[:].indirect(part_of(slot_list, half, HALF)))
 
         def gather_e(engine, j, halves=(0, 1)):
             by_slots(engine, e_slots[j], e_sb[j], halves)
@@ -227,18 +230,18 @@ def tile_attend_gblkatt_kernel(tc, qT, kT, us, ts, wb, dp, offs, blkoffs, slotof
         def gather_f(engine, j, halves=(0, 1)):
             by_slots(engine, f_slots[j], f_sb[j], halves)
 
-        def pair_sums_turned(picked, index, name):
-            pairs = picked[:].rearrange("p (x i) -> p x i", i=2)
+        def pair_sums_turned(picked, parted, index, name):
+            pairs = picked[:].rearrange("p (h i x) -> p h x i" if parted else "p (h x i) -> p h x i", h=2, i=2)
             sums = bank(index, name)
             for b in range(CHUNKS):
                 for i in range(2):
-                    turn(sums[:, b, :], pairs[:, cols(b, P), i], start=(i == 0), stop=(i == 1))
+                    turn(sums[:, b, :], pairs[:, b // 2, cols(b % 2, P), i], start=(i == 0), stop=(i == 1))
             return flat(sums[:])
 
         s_turned, root, root_back, inverse, t_turned, t_fetched, t_back = {}, {}, {}, {}, {}, {}, {}
 
         def sum_e(j, index):
-            s_turned[j] = pair_sums_turned(e_slots[j], index, "s_turned_%d" % j)
+            s_turned[j] = pair_sums_turned(e_slots[j], j % 2 == 0, index, "s_turned_%d" % j)
 
         def take_root(j):
             root[j] = placed([P, X], F32, AT_K_RAW + (24, 30, 0, 2)[j], "root_%d" % j)
@@ -252,7 +255,7 @@ def tile_attend_gblkatt_kernel(tc, qT, kT, us, ts, wb, dp, offs, blkoffs, slotof
             nc.scalar.activation(inverse[j][:], root_back[j], ACT.Square)
 
         def sum_f(j, index):
-            t_turned[j] = pair_sums_turned(f_slots[j], index, "t_turned_%d" % j)
+            t_turned[j] = pair_sums_turned(f_slots[j], True, index, "t_turned_%d" % j)
 
         def fetch_t(j):
             t_fetched[j] = placed([P, X], F32, (AT_TS_ROWS, AT_TS - 1, AT_W + 8, AT_Z + 2)[j], "t_fetched_%d" % j)

@@ -217,18 +217,18 @@ def tile_attend_gblkatt_kernel(tc, qT, kT, us, ts, wb, dp, offs, blkoffs, slotof
         e_slots.append(placed([P, C], F32, AT_K_RAW + 20, "e_slots_3"))
         f_slots.append(placed([P, C], F32, AT_K_RAW + 20, "f_slots_3"))
 
-        def by_slots(engine, picked, window, halves):
+        def by_slots(engine, picked, window, halves, parted):
             for half in halves:
                 dst = picked[:, cols(half, HALF)]
-                if engine == "vector":
+                if parted:
                     dst = dst.rearrange("p (i x) -> p x i", i=2)
                 move(engine, dst, window[:].indirect(part_of(slot_list, half, HALF)))
 
         def gather_e(engine, j, halves=(0, 1)):
-            by_slots(engine, e_slots[j], e_sb[j], halves)
+            by_slots(engine, e_slots[j], e_sb[j], halves, False)
 
         def gather_f(engine, j, halves=(0, 1)):
-            by_slots(engine, f_slots[j], f_sb[j], halves)
+            by_slots(engine, f_slots[j], f_sb[j], halves, j > 0)
 
         def pair_sums_turned(picked, parted, index, name):
             pairs = picked[:].rearrange("p (h i x) -> p h x i" if parted else "p (h x i) -> p h x i", h=2, i=2)
@@ -241,7 +241,7 @@ def tile_attend_gblkatt_kernel(tc, qT, kT, us, ts, wb, dp, offs, blkoffs, slotof
         s_turned, root, root_back, inverse, t_turned, t_fetched, t_back = {}, {}, {}, {}, {}, {}, {}
 
         def sum_e(j, index):
-            s_turned[j] = pair_sums_turned(e_slots[j], j % 2 == 0, index, "s_turned_%d" % j)
+            s_turned[j] = pair_sums_turned(e_slots[j], False, index, "s_turned_%d" % j)
 
         def take_root(j):
             root[j] = placed([P, X], F32, AT_K_RAW + (24, 30, 0, 2)[j], "root_%d" % j)
@@ -255,7 +255,7 @@ def tile_attend_gblkatt_kernel(tc, qT, kT, us, ts, wb, dp, offs, blkoffs, slotof
             nc.scalar.activation(inverse[j][:], root_back[j], ACT.Square)
 
         def sum_f(j, index):
-            t_turned[j] = pair_sums_turned(f_slots[j], True, index, "t_turned_%d" % j)
+            t_turned[j] = pair_sums_turned(f_slots[j], j > 0, index, "t_turned_%d" % j)
 
         def fetch_t(j):
             t_fetched[j] = placed([P, X], F32, (AT_TS_ROWS, AT_TS - 1, AT_W + 8, AT_Z + 2)[j], "t_fetched_%d" % j)

@@ -183,7 +183,7 @@ def tile_attend_gblkatt_kernel(tc, qT, kT, us, ts, wb, dp, offs, blkoffs, slotof
             )
 
         e_sb = [placed([P, C], F32, AT_E + 4 * j, "e_%d" % j) for j in range(PACK)]
-        f_sb = [placed([P, C], F32, AT_F + 4 * j, "f_%d" % j) for j in range(PACK)]
+        f_sb = [placed([P, C], F32, AT_F + 4 * j if j < LAST else AT_TS + 8, "f_%d" % j) for j in range(PACK)]
         ue_sb = {j: placed([P, C], F32, AT_W + 4 * j, "ue_%d" % j) for j in range(2)}
         def score(j, half, index, kib):
             scores = flat(bank(index, "scores_%d_%d" % (j, half))[:])
@@ -192,19 +192,21 @@ def tile_attend_gblkatt_kernel(tc, qT, kT, us, ts, wb, dp, offs, blkoffs, slotof
             nc.vector.tensor_tensor(z_sb[:], scores, ts_rows[:, cols(half, HALF)], ALU.mult)
             nc.scalar.activation(e_sb[j][:, cols(half, HALF)], z_sb[:], ACT.Exp, scale=us_sb[:, cols(j, 1)])
 
-        def form_f(j):
-            nc.gpsimd.tensor_tensor(f_sb[j][:], e_sb[j][:], dp_sb[j][:], ALU.mult)
+        def form_f(j, part=slice(0, C)):
+            nc.gpsimd.tensor_tensor(f_sb[j][:, part], e_sb[j][:, part], dp_sb[j][:, part], ALU.mult)
 
         quantize_keys(0)
         quantize_keys(1)
         quantize_keys(2)
         score(0, 0, 0, AT_K_PLANES + 4)
+        form_f(0, cols(0, HALF))
         quantize_keys(3)
         score(1, 0, 1, AT_K_PLANES + 6)
+        form_f(1, cols(0, HALF))
         score(0, 1, 2, AT_K_RAW)
-        form_f(0)
+        form_f(0, cols(1, HALF))
         score(1, 1, 3, AT_K_RAW + 4)
-        form_f(1)
+        form_f(1, cols(1, HALF))
         score(2, 0, 4, AT_K_PLANES + 6)
         score(2, 1, 5, AT_K_RAW + 8)
         form_f(2)
@@ -212,121 +214,86 @@ def tile_attend_gblkatt_kernel(tc, qT, kT, us, ts, wb, dp, offs, blkoffs, slotof
         score(3, 1, 7, AT_K_RAW + 23)
         form_f(3)
 
-        e_slots = [placed([P, C], F32, AT_K_RAW + (26, 20, 8)[j], "e_slots_%d" % j) for j in range(LAST)]
-        f_slots = [placed([P, C], F32, AT_K_RAW + (4, 12, 16)[j], "f_slots_%d" % j) for j in range(LAST)]
-        e_slots.append(placed([P, C], F32, AT_K_RAW + 20, "e_slots_3"))
-        f_slots.append(placed([P, C], F32, AT_K_RAW + 20, "f_slots_3"))
+        e_slots, s_turned, root, root_back, inverse = {}, {}, {}, {}, {}
+        f_slots = [placed([P, 2, 2, PART], F32, AT_K_RAW + (4, 12, 16, 8)[j], "f_slots_%d" % j) for j in range(PACK)]
 
-        def by_slots(engine, picked, window, halves, parted):
-            for half in halves:
-                dst = picked[:, cols(half, HALF)]
-                if parted:
-                    dst = dst.rearrange("p (i x) -> p x i", i=2)
-                move(engine, dst, window[:].indirect(part_of(slot_list, half, HALF)))
-
-        def gather_e(engine, j, halves=(0, 1)):
-            by_slots(engine, e_slots[j], e_sb[j], halves, False)
-
-        def gather_f(engine, j, halves=(0, 1)):
-            by_slots(engine, f_slots[j], f_sb[j], halves, j > 0)
-
-        def pair_sums_turned(picked, parted, index, name):
-            pairs = picked[:].rearrange("p (h i x) -> p h x i" if parted else "p (h x i) -> p h x i", h=2, i=2)
-            sums = bank(index, name)
+        def sum_e(engine, j, index):
+            e_slots[j] = placed([P, C], F32, AT_K_RAW + (20 if j else 26), "e_slots_%d" % j)
+            for half in range(2):
+                move(engine, e_slots[j][:, cols(half, HALF)], e_sb[j][:].indirect(part_of(slot_list, half, HALF)))
+            pairs = e_slots[j][:].rearrange("p (x i) -> p x i", i=2)
+            sums = bank(index, "s_turned_%d" % j)
             for b in range(CHUNKS):
                 for i in range(2):
-                    turn(sums[:, b, :], pairs[:, b // 2, cols(b % 2, P), i], start=(i == 0), stop=(i == 1))
-            return flat(sums[:])
+                    turn(sums[:, b, :], pairs[:, cols(b, P), i], start=(i == 0), stop=(i == 1))
+            s_turned[j] = flat(sums[:])
 
-        s_turned, root, root_back, inverse, t_turned, t_fetched, t_back = {}, {}, {}, {}, {}, {}, {}
+        def gather_f(j):
+            for half in range(2):
+                nc.vector.tensor_copy(f_slots[j][:, half, :, :].rearrange("p i x -> p x i"), f_sb[j][:].indirect(part_of(slot_list, half, HALF)))
 
-        def sum_e(j, index):
-            s_turned[j] = pair_sums_turned(e_slots[j], False, index, "s_turned_%d" % j)
-
-        def take_root(j):
+        def take_root(j, index):
             root[j] = placed([P, X], F32, AT_K_RAW + (24, 30, 0, 2)[j], "root_%d" % j)
             nc.scalar.activation(root[j][:], s_turned[j], ACT.Abs_reciprocal_sqrt)
-
-        def return_root(j, index):
             root_back[j] = turn_back(root[j], index, "root_back_%d" % j)
 
         def take_inverse(j):
-            inverse[j] = placed([P, X], F32, (AT_INV, AT_INV + 2, AT_TS_LISTED, AT_TS - 1)[j], "inverse_%d" % j)
+            inverse[j] = placed([P, X], F32, (AT_INV, AT_INV + 2, AT_TS + 9, AT_TS + 7)[j], "inverse_%d" % j)
             nc.scalar.activation(inverse[j][:], root_back[j], ACT.Square)
 
-        def sum_f(j, index):
-            t_turned[j] = pair_sums_turned(f_slots[j], j > 0, index, "t_turned_%d" % j)
-
-        def fetch_t(j):
-            t_fetched[j] = placed([P, X], F32, (AT_TS_ROWS, AT_TS - 1, AT_W + 8, AT_Z + 2)[j], "t_fetched_%d" % j)
-            nc.scalar.copy(t_fetched[j][:], t_turned[j])
-
-        def return_t(j, index):
-            t_back[j] = turn_back(t_fetched[j], index, "t_back_%d" % j)
+        def sum_f(j):
+            nc.vector.tensor_tensor(t_sb[:, j, :].rearrange("p (h x) -> p h x", h=2), f_slots[j][:, :, 0, :], f_slots[j][:, :, 1, :], ALU.add)
 
         def form_m(j):
-            nc.vector.tensor_tensor(m_window[j][:, :X], t_back[j], inverse[j][:], ALU.mult)
+            nc.vector.tensor_tensor(m_window[j][:, :X], t_sb[:, j, :], inverse[j][:], ALU.mult)
 
-        def form_h(j):
-            nc.gpsimd.tensor_tensor(h_window[j][:, :X], inverse[j][:], wb_sb[:, j, :], ALU.mult)
+        def form_h(engine, j):
+            engine.tensor_tensor(h_window[j][:, :X], inverse[j][:], wb_sb[:, j, :], ALU.mult)
 
         def form_ue(j):
             nc.gpsimd.tensor_scalar(ue_sb[j][:], e_sb[j][:], us_sb[:, cols(j, 1)], 0.0, ALU.mult, ALU.add)
 
-        gather_e("vector", 0)
-        gather_e("scalar", 1)
-        sum_e(0, 0)
-        sum_e(1, 1)
-        gather_f("vector", 0)
-        sum_f(0, 6)
-        take_root(0)
-        take_root(1)
-        return_root(0, 2)
-        return_root(1, 3)
-        gather_e("vector", 2)
-        gather_e("scalar", 3)
+        sum_e("vector", 0, 0)
+        sum_e("scalar", 1, 1)
+        gather_f(0)
+        take_root(0, 2)
+        take_root(1, 3)
+        gather_f(1)
         form_ue(0)
         form_ue(1)
-        sum_e(2, 1)
-        sum_e(3, 4)
-        gather_f("vector", 1)
+        sum_e("scalar", 2, 4)
         take_inverse(0)
         take_inverse(1)
-        form_h(0)
-        form_h(1)
-        sum_f(1, 2)
-        take_root(2)
-        take_root(3)
-        return_root(2, 3)
-        return_root(3, 5)
-        fetch_t(0)
-        fetch_t(1)
-        gather_f("vector", 2)
-        sum_f(2, 4)
-        return_t(0, 0)
-        return_t(1, 7)
+        form_h(nc.gpsimd, 0)
+        form_h(nc.gpsimd, 1)
+        gather_f(2)
+        take_root(2, 5)
+        gather_f(3)
+        sum_e("scalar", 3, 6)
         take_inverse(2)
-        form_h(2)
-        gather_f("vector", 3)
-        ue_sb[LAST] = placed([P, C], F32, AT_K_RAW, "ue_3")
+        take_root(3, 7)
+        ue_sb[LAST] = placed([P, C], F32, AT_K_RAW + 20, "ue_3")
         nc.scalar.activation(ue_sb[LAST][:], e_sb[LAST][:], ACT.Copy, scale=us_sb[:, cols(LAST, 1)])
-        fetch_t(2)
         take_inverse(3)
-        sum_f(3, 2)
-        return_t(2, 1)
-        fetch_t(3)
-        return_t(3, 6)
-        for j in range(LAST):
-            form_m(j)
-        ue_sb[2] = placed([P, C], F32, AT_W + 8, "ue_2")
+        t_sb = placed([P, PACK, X], F32, AT_TS + 11, "t_sb")
+        sum_f(0)
+        sum_f(1)
+        form_m(0)
+        form_m(1)
+        sum_f(2)
+        sum_f(3)
+        form_m(2)
+        form_h(nc.vector, 2)
+        form_h(nc.vector, 3)
+        form_m(3)
+        ue_sb[2] = placed([P, C], F32, AT_TS + 15, "ue_2")
         nc.vector.tensor_scalar(ue_sb[2][:], e_sb[2][:], us_sb[:, cols(2, 1)], None, ALU.mult)
-        nc.vector.tensor_tensor(h_window[LAST][:, :X], inverse[LAST][:], wb_sb[:, LAST, :], ALU.mult)
-        form_m(LAST)
 
-        neg_m_first = [placed([P, HALF], F32, AT_K_RAW + (20, 22, 8, 5)[j], "neg_m_first_%d" % j) for j in range(PACK)]
-        neg_m_third = [placed([P, PART], F32, AT_K_RAW + 3.0625 + j if j else AT_TS - 1, "neg_m_third_%d" % j) for j in range(PACK)]
+        neg_m_early = placed([P, LAST, HALF], F32, AT_K_RAW + 2, "neg_m_early")
+        neg_m_first = [neg_m_early[:, j, :] for j in range(LAST)] + [placed([P, HALF], F32, AT_K_RAW + 9, "neg_m_last")[:]]
+        neg_m_third = [placed([P, PART], F32, AT_K_RAW + 7.0625 + j if j else AT_TS + 8, "neg_m_third_%d" % j) for j in range(PACK)]
         g_grouped = [placed([P, PART, PACK], BF16, AT_K_PLANES + 2 * n if n < LAST else AT_UTS + 8, "g_grouped_%d" % n) for n in range(PARTS)]
-        m_less_dp = [placed([P, PART], F32, (AT_TS_LISTED, AT_K_RAW + 20, AT_E + 2, AT_E + 4)[j], "m_less_dp_%d" % j) for j in range(PACK)]
+        m_less_dp = [placed([P, PART], F32, (AT_TS + 9, AT_E + 2, AT_E + 4, AT_E + 5)[j], "m_less_dp_%d" % j) for j in range(PACK)]
         weighted = [placed([P, PACK, HALF], F32, (AT_TS, AT_E + 6)[half], "weighted_%d" % half) for half in range(2)]
         g_codes = [keep.tile([P, PART], U32, name="g_codes_%d" % n, align_bytes=64) for n in range(PARTS)]
         g_scales = [keep.tile([P, PART], U8, name="g_scales_%d" % n, align_bytes=64) for n in range(PARTS)]
@@ -341,25 +308,27 @@ def tile_attend_gblkatt_kernel(tc, qT, kT, us, ts, wb, dp, offs, blkoffs, slotof
         def look_up_m_less_dp(j):
             nc.vector.tensor_tensor(m_less_dp[j][:], m_window[j][:].indirect(part_of(blk_list, LAST, PART)), dp_sb[j][:, cols(LAST, PART)], ALU.subtract)
 
-        def turn_centred(chunks, j):
+        def turn_dp(chunk):
+            centred_turned[chunk] = bank(chunk if chunk < CHUNKS else chunk + 2, "centred_turned_%d" % chunk)
+            for j in range(PACK):
+                turn(centred_turned[chunk][:, j, :], dp_sb[j][:, cols(chunk, P)], start=(j == 0), stop=False)
+
+        def turn_neg_m(chunks, j):
             for chunk in chunks:
-                if j == 0:
-                    centred_turned[chunk] = bank((2, 4, 3, 5, 2, 4, 2, 4)[chunk], "centred_turned_%d" % chunk)
-                if chunk < 6:
-                    turn(centred_turned[chunk][:, j, :], dp_sb[j][:, cols(chunk, P)], start=True, stop=False)
-            for chunk in chunks:
-                if chunk >= 6:
-                    term = m_less_dp[j][:, cols(chunk - 6, P)]
-                else:
-                    term = neg_m_first[j][:, cols(chunk, P)] if chunk < CHUNKS else neg_m_third[j][:, cols(chunk - CHUNKS, P)]
-                turn(centred_turned[chunk][:, j, :], term, start=(chunk >= 6), stop=True)
+                neg_m = neg_m_first[j][:, cols(chunk, P)] if chunk < CHUNKS else neg_m_third[j][:, cols(chunk - CHUNKS, P)]
+                turn(centred_turned[chunk][:, j, :], neg_m, start=False, stop=(j == LAST))
+
+        def turn_m_less_dp(chunk):
+            centred_turned[chunk] = bank(chunk, "centred_turned_%d" % chunk)
+            for j in range(PACK):
+                turn(centred_turned[chunk][:, j, :], m_less_dp[j][:, cols(chunk - 6, P)])
 
         def scale_centred(chunk):
             centred[chunk] = placed([P, HALF], F32, AT_E + 2 * chunk if chunk < CHUNKS else AT_UTS + 2 * chunk - 2 * CHUNKS, "centred_%d" % chunk)
             nc.scalar.activation(centred[chunk][:], flat(centred_turned[chunk][:]), ACT.Copy, scale=neg_ts_col[:, cols(chunk - CHUNKS, 1)] if chunk >= 6 else ts_col[:, cols(chunk, 1)])
 
         def return_centred(chunk):
-            centred_back[chunk] = turn_back(centred[chunk], (0, 7, 1, 6, 3, 5, 2, 4)[chunk], "centred_back_%d" % chunk).rearrange("p (j c) -> p j c", j=PACK)
+            centred_back[chunk] = turn_back(centred[chunk], (4, 5, 4, 5, 2, 3, 6, 7)[chunk], "centred_back_%d" % chunk).rearrange("p (j c) -> p j c", j=PACK)
 
         def gradient(chunk):
             half, b = divmod(chunk, CHUNKS)
@@ -373,7 +342,7 @@ def tile_attend_gblkatt_kernel(tc, qT, kT, us, ts, wb, dp, offs, blkoffs, slotof
         dk_late = placed([P, 2, C], F32, AT_F, "dk_late")
 
         def multiply(n, pair):
-            product = flat(bank(((0, 7, 1, 6), (0, 3, 5, 2))[pair][n], "dk_psum_%d_%d" % (n, pair))[:])
+            product = flat(bank(((0, 1, 4, 5), (0, 1, 3, 6))[pair][n], "dk_psum_%d_%d" % (n, pair))[:])
             for i in range(2):
                 t = 2 * pair + i
                 product_mx(product[:, cols(i, PART)], q2_codes[:, cols(t, P)], q2_scales[:, cols(t, P)], g_codes[n][:], g_scales[n][:], E5M2)
@@ -389,19 +358,21 @@ def tile_attend_gblkatt_kernel(tc, qT, kT, us, ts, wb, dp, offs, blkoffs, slotof
             values = dk_late[:, t % 2, first:last] if t // 2 else dk_early[first // PART][:, t, :]
             move(engine, out_window[t][:].indirect(tok_list[:, first // 16 : last // 16]), values)
 
-        def store(t):
-            nc.sync.dma_start(out=out_rows[t], in_=out_window[t][:])
+        def store(t, queue=nc.sync):
+            queue.dma_start(out=out_rows[t], in_=out_window[t][:])
 
         def place_part(engine, t, n):
             place(engine, t, n * PART, (n + 1) * PART)
 
         def first_half(j):
-            look_up_neg_m(neg_m_first[j][:], j, part_of(blk_list, 0, HALF))
-            turn_centred(range(CHUNKS), j)
+            look_up_neg_m(neg_m_first[j], j, part_of(blk_list, 0, HALF))
+            turn_neg_m(range(CHUNKS), j)
 
         def third_part(j):
             look_up_neg_m(neg_m_third[j][:], j, part_of(blk_list, 2, PART))
 
+        for chunk in range(CHUNKS + 2):
+            turn_dp(chunk)
         for j in range(PACK):
             first_half(j)
         look_up_m_less_dp(0)
@@ -410,26 +381,29 @@ def tile_attend_gblkatt_kernel(tc, qT, kT, us, ts, wb, dp, offs, blkoffs, slotof
         third_part(0)
         for chunk in range(CHUNKS):
             scale_centred(chunk)
-            return_centred(chunk)
-        turn_centred((4, 5), 0)
+        return_centred(0)
+        return_centred(1)
+        turn_neg_m((4, 5), 0)
         for j in range(1, PACK):
             third_part(j)
-            turn_centred((4, 5), j)
-        look_up_m_less_dp(1)
+            turn_neg_m((4, 5), j)
         gradient(0)
+        return_centred(2)
         gradient(1)
-        gradient(2)
+        return_centred(3)
         quantize_gradient(0)
+        look_up_m_less_dp(1)
+        gradient(2)
+        multiply(0, 0)
         look_up_m_less_dp(2)
         gradient(3)
-        multiply(0, 0)
         look_up_m_less_dp(3)
         quantize_gradient(1)
         fetch_dk("scalar", 0, 0)
         for chunk in (4, 5):
             scale_centred(chunk)
-        for j in range(PACK):
-            turn_centred((6, 7), j)
+        turn_m_less_dp(6)
+        turn_m_less_dp(7)
         place_part("scalar", 0, 0)
         for chunk in (6, 7):
             scale_centred(chunk)
@@ -442,9 +416,13 @@ def tile_attend_gblkatt_kernel(tc, qT, kT, us, ts, wb, dp, offs, blkoffs, slotof
         place_part("scalar", 1, 0)
         place_part("scalar", 0, 1)
         place_part("scalar", 1, 1)
+        multiply(0, 1)
+        multiply(1, 1)
+        fetch_dk("scalar", 0, 1)
+        fetch_dk("scalar", 1, 1)
+        place_part("scalar", 2, 0)
         gradient(4)
         gradient(5)
-        multiply(1, 1)
         gradient(6)
         quantize_gradient(2)
         gradient(7)
@@ -454,21 +432,17 @@ def tile_attend_gblkatt_kernel(tc, qT, kT, us, ts, wb, dp, offs, blkoffs, slotof
         quantize_gradient(3)
         multiply(3, 0)
         multiply(3, 1)
-        fetch_dk("scalar", 1, 1)
-        multiply(0, 1)
+        place_part("scalar", 1, 2)
         fetch_dk("scalar", 2, 1)
         fetch_dk("scalar", 3, 1)
-        fetch_dk("scalar", 0, 1)
         place_part("vector", 0, 2)
         fetch_dk("vector", 3, 0)
         place_part("vector", 0, 3)
         store(0)
         place_part("scalar", 1, 3)
+        store(1, nc.scalar)
         place_part("scalar", 3, 3)
-        place_part("scalar", 1, 2)
-        store(1)
-        place_part("vector", 2, 3)
-        place("vector", 2, 0, 768)
+        place("vector", 2, PART, C)
         store(2)
         place("scalar", 3, 0, 384)
         place("scalar", 3, 384, 768)

@@ -214,11 +214,11 @@ def tile_attend_gblkatt_kernel(tc, qT, kT, us, ts, wb, dp, offs, blkoffs, slotof
         score(3, 1, 7, AT_K_RAW + 23)
         form_f(3)
 
-        e_slots, s_turned, root, root_back, inverse = {}, {}, {}, {}, {}
-        f_slots = [placed([P, 2, 2, PART], F32, AT_K_RAW + (4, 12, 16, 8)[j], "f_slots_%d" % j) for j in range(PACK)]
+        e_slots, s_turned, root, root_back, inverse, t_sums = {}, {}, {}, {}, {}, {}
+        f_slots = [placed([P, 2, 2, PART], F32, AT_K_RAW + (4, 12, 16, 0)[j], "f_slots_%d" % j) for j in range(PACK)]
 
         def sum_e(engine, j, index):
-            e_slots[j] = placed([P, C], F32, AT_K_RAW + (20 if j else 26), "e_slots_%d" % j)
+            e_slots[j] = placed([P, C], F32, AT_K_RAW + (26, 20, 8, 20)[j], "e_slots_%d" % j)
             for half in range(2):
                 move(engine, e_slots[j][:, cols(half, HALF)], e_sb[j][:].indirect(part_of(slot_list, half, HALF)))
             pairs = e_slots[j][:].rearrange("p (x i) -> p x i", i=2)
@@ -232,20 +232,33 @@ def tile_attend_gblkatt_kernel(tc, qT, kT, us, ts, wb, dp, offs, blkoffs, slotof
             for half in range(2):
                 nc.vector.tensor_copy(f_slots[j][:, half, :, :].rearrange("p i x -> p x i"), f_sb[j][:].indirect(part_of(slot_list, half, HALF)))
 
+        def sum_f_turned(j, index):
+            sums = bank(index, "t_turned_%d" % j)
+            for b in range(CHUNKS):
+                for i in range(2):
+                    turn(sums[:, b, :], f_slots[j][:, b // 2, i, cols(b % 2, P)], start=(i == 0), stop=(i == 1))
+            t_sums[j] = flat(sums[:])
+
+        def fetch_t(j):
+            fetched = placed([P, X], F32, AT_TS + (13, 5.5)[j], "t_fetched_%d" % j)
+            nc.scalar.copy(fetched[:], t_sums[j])
+            t_sums[j] = turn_back(fetched, j, "t_back_%d" % j)
+
         def take_root(j, index):
-            root[j] = placed([P, X], F32, AT_K_RAW + (24, 30, 0, 2)[j], "root_%d" % j)
+            root[j] = placed([P, X], F32, AT_K_RAW + (24, 30, 10, 23)[j], "root_%d" % j)
             nc.scalar.activation(root[j][:], s_turned[j], ACT.Abs_reciprocal_sqrt)
             root_back[j] = turn_back(root[j], index, "root_back_%d" % j)
 
         def take_inverse(j):
-            inverse[j] = placed([P, X], F32, (AT_INV, AT_INV + 2, AT_TS + 9, AT_TS + 7)[j], "inverse_%d" % j)
+            inverse[j] = placed([P, X], F32, (AT_INV + 2, AT_INV, AT_INV + 6, AT_TS + 7)[j], "inverse_%d" % j)
             nc.scalar.activation(inverse[j][:], root_back[j], ACT.Square)
 
         def sum_f(j):
-            nc.vector.tensor_tensor(t_sb[:, j, :].rearrange("p (h x) -> p h x", h=2), f_slots[j][:, :, 0, :], f_slots[j][:, :, 1, :], ALU.add)
+            t_sums[j] = t_sb[:, j - 2, :]
+            nc.vector.tensor_tensor(t_sums[j].rearrange("p (h x) -> p h x", h=2), f_slots[j][:, :, 0, :], f_slots[j][:, :, 1, :], ALU.add)
 
         def form_m(j):
-            nc.vector.tensor_tensor(m_window[j][:, :X], t_sb[:, j, :], inverse[j][:], ALU.mult)
+            nc.vector.tensor_tensor(m_window[j][:, :X], t_sums[j], inverse[j][:], ALU.mult)
 
         def form_h(engine, j):
             engine.tensor_tensor(h_window[j][:, :X], inverse[j][:], wb_sb[:, j, :], ALU.mult)
@@ -256,44 +269,46 @@ def tile_attend_gblkatt_kernel(tc, qT, kT, us, ts, wb, dp, offs, blkoffs, slotof
         sum_e("vector", 0, 0)
         sum_e("scalar", 1, 1)
         gather_f(0)
+        sum_f_turned(0, 6)
         take_root(0, 2)
         take_root(1, 3)
-        gather_f(1)
+        sum_e("vector", 2, 4)
         form_ue(0)
         form_ue(1)
-        sum_e("scalar", 2, 4)
+        sum_e("scalar", 3, 7)
+        gather_f(1)
         take_inverse(0)
         take_inverse(1)
         form_h(nc.gpsimd, 0)
         form_h(nc.gpsimd, 1)
-        gather_f(2)
+        sum_f_turned(1, 2)
         take_root(2, 5)
-        gather_f(3)
-        sum_e("scalar", 3, 6)
+        take_root(3, 4)
+        fetch_t(0)
+        fetch_t(1)
+        gather_f(2)
         take_inverse(2)
-        take_root(3, 7)
+        form_h(nc.gpsimd, 2)
+        gather_f(3)
         ue_sb[LAST] = placed([P, C], F32, AT_K_RAW + 20, "ue_3")
         nc.scalar.activation(ue_sb[LAST][:], e_sb[LAST][:], ACT.Copy, scale=us_sb[:, cols(LAST, 1)])
         take_inverse(3)
-        t_sb = placed([P, PACK, X], F32, AT_TS + 11, "t_sb")
-        sum_f(0)
-        sum_f(1)
+        t_sb = placed([P, 2, X], F32, AT_TS + 11, "t_sb")
         form_m(0)
         form_m(1)
         sum_f(2)
         sum_f(3)
         form_m(2)
-        form_h(nc.vector, 2)
         form_h(nc.vector, 3)
         form_m(3)
-        ue_sb[2] = placed([P, C], F32, AT_TS + 15, "ue_2")
+        ue_sb[2] = placed([P, C], F32, AT_K_RAW + 16, "ue_2")
         nc.vector.tensor_scalar(ue_sb[2][:], e_sb[2][:], us_sb[:, cols(2, 1)], None, ALU.mult)
 
-        neg_m_early = placed([P, LAST, HALF], F32, AT_K_RAW + 2, "neg_m_early")
-        neg_m_first = [neg_m_early[:, j, :] for j in range(LAST)] + [placed([P, HALF], F32, AT_K_RAW + 9, "neg_m_last")[:]]
-        neg_m_third = [placed([P, PART], F32, AT_K_RAW + 7.0625 + j if j else AT_TS + 8, "neg_m_third_%d" % j) for j in range(PACK)]
+        neg_m_early = placed([P, LAST, HALF], F32, AT_K_RAW + 24, "neg_m_early")
+        neg_m_first = [neg_m_early[:, j, :] for j in range(LAST)] + [placed([P, HALF], F32, AT_K_RAW + 1, "neg_m_last")[:]]
+        neg_m_third = [placed([P, PART], F32, AT_K_RAW + j - 0.9375 if j else AT_TS + 8, "neg_m_third_%d" % j) for j in range(PACK)]
         g_grouped = [placed([P, PART, PACK], BF16, AT_K_PLANES + 2 * n if n < LAST else AT_UTS + 8, "g_grouped_%d" % n) for n in range(PARTS)]
-        m_less_dp = [placed([P, PART], F32, (AT_TS + 9, AT_E + 2, AT_E + 4, AT_E + 5)[j], "m_less_dp_%d" % j) for j in range(PACK)]
+        m_less_dp = [placed([P, PART], F32, (AT_INV + 6, AT_E + 2, AT_E + 4, AT_E + 5)[j], "m_less_dp_%d" % j) for j in range(PACK)]
         weighted = [placed([P, PACK, HALF], F32, (AT_TS, AT_E + 6)[half], "weighted_%d" % half) for half in range(2)]
         g_codes = [keep.tile([P, PART], U32, name="g_codes_%d" % n, align_bytes=64) for n in range(PARTS)]
         g_scales = [keep.tile([P, PART], U8, name="g_scales_%d" % n, align_bytes=64) for n in range(PARTS)]
@@ -309,7 +324,7 @@ def tile_attend_gblkatt_kernel(tc, qT, kT, us, ts, wb, dp, offs, blkoffs, slotof
             nc.vector.tensor_tensor(m_less_dp[j][:], m_window[j][:].indirect(part_of(blk_list, LAST, PART)), dp_sb[j][:, cols(LAST, PART)], ALU.subtract)
 
         def turn_dp(chunk):
-            centred_turned[chunk] = bank(chunk if chunk < CHUNKS else chunk + 2, "centred_turned_%d" % chunk)
+            centred_turned[chunk] = bank((3, 7, 6, 2, 5, 4)[chunk], "centred_turned_%d" % chunk)
             for j in range(PACK):
                 turn(centred_turned[chunk][:, j, :], dp_sb[j][:, cols(chunk, P)], start=(j == 0), stop=False)
 
@@ -319,7 +334,7 @@ def tile_attend_gblkatt_kernel(tc, qT, kT, us, ts, wb, dp, offs, blkoffs, slotof
                 turn(centred_turned[chunk][:, j, :], neg_m, start=False, stop=(j == LAST))
 
         def turn_m_less_dp(chunk):
-            centred_turned[chunk] = bank(chunk, "centred_turned_%d" % chunk)
+            centred_turned[chunk] = bank(11 - chunk, "centred_turned_%d" % chunk)
             for j in range(PACK):
                 turn(centred_turned[chunk][:, j, :], m_less_dp[j][:, cols(chunk - 6, P)])
 
@@ -328,7 +343,7 @@ def tile_attend_gblkatt_kernel(tc, qT, kT, us, ts, wb, dp, offs, blkoffs, slotof
             nc.scalar.activation(centred[chunk][:], flat(centred_turned[chunk][:]), ACT.Copy, scale=neg_ts_col[:, cols(chunk - CHUNKS, 1)] if chunk >= 6 else ts_col[:, cols(chunk, 1)])
 
         def return_centred(chunk):
-            centred_back[chunk] = turn_back(centred[chunk], (4, 5, 4, 5, 2, 3, 6, 7)[chunk], "centred_back_%d" % chunk).rearrange("p (j c) -> p j c", j=PACK)
+            centred_back[chunk] = turn_back(centred[chunk], (0, 1, 3, 7, 6, 2, 5, 4)[chunk], "centred_back_%d" % chunk).rearrange("p (j c) -> p j c", j=PACK)
 
         def gradient(chunk):
             half, b = divmod(chunk, CHUNKS)
@@ -342,7 +357,7 @@ def tile_attend_gblkatt_kernel(tc, qT, kT, us, ts, wb, dp, offs, blkoffs, slotof
         dk_late = placed([P, 2, C], F32, AT_F, "dk_late")
 
         def multiply(n, pair):
-            product = flat(bank(((0, 1, 4, 5), (0, 1, 3, 6))[pair][n], "dk_psum_%d_%d" % (n, pair))[:])
+            product = flat(bank(((0, 1, 3, 7), (0, 1, 2, 5))[pair][n], "dk_psum_%d_%d" % (n, pair))[:])
             for i in range(2):
                 t = 2 * pair + i
                 product_mx(product[:, cols(i, PART)], q2_codes[:, cols(t, P)], q2_scales[:, cols(t, P)], g_codes[n][:], g_scales[n][:], E5M2)
@@ -381,16 +396,13 @@ def tile_attend_gblkatt_kernel(tc, qT, kT, us, ts, wb, dp, offs, blkoffs, slotof
         third_part(0)
         for chunk in range(CHUNKS):
             scale_centred(chunk)
-        return_centred(0)
-        return_centred(1)
+            return_centred(chunk)
         turn_neg_m((4, 5), 0)
         for j in range(1, PACK):
             third_part(j)
             turn_neg_m((4, 5), j)
         gradient(0)
-        return_centred(2)
         gradient(1)
-        return_centred(3)
         quantize_gradient(0)
         look_up_m_less_dp(1)
         gradient(2)
@@ -405,6 +417,7 @@ def tile_attend_gblkatt_kernel(tc, qT, kT, us, ts, wb, dp, offs, blkoffs, slotof
         turn_m_less_dp(6)
         turn_m_less_dp(7)
         place_part("scalar", 0, 0)
+        place_part("scalar", 1, 0)
         for chunk in (6, 7):
             scale_centred(chunk)
         multiply(1, 0)
@@ -413,14 +426,12 @@ def tile_attend_gblkatt_kernel(tc, qT, kT, us, ts, wb, dp, offs, blkoffs, slotof
         for j in range(PACK):
             look_up_h(j, 1)
         fetch_dk("scalar", 1, 0)
-        place_part("scalar", 1, 0)
         place_part("scalar", 0, 1)
         place_part("scalar", 1, 1)
         multiply(0, 1)
         multiply(1, 1)
         fetch_dk("scalar", 0, 1)
         fetch_dk("scalar", 1, 1)
-        place_part("scalar", 2, 0)
         gradient(4)
         gradient(5)
         gradient(6)
@@ -432,8 +443,8 @@ def tile_attend_gblkatt_kernel(tc, qT, kT, us, ts, wb, dp, offs, blkoffs, slotof
         quantize_gradient(3)
         multiply(3, 0)
         multiply(3, 1)
-        place_part("scalar", 1, 2)
         fetch_dk("scalar", 2, 1)
+        place_part("scalar", 1, 2)
         fetch_dk("scalar", 3, 1)
         place_part("vector", 0, 2)
         fetch_dk("vector", 3, 0)
@@ -442,7 +453,7 @@ def tile_attend_gblkatt_kernel(tc, qT, kT, us, ts, wb, dp, offs, blkoffs, slotof
         place_part("scalar", 1, 3)
         store(1, nc.scalar)
         place_part("scalar", 3, 3)
-        place("vector", 2, PART, C)
+        place("vector", 2, 0, C)
         store(2)
         place("scalar", 3, 0, 384)
         place("scalar", 3, 384, 768)

from contextlib import ExitStack

import concourse.mybir as mybir
from concourse.masks import make_identity

D, R, C, T, X = 512, 512, 1024, 2048, 512
FLOPS = 2 * 2 * D * R * C

F32 = mybir.dt.float32
BF16 = mybir.dt.bfloat16
U32 = mybir.dt.uint32
I32 = mybir.dt.int32
U16 = mybir.dt.uint16
U8 = mybir.dt.uint8
E4M3 = mybir.dt.float8_e4m3fn_x4
E5M2 = mybir.dt.float8_e5m2_x4
ACT = mybir.ActivationFunctionType
ALU = mybir.AluOpType

P = 128
PACK = 4
LAST = PACK - 1
HALF = 512
PART = 256
PARTS = C // PART
CHUNKS = HALF // P
Q_PIECE = R // 2
TS_ROW = P - 1
BANK_BYTES = 2048
BLK_WINDOW = X + 8
BLK_WINDOW_KIB = 2.125

AT_K_RAW, AT_OUT, AT_E, AT_F, AT_W, AT_DP, AT_UTS, AT_WB, AT_INV = 0, 32, 64, 80, 96, 112, 128, 144, 152
AT_K_PLANES, AT_TS, AT_TS_LISTED, AT_TS_ROWS, AT_Q_RAW, AT_Q_GROUPED, AT_K_CODES, AT_Z, AT_LATE = 160, 168, 176, 180, 184, 192, 196, 200, 204
AT_H, AT_M = 208, 216.5


def tile_attend_gblkatt_kernel(tc, qT, kT, us, ts, wb, dp, offs, blkoffs, slotoffs, out):
    nc = tc.nc
    with ExitStack() as ctx:
        keep = ctx.enter_context(tc.tile_pool(name="keep", bufs=1))
        arena = ctx.enter_context(tc.tile_pool(name="arena", bufs=1))
        psum = ctx.enter_context(tc.psum_pool(name="psum", bufs=1))

        def placed(shape, dtype, kib, name):
            return arena.tile(shape, dtype, name=name, align_bytes=64, offset=int(kib * 1024))

        def bank(index, name):
            return psum.tile([P, CHUNKS, P], F32, name=name, offset=index * BANK_BYTES)

        def flat(view):
            return view.rearrange("p a b -> p (a b)")

        def cols(index, width):
            return slice(index * width, (index + 1) * width)

        def part_of(offsets, index, width):
            return offsets[:, cols(index, width // 16)]

        def turn(dst, src, start=True, stop=True):
            nc.tensor.matmul(dst, lhsT=src, rhs=ident[:], is_transpose=True, start=start, stop=stop)

        def turn_back(src, index, name):
            back = bank(index, name)
            for b in range(CHUNKS):
                turn(back[:, b, :], src[:, cols(b, P)])
            return flat(back[:])

        def product_mx(dst, stationary, stationary_scales, moving, moving_scales, moving_format=E4M3):
            nc.tensor.matmul_mx(
                out=dst,
                lhsT=stationary.bitcast(E4M3),
                lhsT_scale=stationary_scales,
                rhs=moving.bitcast(moving_format),
                rhs_scale=moving_scales,
                start=True,
                stop=True,
            )

        def move(engine, dst, src):
            if engine == "vector":
                nc.vector.tensor_copy(dst, src)
            else:
                nc.scalar.activation(dst, src, ACT.Copy)

        def by_fours(woven, planes):
            return woven.rearrange("p (c i) t -> p c t i", i=4), planes.rearrange("p t (c i) -> p c t i", i=4)

        tok_list = keep.tile([P, C // 16], U16, name="tok_list")
        blk_list = keep.tile([P, C // 16], U16, name="blk_list")
        slot_list = keep.tile([P, C // 16], U16, name="slot_list")
        ident = keep.tile([P, P], F32, name="ident")
        us_sb = keep.tile([P, 8], F32, name="us_sb")

        ts_window = placed([P, T], F32, AT_UTS, "ts_window")
        nc.scalar.dma_start(out=ts_window[TS_ROW:P, :], in_=ts[0:1, :])
        nc.vector.memset(ts_window[0:TS_ROW, :].bitcast(I32), 0)
        nc.sync.dma_start(tok_list[:], offs)
        make_identity(nc, ident[:])
        q_raw = placed([P, PACK, R], F32, AT_Q_RAW, "q_raw")
        nc.sync.dma_start(out=q_raw[:], in_=qT.rearrange("(p t) r -> p t r", t=PACK))
        nc.sync.dma_start(out=us_sb[:, :PACK], in_=us.rearrange("(p j) o -> p (j o)", j=PACK))
        k_rows = kT.rearrange("(p t) n -> t p n", t=PACK)
        k_raw = [placed([P, T], F32, AT_K_RAW + 8 * t, "k_raw_%d" % t) for t in range(PACK)]
        for t in range(PACK):
            nc.sync.dma_start(out=k_raw[t][:], in_=k_rows[t])
        dp_rows = dp.rearrange("(p j) c -> j p c", j=PACK)
        dp_sb = [placed([P, C], F32, AT_DP + 4 * j, "dp_%d" % j) for j in range(PACK)]
        nc.sync.dma_start(out=dp_sb[0][:], in_=dp_rows[0])
        nc.sync.dma_start(slot_list[:], slotoffs)
        for j in range(1, PACK):
            nc.sync.dma_start(out=dp_sb[j][:], in_=dp_rows[j])
        wb_sb = placed([P, PACK, X], F32, AT_WB, "wb_sb")
        nc.sync.dma_start(out=wb_sb[:], in_=wb.rearrange("(p j) x -> p j x", j=PACK))
        nc.sync.dma_start(blk_list[:], blkoffs)

        out_window = [placed([P, T], F32, AT_OUT + 8 * t, "out_window_%d" % t) for t in range(PACK)]
        nc.vector.memset(out_window[0][:].bitcast(I32), 0)
        ts_listed = placed([P, C], F32, AT_TS, "ts_listed")
        move("scalar", ts_listed[:], ts_window[:].indirect(tok_list[:]))
        h_window = [placed([P, BLK_WINDOW], F32, AT_H + BLK_WINDOW_KIB * j, "h_window_%d" % j) for j in range(PACK)]
        m_window = [placed([P, BLK_WINDOW], F32, AT_M + BLK_WINDOW_KIB * j, "m_window_%d" % j) for j in range(PACK)]
        nc.gpsimd.memset(out_window[1][:], 0.0)

        q_grouped = placed([P, PACK, P, PACK], BF16, AT_OUT + 16, "q_grouped")
        q_codes = keep.tile([P, R], U32, name="q_codes", align_bytes=64)
        q_scales = keep.tile([P, R], U8, name="q_scales", align_bytes=64)
        nc.vector.tensor_copy(q_grouped[:].rearrange("p j m t -> p m j t"), q_raw[:].rearrange("p t (m j) -> p m j t", j=PACK))

        ts_col = keep.tile([P, C // P], F32, name="ts_col")
        neg_ts_col = keep.tile([P, CHUNKS], F32, name="neg_ts_col")
        for half in range(2):
            turned = bank(half, "ts_turned_%d" % half)
            for b in range(CHUNKS):
                turn(turned[:, b, :], ts_listed[:, cols(half * CHUNKS + b, P)])
            nc.vector.tensor_copy(ts_col[:, cols(half, CHUNKS)], turned[:, :, TS_ROW])
        nc.vector.tensor_scalar(neg_ts_col[:], turned[:, :, TS_ROW], -1.0, None, ALU.mult)
        nc.vector.quantize_mx(out=q_codes[:].bitcast(E4M3), scales=q_scales[:], in_=q_grouped[:].rearrange("p j m t -> p (j m t)"))

        ts_rows = placed([P, C], F32, AT_LATE, "ts_rows")
        for half in range(2):
            spread = bank(2 + half, "ts_spread_%d" % half)
            for b in range(CHUNKS):
                turn(spread[:, b, :], ts_col[:, cols(half * CHUNKS + b, 1)].to_broadcast([P, P]))
            nc.scalar.copy(ts_rows[:, cols(half, HALF)], flat(spread[:]))

        q_words = q_grouped[:].rearrange("p j m t -> p (j m t)").bitcast(F32).rearrange("p (j m u) -> p j m u", j=PACK, u=2)
        q2_codes = keep.tile([P, D], U32, name="q2_codes", align_bytes=64)
        q2_scales = keep.tile([P, D], U8, name="q2_scales", align_bytes=64)
        q2_grouped = placed([P, PACK, P, PACK], BF16, AT_OUT + 24, "q2_grouped")
        for u in range(2):
            turned = bank(4 + u, "q_turned_%d" % u)
            for j in range(PACK):
                turn(turned[:, j, :], q_words[:, j, :, u])
            nc.scalar.copy(q2_grouped[:, cols(u, 2), :, :], flat(turned[:]).bitcast(BF16).rearrange("m (j p e) -> m e p j", j=PACK, e=2))

        k_grouped = [placed([P, PART, PACK], BF16, AT_TS + 2 * n, "k_grouped_%d" % n) for n in range(PARTS)]
        k_planes = {n: placed([P, PACK, PART], BF16, AT_K_PLANES + 2 * n, "k_planes_%d" % n) for n in (2, 3)}
        k_codes = [placed([P, HALF], U32, AT_K_CODES + 2 * half, "k_codes_%d" % half) for half in range(2)]
        k_scales = [keep.tile([P, HALF], U8, name="k_scales_%d" % half, align_bytes=64) for half in range(2)]

        def gather_keys(t):
            for n in (0, 1):
                nc.vector.tensor_copy(k_grouped[n][:, :, t], k_raw[t][:].indirect(part_of(tok_list, n, PART)))
            for n in (2, 3):
                move("scalar" if t else "vector", k_planes[n][:, t, :], k_raw[t][:].indirect(part_of(tok_list, n, PART)))

        gather_keys(0)
        nc.gpsimd.memset(out_window[2][:], 0.0)
        gather_keys(1)
        nc.vector.quantize_mx(out=q2_codes[:].bitcast(E4M3), scales=q2_scales[:], in_=q2_grouped[:].rearrange("m t p j -> m (t p j)"))
        nc.gpsimd.memset(out_window[LAST][:], 0.0)
        for window in h_window + m_window:
            nc.gpsimd.memset(window[:, X:], 0.0)
        gather_keys(2)
        gather_keys(3)
        for n in (2, 3):
            nc.scalar.copy(*by_fours(k_grouped[n][:], k_planes[n][:]))

        def quantize_keys(n):
            nc.vector.quantize_mx(
                out=k_codes[n // 2][:, cols(n % 2, PART)].bitcast(E4M3), scales=k_scales[n // 2][:, cols(n % 2, PART)], in_=flat(k_grouped[n][:])
            )

        e_sb = [placed([P, C], F32, AT_E + 4 * j, "e_%d" % j) for j in range(PACK)]
        f_sb = [placed([P, C], F32, AT_F + 4 * j if j < LAST else AT_TS + 8, "f_%d" % j) for j in range(PACK)]
        ue_sb = {j: placed([P, C], F32, AT_W + 4 * j, "ue_%d" % j) for j in range(2)}
        def score(j, half, index, kib):
            scores = flat(bank(index, "scores_%d_%d" % (j, half))[:])
            product_mx(scores, q_codes[:, cols(j, P)], q_scales[:, cols(j, P)], k_codes[half][:], k_scales[half][:])
            z_sb = placed([P, HALF], F32, kib, "z_sb_%d_%d" % (j, half))
            nc.vector.tensor_tensor(z_sb[:], scores, ts_rows[:, cols(half, HALF)], ALU.mult)
            nc.scalar.activation(e_sb[j][:, cols(half, HALF)], z_sb[:], ACT.Exp, scale=us_sb[:, cols(j, 1)])

        def form_f(j, part=slice(0, C)):
            nc.gpsimd.tensor_tensor(f_sb[j][:, part], e_sb[j][:, part], dp_sb[j][:, part], ALU.mult)

        quantize_keys(0)
        quantize_keys(1)
        quantize_keys(2)
        score(0, 0, 0, AT_K_PLANES + 4)
        form_f(0, cols(0, HALF))
        quantize_keys(3)
        score(1, 0, 1, AT_K_PLANES + 6)
        form_f(1, cols(0, HALF))
        score(0, 1, 2, AT_K_RAW)
        form_f(0, cols(1, HALF))
        score(1, 1, 3, AT_K_RAW + 4)
        form_f(1, cols(1, HALF))
        score(2, 0, 4, AT_K_PLANES + 6)
        score(2, 1, 5, AT_K_RAW + 8)
        form_f(2)
        score(3, 0, 6, AT_K_RAW)
        score(3, 1, 7, AT_K_RAW + 23)
        form_f(3)

        e_slots, s_turned, root, root_back, inverse, t_sums = {}, {}, {}, {}, {}, {}
        f_slots = [placed([P, 2, 2, PART], F32, AT_K_RAW + (4, 12, 16, 0)[j], "f_slots_%d" % j) for j in range(PACK)]

        def sum_e(engine, j, index):
            e_slots[j] = placed([P, C], F32, AT_K_RAW + (26, 20, 8, 20)[j], "e_slots_%d" % j)
            for half in range(2):
                move(engine, e_slots[j][:, cols(half, HALF)], e_sb[j][:].indirect(part_of(slot_list, half, HALF)))
            pairs = e_slots[j][:].rearrange("p (x i) -> p x i", i=2)
            sums = bank(index, "s_turned_%d" % j)
            for b in range(CHUNKS):
                for i in range(2):
                    turn(sums[:, b, :], pairs[:, cols(b, P), i], start=(i == 0), stop=(i == 1))
            s_turned[j] = flat(sums[:])

        def gather_f(j):
            for half in range(2):
                nc.vector.tensor_copy(f_slots[j][:, half, :, :].rearrange("p i x -> p x i"), f_sb[j][:].indirect(part_of(slot_list, half, HALF)))

        def sum_f_turned(j, index):
            sums = bank(index, "t_turned_%d" % j)
            for b in range(CHUNKS):
                for i in range(2):
                    turn(sums[:, b, :], f_slots[j][:, b // 2, i, cols(b % 2, P)], start=(i == 0), stop=(i == 1))
            t_sums[j] = flat(sums[:])

        def fetch_t(j):
            fetched = placed([P, X], F32, AT_TS + (13, 5.5)[j], "t_fetched_%d" % j)
            nc.scalar.copy(fetched[:], t_sums[j])
            t_sums[j] = turn_back(fetched, j, "t_back_%d" % j)

        def take_root(j, index):
            root[j] = placed([P, X], F32, AT_K_RAW + (24, 30, 10, 23)[j], "root_%d" % j)
            nc.scalar.activation(root[j][:], s_turned[j], ACT.Abs_reciprocal_sqrt)
            root_back[j] = turn_back(root[j], index, "root_back_%d" % j)

        def take_inverse(j):
            inverse[j] = placed([P, X], F32, (AT_INV + 2, AT_INV, AT_INV + 6, AT_TS + 7)[j], "inverse_%d" % j)
            nc.scalar.activation(inverse[j][:], root_back[j], ACT.Square)

        def sum_f(j):
            t_sums[j] = t_sb[:, j - 2, :]
            nc.vector.tensor_tensor(t_sums[j].rearrange("p (h x) -> p h x", h=2), f_slots[j][:, :, 0, :], f_slots[j][:, :, 1, :], ALU.add)

        def form_m(j):
            nc.vector.tensor_tensor(m_window[j][:, :X], t_sums[j], inverse[j][:], ALU.mult)

        def form_h(engine, j):
            engine.tensor_tensor(h_window[j][:, :X], inverse[j][:], wb_sb[:, j, :], ALU.mult)

        def form_ue(j):
            nc.gpsimd.tensor_scalar(ue_sb[j][:], e_sb[j][:], us_sb[:, cols(j, 1)], 0.0, ALU.mult, ALU.add)

        sum_e("vector", 0, 0)
        sum_e("scalar", 1, 1)
        gather_f(0)
        sum_f_turned(0, 6)
        take_root(0, 2)
        take_root(1, 3)
        sum_e("vector", 2, 4)
        form_ue(0)
        form_ue(1)
        sum_e("scalar", 3, 7)
        gather_f(1)
        take_inverse(0)
        take_inverse(1)
        form_h(nc.gpsimd, 0)
        form_h(nc.gpsimd, 1)
        sum_f_turned(1, 2)
        take_root(2, 5)
        take_root(3, 4)
        fetch_t(0)
        fetch_t(1)
        gather_f(2)
        take_inverse(2)
        form_h(nc.gpsimd, 2)
        gather_f(3)
        ue_sb[LAST] = placed([P, C], F32, AT_K_RAW + 20, "ue_3")
        nc.scalar.activation(ue_sb[LAST][:], e_sb[LAST][:], ACT.Copy, scale=us_sb[:, cols(LAST, 1)])
        take_inverse(3)
        t_sb = placed([P, 2, X], F32, AT_TS + 11, "t_sb")
        form_m(0)
        form_m(1)
        sum_f(2)
        sum_f(3)
        form_m(2)
        form_h(nc.vector, 3)
        form_m(3)
        ue_sb[2] = placed([P, C], F32, AT_K_RAW + 16, "ue_2")
        nc.vector.tensor_scalar(ue_sb[2][:], e_sb[2][:], us_sb[:, cols(2, 1)], None, ALU.mult)

        neg_m_early = placed([P, LAST, HALF], F32, AT_K_RAW + 24, "neg_m_early")
        neg_m_first = [neg_m_early[:, j, :] for j in range(LAST)] + [placed([P, HALF], F32, AT_K_RAW + 1, "neg_m_last")[:]]
        neg_m_third = [placed([P, PART], F32, AT_K_RAW + j - 0.9375 if j else AT_TS + 8, "neg_m_third_%d" % j) for j in range(PACK)]
        g_grouped = [placed([P, PART, PACK], BF16, AT_K_PLANES + 2 * n if n < LAST else AT_UTS + 8, "g_grouped_%d" % n) for n in range(PARTS)]
        m_less_dp = [placed([P, PART], F32, (AT_INV + 6, AT_E + 2, AT_E + 4, AT_E + 5)[j], "m_less_dp_%d" % j) for j in range(PACK)]
        weighted = [placed([P, PACK, HALF], F32, (AT_TS, AT_E + 6)[half], "weighted_%d" % half) for half in range(2)]
        g_codes = [keep.tile([P, PART], U32, name="g_codes_%d" % n, align_bytes=64) for n in range(PARTS)]
        g_scales = [keep.tile([P, PART], U8, name="g_scales_%d" % n, align_bytes=64) for n in range(PARTS)]
        centred_turned, centred, centred_back, dk_banks = {}, {}, {}, {}

        def look_up_h(j, half):
            nc.vector.tensor_tensor(weighted[half][:, j, :], h_window[j][:].indirect(part_of(blk_list, half, HALF)), ue_sb[j][:, cols(half, HALF)], ALU.mult)

        def look_up_neg_m(dst, j, offsets):
            nc.scalar.activation(dst, m_window[j][:].indirect(offsets), ACT.Copy, scale=-1.0)

        def look_up_m_less_dp(j):
            nc.vector.tensor_tensor(m_less_dp[j][:], m_window[j][:].indirect(part_of(blk_list, LAST, PART)), dp_sb[j][:, cols(LAST, PART)], ALU.subtract)

        def turn_dp(chunk):
            centred_turned[chunk] = bank((3, 7, 6, 2, 5, 4)[chunk], "centred_turned_%d" % chunk)
            for j in range(PACK):
                turn(centred_turned[chunk][:, j, :], dp_sb[j][:, cols(chunk, P)], start=(j == 0), stop=False)

        def turn_neg_m(chunks, j):
            for chunk in chunks:
                neg_m = neg_m_first[j][:, cols(chunk, P)] if chunk < CHUNKS else neg_m_third[j][:, cols(chunk - CHUNKS, P)]
                turn(centred_turned[chunk][:, j, :], neg_m, start=False, stop=(j == LAST))

        def turn_m_less_dp(chunk):
            centred_turned[chunk] = bank(11 - chunk, "centred_turned_%d" % chunk)
            for j in range(PACK):
                turn(centred_turned[chunk][:, j, :], m_less_dp[j][:, cols(chunk - 6, P)])

        def scale_centred(chunk):
            centred[chunk] = placed([P, HALF], F32, AT_E + 2 * chunk if chunk < CHUNKS else AT_UTS + 2 * chunk - 2 * CHUNKS, "centred_%d" % chunk)
            nc.scalar.activation(centred[chunk][:], flat(centred_turned[chunk][:]), ACT.Copy, scale=neg_ts_col[:, cols(chunk - CHUNKS, 1)] if chunk >= 6 else ts_col[:, cols(chunk, 1)])

        def return_centred(chunk):
            centred_back[chunk] = turn_back(centred[chunk], (0, 1, 3, 7, 6, 2, 5, 4)[chunk], "centred_back_%d" % chunk).rearrange("p (j c) -> p j c", j=PACK)

        def gradient(chunk):
            half, b = divmod(chunk, CHUNKS)
            woven, planes = by_fours(g_grouped[chunk // 2][:, cols(chunk % 2, P), :], centred_back[chunk])
            nc.vector.tensor_tensor(woven, planes, weighted[half][:, :, cols(b, P)].rearrange("p t (c i) -> p c t i", i=4), ALU.mult)

        def quantize_gradient(n):
            nc.vector.quantize_mx(out=g_codes[n][:].bitcast(E5M2), scales=g_scales[n][:], in_=flat(g_grouped[n][:]))

        dk_early = [placed([P, 2, PART], F32, (AT_F + 12, AT_E + 4, AT_F + 8, AT_F + 10)[n], "dk_early_%d" % n) for n in range(PARTS)]
        dk_late = placed([P, 2, C], F32, AT_F, "dk_late")

        def multiply(n, pair):
            product = flat(bank(((0, 1, 3, 7), (0, 1, 2, 5))[pair][n], "dk_psum_%d_%d" % (n, pair))[:])
            for i in range(2):
                t = 2 * pair + i
                product_mx(product[:, cols(i, PART)], q2_codes[:, cols(t, P)], q2_scales[:, cols(t, P)], g_codes[n][:], g_scales[n][:], E5M2)
            dk_banks[(n, pair)] = product.rearrange("p (i c) -> p i c", i=2)

        def fetch_dk(engine, n, pair):
            engine_copy = nc.vector.tensor_copy if engine == "vector" else nc.scalar.copy
            engine_copy(dk_late[:, :, cols(n, PART)] if pair else dk_early[n][:], dk_banks[(n, pair)])

        out_rows = out.rearrange("(p t) n -> t p n", t=PACK)

        def place(engine, t, first, last):
            values = dk_late[:, t % 2, first:last] if t // 2 else dk_early[first // PART][:, t, :]
            move(engine, out_window[t][:].indirect(tok_list[:, first // 16 : last // 16]), values)

        def store(t, queue=nc.sync):
            queue.dma_start(out=out_rows[t], in_=out_window[t][:])

        def place_part(engine, t, n):
            place(engine, t, n * PART, (n + 1) * PART)

        def first_half(j):
            look_up_neg_m(neg_m_first[j], j, part_of(blk_list, 0, HALF))
            turn_neg_m(range(CHUNKS), j)

        def third_part(j):
            look_up_neg_m(neg_m_third[j][:], j, part_of(blk_list, 2, PART))

        for chunk in range(CHUNKS + 2):
            turn_dp(chunk)
        for j in range(PACK):
            first_half(j)
        look_up_m_less_dp(0)
        for j in range(PACK):
            look_up_h(j, 0)
        third_part(0)
        for chunk in range(CHUNKS):
            scale_centred(chunk)
            return_centred(chunk)
        turn_neg_m((4, 5), 0)
        for j in range(1, PACK):
            third_part(j)
            turn_neg_m((4, 5), j)
        gradient(0)
        gradient(1)
        quantize_gradient(0)
        look_up_m_less_dp(1)
        gradient(2)
        multiply(0, 0)
        look_up_m_less_dp(2)
        gradient(3)
        look_up_m_less_dp(3)
        quantize_gradient(1)
        fetch_dk("scalar", 0, 0)
        for chunk in (4, 5):
            scale_centred(chunk)
        turn_m_less_dp(6)
        turn_m_less_dp(7)
        place_part("scalar", 0, 0)
        place_part("scalar", 1, 0)
        for chunk in (6, 7):
            scale_centred(chunk)
        multiply(1, 0)
        for chunk in range(CHUNKS, 2 * CHUNKS):
            return_centred(chunk)
        for j in range(PACK):
            look_up_h(j, 1)
        fetch_dk("scalar", 1, 0)
        place_part("scalar", 0, 1)
        place_part("scalar", 1, 1)
        multiply(0, 1)
        multiply(1, 1)
        fetch_dk("scalar", 0, 1)
        fetch_dk("scalar", 1, 1)
        gradient(4)
        gradient(5)
        gradient(6)
        quantize_gradient(2)
        gradient(7)
        multiply(2, 0)
        multiply(2, 1)
        fetch_dk("vector", 2, 0)
        quantize_gradient(3)
        multiply(3, 0)
        multiply(3, 1)
        fetch_dk("scalar", 2, 1)
        place_part("scalar", 1, 2)
        fetch_dk("scalar", 3, 1)
        place_part("vector", 0, 2)
        fetch_dk("vector", 3, 0)
        place_part("vector", 0, 3)
        store(0)
        place_part("scalar", 1, 3)
        store(1, nc.scalar)
        place_part("scalar", 3, 3)
        place("vector", 2, 0, C)
        store(2)
        place("scalar", 3, 0, 384)
        place("scalar", 3, 384, 768)
        store(3)
